import numpy as np, ml_dtypes
CORES = [16,18,20,22]
N = 4
BF = ml_dtypes.bfloat16
V, U, H, S, Q, P, ST, RO, NEED = 3072, 768, 128, 192, 3, 256, 128, 5, 9
def noisy(rng, base, part):
    return base[:, :, None, :] * (1 + part * (2 * rng.random((N, 8, 16, V)) - 1))
def detours(rng, m, share):
    hub = rng.integers(0, V, (N, 8, m)); h = np.take_along_axis(hub, rng.integers(0, m, (N, 8, 16 * U)), 2).reshape(N, 8, 16, U)
    p = np.where(rng.random((N, 8, 16, U)) < share, h, rng.integers(0, V, (N, 8, 16, U)))
    return p, rng.integers(0, V, (N, 8, 16, U))
def pack(x, p, q):
    x = x.astype(np.float32); x[..., V - H:] = np.roll(x, -1, axis=0)[..., :H]
    e = np.arange(U); p = np.where(p == e, (p + 1) % V, p)
    for i in range(2): q = np.where((q == e) | (q == p), (q + 1) % V, q)
    return {"dist": np.ascontiguousarray(x.reshape(N, 128, V)), "b1": np.ascontiguousarray(p.reshape(N, 128, U)).astype(np.int32), "b2": np.ascontiguousarray(q.reshape(N, 128, U)).astype(np.int32)}
def plain(rng):
    hot = rng.permuted(np.tile(np.array([0.03, 0.05, 0.07, 0.09, 0.12, 0.16, 0.25, 0.4]), (N, 1)), axis=1)[..., None]
    u, w = rng.random((N, 8, V)), rng.random((N, 8, V)); base = 0.8 + 0.4 * rng.random((N, 8, V))
    base = np.where(u < hot, 2 + 2.5 * w * w, np.where(u > 0.97, 0.25 + 0.25 * w, base))
    p, q = detours(rng, 24, 0.5)
    return noisy(rng, base, 0.15), p, q
def quiet(rng, n):
    x = 1 + 0.03 * (2 * rng.random((N, 16, V)) - 1); mid = U + np.argsort(rng.random((N, V - H - U)), axis=1); h = (V - H - U - n) // 2
    p = np.take_along_axis(mid[:, n:n + h], rng.integers(0, h, (N, 16 * U)), 1).reshape(N, 16, U)
    q = np.take_along_axis(mid[:, n + h:n + 2 * h], rng.integers(0, h, (N, 16 * U)), 1).reshape(N, 16, U)
    return x, p, q, mid[:, :n]
def ties(rng, size):
    n = 32; x, p, q, o = quiet(rng, 2 * n); kind = np.arange(n) % 4
    for r in range(N):
        e = rng.permutation(U)[:n]; one, two = o[r, :n], o[r, n:]
        m = rng.integers(192, 256, (16, n)) * 2 ** 16 + rng.integers(2 ** 10, 2 ** 15 - 2 ** 10, (16, n)) + 2 ** 15 * (kind == 3)
        j = rng.integers(2 ** 21, 2 ** 22, (16, n)); up = np.argsort(rng.random((16, n)), axis=0) < np.array([0, 8, 9, 16])[kind]
        x[r][:, e] = (m + up) * 2.0 ** -23; x[r][:, one] = (m - j - 1) * 2.0 ** -23; x[r][:, two] = (4 * j + 3) * 2.0 ** -25
        p[r][:, e] = one; q[r][:, e] = two
    return x * size, p, q
def still(rng):
    x, p, q, o = quiet(rng, Q + 3); f = 1 + 0.05 * rng.random((16, 1)); turn = int(rng.integers(0, 2))
    for r in range(N):
        if r % 2 != turn: continue
        i = rng.permutation(H)[:2 * Q]; a, b = np.sort(i[:Q]), i[Q:]
        x[r][:, a] = 10 * f; x[r][:, b] = f; x[r][:, o[r, :Q]] = f; p[r][:, a] = b; q[r][:, a] = o[r, :Q]
        x[r][:, o[r, Q:Q + 2]] = 8.0; p[r][:, b] = o[r, Q]; q[r][:, b] = o[r, Q + 1]
        s = (r - 1) % N; m = rng.random(U) < 0.05; m[:P * (RO - 1 - Q)] = False; m[ST * (RO - 1) % U] = True; m[U - 1] = True; e = np.nonzero(m)[0]
        x[s][:, e] = 5 * f; x[s, :, o[s, Q + 2]] = f[:, 0]; p[s][:, e] = V - H + b[(RO - 2) % Q]; q[s][:, e] = o[s, Q + 2]
    return x, p, q
def below(rng):
    n = 20; w = 2 * Q; k = 5 + 2 * (w - 3); x, p, q, o = quiet(rng, n * k); odd = np.arange(16) % 2
    for r in range(N):
        f = 1 + 0.05 * rng.random(16); e = np.sort(rng.permutation(ST)[:n * w]).reshape(n, w); spare = rng.permutation(n); d = o[r].reshape(n, k)
        for i in range(n):
            a, b, far = e[i, 0], e[i, 1], e[i, Q + 1]; c, y1, y2, w1, v = d[i, :5]; late = U - 1 - i
            for edge, size in ((a, 8.0), (b, 1.0), (far, 100.0), (c, 1.0), (y1, 0.25), (y2, 0.25), (w1, 1.0), (v, 8.4), (late, 8.0)): x[r, :, edge] = size * f
            if spare[i] < 16: x[r, spare[i], far] = 1.5 * f[spare[i]]
            p[r, :, a] = b; q[r, :, a] = np.where(odd == 1, v, c); p[r, :, b] = y1; q[r, :, b] = y2
            p[r, :, far] = c; q[r, :, far] = w1; p[r, :, late] = b; q[r, :, late] = v
            for j, edge in enumerate(np.delete(e[i], [0, 1, Q + 1])):
                x[r, :, edge] = 4 * f; p[r, :, edge] = d[i, 5 + 2 * j]; q[r, :, edge] = d[i, 6 + 2 * j]
    return x, p, q
def setup_inputs(rng):
    x, p, q = plain(rng)
    return pack(x, p, q)
def setup_inputs_spread(rng):
    base = np.exp2(6 * rng.random((N, 8, V)) - 3) * (rng.random((N, 8, V)) > 0.03125)
    p, q = detours(rng, 48, 0.3); x = noisy(rng, base, 0.25); gs = rng.permutation(8)
    x[:, gs[0]] *= 64.0; x[:, gs[1]] *= 2.0 ** -24
    for g, size in ((gs[2], 512.0), (gs[3], 2.0 ** -22)):
        x[:, g], p[:, g], q[:, g] = ties(rng, size)
    return pack(x, p, q)
def setup_inputs_ends(rng):
    typ = (np.arange(N)[:, None] + np.arange(8)[None, :]) % 2
    base = np.where(rng.random((N, 8, V)) < 0.35, 8.0, 0.125); base[:, 7, :P] = 8.0; base[:, :, U - 1] = 8.0
    base[:, :, 0] = np.where(typ == 0, 8.0, 0.125); base[:, :, H - 1] = np.where(typ == 1, 8.0, 0.125)
    x = base[:, :, None, :] * (1 - 0.05 * rng.random((N, 8, 16, V)))
    p, q = detours(rng, 24, 0.1)
    m = np.argsort(rng.random((N, 8, 16, U)), axis=2) < 11; a = (V - 1) * rng.integers(0, 2, (N, 8, 16, U))
    return pack(x, np.where(m, a, p), np.where(m, V - 1 - a, q))
def setup_inputs_corners(rng):
    wall = V - H - 1; x = noisy(rng, 0.7 + 0.2 * rng.random((N, 8, V)), 0.05)
    hub = rng.integers(U, wall, (N, 8, 16)); h = np.take_along_axis(hub, rng.integers(0, 16, (N, 8, 16 * U)), 2).reshape(N, 8, 16, U)
    p = np.where(rng.random((N, 8, 16, U)) < 0.5, h, rng.integers(U, wall, (N, 8, 16, U))); q = rng.integers(U, wall, (N, 8, 16, U))
    p = np.where(np.arange(16)[:, None] < rng.integers(0, 16, (N, 8, 1, U)), wall, p)
    m = rng.random((N, 8, U)) < 0.1; m[..., :P] = False; rows = np.ones((N, 8, 16, U), bool); w = rng.random((N, 8, 1, U))
    long = (2.2 + 3 * w * w) * (1 + 0.05 * (2 * rng.random((N, 8, 16, U)) - 1)); pairs = np.arange(32)
    late = int(rng.integers(0, 8)); fr = min(RO - 2, (U - 1) // P); e = slice(P * fr, P * fr + 16 * Q)
    for r in range(N):
        order = rng.permutation(8); i = int(np.argmax(order == 5)); order[i] = order[late]; order[late] = 5
        for g in range(8):
            kind = order[g]
            if kind < 5: m[r, g, rng.permutation(P)[:(S - 1, S, S + 1, P, 1)[kind]]] = True
            elif kind == 5 and r % 2 == 0:
                flip = np.repeat(rng.integers(0, 2, 16), 2); m[r, g, :32] = True
                p[r, g, :, :32] = U + np.repeat(rng.permutation(wall - U)[:16], 2)
                long[r, g, :, :32] = np.where(pairs % 2 == flip, 6.0, 2.2) * (1 + 0.05 * (2 * rng.random((16, 32)) - 1))
            elif kind == 5:
                m[r, g] = False; m[r, g, e] = True; o = U + rng.permutation(wall - U)[:16 + 16 * Q]
                c = o[16:].copy(); c[(RO - 1) % Q::Q] = V - H + 32 + rng.permutation(H - 32)[:16]
                p[r, g, :, e] = np.repeat(o[:16], Q); q[r, g, :, e] = c
                long[r, g, :, e] = np.where(np.arange(16 * Q) % Q == fr % Q, 6.0, 2.2) * (1 + 0.05 * (2 * rng.random((16, 16 * Q)) - 1))
            else:
                m[r, g, :P] = True; c = rng.choice(np.array([8, 9] if kind == 6 else [0, 9, 15, 16]), P)
                rows[r, g, :, :P] = np.argsort(rng.random((16, P)), axis=0) < c
    x[..., :U] = np.where(m[:, :, None, :] & rows, long, x[..., :U]); x[..., wall] = 8.0
    return pack(x, p, q)
def setup_inputs_calm(rng):
    x, p, q = plain(rng); og = rng.permutation(8); gs = og[:4]
    x[:, gs] = noisy(rng, 0.9 + 0.2 * rng.random((N, 8, V)), 0.05)[:, gs]
    for r in range(N):
        for i in range(4):
            c = np.concatenate([rng.permutation(ST)[:(i + r) % 4], U - 1 - rng.permutation(64)[:1]])
            x[r, gs[i], :, c] = 2.6 * (1 + 0.03 * (2 * rng.random((len(c), 16)) - 1))
    x[:, og[4]], p[:, og[4]], q[:, og[4]] = still(rng)
    x[:, og[5]], p[:, og[5]], q[:, og[5]] = below(rng)
    return pack(x, p, q)
def setup_inputs_crowd(rng):
    x = 0.25 * (rng.integers(4, 17, (N, 8, 1, V)) + rng.integers(0, 2, (N, 8, 16, V)))
    p, q = detours(rng, 24, 0.2)
    for r in range(N):
        for g in range(8):
            kind = (g + r) % 4; hs = U + rng.permutation(V - H - U)[:8]
            x[r, g, :, hs] = 0.25 * (1 + rng.integers(0, 2, (8, 16)))
            if kind < 2:
                e = rng.integers(0, P); a, b = p[r, g, :, e].copy(), q[r, g, :, e].copy()
                p[r, g] = hs[0]; q[r, g] = hs[1]
                if kind == 1: p[r, g, :, e] = a; q[r, g, :, e] = b
            elif kind == 2: p[r, g] = hs[0]
            else: p[r, g] = hs[rng.integers(0, 8, (16, U))]; q[r, g] = hs[rng.integers(0, 8, (16, U))]
    return pack(x, p, q)
def check_inputs(d):
    bad = []; x, p, q = np.asarray(d["dist"]), np.asarray(d["b1"]), np.asarray(d["b2"]); e = np.arange(U)
    if not np.all((x >= 0) & (x <= 1024)): bad.append("range of dist")
    if np.min(p) < 0 or np.max(p) > V - 1: bad.append("range of b1")
    if np.min(q) < 0 or np.max(q) > V - 1: bad.append("range of b2")
    if np.any((p == e) | (q == e) | (p == q)): bad.append("the three edges of a triple in b1 and b2 differ")
    if not np.array_equal(np.roll(x, -1, axis=0)[..., :H], x[..., V - H:]): bad.append("shared columns of dist")
    return bad
def reference(dist, b1, b2):
    D = dist.astype(np.float32).reshape(N, 8, 16, V); B1 = b1.astype(np.int64).reshape(N, 8, 16, U); B2 = b2.astype(np.int64).reshape(N, 8, 16, U)
    flag = np.ones((N, 8, U), bool); fill = np.zeros((N, 8, S), bool); tri = np.full((N, 8, 3, S), -1, np.int64); z = np.zeros((N, 8, 16, S), np.float32)
    for t in range(RO):
        corr = np.zeros((N, 8, 16, V), np.float32); touch = np.zeros((N, 8, V), bool); order = (ST * t + np.arange(U)) % U
        for r in range(N):
            for g in range(8):
                x = D[r, g]
                look = order[flag[r, g, order]][:P]; flag[r, g, look] = False
                c1, c2 = B1[r, g][:, look], B2[r, g][:, look]
                n = np.sum(x[:, look][:, None, :] > x[:, c1] + x[:, c2], axis=0)
                k = np.argmax(n, axis=0)
                who = np.nonzero(np.max(n, axis=0) >= NEED)[0]; free = np.nonzero(~fill[r, g])[0]
                m = min(len(who), len(free)); who, s = who[:m], free[:m]
                tri[r, g][0, s] = look[who]; tri[r, g][1, s] = c1[k[who], who]; tri[r, g][2, s] = c2[k[who], who]
                fill[r, g, s] = True; z[r, g][:, s] = 0
                vis = np.arange(t % Q, S, Q); vis = vis[fill[r, g, vis]]; w = tri[r, g][:, vis]
                least = np.full(V, S, np.int64); np.minimum.at(least, w, np.broadcast_to(vis, w.shape))
                st = vis[np.all(least[w] == vis, axis=0)]
                a, b, c = tri[r, g][:, st]; old = z[r, g][:, st]
                theta = ((x[:, a] - x[:, b]) - x[:, c]) * np.float32(0.5)
                delta = np.maximum(theta, -old); new = old + delta
                z[r, g][:, st] = new
                corr[r, g][:, a] = -delta; corr[r, g][:, b] = delta; corr[r, g][:, c] = delta
                touch[r, g, a] = True; touch[r, g, b] = True; touch[r, g, c] = True
                gone = st[np.all(new == 0, axis=0)]; fill[r, g, gone] = False; tri[r, g][:, gone] = -1
        nxt = D + corr
        for r in range(N):
            for q, mine, other in (((r - 1) % N, slice(0, H), slice(V - H, V)), ((r + 1) % N, slice(V - H, V), slice(0, H))):
                own, his = corr[r][..., mine], corr[q][..., other]
                one, two = (own, his) if r < q else (his, own)
                nxt[r][..., mine] = (D[r][..., mine] + one) + two
        D = nxt
        flag = flag | touch[..., :U]
        flag[:, :, :H] = flag[:, :, :H] | np.roll(touch, 1, axis=0)[..., V - H:]
    return {"yd": D.reshape(N, 128, V), "yz": z.reshape(N, 128, S), "yt": tri.reshape(N, 8, 3 * S).astype(np.float32), "yf": flag.astype(np.float32)}

@@ -1,0 +1,676 @@
+from concourse.bass import DstId, RemoteDMATransfer
+from concourse.mybir import AluOpType as A, ActivationFunctionType as AF, AxisListType
+
+AXX = AxisListType.X
+
+V, U, H, S, P, RO = 3072, 768, 128, 192, 256, 5
+J, WALL, DW = 3072, 3136, 3144
+EXT, DUM = 1288, 1280
+MAG = 12582912.0
+MARK = 3583
+PARTS = "at wt pca pcb wc cmp_0 cmp_1 cmp_2 ab2 ab3 d4 zo pct fo thr".split()
+F32, BF, F16, I32, U16 = "float32", "bfloat16", "float16", "int32", "uint16"
+
+
+def sb(n, d):
+    return ("sbuf", [128] + (n if isinstance(n, list) else [n]), d)
+
+
+SCRATCH = {
+    "D": sb(DW, F32), "b1t": sb(EXT, I32), "b2t": sb(EXT, I32), "bp": sb(EXT, F32), "at": sb(EXT, F32), "pos": sb(EXT, F32),
+    "g2": sb(4096, F32), "sm": sb(4096, F32), "cmp": sb([256, 16], BF),
+    "o1": sb(256, U16), "o2": sb(256, U16), "lw": sb(16, U16), "le": sb(16, U16), "lt": sb(16, F32), "lt2": sb(16, F32),
+    "dl": sb(256, F32), "bl": sb(256, F32), "al": sb(256, F32), "yy": sb(256, F32), "sc": sb(256, F32),
+    "prop": sb(16, BF), "scb": sb(16, BF), "pu": sb(16, BF), "pcs": sb(24, BF), "ofl": sb(16, U16),
+    "w0": sb(1216, F32), "w1": sb(1216, F32), "ofs": sb(12, U16), "ofs32": sb(12, F32),
+    "h32": sb(192, F32), "h16": sb(192, F16), "q16": sb(192, F16), "l16": sb(192, F16),
+    "ra": sb(192, F32), "ew": sb(12, F32), "eq": sb(1440, BF), "ts": sb(192, F32), "off": sb(12, U16),
+    "d4": sb(256, F32), "d3": sb(192, F32), "th": sb(256, F32), "dlt": sb(64, F32), "nz": sb(192, F32),
+    "tw": sb(DW, BF), "one": sb(64, BF), "gr": sb(192, BF), "fil": sb(4, F32), "blk": sb(4, BF),
+    "fre": sb(12, BF), "fcs": sb(12, BF),
+    "fown": sb(8, BF), "fls": sb(48, BF), "fl": sb(48, BF), "fu": sb(48, BF), "lcs": sb(56, BF), "ofe": sb(48, U16), "lwin": sb(4608, F32), "lx": sb(256, F32),
+    "rd": sb([RO, 256], F32), "rt": sb([RO, 128], BF),
+    "zo": sb(192, F32), "t1": sb(576, F32), "t2": sb(192, F32), "fo": sb(768, F32),
+    "ip": sb(8, I32), "col": sb(16, F32), "cm": sb(256, F32), "i128": sb(144, F32), "gi": sb(128, F32), "tmp": sb(16, F32), "tmp2": sb(128, F32),
+    "dg": sb(256, F32), "mx": sb(256, F32), "rs": sb(256, F32), "mul4": sb(256, F32), "r4": sb(12, F32),
+    "eye": sb(128, BF), "neye": sb(128, BF), "bo": sb(128, BF), "tri": sb(128, BF), "zz": sb(144, BF), "wt": sb([16, 128], BF),
+    "dfill": sb(128, BF), "dflag": sb(128, BF), "e1k": sb(128, BF), "e512": sb(128, BF), "mgt": sb(128, BF), "ab": sb(432, F32),
+    "hq": sb(128, F16), "hh": sb(128, F16), "hl": sb(128, F16), "hn": sb(128, F16),
+    "ckw": sb(256, BF), "cka": sb(256, BF), "c32": sb(16, BF), "c64": sb(48, BF), "cf1": sb(16, BF), "ce1": sb(48, BF),
+    "mka": sb(192, BF), "pca": sb(192, BF), "pcb": sb(192, BF), "pct": sb(576, BF), "wr": sb(64, F32), "thr": sb(192, BF),
+    "r48": sb(192, F32), "h1": sb(128, F16), "hm": sb(128, F16), "hf": sb(128, F16), "hfa": sb(128, F16), "kb": sb(2, F32), "f16": sb(192, F16),
+    "wc": sb(8, F32), "jk": sb(4, F32), "own": sb(12, F32), "cpd": sb(192, F32), "zb": sb(384, BF),
+    "p0": ("psum", [128, 512], F32), "p1": ("psum", [128, 512], F32), "p2": ("psum", [128, 512], F32), "p3": ("psum", [128, 512], F32),
+    "p4": ("psum", [128, 512], F32), "p5": ("psum", [128, 512], F32), "p6": ("psum", [128, 512], F32), "p7": ("psum", [128, 512], F32),
+}
+SEMAPHORES = (["sv", "ss", "st", "sg"] + ["dm%d" % i for i in range(24)]
+              + [k + str(t) for k in ("ld", "lt", "rd", "rt") for t in range(RO)])
+
+
+def bank(k):
+    return k[0] == "p" and k[1:].isdigit()
+
+
+is_bank = bank
+
+
+def emit(g, T, ops):
+    Q = {"v": g.vector, "s": g.scalar, "t": g.tensor, "g": g, "y": g.sync}
+    lastw, readers, need, seen = {}, {}, [], {}
+    for i, o in enumerate(ops):
+        deps = set()
+        for k in o["r"]:
+            if k in lastw:
+                deps.add((lastw[k], not bank(k)))
+        for k in o["w"]:
+            if k in lastw:
+                deps.add((lastw[k], not (bank(k) or (k in PARTS and not readers[k]))))
+            for j in readers.get(k, []):
+                deps.add((j, not bank(k)))
+        best = {}
+        for j, hard in deps:
+            p = ops[j]
+            if j == i:
+                continue
+            if p["sem"] is None:
+                if p["q"] == o["q"] and o["sem"] is None and (o["q"] == "t" or not hard):
+                    continue
+                key = p["q"]
+            else:
+                key = ("own", j)
+            best[key] = max(best.get(key, -1), j)
+        mine = []
+        for key, j in best.items():
+            if seen.get((o["q"], key), -1) < j:
+                seen[(o["q"], key)] = j
+                mine.append(j)
+        need.append(sorted(mine))
+        for k in o["r"]:
+            readers.setdefault(k, []).append(i)
+        for k in o["w"]:
+            lastw[k] = i
+            readers[k] = []
+    wanted = set(j for m in need for j in m)
+    count, token, total = {}, {}, {}
+    for i, o in enumerate(ops):
+        if o["sem"] is not None:
+            token[i] = o["sem"]
+            total[o["sem"][0]] = o["sem"][1]
+        elif i in wanted:
+            count[o["q"]] = count.get(o["q"], 0) + 1
+            token[i] = ("s" + o["q"], count[o["q"]])
+            total["s" + o["q"]] = count[o["q"]]
+    for i, o in enumerate(ops):
+        if o["f"] is None:
+            continue
+        for j in need[i]:
+            Q[o["q"]].wait_ge(T.sem[token[j][0]], token[j][1])
+        ins = o["f"]()
+        if o["dma"]:
+            ins.then_inc(T.sem[o["sem"][0]], 16)
+        elif o["sem"] is None and i in token:
+            ins.then_inc(T.sem[token[i][0]], 1)
+    for name, n in total.items():
+        g.wait_ge(T.sem[name], n)
+
+
+def rank_program(g, core, T, topo):
+    rank = T.rank_of(core)
+    if rank is None:
+        return
+    n_ranks = len(T.cores)
+    before, after = T.cores[(rank - 1) % n_ranks], T.cores[(rank + 1) % n_ranks]
+    ops, nd = [], [0]
+    v, s, pe = g.vector, g.scalar, g.tensor
+
+    def op(q, f, r, w, sem=None, dma=False):
+        r, w = r.split(), w.split()
+        for k in list(r):
+            if is_bank(k):
+                w.append(k)
+        ops.append({"q": q, "f": f, "r": r, "w": w, "sem": sem, "dma": dma})
+
+    def dma(q, out, in_, r, w):
+        e = g.sync if q == "y" else g.scalar
+        op(q, lambda: e.dma_start(out, in_), r, w, ("dm%d" % nd[0], 16), True)
+        nd[0] += 1
+
+    def ts(out, in0, s1, o0, r, w, s2=None, o1=None):
+        if o1 is None:
+            op("v", lambda: v.tensor_scalar(out, in0, s1, None, o0), r, w)
+        else:
+            op("v", lambda: v.tensor_scalar(out, in0, s1, s2, o0, o1), r, w)
+
+    def tt(out, a, b, o, r, w):
+        op("v", lambda: v.tensor_tensor(out, a, b, o), r, w)
+
+    def cp(out, a, r, w):
+        op("v", lambda: v.tensor_copy(out, a), r, w)
+
+    def scan(out, d0, d1, o0, o1, r, w, first=0.0):
+        op("v", lambda: v.tensor_tensor_scan(out, d0, d1, first, o0, o1), r, w)
+
+    def ms(out, c, w):
+        op("v", lambda: v.memset(out, c), "", w)
+
+    def act(out, a, r, w, func=None, scale=None, bias=None):
+        fn = AF.Copy if func is None else func
+        if scale is None:
+            op("s", lambda: s.activation(out, a, fn), r, w)
+        elif bias is not None:
+            op("s", lambda: s.activation(out, a, fn, bias=bias, scale=scale), r, w)
+        else:
+            op("s", lambda: s.activation(out, a, fn, scale=scale), r, w)
+
+    def mm(out, l, rh, r, w, start=False, stop=False):
+        op("t", lambda: pe.matmul(out, l, rh, start, stop), r, w)
+
+    def iota(out, pat, base, cmul, w, r=""):
+        op("g", lambda: g.iota(out, pat, base, cmul, allow_small_or_imprecise_dtypes=True), r, w)
+
+    def sel(r):
+        return T.zz[:, 15 - r:143 - r]
+
+    Dw = T.D[:, 0:DW]
+    DK = "Da Dm Dz Dj"
+    col = lambda i: T.col[:, i:i + 1]
+
+    def slot_list():
+        scan(T.fcs[:], T.r4[:], T.fre[:], A.mult, A.add, "r4 fre", "fcs")
+        for u in range(3):
+            for w in range(3):
+                mm(T.p5[:, 16 + 4 * u:20 + 4 * u], T.mgt[:], T.fre[:, 4 * w:4 * w + 4], "mgt fre", "p5", start=(w == 0))
+                if w <= u:
+                    m = "e512" if w == u else "eye"
+                    mm(T.p5[:, 16 + 4 * u:20 + 4 * u], T[m][:], T.fre[:, 4 * w:4 * w + 4], m + " fre", "p5")
+                mm(T.p5[:, 16 + 4 * u:20 + 4 * u], T.bo[:], T.fcs[:, 4 * w:4 * w + 4], "bo fcs", "p5", stop=(w == 2))
+
+    dma("y", T.b2t[:, 0:P], T.b2[:, 0:P], "", "b2a")
+    dma("y", T.b1t[:, 0:P], T.b1[:, 0:P], "", "b1a")
+    dma("y", T.D[:, 0:V // 2], T.dist[:, 0:V // 2], "", "Da Dm")
+    dma("y", T.D[:, V // 2:V], T.dist[:, V // 2:V], "", "Dz Dm2")
+    dma("y", T.b1t[:, P:U], T.b1[:, P:U], "", "b1b")
+    dma("y", T.b2t[:, P:U], T.b2[:, P:U], "", "b2b")
+    dma("y", T.b1t[:, U:DUM], T.b1[:, 0:DUM - U], "", "b1c")
+    dma("y", T.b2t[:, U:DUM], T.b2[:, 0:DUM - U], "", "b2c")
+
+    op("g", lambda: g.iota(T.ip[:, 0:1], [[0, 1]], 0, 1), "", "ip0")
+    iota(T.cm[:], [[0, 16], [1, 16]], 0, 0, "cm")
+    iota(T.i128[:], [[1, 144]], 0, 0, "i128")
+    iota(T.gi[:], [[16, 8], [0, 16]], 0, 0, "gi")
+    iota(T.c32[:], [[32, 16]], 0, 0, "c32")
+    iota(T.c64[:], [[64, 48]], 0, 0, "c64")
+    iota(T.pos[:], [[1, EXT]], 0, 0, "pos")
+    ts(T.ip[:, 1:2], T.ip[:, 0:1], 15, A.bitwise_and, "ip0", "ip1")
+    cp(col(0), T.ip[:, 0:1], "ip0", "c0")
+    cp(col(1), T.ip[:, 1:2], "ip1", "c1")
+    iota(T.nz[:], [[0, S]], 0, 0, "nz0 nz1 nz2")
+    iota(T.d4[:, 3::4], [[0, 64]], 0, 0, "d4")
+    iota(T.w0[:, 0:S], [[0, S]], 0, 0, "tr0")
+    ms(T.D[:, J:WALL], 0.0, "Dj0")
+    ms(T.one[:], 1.0, "one")
+    tt(col(2), col(0), col(1), A.subtract, "c0 c1", "c2")
+    ts(col(4), col(1), 0.0, A.is_equal, "c1", "c4")
+    ts(col(5), col(1), 1.0, A.is_equal, "c1", "c5", -15.0, A.mult)
+    ts(col(6), col(1), 2.0, A.mult, "c1", "c6", 256.0, A.add)
+    ts(col(7), col(1), 4.0, A.mult, "c1", "c7", 768.0, A.add)
+    ts(col(8), col(1), -4096.0, A.mult, "c1", "c8", -129.0 * 4096, A.add)
+    ts(col(13), col(1), -2.0, A.mult, "c1", "c13", -256.0, A.add)
+    ts(col(14), col(1), -4.0, A.mult, "c1", "c14", -768.0, A.add)
+    ts(T.tmp[:], T.cm[:, 0:16], col(1), A.is_equal, "cm c1", "tmp", -4096.0, A.mult)
+    ts(col(3), col(2), 15.0, A.add, "c2", "c3")
+    ts(col(9), col(4), float(MARK + 1), A.mult, "c4", "c9", (MARK - 1536) / 4096.0, A.add)
+    act(T.ckw[:], T.cm[:], "cm", "ckw", AF.Identity, -4096.0, 15.0 * 4096)
+    act(T.cka[:], T.cm[:], "cm c8", "cka", AF.Identity, 0.0, col(8))
+    ts(T.eye[:], T.i128[:, 0:128], col(0), A.is_equal, "i128 c0", "eye")
+    ts(T.bo[:], T.gi[:], col(2), A.is_equal, "gi c2", "bo")
+    ts(T.dg[:], T.cm[:], col(1), A.is_equal, "cm c1", "dg")
+    act(T.cpd[:], T.cm[:, 0:S], "cm c9", "cpd", AF.Identity, 0.0, col(9))
+    act(T.e512[:], T.eye[:], "eye", "e512", AF.Identity, 512.0)
+    for r in range(16):
+        act(T.wt[:, r, :], T.bo[:], "bo tmp", "wt", AF.Identity, T.tmp[:, r:r + 1])
+    act(T.neye[:], T.eye[:], "eye", "neye", AF.Identity, -1.0)
+    act(T.e1k[:], T.eye[:], "eye", "e1k", AF.Identity, 1024.0)
+    act(T.dfill[:], T.eye[:], "eye c13", "dfill", AF.Identity, col(13))
+    act(T.dflag[:], T.eye[:], "eye c14", "dflag", AF.Identity, col(14))
+    act(T.mx[:], T.dg[:], "dg", "mx", AF.Identity, 20000.0, -10000.0)
+    act(T.mka[:], T.dg[:, 0:S], "dg", "mka", AF.Identity, 1048576.0, -1048576.0)
+    ts(T.tmp2[:], T.cm[:, 0:128], col(1), A.is_gt, "cm c1", "tmp2")
+    ts(T.zz[:], T.i128[:], col(3), A.is_equal, "i128 c3", "zz", 65536.0, A.mult)
+    ms(T.r4[:], 1.0, "r4")
+    ms(T.fre[:], 1.0, "fre")
+    tt(T.tri[:], T.tmp2[:], T.bo[:], A.mult, "tmp2 bo", "tri")
+    op("v", lambda: v.memset(T.r4[:, 0::4], 0.0), "r4", "r4")
+    ts(T.rs[:], T.cm[:], 0.0, A.not_equal, "cm", "rs")
+    tt(T.mgt[:], T.tri[:], T.bo[:], A.subtract, "tri bo", "mgt")
+    slot_list()
+    op("v", lambda: v.memset(T.D[:, WALL:DW], 1e29), "Dj0", "Dj")
+    ms(T.b1t[:, DUM:EXT], WALL, "b1d")
+    ms(T.b2t[:, DUM:EXT], WALL, "b2d")
+    ms(T.bp[:, DUM:EXT], 1.0, "bpd")
+    ms(T.pcs[:, 0:1], 0.0, "pcs0")
+    ms(T.lcs[:, 0:1], 0.0, "lcs0")
+    ms(T.fls[:, 0:16], 0.0, "flsb")
+    ms(T.fls[:, 16:48], 1.0, "fls")
+    for q, c in enumerate((0.0, -1.0, 1.0, 0.5)):
+        ms(T.mul4[:, q::4], c, "mul4_%d" % q)
+    ts(T.cf1[:], T.cm[:, 0:16], 0.0, A.mult, "cm c6", "cf1", col(6), A.add)
+    ts(T.ce1[:], T.cm[:, 0:48], 0.0, A.mult, "cm c7", "ce1", col(7), A.add)
+    cp(T.o2[:], T.b2t[:, 0:P], "b2a", "o2")
+    cp(T.o1[:], T.b1t[:, 0:P], "b1a", "o1")
+    for name, c in (("hq", 4096.0), ("hh", 15.0), ("hl", 61440.0), ("hn", -61440.0)):
+        ts(T[name][:], T.bo[:], c, A.mult, "bo", name)
+    for q, c in enumerate((20992.0, 245760.0, 53760.0)):
+        ts(col(10 + q), col(4), c, A.mult, "c4 c5", "k%d" % q, col(5) if q == 1 else 0.0, A.add)
+    for q in range(3):
+        ts(T.pca[:, 64 * q:64 * q + 64], T.cm[:, 0:64], 0.0, A.mult, "cm k%d" % q, "pca", col(10 + q), A.add)
+        ts(T.pcb[:, q::3], T.cm[:, 0:64], 0.0, A.mult, "cm k%d" % q, "pcb", col(10 + q), A.add)
+    ms(T.th[:, 0:64], 1.0 / 3.0, "th")
+    op("v", lambda: v.tensor_tensor_scan(T.ts[:, 0:64], T.th[:, 0:64], T.nz[:, 0:64], 1e29, A.mult, A.add), "th nz0", "ts")
+    ms(T.r48[:], 1.0, "r48")
+    ts(T.wr[:], T.ts[:, 0:64], 3.0 ** 64 * 2.0 ** 14 / 1e29, A.mult, "ts", "wr")
+    op("v", lambda: v.memset(T.r48[:, 0::48], 0.0), "r48", "r48")
+    tt(T.ts[:, 0:64], T.wr[:], T.dg[:, 0:64], A.mult, "wr dg", "ts")
+    ts(T.th[:, 0:64], T.dg[:, 0:64], -1.0, A.add, "dg wr", "th", 1e29, A.mult)
+    for c in range(4):
+        op("v", lambda c=c: v.tensor_reduce(T.wc[:, c:c + 1], T.ts[:, 16 * c:16 * c + 16], AXX, A.add), "ts", "wc")
+    ts(T.th[:, 64:128], T.th[:, 0:64], 1e7, A.mult, "th", "th2")
+    ts(T.th[:, 128:192], T.ts[:, 0:64], -2.25, A.mult, "ts", "th3")
+    ts(T.jk[:], T.cm[:, 0:4], 16.0, A.mult, "cm c1", "jk0", col(1), A.add)
+    ts(T.own[:], T.cm[:, 0:12], 16.0, A.mult, "cm c1", "own0", col(1), A.add)
+    for q in range(3):
+        tt(T.thr[:, q::3], T.th[:, 64:128], T.th[:, 128:192], A.add, "th2 th3", "thr")
+    for name, c in (("h1", 1.0), ("hm", -4096.0), ("hf", -224.0), ("hfa", -3360.0)):
+        ts(T[name][:], T.bo[:], c, A.mult, "bo", name)
+    ts(col(15), col(5), 1.0 / 15, A.mult, "c5", "c15")
+    ts(T.kb[:, 0:1], col(4), 16384.0, A.mult, "c4 c15", "kb", col(15), A.add)
+    ts(T.kb[:, 1:2], col(4), 3584.0, A.mult, "c4", "kc")
+    ts(T.jk[:], T.jk[:], float(J), A.add, "jk0", "jk")
+    ts(T.own[:], T.own[:], 320.0, A.add, "own0", "own")
+    ts(T.wc[:, 4:8], T.wc[:, 0:4], -1.0, A.mult, "wc", "nwc")
+    act(T.at[:, 0:U], T.pos[:, 0:U], "pos", "at", AF.Identity, 1.0 / 4096, -1536.0 / 4096)
+    act(T.at[:, U:EXT], T.pos[:, U:EXT], "pos", "at", AF.Identity, 1.0 / 4096, (-1536.0 - U) / 4096)
+
+    def pack(a, b, r, w):
+        ts(T.bp[:, a:b], T.b2t[:, a:b], 2560.0, A.add, r, w + "x", 1.0 / 4096, A.mult)
+        tt(T.bp[:, a:b], T.bp[:, a:b], T.b1t[:, a:b], A.add, r + " " + w + "x", w)
+
+    pack(0, P, "b1a b2a", "bpa")
+
+    def slot_list_end():
+        tt(T.ofs32[:], T.p5[:, 16:28], T.own[:], A.max, "p5 own", "ofs32")
+        ts(T.ofs[:], T.ofs32[:], -320.0, A.add, "ofs32", "ofs")
+
+    def planes(src, n, r):
+        ts(T.h32[:, 0:n], src(), MAG, A.add, r, "h32", MAG, A.subtract)
+        ts(T.h16[:, 0:n], src(), MAG, A.add, r, "h16", MAG + 1024.0, A.subtract)
+        ts(T.q16[:, 0:n], src(), 0.5, A.min, r, "q16")
+        tt(T.l16[:, 0:n], src(), T.h32[:, 0:n], A.subtract, r + " h32", "l16")
+
+    def rows(outs, a, b, bank, stop):
+        mm(outs[1], T.hh[:], T.h16[:, a:b], "hh h16", bank[1])
+        mm(outs[0], T.hq[:], T.q16[:, a:b], "hq q16", bank[0], stop=stop and bank[0] != bank[2])
+        mm(outs[2], T.hn[:], T.q16[:, a:b], "hn q16", bank[2])
+        mm(outs[2], T.hl[:], T.l16[:, a:b], "hl l16", bank[2], stop=stop)
+
+    eng_b, eng_a = topo.engines(core, before), topo.engines(core, after)
+    half_b = eng_b[:len(eng_b) // 2]
+    half_a = [e for e in eng_a if e not in half_b][:len(half_b)]
+    bits = lambda es: sum(1 << e for e in es)
+    dst = lambda c: DstId(rid=topo.addr(c)[0], pnc=topo.addr(c)[1])
+    n_in_t = len(topo.engines(before, core))
+    n_in_d = len(topo.engines(before, core)) // 2 + len(topo.engines(after, core)) // 2
+
+    for t in range(RO):
+        u = t % 3
+        wa, wb = (T.w0, T.w1) if t % 2 == 0 else (T.w1, T.w0)
+        tra, trb = ("tr0", "tr1") if t % 2 == 0 else ("tr1", "tr0")
+        cpa = "cp%d" % (t % 2)
+        last = t == RO - 1
+        op("g", lambda wa=wa: g.affine_select(wa[:, S:2 * S], T.cpd[:], [[0, S]], A.is_ge, 0.0, 0, 0), "cpd", cpa)
+        iota(T.tw[:, V - H:V], [[0, H]], 0, 0, "twz")
+        iota(T.tw[:, 0:U], [[0, U]], 0, 0, "twa")
+        if not last:
+            iota(T.lwin[:, 0:P], [[0, P]], DUM, 0, "lwin")
+        else:
+            iota(T.zb[:], [[0, 384]], 0, 0, "zb")
+            op("g", lambda wb=wb: g.affine_select(wb[:, S:2 * S], T.cpd[:], [[0, S]], A.is_ge, 0.0, 0, 0), "cpd", "cp%d" % (1 - t % 2))
+        dk = DK + (" Dm2" if t == 0 else "")
+        cuts = (0, 16, 64, 128, 192, 256)
+
+        def gath(i):
+            a, b = cuts[i], cuts[i + 1]
+            act(T.g2[:, 16 * a:16 * b], Dw.indirect(T.o2[:, a:b]), dk + " o2", "g2_%d" % i)
+
+        def add(i):
+            a, b = cuts[i], cuts[i + 1]
+            tt(T.sm[:, 16 * a:16 * b], Dw.indirect(T.o1[:, a:b]), T.g2[:, 16 * a:16 * b], A.add, dk + " o1 g2_%d" % i, "sm_%d" % i)
+
+        def rep(h):
+            bank = T.p6 if h == 0 else T.p7
+            src = T.D if t == 0 else T.dl
+            for q in range(4):
+                act(bank[:, q::4], src[:, 128 * h:128 * h + 128], dk if t == 0 else "dl", "p%d" % (6 + h))
+
+        def compare(j):
+            a, b = 64 * j, 64 * j + 64
+            bank = T.p6 if j < 2 else T.p7
+            keys = ("sm_0 sm_1", "sm_2", "sm_3", "sm_4")[j]
+            for q in range(4):
+                tt(T.cmp[:, a:b, q::4], bank[:, 256 * (j % 2):256 * (j % 2) + 256], T.sm[:, 16 * a + q:16 * b:4], A.is_gt,
+                   "p%d %s" % (6 + j // 2, keys), "cmp_%d" % j)
+            for r in range(16):
+                mm(T.p0[:, a:b], sel(r), T.cmp[:, a + r:b:16, :], "zz cmp_%d" % j, "p0", stop=(j == 2 and r == 15))
+            for k in range(16):
+                mm(T.p1[:, a:b], sel(k), T.cmp[:, a:b, k], "zz cmp_%d" % j, "p1")
+
+        mm(T.p0[:, 0:192], T.eye[:], T.ckw[:, 0:192], "eye ckw", "p0", start=True)
+        mm(T.p1[:, 0:192], T.eye[:], T.cka[:, 0:192], "eye cka", "p1", start=True)
+        mm(T.p4[:, 0:64], T.eye[:], T.cka[:, 0:64], "eye cka", "p4", start=True)
+        gath(0)
+        gath(1)
+        add(0)
+        slot_list_end()
+        if t > 0:
+            lst = T.lw
+            if t >= 3:
+                ts(T.lt[:], T.lx[:, 15::16], U - 0.5, A.is_ge, "lx", "lt", -float(U), A.mult)
+                tt(T.lt2[:], T.lt[:], T.lx[:, 15::16], A.add, "lt lx", "lt2")
+                ts(T.le[:], T.lt2[:], 0.25, A.add, "lt2", "le")
+                lst = T.le
+            cp(T.dl[:], Dw.indirect(lst[:]), dk + " lw le", "dl")
+        rep(0)
+        gath(2)
+        add(1)
+        compare(0)
+        rep(1)
+        gath(3)
+        add(2)
+        compare(1)
+        gath(4)
+        add(3)
+        compare(2)
+        if t > 0:
+            act(T.bl[:], T.bp[:, 0:(512, U, EXT, EXT)[t - 1]].indirect(T.lw[:]), "bpa bpb bpc bpe bpd lw", "bl")
+            act(T.al[:], T.at[:, 0:EXT].indirect(T.lw[:]), "at lw", "al")
+            bl, al, blk, alk = T.bl, T.al, "bl", "al"
+            if last:
+                for q, (c, k) in enumerate(((col(10), "k0"), (T.kb[:, 0:1], "kb"), (T.kb[:, 1:2], "kc"))):
+                    act(T.pct[:, S * q:S * q + S], T.cm[:, 0:S], "cm " + k, "pct", AF.Identity, 0.0, c)
+            if t == 2:
+                act(T.bp[:, U:DUM], T.bp[:, 0:DUM - U], "bpa bpb", "bpe")
+        else:
+            bl, al, blk, alk = T.bp, T.at, "bpa", "at"
+        add(4)
+        span = ((0, 12), (12, 16))
+        rank_ps, rank_k = (T.p2[:, 0:12], T.p5[:, 32:36]), ("p2", "p5")
+        win_ps, win_k = (T.p1, T.p4), ("p1", "p4")
+
+        def best(h):
+            a, b = span[h]
+            scan(T.sc[:, 16 * a:16 * b], T.rs[:, 16 * a:16 * b], T.p0[:, 16 * a:16 * b], A.mult, A.max, "rs p0", "sc%d" % h)
+            mm(rank_ps[h], T.eye[:], T.cf1[:, a:b], "eye cf1", rank_k[h], start=True)
+            mm(rank_ps[h], T.eye[:], T.c32[:, a:b], "eye c32", rank_k[h])
+
+        def propose(h):
+            a, b = span[h]
+            top = T.sc[:, 16 * a + 15:16 * b:16]
+            ts(T.scb[:, a:b], top, 1.0 / 4096, A.mult, "sc%d" % h, "scb%d" % h, -144.0, A.add)
+            ts(T.prop[:, a:b], top, 143.5 * 4096, A.is_gt, "sc%d" % h, "prop%d" % h)
+            for r in range(16):
+                mm(win_ps[h][:, r:16 * (b - a):16], T.wt[:, r, :], T.scb[:, a:b], "wt scb%d" % h, win_k[h], stop=(r == 15))
+
+        def order(h):
+            a, b = span[h]
+            scan(T.pcs[:, a + 1:b + 1], T.one[:, a:b], T.prop[:, a:b], A.mult, A.add, "one pcs0 prop%d" % h, "pcs%d" % h,
+                 0.0 if h == 0 else T.pcs[:, a:a + 1])
+            tt(T.pu[:, a:b], T.prop[:, a:b], T.c32[:, a:b], A.mult, "c32 prop%d" % h, "pu%d" % h)
+            mm(rank_ps[h], T.tri[:], T.prop[:, a:b], "tri prop%d" % h, rank_k[h])
+            mm(rank_ps[h], T.dfill[:], T.prop[:, a:b], "dfill prop%d" % h, rank_k[h])
+            mm(rank_ps[h], T.bo[:], T.pcs[:, a:b], "bo pcs0 pcs%d" % h, rank_k[h])
+            mm(rank_ps[h], T.neye[:], T.pu[:, a:b], "neye pu%d" % h, rank_k[h], stop=True)
+
+        def winners(h):
+            a, b = span[h]
+            tt(T.yy[:, 16 * a:16 * b], win_ps[h][:, 0:16 * (b - a)], bl[:, 16 * a:16 * b], A.add, win_k[h] + " " + blk, "yy%d" % h)
+            cp(T.ofl[:, a:b], rank_ps[h], rank_k[h], "ofl%d" % h)
+
+        def place(h, a, b):
+            tt(wa[:, S:S + 1024].indirect(T.ofl[:, a:b]), T.yy[:, 16 * a:16 * b], al[:, 16 * a:16 * b], A.max,
+               "ofl%d yy%d %s" % (h, h, alk), cpa)
+
+        def tail(q):
+            tt(T.cmp[:, 192:P, q::4], T.p7[:, 256:512], T.sm[:, 16 * 192 + q:16 * P:4], A.is_gt, "p7 sm_4", "cmp_3%d" % q)
+
+        def tail_counts(q):
+            for k in range(q, 16, 4):
+                mm(T.p4[:, 0:64], sel(k), T.cmp[:, 192:P, k], "zz cmp_3%d" % q, "p4")
+
+        best(0)
+        mm(T.p0[:, 192:P], T.eye[:], T.ckw[:, 192:P], "eye ckw", "p0", start=True)
+        tail(0)
+        propose(0)
+        tail(1)
+        order(0)
+        tail(2)
+        for q in range(3):
+            tail_counts(q)
+        tail(3)
+        for r in range(16):
+            mm(T.p0[:, 192:P], sel(r), T.cmp[:, 192 + r:P:16, :], "zz cmp_30 cmp_31 cmp_32 cmp_33", "p0", stop=(r == 15))
+        tail_counts(3)
+        winners(0)
+        place(0, 0, 6)
+        best(1)
+        propose(1)
+        order(1)
+        place(0, 6, 12)
+        winners(1)
+        mm(T.p0[:, 0:S], T.eye[:], T.mka[:], "eye mka", "p0", start=True)
+        mm(T.p0[:, 0:S], T.bo[:], T.pca[:], "bo pca", "p0")
+        mm(T.p1[:, 0:S], T.bo[:], T.pcb[:], "bo pcb", "p1", start=True)
+        mm(T.p3[:, 0:96], T.bo[:], T.pcb[:, 96:S], "bo pcb", "p3", start=True)
+        mm(T.p2[:, 0:S], T.eye[:], T.thr[:], "eye thr", "p2", start=True)
+        place(1, 12, 16)
+        planes(lambda: wa[:, 0:2 * S].indirect(T.ofs[:, 4 * u:4 * u + 4]), 64, "ofs %s %s" % (tra, cpa))
+        act(wb[:, 0:S], wa[:, 0:2 * S].indirect(T.ofs[:]), "ofs %s %s" % (tra, cpa), trb)
+        rows([T.p0[:, 64 * q:64 * q + 64] for q in range(3)], 0, 64, ["p0"] * 3, True)
+        rows([T.p1[:, q:S:3] for q in range(3)], 0, 64, ["p1"] * 3, True)
+        rows([T.p3[:, q:96:3] for q in range(3)], 32, 64, ["p3"] * 3, True)
+        scan(T.ra[:], T.rs[:, 0:S], T.p0[:, 0:S], A.mult, A.max, "rs p0", "ra")
+        starts = (0, 576, 1008, 1296)
+
+        def weigh(c, q, key, stop=False):
+            n = S - 48 * c
+            at = starts[c] + q * n
+            mm(T.p2[:, 48 * c:S], T.bo[:], T.eq[:, at:at + n], "bo " + key, "p2", stop=stop)
+
+        for c in (2, 3):
+            n, at = S - 48 * c, starts[c] - starts[2]
+            for q in range(3):
+                x = 64 * q + 16 * c + 15
+                act(T.ab[:, at + q * n:at + q * n + n], T.p3[:, 48 * c - 96:96], "p3 ra", "ab%d" % c, AF.Abs, -1.0, T.ra[:, x:x + 1])
+        for c in (2, 3):
+            n, at = S - 48 * c, starts[c] - starts[2]
+            act(T.eq[:, starts[c]:starts[c] + 3 * n], T.ab[:, at:at + 3 * n], "wc nwc ab%d" % c, "eq%d" % c, AF.Relu,
+                T.wc[:, 4 + c:5 + c], T.wc[:, c:c + 1])
+        for c in (0, 1):
+            for q in range(3):
+                n, x = S - 48 * c, 64 * q + 16 * c + 15
+                at = starts[c] + q * n
+                ts(T.eq[:, at:at + n], T.p1[:, 48 * c:S], T.ra[:, x:x + 1], A.is_equal, "p1 ra wc", "eq%d%d" % (c, q), T.wc[:, c:c + 1], A.mult)
+                if (c, q) == (1, 2):
+                    for k in range(3):
+                        weigh(2, k, "eq2")
+                weigh(c, q, "eq%d%d" % (c, q))
+        for q in range(3):
+            weigh(3, q, "eq3", q == 2)
+        ts(T.ew[:], T.ra[:, 15::16], 1.0 / 15, A.mult, "ra", "ew", 0.25, A.add)
+        scan(T.ts[:], T.r48[:], T.p2[:, 0:S], A.mult, A.max, "r48 p2", "ts")
+        for c in range(4):
+            ts(T.off[:, c::4], T.ew[:, c::4], T.ts[:, 48 * c + 47:48 * c + 48], A.max, "ew ts jk", "off%d" % c, T.jk[:, c:c + 1], A.min)
+        OFF = "off0 off1 off2 off3"
+        lst = lambda q: T.off[:, 4 * q:4 * q + 4]
+        for q in range(3):
+            act(T.d4[:, q::4], Dw.indirect(lst(q)), DK + " " + OFF, "d4")
+
+        def touch():
+            for q in range(3):
+                cp(T.tw[:, 0:DW].indirect(lst(q)), T.one[:], "one " + OFF, "twa twz")
+            op("g", lambda t=t: g.remote_dma(T.rt[:, t, :], T.tw[:, V - H:V], T.sem["rt%d" % t], T.sem["lt%d" % t],
+                                            topo.addr(after)[1], topo.addr(after)[0], bits(eng_a)), "twz", "", ("lt%d" % t, len(eng_a)))
+            op("g", None, "", "rt%d" % t, ("rt%d" % t, n_in_t))
+
+        if not last:
+            touch()
+        zero = ([("Da", 0)] if rank > (rank - 1) % n_ranks else []) + ([("Dz", V - H)] if rank > (rank + 1) % n_ranks else [])
+        for k, a in zero:
+            act(T.D[:, a:a + H], T.D[:, a:a + H], k + " d4", k, AF.Copy, 0.0)
+        if zero:
+            act(T.d3[:], Dw.indirect(T.off[:]), DK + " " + OFF, "d3")
+            base, bk = (lambda q: T.d3[:, 64 * q:64 * q + 64]), "d3"
+        else:
+            base, bk = (lambda q: T.d4[:, q::4]), "d4"
+        late = [] if t < 2 else ([0, 1, 2] if t == 2 else [t])
+        mm(T.p3[:, 0:48], T.eye[:], T.fls[:], "eye fls flsb", "p3", start=True)
+        for x in late[:-1]:
+            for r in range(16):
+                mm(T.p3[:, 0:8], sel(r), T.rt[:, x, r::16], "zz rt%d" % x, "p3")
+
+        def own_touch():
+            for r in range(16):
+                mm(T.p3[:, 0:48], sel(r), T.tw[:, r:U:16], "zz twa", "p3", stop=(r == 15))
+
+        if not last:
+            own_touch()
+
+        def their_touch():
+            mm(T.p6[:, 0:8], T.eye[:], T.fown[:], "eye fown", "p6", start=True)
+            for r in range(16):
+                mm(T.p6[:, 0:8], sel(r), T.rt[:, t, r::16], "zz rt%d" % t, "p6", stop=(r == 15))
+
+        nzu, nk = T.nz[:, 64 * u:64 * u + 64], "nz%d" % u
+        scan(T.th[:], T.mul4[:], T.d4[:], A.mult, A.subtract, "mul4_0 mul4_1 mul4_2 mul4_3 d4", "th")
+        tt(T.dlt[:], T.th[:, 3::4], nzu, A.max, "th " + nk, "dlt")
+        for q in range(3):
+            tt(Dw.indirect(lst(q)), base(q), T.dlt[:], A.subtract if q == 0 else A.add, "dlt %s %s" % (bk, OFF), DK)
+        op("g", lambda t=t: g.remote_dma_fused([
+            RemoteDMATransfer(dst_ids=[dst(before)], dma_engine_mask=bits(half_b), remote_sem=T.sem["rd%d" % t],
+                              src=T.D[:, 0:H], dst=T.rd[:, t, H:2 * H]),
+            RemoteDMATransfer(dst_ids=[dst(after)], dma_engine_mask=bits(half_a), remote_sem=T.sem["rd%d" % t],
+                              src=T.D[:, V - H:V], dst=T.rd[:, t, 0:H])], local_sem=T.sem["ld%d" % t]),
+           "Da Dz", "", ("ld%d" % t, len(half_a) + len(half_b)))
+        op("g", None, "", "rd%d" % t, ("rd%d" % t, n_in_d))
+        if last:
+            dma("y", T.yd[:, H:V // 2], T.D[:, H:V // 2], "Dm", "")
+            dma("s", T.yd[:, V // 2:V - H], T.D[:, V // 2:V - H], "Dm", "")
+            touch()
+            own_touch()
+
+        def forget():
+            tt(nzu, nzu, T.dlt[:], A.subtract, "dlt " + nk, nk)
+            ts(T.fil[:], T.ew[:, 0:4], float(V), A.is_lt, "ew", "fil")
+            ts(T.gr[:], wb[:, 0:S], col(9), A.not_equal, trb + " c9", "gr")
+            tt(T.blk[:], T.ts[:, 47::48], T.fil[:], A.min, "ts fil", "blk")
+            ts(T.gr[:, 64 * u:64 * u + 64], nzu, 0.0, A.not_equal, nk + " gr", "gr")
+            for r in range(16):
+                mm(T.p5[:, 0:12], sel(r), T.gr[:, r::16], "zz gr", "p5", start=(r == 0))
+            mm(T.p5[:, 4 * u:4 * u + 4], T.eye[:], T.blk[:], "eye blk", "p5", stop=True)
+
+        def forget2():
+            ts(T.fre[:], T.p5[:, 0:12], 0.0, A.is_equal, "p5", "fre")
+            slot_list()
+
+        def take():
+            tt(T.D[:, 0:H], T.D[:, 0:H], T.rd[:, t, 0:H], A.add, "Da rd%d" % t, "Da")
+            tt(T.D[:, V - H:V], T.D[:, V - H:V], T.rd[:, t, H:2 * H], A.add, "Dz rd%d" % t, "Dz")
+
+        if not last:
+            c0, nc = 8 * (t + 1), (24, 32, 48, 48)[t]
+            na = min(nc, 48 - c0)
+
+            def compact(h, a, b, keys, home):
+                ps, pk, ps2, pk2 = (T.p4, "p4", T.p3, "p3") if h == 0 else (T.p7, "p7", T.p6, "p6")
+                mm(ps[:, a:b], T.eye[:], T.ce1[:, a:b], "eye ce1", pk, start=True)
+                mm(ps[:, a:b], T.eye[:], T.c64[:, a:b], "eye c64", pk)
+                scan(T.lcs[:, a + 1:b + 1], T.one[:, a:b], T.fl[:, a:b], A.mult, A.add, "one lcs0 " + keys, "lcs%d" % h,
+                     0.0 if h == 0 else T.lcs[:, a:a + 1])
+                tt(T.fu[:, a:b], T.fl[:, a:b], T.c64[:, a:b], A.mult, "c64 " + keys, "fu%d" % h)
+                mm(ps[:, a:b], T.tri[:], T.fl[:, a:b], "tri " + keys, pk)
+                mm(ps[:, a:b], T.dflag[:], T.fl[:, a:b], "dflag " + keys, pk)
+                mm(ps[:, a:b], T.bo[:], T.lcs[:, a:b], "bo lcs0 lcs%d" % h, pk)
+                mm(ps[:, a:b], T.neye[:], T.fu[:, a:b], "neye fu%d" % h, pk, stop=True)
+                mm(ps2[:, 64 + a:64 + b], T.tri[:], T.fl[:, a:b], "tri " + keys, pk2, start=True)
+                mm(ps2[:, 64 + a:64 + b], T.e1k[:], T.fl[:, a:b], "e1k " + keys, pk2)
+                mm(ps2[:, 64 + a:64 + b], T.bo[:], T.lcs[:, a:b], "bo lcs0 lcs%d" % h, pk2, stop=True)
+                cp(T.ofe[:, a:b], ps[:, a:b], pk, "ofe%d" % h)
+                act(T.lwin[:, 0:4608].indirect(T.ofe[:, a:b]), T.pos[:, 16 * (c0 + a):16 * (c0 + b)], "pos ofe%d" % h, "lwin", AF.Silu)
+                return lambda: ts(T.fls[:, home:home + b - a], ps2[:, 64 + a:64 + b], 1024 + P - 0.5, A.is_gt, pk2, "fls" + "b" * h)
+
+            def next_lists():
+                scan(T.lx[:], T.mx[:], T.lwin[:, 0:P], A.max, A.min, "mx lwin", "lx")
+                ts(T.lw[:], T.lx[:, 15::16], 0.25, A.add, "lx", "lw")
+                cp(T.o2[:], T.b2t[:, 0:EXT].indirect(T.lw[:]), "b2a b2b b2c b2d lw", "o2")
+
+            ts(T.fl[:, 0:na], T.p3[:, c0:c0 + na], 0.0, A.is_gt, "p3", "fla")
+            if t < 2:
+                ts(T.fls[:], T.p3[:, 0:48], 0.0, A.is_gt, "p3", "fls")
+                keep = compact(0, 0, na, "fla", c0)
+                forget()
+                keep()
+                pack(P + 256 * t, 2 * P + 256 * t, "b1b b2b", ("bpb", "bpc")[t])
+                forget2()
+                next_lists()
+                cp(T.o1[:], T.b1t[:, 0:EXT].indirect(T.lw[:]), "b1a b1b b1c b1d lw", "o1")
+                take()
+            else:
+                ts(T.fown[:], T.p3[:, 0:8], 0.0, A.is_gt, "p3", "fown")
+                ts(T.fl[:, na + 8:48], T.p3[:, 8:c0], 0.0, A.is_gt, "p3", "flc")
+                keep = compact(0, 0, na, "fla", c0)
+                their_touch()
+                keep()
+                ts(T.fl[:, na:na + 8], T.p6[:, 0:8], 0.0, A.is_gt, "p6", "flb")
+                keep = compact(1, na, 48, "flb flc", 0)
+                forget()
+                keep()
+                take()
+                forget2()
+                next_lists()
+                cp(T.o1[:], T.b1t[:, 0:EXT].indirect(T.lw[:]), "b1a b1b b1c b1d lw", "o1")
+        else:
+            forget()
+            ts(T.fown[:], T.p3[:, 0:8], 0.0, A.is_gt, "p3", "fown")
+            ts(T.fl[:, 8:48], T.p3[:, 8:48], 0.0, A.is_gt, "p3", "fla")
+            forget2()
+            take()
+            dma("y", T.yd[:, 0:H], T.D[:, 0:H], "Da", "")
+            dma("y", T.yd[:, V - H:V], T.D[:, V - H:V], "Dz", "")
+            their_touch()
+            for x in range(3):
+                act(T.zo[:, x::3], T.nz[:, 64 * x:64 * x + 64], "nz%d" % x, "zo", AF.Copy, -1.0)
+            dma("y", T.yz[:], T.zo[:], "zo", "")
+            slot_list_end()
+            ts(T.fl[:, 0:8], T.p6[:, 0:8], 0.0, A.is_gt, "p6 fla", "fl0")
+            for h in range(2):
+                bank, bk2 = (T.p6, "p6") if h == 0 else (T.p7, "p7")
+                mm(bank[:, 0:384], T.eye[:], T.zb[:], "eye zb", bk2, start=True)
+                for r in range(16):
+                    mm(bank[:, r:384:16], T.wt[:, r, :], T.fl[:, 24 * h:24 * h + 24], "wt fl0", bk2, stop=(r == 15))
+            for h in range(2):
+                act(T.fo[:, 384 * h:384 * h + 384], (T.p6 if h == 0 else T.p7)[:, 0:384], "p%d" % (6 + h), "fo", AF.Copy, -1.0 / 4096)
+            dma("s", T.yf[:], T.fo[0:128:16, :], "fo", "")
+            src, keys = (lambda: wb[:, 0:2 * S].indirect(T.ofs[:])), "ofs %s cp%d" % (trb, 1 - t % 2)
+            ts(T.f16[:], src(), col(9), A.is_equal, keys + " c9", "f16")
+            planes(src, S, keys)
+            mm(T.p0[:, 0:S], T.bo[:], T.pct[:, 0:S], "bo pct", "p0", start=True)
+            mm(T.p1[:, 0:2 * S], T.bo[:], T.pct[:, S:3 * S], "bo pct", "p1", start=True)
+            for m, d, o in (("hfa", "f16", 0), ("hq", "q16", 0), ("hf", "f16", 1), ("hf", "f16", 2), ("h1", "h16", 1), ("hm", "q16", 2), ("hq", "l16", 2)):
+                for x in range(3):
+                    out = T.p0[:, x:S:3] if o == 0 else T.p1[:, S * (o - 1) + x:S * o:3]
+                    mm(out, T[m][:], T[d][:, 64 * x:64 * x + 64], m + " " + d, "p0" if o == 0 else "p1",
+                       stop=(x == 2 and m == "hq"))
+            ts(T.t2[:], T.p0[:, 0:S], 1.0 / 15, A.mult, "p0", "t2", MAG, A.add)
+            act(T.t1[:, S:3 * S], T.p1[:, 0:2 * S], "p1", "t1b")
+            ts(T.t1[:, 0:S], T.t2[:], MAG, A.subtract, "t2", "t1a")
+            dma("y", T.yt[:], T.t1[0:128:16, :], "t1a t1b", "")
+    emit(g, T, ops)

@@ -6,6 +6,7 @@ AXX = AxisListType.X
 V, U, H, S, P, RO = 3072, 768, 128, 192, 256, 5
 J, WALL, DW = 3072, 3136, 3144
 EXT, DUM = 1288, 1280
+XL, XM = 224, 240
 MAG = 12582912.0
 MARK = 3583
 PARTS = "at wt pca pcb wc cmp_0 cmp_1 cmp_2 ab2 ab3 d4 zo pct fo thr".split()
@@ -44,7 +45,7 @@ SCRATCH = {
     "p4": ("psum", [128, 512], F32), "p5": ("psum", [128, 512], F32), "p6": ("psum", [128, 512], F32), "p7": ("psum", [128, 512], F32),
 }
 SEMAPHORES = (["sv", "ss", "st", "sg"] + ["dm%d" % i for i in range(24)]
-              + [k + str(t) for k in ("ld", "lt", "rd", "rt") for t in range(RO)])
+              + [k + str(t) for k in ("ld", "lt", "rd", "rt", "ac", "ad") for t in range(RO)])
 
 
 def bank(k):
@@ -185,14 +186,12 @@ def rank_program(g, core, T, topo):
                     mm(T.p5[:, 16 + 4 * u:20 + 4 * u], T[m][:], T.fre[:, 4 * w:4 * w + 4], m + " fre", "p5")
                 mm(T.p5[:, 16 + 4 * u:20 + 4 * u], T.bo[:], T.fcs[:, 4 * w:4 * w + 4], "bo fcs", "p5", stop=(w == 2))
 
-    dma("y", T.b2t[:, 0:P], T.b2[:, 0:P], "", "b2a")
-    dma("y", T.b1t[:, 0:P], T.b1[:, 0:P], "", "b1a")
+    dma("s", T.b2t[:, 0:P], T.b2[:, 0:P], "", "b2a")
+    dma("s", T.b1t[:, 0:P], T.b1[:, 0:P], "", "b1a")
     dma("y", T.D[:, 0:V // 2], T.dist[:, 0:V // 2], "", "Da Dm")
     dma("y", T.D[:, V // 2:V], T.dist[:, V // 2:V], "", "Dz Dm2")
-    dma("y", T.b1t[:, P:U], T.b1[:, P:U], "", "b1b")
+    dma("y", T.b1t[:, P:U], T.b1[:, P:U], "Da Dz", "b1b")
     dma("y", T.b2t[:, P:U], T.b2[:, P:U], "", "b2b")
-    dma("y", T.b1t[:, U:DUM], T.b1[:, 0:DUM - U], "", "b1c")
-    dma("y", T.b2t[:, U:DUM], T.b2[:, 0:DUM - U], "", "b2c")
 
     op("g", lambda: g.iota(T.ip[:, 0:1], [[0, 1]], 0, 1), "", "ip0")
     iota(T.cm[:], [[0, 16], [1, 16]], 0, 0, "cm")
@@ -230,11 +229,7 @@ def rank_program(g, core, T, topo):
     for r in range(16):
         act(T.wt[:, r, :], T.bo[:], "bo tmp", "wt", AF.Identity, T.tmp[:, r:r + 1])
     act(T.neye[:], T.eye[:], "eye", "neye", AF.Identity, -1.0)
-    act(T.e1k[:], T.eye[:], "eye", "e1k", AF.Identity, 1024.0)
     act(T.dfill[:], T.eye[:], "eye c13", "dfill", AF.Identity, col(13))
-    act(T.dflag[:], T.eye[:], "eye c14", "dflag", AF.Identity, col(14))
-    act(T.mx[:], T.dg[:], "dg", "mx", AF.Identity, 20000.0, -10000.0)
-    act(T.mka[:], T.dg[:, 0:S], "dg", "mka", AF.Identity, 1048576.0, -1048576.0)
     ts(T.tmp2[:], T.cm[:, 0:128], col(1), A.is_gt, "cm c1", "tmp2")
     ts(T.zz[:], T.i128[:], col(3), A.is_equal, "i128 c3", "zz", 65536.0, A.mult)
     ms(T.r4[:], 1.0, "r4")
@@ -253,9 +248,9 @@ def rank_program(g, core, T, topo):
     ms(T.fls[:, 0:16], 0.0, "flsb")
     ms(T.fls[:, 16:48], 1.0, "fls")
     for q, c in enumerate((0.0, -1.0, 1.0, 0.5)):
-        ms(T.mul4[:, q::4], c, "mul4_%d" % q)
-    ts(T.cf1[:], T.cm[:, 0:16], 0.0, A.mult, "cm c6", "cf1", col(6), A.add)
-    ts(T.ce1[:], T.cm[:, 0:48], 0.0, A.mult, "cm c7", "ce1", col(7), A.add)
+        act(T.mul4[:, q::4], T.cm[:, 0:64], "cm", "mul4_%d" % q, AF.Identity, 0.0, c)
+    act(T.cf1[:], T.cm[:, 0:16], "cm c6", "cf1", AF.Identity, 0.0, col(6))
+    act(T.ce1[:], T.cm[:, 0:48], "cm c7", "ce1", AF.Identity, 0.0, col(7))
     cp(T.o2[:], T.b2t[:, 0:P], "b2a", "o2")
     cp(T.o1[:], T.b1t[:, 0:P], "b1a", "o1")
     for name, c in (("hq", 4096.0), ("hh", 15.0), ("hl", 61440.0), ("hn", -61440.0)):
@@ -263,8 +258,8 @@ def rank_program(g, core, T, topo):
     for q, c in enumerate((20992.0, 245760.0, 53760.0)):
         ts(col(10 + q), col(4), c, A.mult, "c4 c5", "k%d" % q, col(5) if q == 1 else 0.0, A.add)
     for q in range(3):
-        ts(T.pca[:, 64 * q:64 * q + 64], T.cm[:, 0:64], 0.0, A.mult, "cm k%d" % q, "pca", col(10 + q), A.add)
-        ts(T.pcb[:, q::3], T.cm[:, 0:64], 0.0, A.mult, "cm k%d" % q, "pcb", col(10 + q), A.add)
+        act(T.pca[:, 64 * q:64 * q + 64], T.cm[:, 0:64], "cm k%d" % q, "pca", AF.Identity, 0.0, col(10 + q))
+        act(T.pcb[:, q::3], T.cm[:, 0:64], "cm k%d" % q, "pcb", AF.Identity, 0.0, col(10 + q))
     ms(T.th[:, 0:64], 1.0 / 3.0, "th")
     op("v", lambda: v.tensor_tensor_scan(T.ts[:, 0:64], T.th[:, 0:64], T.nz[:, 0:64], 1e29, A.mult, A.add), "th nz0", "ts")
     ms(T.r48[:], 1.0, "r48")
@@ -278,28 +273,32 @@ def rank_program(g, core, T, topo):
     ts(T.th[:, 128:192], T.ts[:, 0:64], -2.25, A.mult, "ts", "th3")
     ts(T.jk[:], T.cm[:, 0:4], 16.0, A.mult, "cm c1", "jk0", col(1), A.add)
     ts(T.own[:], T.cm[:, 0:12], 16.0, A.mult, "cm c1", "own0", col(1), A.add)
-    for q in range(3):
-        tt(T.thr[:, q::3], T.th[:, 64:128], T.th[:, 128:192], A.add, "th2 th3", "thr")
-    for name, c in (("h1", 1.0), ("hm", -4096.0), ("hf", -224.0), ("hfa", -3360.0)):
-        ts(T[name][:], T.bo[:], c, A.mult, "bo", name)
-    ts(col(15), col(5), 1.0 / 15, A.mult, "c5", "c15")
-    ts(T.kb[:, 0:1], col(4), 16384.0, A.mult, "c4 c15", "kb", col(15), A.add)
-    ts(T.kb[:, 1:2], col(4), 3584.0, A.mult, "c4", "kc")
+    tt(T.th[:, 192:256], T.th[:, 64:128], T.th[:, 128:192], A.add, "th2 th3", "th4")
+
+    def output_constants():
+        ts(col(15), col(5), 1.0 / 15, A.mult, "c5", "c15")
+        for name, c in (("h1", 1.0), ("hm", -4096.0), ("hf", -224.0), ("hfa", -3360.0)):
+            ts(T[name][:], T.bo[:], c, A.mult, "bo", name)
+        ts(T.kb[:, 0:1], col(4), 16384.0, A.mult, "c4 c15", "kb", col(15), A.add)
+        ts(T.kb[:, 1:2], col(4), 3584.0, A.mult, "c4", "kc")
+
     ts(T.jk[:], T.jk[:], float(J), A.add, "jk0", "jk")
     ts(T.own[:], T.own[:], 320.0, A.add, "own0", "own")
     ts(T.wc[:, 4:8], T.wc[:, 0:4], -1.0, A.mult, "wc", "nwc")
-    act(T.at[:, 0:U], T.pos[:, 0:U], "pos", "at", AF.Identity, 1.0 / 4096, -1536.0 / 4096)
-    act(T.at[:, U:EXT], T.pos[:, U:EXT], "pos", "at", AF.Identity, 1.0 / 4096, (-1536.0 - U) / 4096)
+
 
     def pack(a, b, r, w):
         ts(T.bp[:, a:b], T.b2t[:, a:b], 2560.0, A.add, r, w + "x", 1.0 / 4096, A.mult)
         tt(T.bp[:, a:b], T.bp[:, a:b], T.b1t[:, a:b], A.add, r + " " + w + "x", w)
 
+
     pack(0, P, "b1a b2a", "bpa")
 
-    def slot_list_end():
-        tt(T.ofs32[:], T.p5[:, 16:28], T.own[:], A.max, "p5 own", "ofs32")
-        ts(T.ofs[:], T.ofs32[:], -320.0, A.add, "ofs32", "ofs")
+    def slot_list_end(step):
+        if step == 0:
+            tt(T.ofs32[:], T.p5[:, 16:28], T.own[:], A.max, "p5 own", "ofs32")
+        else:
+            ts(T.ofs[:], T.ofs32[:], -320.0, A.add, "ofs32", "ofs")
 
     def planes(src, n, r):
         ts(T.h32[:, 0:n], src(), MAG, A.add, r, "h32", MAG, A.subtract)
@@ -314,7 +313,7 @@ def rank_program(g, core, T, topo):
         mm(outs[2], T.hl[:], T.l16[:, a:b], "hl l16", bank[2], stop=stop)
 
     eng_b, eng_a = topo.engines(core, before), topo.engines(core, after)
-    half_b = eng_b[:len(eng_b) // 2]
+    half_b = eng_b[0::2]
     half_a = [e for e in eng_a if e not in half_b][:len(half_b)]
     bits = lambda es: sum(1 << e for e in es)
     dst = lambda c: DstId(rid=topo.addr(c)[0], pnc=topo.addr(c)[1])
@@ -336,7 +335,7 @@ def rank_program(g, core, T, topo):
             iota(T.zb[:], [[0, 384]], 0, 0, "zb")
             op("g", lambda wb=wb: g.affine_select(wb[:, S:2 * S], T.cpd[:], [[0, S]], A.is_ge, 0.0, 0, 0), "cpd", "cp%d" % (1 - t % 2))
         dk = DK + (" Dm2" if t == 0 else "")
-        cuts = (0, 16, 64, 128, 192, 256)
+        cuts = (0, 16, 40, 64, 128, 192, XL, XM, 256)
 
         def gath(i):
             a, b = cuts[i], cuts[i + 1]
@@ -344,21 +343,20 @@ def rank_program(g, core, T, topo):
 
         def add(i):
             a, b = cuts[i], cuts[i + 1]
-            tt(T.sm[:, 16 * a:16 * b], Dw.indirect(T.o1[:, a:b]), T.g2[:, 16 * a:16 * b], A.add, dk + " o1 g2_%d" % i, "sm_%d" % i)
+            tt(T.sm[:, 16 * a:16 * b], Dw.indirect(T.o1[:, a:b]), T.g2[:, 16 * a:16 * b], A.add,
+               dk + " o1 g2_%d" % i, "sm_%d" % i)
 
-        def rep(h):
-            bank = T.p6 if h == 0 else T.p7
+        def rep(a, b, bk3):
             src = T.D if t == 0 else T.dl
             for q in range(4):
-                act(bank[:, q::4], src[:, 128 * h:128 * h + 128], dk if t == 0 else "dl", "p%d" % (6 + h))
+                act(T[bk3][:, q:4 * (b - a):4], src[:, a:b], dk if t == 0 else "dl", bk3)
 
         def compare(j):
             a, b = 64 * j, 64 * j + 64
-            bank = T.p6 if j < 2 else T.p7
-            keys = ("sm_0 sm_1", "sm_2", "sm_3", "sm_4")[j]
+            bk3 = ("p6", "p3", "p7")[j]
+            keys = ("sm_0 sm_1 sm_2", "sm_3", "sm_4")[j]
             for q in range(4):
-                tt(T.cmp[:, a:b, q::4], bank[:, 256 * (j % 2):256 * (j % 2) + 256], T.sm[:, 16 * a + q:16 * b:4], A.is_gt,
-                   "p%d %s" % (6 + j // 2, keys), "cmp_%d" % j)
+                tt(T.cmp[:, a:b, q::4], T[bk3][:, 0:256], T.sm[:, 16 * a + q:16 * b:4], A.is_gt, bk3 + " " + keys, "cmp_%d" % j)
             for r in range(16):
                 mm(T.p0[:, a:b], sel(r), T.cmp[:, a + r:b:16, :], "zz cmp_%d" % j, "p0", stop=(j == 2 and r == 15))
             for k in range(16):
@@ -369,30 +367,47 @@ def rank_program(g, core, T, topo):
         mm(T.p4[:, 0:64], T.eye[:], T.cka[:, 0:64], "eye cka", "p4", start=True)
         gath(0)
         gath(1)
-        add(0)
-        slot_list_end()
-        if t > 0:
-            lst = T.lw
-            if t >= 3:
-                ts(T.lt[:], T.lx[:, 15::16], U - 0.5, A.is_ge, "lx", "lt", -float(U), A.mult)
-                tt(T.lt2[:], T.lt[:], T.lx[:, 15::16], A.add, "lt lx", "lt2")
-                ts(T.le[:], T.lt2[:], 0.25, A.add, "lt2", "le")
-                lst = T.le
-            cp(T.dl[:], Dw.indirect(lst[:]), dk + " lw le", "dl")
-        rep(0)
         gath(2)
-        add(1)
-        compare(0)
-        rep(1)
+        if t > 0:
+            if t >= 3:
+                ts(T.le[:], T.lt2[:], 0.25, A.add, "lt2", "le")
+                add(0)
+                cp(T.dl[:], Dw.indirect(T.le[:]), dk + " le", "dl")
+                slot_list_end(0)
+            else:
+                cp(T.dl[:], Dw.indirect(T.lw[:]), dk + " lw", "dl")
+                slot_list_end(0)
+                add(0)
+        else:
+            slot_list_end(0)
+            add(0)
+        rep(0, 64, "p6")
         gath(3)
+        add(1)
+        slot_list_end(1)
         add(2)
-        compare(1)
+        compare(0)
+        rep(64, 128, "p3")
+
+        def both(i):
+            a, b = cuts[i], cuts[i + 1]
+            gath(i)
+            act(T.sm[:, 16 * a:16 * b], Dw.indirect(T.o1[:, a:b]), dk + " o1", "sm_%d" % i)
+            op("g", lambda: g.dma_start(T.sm[:, 16 * a:16 * b], T.g2[:, 16 * a:16 * b], accum_op=A.add), "g2_%d sm_%d" % (i, i),
+               "sm_%d" % i, ("%s%d" % (("ac", "ad")[i - 6], t), 16), True)
+
+        both(6)
         gath(4)
+        both(7)
         add(3)
+        compare(1)
+        rep(128, 256, "p7")
+        gath(5)
+        add(4)
         compare(2)
         if t > 0:
             act(T.bl[:], T.bp[:, 0:(512, U, EXT, EXT)[t - 1]].indirect(T.lw[:]), "bpa bpb bpc bpe bpd lw", "bl")
-            act(T.al[:], T.at[:, 0:EXT].indirect(T.lw[:]), "at lw", "al")
+            act(T.al[:], T.at[:, 0:EXT].indirect(T.lw[:]), "at0 at lw", "al")
             bl, al, blk, alk = T.bl, T.al, "bl", "al"
             if last:
                 for q, (c, k) in enumerate(((col(10), "k0"), (T.kb[:, 0:1], "kb"), (T.kb[:, 1:2], "kc"))):
@@ -400,8 +415,17 @@ def rank_program(g, core, T, topo):
             if t == 2:
                 act(T.bp[:, U:DUM], T.bp[:, 0:DUM - U], "bpa bpb", "bpe")
         else:
-            bl, al, blk, alk = T.bp, T.at, "bpa", "at"
-        add(4)
+            bl, al, blk, alk = T.bp, T.at, "bpa", "at0"
+            act(T.at[:, 0:P], T.pos[:, 0:P], "pos", "at0", AF.Identity, 1.0 / 4096, -1536.0 / 4096)
+            for q in range(3):
+                act(T.thr[:, q::3], T.th[:, 192:256], "th4 th", "thr")
+            act(T.mka[:], T.dg[:, 0:S], "dg", "mka", AF.Identity, 1048576.0, -1048576.0)
+            act(T.e1k[:], T.eye[:], "eye", "e1k", AF.Identity, 1024.0)
+            act(T.dflag[:], T.eye[:], "eye c14", "dflag", AF.Identity, col(14))
+            act(T.mx[:], T.dg[:], "dg", "mx", AF.Identity, 20000.0, -10000.0)
+            act(T.at[:, P:U], T.pos[:, P:U], "pos", "at", AF.Identity, 1.0 / 4096, -1536.0 / 4096)
+            act(T.at[:, U:EXT], T.pos[:, U:EXT], "pos", "at", AF.Identity, 1.0 / 4096, (-1536.0 - U) / 4096)
+        add(5)
         span = ((0, 12), (12, 16))
         rank_ps, rank_k = (T.p2[:, 0:12], T.p5[:, 32:36]), ("p2", "p5")
         win_ps, win_k = (T.p1, T.p4), ("p1", "p4")
@@ -440,7 +464,7 @@ def rank_program(g, core, T, topo):
                "ofl%d yy%d %s" % (h, h, alk), cpa)
 
         def tail(q):
-            tt(T.cmp[:, 192:P, q::4], T.p7[:, 256:512], T.sm[:, 16 * 192 + q:16 * P:4], A.is_gt, "p7 sm_4", "cmp_3%d" % q)
+            tt(T.cmp[:, 192:P, q::4], T.p7[:, 256:512], T.sm[:, 16 * 192 + q:16 * P:4], A.is_gt, "p7 sm_5 sm_6 sm_7", "cmp_3%d" % q)
 
         def tail_counts(q):
             for k in range(q, 16, 4):
@@ -448,10 +472,10 @@ def rank_program(g, core, T, topo):
 
         best(0)
         mm(T.p0[:, 192:P], T.eye[:], T.ckw[:, 192:P], "eye ckw", "p0", start=True)
-        tail(0)
         propose(0)
-        tail(1)
+        tail(0)
         order(0)
+        tail(1)
         tail(2)
         for q in range(3):
             tail_counts(q)
@@ -462,6 +486,9 @@ def rank_program(g, core, T, topo):
         winners(0)
         place(0, 0, 6)
         best(1)
+        if t == 1:
+            dma("y", T.b1t[:, U:DUM], T.b1[:, 0:DUM - U], "sc1", "b1c")
+            dma("y", T.b2t[:, U:DUM], T.b2[:, 0:DUM - U], "", "b2c")
         propose(1)
         order(1)
         place(0, 6, 12)
@@ -490,8 +517,6 @@ def rank_program(g, core, T, topo):
             for q in range(3):
                 x = 64 * q + 16 * c + 15
                 act(T.ab[:, at + q * n:at + q * n + n], T.p3[:, 48 * c - 96:96], "p3 ra", "ab%d" % c, AF.Abs, -1.0, T.ra[:, x:x + 1])
-        for c in (2, 3):
-            n, at = S - 48 * c, starts[c] - starts[2]
             act(T.eq[:, starts[c]:starts[c] + 3 * n], T.ab[:, at:at + 3 * n], "wc nwc ab%d" % c, "eq%d" % c, AF.Relu,
                 T.wc[:, 4 + c:5 + c], T.wc[:, c:c + 1])
         for c in (0, 1):
@@ -499,7 +524,7 @@ def rank_program(g, core, T, topo):
                 n, x = S - 48 * c, 64 * q + 16 * c + 15
                 at = starts[c] + q * n
                 ts(T.eq[:, at:at + n], T.p1[:, 48 * c:S], T.ra[:, x:x + 1], A.is_equal, "p1 ra wc", "eq%d%d" % (c, q), T.wc[:, c:c + 1], A.mult)
-                if (c, q) == (1, 2):
+                if (c, q) == (1, 1):
                     for k in range(3):
                         weigh(2, k, "eq2")
                 weigh(c, q, "eq%d%d" % (c, q))
@@ -552,8 +577,47 @@ def rank_program(g, core, T, topo):
         nzu, nk = T.nz[:, 64 * u:64 * u + 64], "nz%d" % u
         scan(T.th[:], T.mul4[:], T.d4[:], A.mult, A.subtract, "mul4_0 mul4_1 mul4_2 mul4_3 d4", "th")
         tt(T.dlt[:], T.th[:, 3::4], nzu, A.max, "th " + nk, "dlt")
-        for q in range(3):
+        c0, nc = 8 * (t + 1), (24, 32, 48, 48, 48)[t]
+        na = min(nc, 48 - c0)
+
+        def ranks(h, a, b, keys):
+            ps, pk, ps2, pk2 = (T.p4, "p4", T.p3, "p3") if h == 0 else (T.p7, "p7", T.p6, "p6")
+            mm(ps[:, a:b], T.eye[:], T.ce1[:, a:b], "eye ce1", pk, start=True)
+            mm(ps[:, a:b], T.eye[:], T.c64[:, a:b], "eye c64", pk)
+            scan(T.lcs[:, a + 1:b + 1], T.one[:, a:b], T.fl[:, a:b], A.mult, A.add, "one lcs0 " + keys, "lcs%d" % h,
+                 0.0 if h == 0 else T.lcs[:, a:a + 1])
+            tt(T.fu[:, a:b], T.fl[:, a:b], T.c64[:, a:b], A.mult, "c64 " + keys, "fu%d" % h)
+            mm(ps[:, a:b], T.tri[:], T.fl[:, a:b], "tri " + keys, pk)
+            mm(ps[:, a:b], T.dflag[:], T.fl[:, a:b], "dflag " + keys, pk)
+            mm(ps[:, a:b], T.bo[:], T.lcs[:, a:b], "bo lcs0 lcs%d" % h, pk)
+            mm(ps[:, a:b], T.neye[:], T.fu[:, a:b], "neye fu%d" % h, pk, stop=True)
+            mm(ps2[:, 64 + a:64 + b], T.tri[:], T.fl[:, a:b], "tri " + keys, pk2, start=True)
+            mm(ps2[:, 64 + a:64 + b], T.e1k[:], T.fl[:, a:b], "e1k " + keys, pk2)
+            mm(ps2[:, 64 + a:64 + b], T.bo[:], T.lcs[:, a:b], "bo lcs0 lcs%d" % h, pk2, stop=True)
+
+        def compact(h, a, b, home):
+            ps, pk, ps2, pk2 = (T.p4, "p4", T.p3, "p3") if h == 0 else (T.p7, "p7", T.p6, "p6")
+            cp(T.ofe[:, a:b], ps[:, a:b], pk, "ofe%d" % h)
+            act(T.lwin[:, 0:4608].indirect(T.ofe[:, a:b]), T.pos[:, 16 * (c0 + a):16 * (c0 + b)], "pos ofe%d" % h, "lwin", AF.Silu)
+            return lambda: ts(T.fls[:, home:home + b - a], ps2[:, 64 + a:64 + b], 1024 + P - 0.5, A.is_gt, pk2, "fls" + "b" * h)
+
+        def correct(q):
             tt(Dw.indirect(lst(q)), base(q), T.dlt[:], A.subtract if q == 0 else A.add, "dlt %s %s" % (bk, OFF), DK)
+
+        correct(0)
+        if not last:
+            ts(T.fl[:, 0:na], T.p3[:, c0:c0 + na], 0.0, A.is_gt, "p3", "fla")
+            if t < 2:
+                ts(T.fls[:], T.p3[:, 0:48], 0.0, A.is_gt, "p3", "fls")
+            else:
+                ts(T.fown[:], T.p3[:, 0:8], 0.0, A.is_gt, "p3", "fown")
+                ts(T.fl[:, na + 8:48], T.p3[:, 8:c0], 0.0, A.is_gt, "p3", "flc")
+        correct(1)
+        if not last:
+            ranks(0, 0, na, "fla")
+        correct(2)
+        if not last:
+            keep = compact(0, 0, na, c0)
         op("g", lambda t=t: g.remote_dma_fused([
             RemoteDMATransfer(dst_ids=[dst(before)], dma_engine_mask=bits(half_b), remote_sem=T.sem["rd%d" % t],
                               src=T.D[:, 0:H], dst=T.rd[:, t, H:2 * H]),
@@ -573,6 +637,8 @@ def rank_program(g, core, T, topo):
             ts(T.gr[:], wb[:, 0:S], col(9), A.not_equal, trb + " c9", "gr")
             tt(T.blk[:], T.ts[:, 47::48], T.fil[:], A.min, "ts fil", "blk")
             ts(T.gr[:, 64 * u:64 * u + 64], nzu, 0.0, A.not_equal, nk + " gr", "gr")
+
+        def forget_count():
             for r in range(16):
                 mm(T.p5[:, 0:12], sel(r), T.gr[:, r::16], "zz gr", "p5", start=(r == 0))
             mm(T.p5[:, 4 * u:4 * u + 4], T.eye[:], T.blk[:], "eye blk", "p5", stop=True)
@@ -586,59 +652,43 @@ def rank_program(g, core, T, topo):
             tt(T.D[:, V - H:V], T.D[:, V - H:V], T.rd[:, t, H:2 * H], A.add, "Dz rd%d" % t, "Dz")
 
         if not last:
-            c0, nc = 8 * (t + 1), (24, 32, 48, 48)[t]
-            na = min(nc, 48 - c0)
-
-            def compact(h, a, b, keys, home):
-                ps, pk, ps2, pk2 = (T.p4, "p4", T.p3, "p3") if h == 0 else (T.p7, "p7", T.p6, "p6")
-                mm(ps[:, a:b], T.eye[:], T.ce1[:, a:b], "eye ce1", pk, start=True)
-                mm(ps[:, a:b], T.eye[:], T.c64[:, a:b], "eye c64", pk)
-                scan(T.lcs[:, a + 1:b + 1], T.one[:, a:b], T.fl[:, a:b], A.mult, A.add, "one lcs0 " + keys, "lcs%d" % h,
-                     0.0 if h == 0 else T.lcs[:, a:a + 1])
-                tt(T.fu[:, a:b], T.fl[:, a:b], T.c64[:, a:b], A.mult, "c64 " + keys, "fu%d" % h)
-                mm(ps[:, a:b], T.tri[:], T.fl[:, a:b], "tri " + keys, pk)
-                mm(ps[:, a:b], T.dflag[:], T.fl[:, a:b], "dflag " + keys, pk)
-                mm(ps[:, a:b], T.bo[:], T.lcs[:, a:b], "bo lcs0 lcs%d" % h, pk)
-                mm(ps[:, a:b], T.neye[:], T.fu[:, a:b], "neye fu%d" % h, pk, stop=True)
-                mm(ps2[:, 64 + a:64 + b], T.tri[:], T.fl[:, a:b], "tri " + keys, pk2, start=True)
-                mm(ps2[:, 64 + a:64 + b], T.e1k[:], T.fl[:, a:b], "e1k " + keys, pk2)
-                mm(ps2[:, 64 + a:64 + b], T.bo[:], T.lcs[:, a:b], "bo lcs0 lcs%d" % h, pk2, stop=True)
-                cp(T.ofe[:, a:b], ps[:, a:b], pk, "ofe%d" % h)
-                act(T.lwin[:, 0:4608].indirect(T.ofe[:, a:b]), T.pos[:, 16 * (c0 + a):16 * (c0 + b)], "pos ofe%d" % h, "lwin", AF.Silu)
-                return lambda: ts(T.fls[:, home:home + b - a], ps2[:, 64 + a:64 + b], 1024 + P - 0.5, A.is_gt, pk2, "fls" + "b" * h)
-
             def next_lists():
                 scan(T.lx[:], T.mx[:], T.lwin[:, 0:P], A.max, A.min, "mx lwin", "lx")
                 ts(T.lw[:], T.lx[:, 15::16], 0.25, A.add, "lx", "lw")
-                cp(T.o2[:], T.b2t[:, 0:EXT].indirect(T.lw[:]), "b2a b2b b2c b2d lw", "o2")
+                if t >= 2:
+                    ts(T.lt[:], T.lx[:, 15::16], U - 0.5, A.is_ge, "lx", "lt", -float(U), A.mult)
+                cp(T.o2[:], T.b2t[:, 0:wide].indirect(T.lw[:]), "b2a b2b b2d lw" + " b2c" * (t >= 2), "o2")
+                if t >= 2:
+                    tt(T.lt2[:], T.lt[:], T.lx[:, 15::16], A.add, "lt lx", "lt2")
 
-            ts(T.fl[:, 0:na], T.p3[:, c0:c0 + na], 0.0, A.is_gt, "p3", "fla")
+            wide = U if t < 2 else EXT
+
             if t < 2:
-                ts(T.fls[:], T.p3[:, 0:48], 0.0, A.is_gt, "p3", "fls")
-                keep = compact(0, 0, na, "fla", c0)
-                forget()
                 keep()
+                forget()
+                forget_count()
                 pack(P + 256 * t, 2 * P + 256 * t, "b1b b2b", ("bpb", "bpc")[t])
                 forget2()
                 next_lists()
-                cp(T.o1[:], T.b1t[:, 0:EXT].indirect(T.lw[:]), "b1a b1b b1c b1d lw", "o1")
                 take()
             else:
-                ts(T.fown[:], T.p3[:, 0:8], 0.0, A.is_gt, "p3", "fown")
-                ts(T.fl[:, na + 8:48], T.p3[:, 8:c0], 0.0, A.is_gt, "p3", "flc")
-                keep = compact(0, 0, na, "fla", c0)
                 their_touch()
                 keep()
-                ts(T.fl[:, na:na + 8], T.p6[:, 0:8], 0.0, A.is_gt, "p6", "flb")
-                keep = compact(1, na, 48, "flb flc", 0)
                 forget()
+                ts(T.fl[:, na:na + 8], T.p6[:, 0:8], 0.0, A.is_gt, "p6", "flb")
+                ranks(1, na, 48, "flb flc")
+                forget_count()
+                keep = compact(1, na, 48, 0)
                 keep()
-                take()
+                if t == 3:
+                    output_constants()
                 forget2()
+                take()
                 next_lists()
-                cp(T.o1[:], T.b1t[:, 0:EXT].indirect(T.lw[:]), "b1a b1b b1c b1d lw", "o1")
+            cp(T.o1[:], T.b1t[:, 0:wide].indirect(T.lw[:]), "b1a b1b b1d lw" + " b1c" * (t >= 2), "o1")
         else:
             forget()
+            forget_count()
             ts(T.fown[:], T.p3[:, 0:8], 0.0, A.is_gt, "p3", "fown")
             ts(T.fl[:, 8:48], T.p3[:, 8:48], 0.0, A.is_gt, "p3", "fla")
             forget2()
@@ -649,7 +699,8 @@ def rank_program(g, core, T, topo):
             for x in range(3):
                 act(T.zo[:, x::3], T.nz[:, 64 * x:64 * x + 64], "nz%d" % x, "zo", AF.Copy, -1.0)
             dma("y", T.yz[:], T.zo[:], "zo", "")
-            slot_list_end()
+            slot_list_end(0)
+            slot_list_end(1)
             ts(T.fl[:, 0:8], T.p6[:, 0:8], 0.0, A.is_gt, "p6 fla", "fl0")
             for h in range(2):
                 bank, bk2 = (T.p6, "p6") if h == 0 else (T.p7, "p7")

@@ -4,12 +4,22 @@ from concourse.mybir import AluOpType as A, ActivationFunctionType as AF, AxisLi
 AXX = AxisListType.X
 
 V, U, H, S, P, RO = 3072, 768, 128, 192, 256, 5
-J, WALL, DW = 3072, 3136, 3144
+J, WALL, MARK, DW = 3072, 3136, 3144, 3152
 EXT, DUM = 1288, 1280
-XL, XM = 224, 240
 MAG = 12582912.0
-MARK = 3583
-PARTS = "at wt pca pcb wc cmp_0 cmp_1 cmp_2 ab2 ab3 d4 zo pct fo thr".split()
+CUTS = (0, 16, 40, 64, 96, 128, 160, 192, 224, 240, 256)
+LOOK = "g0 o2 g1 a0 le dl g2 a1 dp g3 o1 s0 a2 b8 g4 c0 s1 g5 b9 a3 a4 c1 g6 g7 a5 a6 c2 bl a7".split()
+OWN = (0,)
+SPLIT = ((8,), (16,), (18, 38), (12, 34))
+EARLY = (2, 2, 0, 0, 2)
+POST = ("0fo1r2", "01for2")
+RELAX = False
+DLS = False
+ARRANGE = True
+CYC, PEC, GA, SCA = 0.95, 0.42, 1.5, 3.5
+EQVS = tuple((0, 1, 3) if e else (0, 1) for e in EARLY)
+TRANS, STREAM = False, (16, 4)
+PARTS = "at wt pca pcb wc ab2 ab3 d4 zo pct thr msk lc xs".split() + ["cmp_%d_%d" % (j, k) for j in range(4) for k in range(16)]
 F32, BF, F16, I32, U16 = "float32", "bfloat16", "float16", "int32", "uint16"
 
 
@@ -20,32 +30,34 @@ def sb(n, d):
 SCRATCH = {
     "D": sb(DW, F32), "b1t": sb(EXT, I32), "b2t": sb(EXT, I32), "bp": sb(EXT, F32), "at": sb(EXT, F32), "pos": sb(EXT, F32),
     "g2": sb(4096, F32), "sm": sb(4096, F32), "cmp": sb([256, 16], BF),
-    "o1": sb(256, U16), "o2": sb(256, U16), "lw": sb(16, U16), "le": sb(16, U16), "lt": sb(16, F32), "lt2": sb(16, F32),
+    "o1": sb(256, U16), "o2": sb(256, U16), "lw": sb(16, U16), "le": sb(16, U16), "lt": sb(32, F32),
     "dl": sb(256, F32), "bl": sb(256, F32), "al": sb(256, F32), "yy": sb(256, F32), "sc": sb(256, F32),
     "prop": sb(16, BF), "scb": sb(16, BF), "pu": sb(16, BF), "pcs": sb(24, BF), "ofl": sb(16, U16),
     "w0": sb(1216, F32), "w1": sb(1216, F32), "ofs": sb(12, U16), "ofs32": sb(12, F32),
-    "h32": sb(192, F32), "h16": sb(192, F16), "q16": sb(192, F16), "l16": sb(192, F16),
-    "ra": sb(192, F32), "ew": sb(12, F32), "eq": sb(1440, BF), "ts": sb(192, F32), "off": sb(12, U16),
+    "h16": sb(192, F16), "q16": sb(192, F16), "l16": sb(192, F16),
+    "ra": sb(192, F32), "ew": sb(12, U16), "eq": sb(1440, BF), "ts": sb(192, F32), "off": sb(12, U16),
     "d4": sb(256, F32), "d3": sb(192, F32), "th": sb(256, F32), "dlt": sb(64, F32), "nz": sb(192, F32),
+    "sw": sb(4, BF), "dm": sb(64, F32), "g0": sb(64, BF), "onef": sb(64, F32),
     "tw": sb(DW, BF), "one": sb(64, BF), "gr": sb(192, BF), "fil": sb(4, F32), "blk": sb(4, BF),
     "fre": sb(12, BF), "fcs": sb(12, BF),
-    "fown": sb(8, BF), "fls": sb(48, BF), "fl": sb(48, BF), "fu": sb(48, BF), "lcs": sb(56, BF), "ofe": sb(48, U16), "lwin": sb(4608, F32), "lx": sb(256, F32),
-    "rd": sb([RO, 256], F32), "rt": sb([RO, 128], BF),
-    "zo": sb(192, F32), "t1": sb(576, F32), "t2": sb(192, F32), "fo": sb(768, F32),
-    "ip": sb(8, I32), "col": sb(16, F32), "cm": sb(256, F32), "i128": sb(144, F32), "gi": sb(128, F32), "tmp": sb(16, F32), "tmp2": sb(128, F32),
-    "dg": sb(256, F32), "mx": sb(256, F32), "rs": sb(256, F32), "mul4": sb(256, F32), "r4": sb(12, F32),
+    "fown": sb(8, F32), "sx": sb(128, BF), "m4": sb(128, BF), "fls": sb(48, BF), "fl": sb(48, BF), "fu": sb(48, BF), "lcs": sb(56, BF), "ofe": sb(48, U16),
+    "lwin": sb(4608, F32), "lwv": sb(4608, F32), "lx": sb(256, F32), "lxv": sb(256, F32), "lm": sb(16, F32),
+    "rd": sb([RO, 256], F32), "rt": sb([2, 128], BF), "rf": sb(128, F32),
+    "zo": sb(192, F32), "t1": sb(576, F32), "t2": sb(576, F32),
+    "ip": sb(8, I32), "col": sb(24, F32), "cm": sb(256, F32), "i128": sb(144, F32), "gi": sb(128, F32), "tmp": sb(16, F32), "tmp2": sb(128, F32),
+    "dg": sb(256, F32), "mx": sb(256, F32), "rs": sb(256, BF), "mul4": sb(256, F32), "r4": sb(12, F32),
     "eye": sb(128, BF), "neye": sb(128, BF), "bo": sb(128, BF), "tri": sb(128, BF), "zz": sb(144, BF), "wt": sb([16, 128], BF),
     "dfill": sb(128, BF), "dflag": sb(128, BF), "e1k": sb(128, BF), "e512": sb(128, BF), "mgt": sb(128, BF), "ab": sb(432, F32),
-    "hq": sb(128, F16), "hh": sb(128, F16), "hl": sb(128, F16), "hn": sb(128, F16),
-    "ckw": sb(256, BF), "cka": sb(256, BF), "c32": sb(16, BF), "c64": sb(48, BF), "cf1": sb(16, BF), "ce1": sb(48, BF),
+    "hx": sb([6, 128], F16), "lc": sb([4, 128], BF), "sk": sb(256, BF), "skt": sb(192, BF), "s32": sb(256, BF), "xs": sb(64, F16),
+    "cka": sb(256, BF), "c32": sb(16, BF), "c64": sb(48, BF), "cf1": sb(16, BF), "ce1": sb(48, BF),
     "mka": sb(192, BF), "pca": sb(192, BF), "pcb": sb(192, BF), "pct": sb(576, BF), "wr": sb(64, F32), "thr": sb(192, BF),
-    "r48": sb(192, F32), "h1": sb(128, F16), "hm": sb(128, F16), "hf": sb(128, F16), "hfa": sb(128, F16), "kb": sb(2, F32), "f16": sb(192, F16),
-    "wc": sb(8, F32), "jk": sb(4, F32), "own": sb(12, F32), "cpd": sb(192, F32), "zb": sb(384, BF),
+    "r48": sb(192, F32), "bq": sb(128, BF),
+    "wc": sb(8, F32), "jk": sb(4, F32), "own": sb(12, F32), "own2": sb(16, F32), "cpd": sb(192, F32),
     "p0": ("psum", [128, 512], F32), "p1": ("psum", [128, 512], F32), "p2": ("psum", [128, 512], F32), "p3": ("psum", [128, 512], F32),
     "p4": ("psum", [128, 512], F32), "p5": ("psum", [128, 512], F32), "p6": ("psum", [128, 512], F32), "p7": ("psum", [128, 512], F32),
 }
 SEMAPHORES = (["sv", "ss", "st", "sg"] + ["dm%d" % i for i in range(24)]
-              + [k + str(t) for k in ("ld", "lt", "rd", "rt", "ac", "ad") for t in range(RO)])
+              + [k + str(t) for k in ("ld", "lt", "rd", "rt", "aa", "ab", "ac", "ad") for t in range(RO)])
 
 
 def bank(k):
@@ -55,7 +67,71 @@ def bank(k):
 is_bank = bank
 
 
+WAKE, TURNS, SLACK = 200.0, 3, 0.0
+
+
+def arrange(ops):
+    n = len(ops)
+    lastw, readers, sent = {}, {}, {}
+    pre, post = [set() for o in ops], [[] for o in ops]
+    for i, o in enumerate(ops):
+        for k in o["r"] + o["w"]:
+            if k in lastw:
+                pre[i].add(lastw[k])
+        for k in o["w"]:
+            pre[i].update(readers.get(k, []))
+        if o["f"] is None:
+            pre[i].add(sent[o["sem"][0][1:]])
+        elif o["sem"] is not None and o["sem"][0][0] == "l":
+            sent[o["sem"][0][1:]] = i
+        pre[i].discard(i)
+        for j in pre[i]:
+            post[j].append(i)
+        for k in o["r"]:
+            readers.setdefault(k, []).append(i)
+        for k in o["w"]:
+            lastw[k] = i
+            readers[k] = []
+
+    def gap(j, i):
+        a, b = ops[j], ops[i]
+        soft = a["q"] == b["q"] and a["sem"] is None and b["sem"] is None and (a["q"] == "t" or not set(a["w"]) & set(b["r"]) - set(b["w"]))
+        return a["late"] + (0.0 if soft or b["f"] is None else WAKE)
+
+    def pack(order, before, wait, first):
+        at, busy = [0.0] * n, {}
+        for i in order:
+            c = ops[i]["cost"]
+            x = max([first(i)] + [at[j] + ops[j]["cost"] + wait(j, i) for j in before[i]])
+            if c > 0:
+                row = busy.setdefault(ops[i]["q"], [])
+                k = len(row)
+                while k > 0 and row[k - 1][1] > x:
+                    k -= 1
+                while k < len(row) and row[k][0] < x + c - SLACK:
+                    x = max(x, row[k][1])
+                    k += 1
+                row.insert(k, (x, x + c))
+            at[i] = x
+        return at
+
+    order = list(range(n))
+    for turn in range(TURNS):
+        at = pack(order, pre, gap, lambda i: 0.0)
+        place = {j: k for k, j in enumerate(order)}
+        order.sort(key=lambda i: (-(at[i] + ops[i]["cost"]), -place[i]))
+        at = pack(order, post, lambda j, i: gap(i, j), lambda i: ops[i]["late"])
+        place = {j: k for k, j in enumerate(order)}
+        order.sort(key=lambda i: (-(at[i] + ops[i]["cost"]), -place[i]))
+    at = pack(order, pre, gap, lambda i: 0.0)
+    place = {j: k for k, j in enumerate(order)}
+    order.sort(key=lambda i: (at[i], place[i]))
+    return [ops[i] for i in order]
+
+
 def emit(g, T, ops):
+    if ARRANGE:
+        ops = arrange(ops)
     Q = {"v": g.vector, "s": g.scalar, "t": g.tensor, "g": g, "y": g.sync}
     lastw, readers, need, seen = {}, {}, [], {}
     for i, o in enumerate(ops):
@@ -65,9 +141,9 @@ def emit(g, T, ops):
                 deps.add((lastw[k], not bank(k)))
         for k in o["w"]:
             if k in lastw:
-                deps.add((lastw[k], not (bank(k) or (k in PARTS and not readers[k]))))
+                deps.add((lastw[k], not (RELAX or k in o["r"] and bank(k) or (k in PARTS and not readers[k]))))
             for j in readers.get(k, []):
-                deps.add((j, not bank(k)))
+                deps.add((j, not (RELAX or k in o["r"] and bank(k))))
         best = {}
         for j, hard in deps:
             p = ops[j]
@@ -124,50 +200,66 @@ def rank_program(g, core, T, topo):
     ops, nd = [], [0]
     v, s, pe = g.vector, g.scalar, g.tensor
 
-    def op(q, f, r, w, sem=None, dma=False):
+    def op(q, f, r, w, sem=None, dma=False, cost=64 * CYC, late=0.0):
         r, w = r.split(), w.split()
         for k in list(r):
             if is_bank(k):
                 w.append(k)
-        ops.append({"q": q, "f": f, "r": r, "w": w, "sem": sem, "dma": dma})
+        ops.append({"q": q, "f": f, "r": r, "w": w, "sem": sem, "dma": dma, "cost": cost if f else 0.0, "late": late})
 
-    def dma(q, out, in_, r, w):
+    def size(x):
+        n = 1
+        for d in x.shape[1:]:
+            n *= d
+        return n
+
+    LISTS = set("o1a o1b o2a o2b lw le ofl0 ofl1 ofs ew off0 ofe0 ofe1".split())
+
+    def price(out, a, r, w, rate=1.0):
+        if LISTS & set(r.split()) and w[:3] not in ("off", "fil"):
+            if w.split()[0] in ("cp0", "cp1", "twa", "lwin", "lwv", "Da"):
+                return 55.0 + SCA * CYC * size(a)
+            return 55.0 + GA * CYC * size(out)
+        return CYC * max(64.0, rate * size(out))
+
+    def dma(q, out, in_, r, w, behind=0):
         e = g.sync if q == "y" else g.scalar
-        op(q, lambda: e.dma_start(out, in_), r, w, ("dm%d" % nd[0], 16), True)
+        op(q, lambda: e.dma_start(out, in_), r, w, ("dm%d" % nd[0], 16), True, 60.0, 1200.0 + 128 * 4 * (size(out) + behind) / 300.0)
         nd[0] += 1
 
     def ts(out, in0, s1, o0, r, w, s2=None, o1=None):
         if o1 is None:
-            op("v", lambda: v.tensor_scalar(out, in0, s1, None, o0), r, w)
+            op("v", lambda: v.tensor_scalar(out, in0, s1, None, o0), r, w, cost=price(out, in0, r, w))
         else:
-            op("v", lambda: v.tensor_scalar(out, in0, s1, s2, o0, o1), r, w)
+            op("v", lambda: v.tensor_scalar(out, in0, s1, s2, o0, o1), r, w, cost=price(out, in0, r, w))
 
     def tt(out, a, b, o, r, w):
-        op("v", lambda: v.tensor_tensor(out, a, b, o), r, w)
+        op("v", lambda: v.tensor_tensor(out, a, b, o), r, w, cost=price(out, b, r, w, 1.0 if any(is_bank(k) for k in r.split()) else 2.0))
 
     def cp(out, a, r, w):
-        op("v", lambda: v.tensor_copy(out, a), r, w)
+        op("v", lambda: v.tensor_copy(out, a), r, w, cost=price(out, a, r, w))
 
     def scan(out, d0, d1, o0, o1, r, w, first=0.0):
-        op("v", lambda: v.tensor_tensor_scan(out, d0, d1, first, o0, o1), r, w)
+        op("v", lambda: v.tensor_tensor_scan(out, d0, d1, first, o0, o1), r, w, cost=price(out, d0, r, w))
 
     def ms(out, c, w):
-        op("v", lambda: v.memset(out, c), "", w)
+        op("v", lambda: v.memset(out, c), "", w, cost=price(out, out, "", w))
 
     def act(out, a, r, w, func=None, scale=None, bias=None):
         fn = AF.Copy if func is None else func
+        c = price(out, a, r, w) + (1300.0 if fn == AF.Silu and bias is not None else 0.0)
         if scale is None:
-            op("s", lambda: s.activation(out, a, fn), r, w)
+            op("s", lambda: s.activation(out, a, fn), r, w, cost=c)
         elif bias is not None:
-            op("s", lambda: s.activation(out, a, fn, bias=bias, scale=scale), r, w)
+            op("s", lambda: s.activation(out, a, fn, bias=bias, scale=scale), r, w, cost=c)
         else:
-            op("s", lambda: s.activation(out, a, fn, scale=scale), r, w)
+            op("s", lambda: s.activation(out, a, fn, scale=scale), r, w, cost=c)
 
     def mm(out, l, rh, r, w, start=False, stop=False):
-        op("t", lambda: pe.matmul(out, l, rh, start, stop), r, w)
+        op("t", lambda: pe.matmul(out, l, rh, start, stop), r, w, cost=PEC * max(64, size(out)))
 
     def iota(out, pat, base, cmul, w, r=""):
-        op("g", lambda: g.iota(out, pat, base, cmul, allow_small_or_imprecise_dtypes=True), r, w)
+        op("g", lambda: g.iota(out, pat, base, cmul, allow_small_or_imprecise_dtypes=True), r, w, cost=130.0 + 2 * CYC * size(out))
 
     def sel(r):
         return T.zz[:, 15 - r:143 - r]
@@ -175,6 +267,7 @@ def rank_program(g, core, T, topo):
     Dw = T.D[:, 0:DW]
     DK = "Da Dm Dz Dj"
     col = lambda i: T.col[:, i:i + 1]
+    HX = {name: T.hx[:, i, :] for i, name in enumerate("hq hh hl hn h1 hm".split())}
 
     def slot_list():
         scan(T.fcs[:], T.r4[:], T.fre[:], A.mult, A.add, "r4 fre", "fcs")
@@ -186,12 +279,12 @@ def rank_program(g, core, T, topo):
                     mm(T.p5[:, 16 + 4 * u:20 + 4 * u], T[m][:], T.fre[:, 4 * w:4 * w + 4], m + " fre", "p5")
                 mm(T.p5[:, 16 + 4 * u:20 + 4 * u], T.bo[:], T.fcs[:, 4 * w:4 * w + 4], "bo fcs", "p5", stop=(w == 2))
 
-    dma("s", T.b2t[:, 0:P], T.b2[:, 0:P], "", "b2a")
-    dma("s", T.b1t[:, 0:P], T.b1[:, 0:P], "", "b1a")
-    dma("y", T.D[:, 0:V // 2], T.dist[:, 0:V // 2], "", "Da Dm")
-    dma("y", T.D[:, V // 2:V], T.dist[:, V // 2:V], "", "Dz Dm2")
+    dma("s", T.b2t[:, 0:P], T.b2[:, 0:P], "", "b2a", V * 5 // 8)
+    dma("s", T.b1t[:, 0:P], T.b1[:, 0:P], "", "b1a", V * 5 // 8)
+    dma("y", T.D[:, 0:V // 2], T.dist[:, 0:V // 2], "", "Da Dm", V // 2)
+    dma("y", T.D[:, V // 2:V], T.dist[:, V // 2:V], "", "Dz Dm2", V // 2)
     dma("y", T.b1t[:, P:U], T.b1[:, P:U], "Da Dz", "b1b")
-    dma("y", T.b2t[:, P:U], T.b2[:, P:U], "", "b2b")
+    dma("y", T.b2t[:, P:U], T.b2[:, P:U], "Da Dz", "b2b")
 
     op("g", lambda: g.iota(T.ip[:, 0:1], [[0, 1]], 0, 1), "", "ip0")
     iota(T.cm[:], [[0, 16], [1, 16]], 0, 0, "cm")
@@ -206,20 +299,30 @@ def rank_program(g, core, T, topo):
     iota(T.nz[:], [[0, S]], 0, 0, "nz0 nz1 nz2")
     iota(T.d4[:, 3::4], [[0, 64]], 0, 0, "d4")
     iota(T.w0[:, 0:S], [[0, S]], 0, 0, "tr0")
-    ms(T.D[:, J:WALL], 0.0, "Dj0")
+    ms(T.D[:, J:DW], 0.0, "Dj0")
     ms(T.one[:], 1.0, "one")
     tt(col(2), col(0), col(1), A.subtract, "c0 c1", "c2")
     ts(col(4), col(1), 0.0, A.is_equal, "c1", "c4")
     ts(col(5), col(1), 1.0, A.is_equal, "c1", "c5", -15.0, A.mult)
     ts(col(6), col(1), 2.0, A.mult, "c1", "c6", 256.0, A.add)
     ts(col(7), col(1), 4.0, A.mult, "c1", "c7", 768.0, A.add)
-    ts(col(8), col(1), -4096.0, A.mult, "c1", "c8", -129.0 * 4096, A.add)
+    ts(col(8), col(1), -4096.0, A.mult, "c1", "c8", -128.0 * 4096, A.add)
     ts(col(13), col(1), -2.0, A.mult, "c1", "c13", -256.0, A.add)
     ts(col(14), col(1), -4.0, A.mult, "c1", "c14", -768.0, A.add)
     ts(T.tmp[:], T.cm[:, 0:16], col(1), A.is_equal, "cm c1", "tmp", -4096.0, A.mult)
     ts(col(3), col(2), 15.0, A.add, "c2", "c3")
-    ts(col(9), col(4), float(MARK + 1), A.mult, "c4", "c9", (MARK - 1536) / 4096.0, A.add)
-    act(T.ckw[:], T.cm[:], "cm", "ckw", AF.Identity, -4096.0, 15.0 * 4096)
+    ts(col(9), col(4), float(MARK + 1), A.mult, "c4", "c9", (MARK - 1536) / 4096.0 - 1536, A.add)
+    if not TRANS:
+        act(T.sk[:], T.cm[:], "cm", "ckw", AF.Identity, -4096.0, 15.0 * 4096)
+    ts(T.ip[:, 2:3], T.ip[:, 0:1], 4, A.logical_shift_right, "ip0", "ip2", 1, A.bitwise_and)
+    cp(col(19), T.ip[:, 2:3], "ip2", "c19")
+    ts(col(20), col(19), 0.0, A.is_equal, "c19", "c20")
+    ts(col(21), col(0), 16.0, A.add, "c0", "c21")
+    ts(col(22), col(0), -16.0, A.add, "c0", "c22")
+    for par in range(2):
+        for half in range(2):
+            ts(T.lc[:, 2 * par + half, :], T.i128[:, 0:128], col((0, 22, 21, 0)[2 * par + half]), A.is_equal, "i128 c0 c19 c20 c21 c22", "lc",
+               col(20 - half), A.mult)
     act(T.cka[:], T.cm[:], "cm c8", "cka", AF.Identity, 0.0, col(8))
     ts(T.eye[:], T.i128[:, 0:128], col(0), A.is_equal, "i128 c0", "eye")
     ts(T.bo[:], T.gi[:], col(2), A.is_equal, "gi c2", "bo")
@@ -239,7 +342,8 @@ def rank_program(g, core, T, topo):
     ts(T.rs[:], T.cm[:], 0.0, A.not_equal, "cm", "rs")
     tt(T.mgt[:], T.tri[:], T.bo[:], A.subtract, "tri bo", "mgt")
     slot_list()
-    op("v", lambda: v.memset(T.D[:, WALL:DW], 1e29), "Dj0", "Dj")
+    op("v", lambda: v.memset(T.D[:, WALL:MARK], 1e29), "Dj0", "Dj")
+    ms(T.onef[:], 1.0, "onef")
     ms(T.b1t[:, DUM:EXT], WALL, "b1d")
     ms(T.b2t[:, DUM:EXT], WALL, "b2d")
     ms(T.bp[:, DUM:EXT], 1.0, "bpd")
@@ -251,11 +355,11 @@ def rank_program(g, core, T, topo):
         act(T.mul4[:, q::4], T.cm[:, 0:64], "cm", "mul4_%d" % q, AF.Identity, 0.0, c)
     act(T.cf1[:], T.cm[:, 0:16], "cm c6", "cf1", AF.Identity, 0.0, col(6))
     act(T.ce1[:], T.cm[:, 0:48], "cm c7", "ce1", AF.Identity, 0.0, col(7))
-    cp(T.o2[:], T.b2t[:, 0:P], "b2a", "o2")
-    cp(T.o1[:], T.b1t[:, 0:P], "b1a", "o1")
-    for name, c in (("hq", 4096.0), ("hh", 15.0), ("hl", 61440.0), ("hn", -61440.0)):
-        ts(T[name][:], T.bo[:], c, A.mult, "bo", name)
-    for q, c in enumerate((20992.0, 245760.0, 53760.0)):
+    cp(T.o2[:], T.b2t[:, 0:P], "b2a", "o2a o2b")
+    cp(T.o1[:], T.b1t[:, 0:P], "b1a", "o1a o1b")
+    for name, c in (("hq", 4096.0), ("hh", 15.0), ("hl", 61440.0), ("hn", -61440.0), ("h1", 1.0), ("hm", -4096.0)):
+        ts(HX[name], T.bo[:], c, A.mult, "bo", name)
+    for q, c in enumerate((20992.0, 368640.0, 53760.0)):
         ts(col(10 + q), col(4), c, A.mult, "c4 c5", "k%d" % q, col(5) if q == 1 else 0.0, A.add)
     for q in range(3):
         act(T.pca[:, 64 * q:64 * q + 64], T.cm[:, 0:64], "cm k%d" % q, "pca", AF.Identity, 0.0, col(10 + q))
@@ -275,24 +379,37 @@ def rank_program(g, core, T, topo):
     ts(T.own[:], T.cm[:, 0:12], 16.0, A.mult, "cm c1", "own0", col(1), A.add)
     tt(T.th[:, 192:256], T.th[:, 64:128], T.th[:, 128:192], A.add, "th2 th3", "th4")
 
-    def output_constants():
-        ts(col(15), col(5), 1.0 / 15, A.mult, "c5", "c15")
-        for name, c in (("h1", 1.0), ("hm", -4096.0), ("hf", -224.0), ("hfa", -3360.0)):
-            ts(T[name][:], T.bo[:], c, A.mult, "bo", name)
-        ts(T.kb[:, 0:1], col(4), 16384.0, A.mult, "c4 c15", "kb", col(15), A.add)
-        ts(T.kb[:, 1:2], col(4), 3584.0, A.mult, "c4", "kc")
+    ts(col(15), col(5), 1.0 / 15, A.mult, "c5", "c15")
+    act(T.bq[:], T.bo[:], "bo", "bq", AF.Identity, 4096.0)
+    ts(col(16), col(4), 24576.0, A.mult, "c4 c15", "kb", col(15), A.add)
+    ts(col(17), col(4), 3584.0, A.mult, "c4", "kc")
+    act(T.m4[:], T.dg[:, 0:H], "dg", "m4", AF.Identity, -4.0, 4.0)
+    ms(T.lt[:, 0:16], 0.25, "lt")
+    scan(T.lt[:, 16:32], T.lt[:, 0:16], T.nz[:, 0:16], A.mult, A.add, "lt nz0", "lt2", 4.0 ** 16 / 2)
+    tt(T.lt[:, 0:16], T.lt[:, 16:32], T.dg[:, 0:16], A.mult, "lt2 dg", "lt")
+    op("v", lambda: v.tensor_reduce(col(18), T.lt[:, 0:16], AXX, A.add), "lt", "c18")
+    act(T.lwin[:, 0:P], T.cm[:], "cm", "lwin", AF.Silu, 0.0, float(DUM))
 
+    ts(T.own2[:], T.cm[:, 0:16], 8.0, A.mult, "cm c1", "own3", col(1), A.add)
+    ts(T.own2[:], T.own2[:], 2.0, A.mult, "own3", "own2")
     ts(T.jk[:], T.jk[:], float(J), A.add, "jk0", "jk")
     ts(T.own[:], T.own[:], 320.0, A.add, "own0", "own")
     ts(T.wc[:, 4:8], T.wc[:, 0:4], -1.0, A.mult, "wc", "nwc")
 
 
     def pack(a, b, r, w):
-        ts(T.bp[:, a:b], T.b2t[:, a:b], 2560.0, A.add, r, w + "x", 1.0 / 4096, A.mult)
-        tt(T.bp[:, a:b], T.bp[:, a:b], T.b1t[:, a:b], A.add, r + " " + w + "x", w)
+        ts(T.p1[:, 0:b - a], T.b2t[:, a:b], -1536.0 - 1535 * 4096, A.add, r, "p1 own_p1", 1.0 / 4096, A.mult)
+        tt(T.bp[:, a:b], T.p1[:, 0:b - a], T.b1t[:, a:b], A.add, r + " p1 own_p1", w)
 
 
     pack(0, P, "b1a b2a", "bpa")
+    act(T.at[:, 0:P], T.pos[:, 0:P], "pos", "at0", AF.Identity, 1.0 / 4096, -1536.0 / 4096 - 1536)
+    for q in range(3):
+        act(T.thr[:, q::3], T.th[:, 192:256], "th4 th", "thr")
+    act(T.mka[:], T.dg[:, 0:S], "dg", "mka", AF.Identity, 1048576.0, -1048576.0)
+    act(T.e1k[:], T.eye[:], "eye", "e1k", AF.Identity, 1024.0)
+    act(T.dflag[:], T.eye[:], "eye c14", "dflag", AF.Identity, col(14))
+    act(T.mx[:], T.dg[:], "dg", "mx", AF.Identity, 20000.0, -10000.0)
 
     def slot_list_end(step):
         if step == 0:
@@ -301,16 +418,15 @@ def rank_program(g, core, T, topo):
             ts(T.ofs[:], T.ofs32[:], -320.0, A.add, "ofs32", "ofs")
 
     def planes(src, n, r):
-        ts(T.h32[:, 0:n], src(), MAG, A.add, r, "h32", MAG, A.subtract)
-        ts(T.h16[:, 0:n], src(), MAG, A.add, r, "h16", MAG + 1024.0, A.subtract)
-        ts(T.q16[:, 0:n], src(), 0.5, A.min, r, "q16")
-        tt(T.l16[:, 0:n], src(), T.h32[:, 0:n], A.subtract, r + " h32", "l16")
+        ts(T.h16[:, 0:n], src(), MAG, A.add, r, "h16", MAG, A.subtract)
+        ts(T.q16[:, 0:n], src(), -1535.5, A.min, r, "q16", 1536.0, A.add)
+        tt(T.l16[:, 0:n], src(), T.h16[:, 0:n], A.subtract, r + " h16", "l16")
 
     def rows(outs, a, b, bank, stop):
-        mm(outs[1], T.hh[:], T.h16[:, a:b], "hh h16", bank[1])
-        mm(outs[0], T.hq[:], T.q16[:, a:b], "hq q16", bank[0], stop=stop and bank[0] != bank[2])
-        mm(outs[2], T.hn[:], T.q16[:, a:b], "hn q16", bank[2])
-        mm(outs[2], T.hl[:], T.l16[:, a:b], "hl l16", bank[2], stop=stop)
+        mm(outs[1], HX["hh"], T.h16[:, a:b], "hh h16", bank[1])
+        mm(outs[0], HX["hq"], T.q16[:, a:b], "hq q16", bank[0], stop=stop and bank[0] != bank[2])
+        mm(outs[2], HX["hn"], T.q16[:, a:b], "hn q16", bank[2])
+        mm(outs[2], HX["hl"], T.l16[:, a:b], "hl l16", bank[2], stop=stop)
 
     eng_b, eng_a = topo.engines(core, before), topo.engines(core, after)
     half_b = eng_b[0::2]
@@ -326,123 +442,158 @@ def rank_program(g, core, T, topo):
         tra, trb = ("tr0", "tr1") if t % 2 == 0 else ("tr1", "tr0")
         cpa = "cp%d" % (t % 2)
         last = t == RO - 1
-        op("g", lambda wa=wa: g.affine_select(wa[:, S:2 * S], T.cpd[:], [[0, S]], A.is_ge, 0.0, 0, 0), "cpd", cpa)
-        iota(T.tw[:, V - H:V], [[0, H]], 0, 0, "twz")
-        iota(T.tw[:, 0:U], [[0, U]], 0, 0, "twa")
-        if not last:
-            iota(T.lwin[:, 0:P], [[0, P]], DUM, 0, "lwin")
-        else:
-            iota(T.zb[:], [[0, 384]], 0, 0, "zb")
-            op("g", lambda wb=wb: g.affine_select(wb[:, S:2 * S], T.cpd[:], [[0, S]], A.is_ge, 0.0, 0, 0), "cpd", "cp%d" % (1 - t % 2))
+        op("g", lambda wa=wa: g.affine_select(wa[:, S:2 * S], T.cpd[:], [[0, S]], A.is_ge, 0.0, 0, 0), "cpd", cpa, cost=540.0)
         dk = DK + (" Dm2" if t == 0 else "")
-        cuts = (0, 16, 40, 64, 128, 192, XL, XM, 256)
+        wide = U if t < 3 else EXT
+        tab = lambda x: "%sa %sb %sd lw" % (x, x, x) + (" %sc" % x) * (t >= 3)
+        part = lambda b: "a" if b <= 64 else "b"
+        sums = lambda j: " ".join("sm_%d" % i for i in range(len(CUTS) - 1) if CUTS[i] // 64 == j)
+        adds = [0]
 
         def gath(i):
-            a, b = cuts[i], cuts[i + 1]
-            act(T.g2[:, 16 * a:16 * b], Dw.indirect(T.o2[:, a:b]), dk + " o2", "g2_%d" % i)
+            a, b = CUTS[i], CUTS[i + 1]
+            (cp if i == 0 and t in OWN else act)(T.g2[:, 16 * a:16 * b], Dw.indirect(T.o2[:, a:b]), dk + " o2" + part(b), "g2_%d" % i)
 
         def add(i):
-            a, b = cuts[i], cuts[i + 1]
+            a, b = CUTS[i], CUTS[i + 1]
             tt(T.sm[:, 16 * a:16 * b], Dw.indirect(T.o1[:, a:b]), T.g2[:, 16 * a:16 * b], A.add,
-               dk + " o1 g2_%d" % i, "sm_%d" % i)
-
-        def rep(a, b, bk3):
-            src = T.D if t == 0 else T.dl
-            for q in range(4):
-                act(T[bk3][:, q:4 * (b - a):4], src[:, a:b], dk if t == 0 else "dl", bk3)
-
-        def compare(j):
-            a, b = 64 * j, 64 * j + 64
-            bk3 = ("p6", "p3", "p7")[j]
-            keys = ("sm_0 sm_1 sm_2", "sm_3", "sm_4")[j]
-            for q in range(4):
-                tt(T.cmp[:, a:b, q::4], T[bk3][:, 0:256], T.sm[:, 16 * a + q:16 * b:4], A.is_gt, bk3 + " " + keys, "cmp_%d" % j)
-            for r in range(16):
-                mm(T.p0[:, a:b], sel(r), T.cmp[:, a + r:b:16, :], "zz cmp_%d" % j, "p0", stop=(j == 2 and r == 15))
-            for k in range(16):
-                mm(T.p1[:, a:b], sel(k), T.cmp[:, a:b, k], "zz cmp_%d" % j, "p1")
-
-        mm(T.p0[:, 0:192], T.eye[:], T.ckw[:, 0:192], "eye ckw", "p0", start=True)
-        mm(T.p1[:, 0:192], T.eye[:], T.cka[:, 0:192], "eye cka", "p1", start=True)
-        mm(T.p4[:, 0:64], T.eye[:], T.cka[:, 0:64], "eye cka", "p4", start=True)
-        gath(0)
-        gath(1)
-        gath(2)
-        if t > 0:
-            if t >= 3:
-                ts(T.le[:], T.lt2[:], 0.25, A.add, "lt2", "le")
-                add(0)
-                cp(T.dl[:], Dw.indirect(T.le[:]), dk + " le", "dl")
-                slot_list_end(0)
-            else:
-                cp(T.dl[:], Dw.indirect(T.lw[:]), dk + " lw", "dl")
-                slot_list_end(0)
-                add(0)
-        else:
-            slot_list_end(0)
-            add(0)
-        rep(0, 64, "p6")
-        gath(3)
-        add(1)
-        slot_list_end(1)
-        add(2)
-        compare(0)
-        rep(64, 128, "p3")
+               dk + " o1%s g2_%d" % (part(b), i), "sm_%d" % i)
 
         def both(i):
-            a, b = cuts[i], cuts[i + 1]
+            a, b = CUTS[i], CUTS[i + 1]
             gath(i)
-            act(T.sm[:, 16 * a:16 * b], Dw.indirect(T.o1[:, a:b]), dk + " o1", "sm_%d" % i)
+            act(T.sm[:, 16 * a:16 * b], Dw.indirect(T.o1[:, a:b]), dk + " o1" + part(b), "sm_%d" % i)
             op("g", lambda: g.dma_start(T.sm[:, 16 * a:16 * b], T.g2[:, 16 * a:16 * b], accum_op=A.add), "g2_%d sm_%d" % (i, i),
-               "sm_%d" % i, ("%s%d" % (("ac", "ad")[i - 6], t), 16), True)
+               "sm_%d" % i, ("a%s%d" % ("abcd"[adds[0]], t), 16), True, 700.0, 1300.0 + 60.0 * (b - a))
+            adds[0] += 1
 
-        both(6)
-        gath(4)
-        both(7)
-        add(3)
-        compare(1)
-        rep(128, 256, "p7")
-        gath(5)
-        add(4)
-        compare(2)
-        if t > 0:
-            act(T.bl[:], T.bp[:, 0:(512, U, EXT, EXT)[t - 1]].indirect(T.lw[:]), "bpa bpb bpc bpe bpd lw", "bl")
-            act(T.al[:], T.at[:, 0:EXT].indirect(T.lw[:]), "at0 at lw", "al")
-            bl, al, blk, alk = T.bl, T.al, "bl", "al"
-            if last:
-                for q, (c, k) in enumerate(((col(10), "k0"), (T.kb[:, 0:1], "kb"), (T.kb[:, 1:2], "kc"))):
-                    act(T.pct[:, S * q:S * q + S], T.cm[:, 0:S], "cm " + k, "pct", AF.Identity, 0.0, c)
-            if t == 2:
-                act(T.bp[:, U:DUM], T.bp[:, 0:DUM - U], "bpa bpb", "bpe")
-        else:
-            bl, al, blk, alk = T.bp, T.at, "bpa", "at0"
-            act(T.at[:, 0:P], T.pos[:, 0:P], "pos", "at0", AF.Identity, 1.0 / 4096, -1536.0 / 4096)
-            for q in range(3):
-                act(T.thr[:, q::3], T.th[:, 192:256], "th4 th", "thr")
-            act(T.mka[:], T.dg[:, 0:S], "dg", "mka", AF.Identity, 1048576.0, -1048576.0)
-            act(T.e1k[:], T.eye[:], "eye", "e1k", AF.Identity, 1024.0)
-            act(T.dflag[:], T.eye[:], "eye c14", "dflag", AF.Identity, col(14))
-            act(T.mx[:], T.dg[:], "dg", "mx", AF.Identity, 20000.0, -10000.0)
-            act(T.at[:, P:U], T.pos[:, P:U], "pos", "at", AF.Identity, 1.0 / 4096, -1536.0 / 4096)
-            act(T.at[:, U:EXT], T.pos[:, U:EXT], "pos", "at", AF.Identity, 1.0 / 4096, (-1536.0 - U) / 4096)
-        add(5)
+        def compare(j, ks=range(16)):
+            a, b = 64 * j, 64 * j + 64
+            out, bk = (T.p1[:, a:b], "p1") if j < 3 else (T.p4[:, 0:64], "p4")
+            step = STREAM[j == 3]
+            for k0 in range(ks[0], ks[-1] + 1, step):
+                key = "cmp_%d_%d" % (j, k0)
+                for k in range(k0, k0 + step):
+                    tt(T.cmp[:, a:b, k], T.p7[:, a:b], T.sm[:, 16 * a + k:16 * b:16], A.is_gt, "p7 " + sums(j), key)
+                if not TRANS and k0 + step == 16:
+                    keys = " ".join("cmp_%d_%d" % (j, x) for x in range(0, 16, step))
+                    for r in range(16):
+                        mm(T.p0[:, a:b], sel(r), T.cmp[:, a + r:b:16, :], "zz " + keys, "p0", stop=(j >= 2 and r == 15))
+                for k in range(k0, k0 + step):
+                    mm(out, sel(k), T.cmp[:, a:b, k], "zz " + key, bk, stop=(TRANS and j >= 2 and k == 15))
+
+        if not TRANS:
+            mm(T.p0[:, 0:192], T.eye[:], T.sk[:, 0:192], "eye ckw", "p0", start=True)
+        mm(T.p1[:, 0:192], T.eye[:], T.cka[:, 0:192], "eye cka", "p1", start=True)
+        mm(T.p4[:, 0:64], T.eye[:], T.cka[:, 0:64], "eye cka", "p4", start=True)
+        if last:
+            for h, bk in enumerate(("p0", "p2") if TRANS else ("p3", "p6")):
+                for r in range(16):
+                    mm(T[bk][:, r:384:16], T.wt[:, r, :], T.fls[:, 24 * h:24 * h + 24], "wt fls flsb", bk, start=True, stop=True)
+
+        def entries():
+            if t > 0:
+                act(T.bl[:], T.bp[:, 0:(512, U, EXT, EXT)[t - 1]].indirect(T.lw[:]), "bpa bpb bpc bpe bpd lw", "bl")
+                act(T.al[:], T.at[:, 0:EXT].indirect(T.lw[:]), "at0 at lw", "al")
+
+        def edges():
+            ts(T.lt[:, 0:16], T.lm[:], U - 0.5, A.is_ge, "lm", "lt", -float(U), A.mult)
+            tt(T.lt[:, 16:32], T.lt[:, 0:16], T.lm[:], A.add, "lt lm", "lt2")
+            ts(T.le[:], T.lt[:, 16:32], 0.25, A.add, "lt2", "le")
+
+        def fills():
+            if t in (0, 3):
+                iota(T.tw[:, V - H:V], [[0, H]], 0, 0, "twz")
+            if not last:
+                iota(T.tw[:, 0:U], [[0, U]], 0, 0, "twa")
+                if t > 0:
+                    iota(T.lwin[:, 0:P], [[0, P]], DUM, 0, "lwin")
+                if t >= 2:
+                    iota(T.lwv[:, 0:P], [[0, P]], DUM, 0, "lwv")
+            else:
+                iota(T.lwin[:, V - H:V], [[0, H]], 0, 0, "lwin")
+
+        later = {"o2": lambda: cp(T.o2[:, 64:P], T.b2t[:, 0:wide].indirect(T.lw[:, 4:16]), tab("b2"), "o2b"),
+                 "o1": lambda: cp(T.o1[:, 64:P], T.b1t[:, 0:wide].indirect(T.lw[:, 4:16]), tab("b1"), "o1b"),
+                 "le": edges if t >= 3 else lambda: None,
+                 "dl": lambda: (act if DLS else cp)(T.dl[:], Dw.indirect((T.le if t >= 3 else T.lw)[:]), dk + " le lw", "dl")}
+        always = {"dp": lambda: (act if t > 0 else cp)(T.p7[:, 0:P], (T.dl if t > 0 else T.D)[:, 0:P], "dl" if t > 0 else dk, "p7"),
+                  "s0": lambda: slot_list_end(0), "s1": lambda: slot_list_end(1), "bl": entries}
+        fills()
+        for step in LOOK:
+            if step in always:
+                always[step]()
+            elif step in later:
+                if t > 0:
+                    later[step]()
+            else:
+                {"g": gath, "a": add, "b": both, "c": compare}[step[0]](int(step[1:]))
+        bl, al, blk, alk = (T.bl, T.al, "bl", "al") if t > 0 else (T.bp, T.at, "bpa", "at0")
+        if t == 0:
+            act(T.at[:, P:U], T.pos[:, P:U], "pos", "at", AF.Identity, 1.0 / 4096, -1536.0 / 4096 - 1536)
+            act(T.at[:, U:EXT], T.pos[:, U:EXT], "pos", "at", AF.Identity, 1.0 / 4096, (-1536.0 - U) / 4096 - 1536)
+        if t == 2:
+            act(T.bp[:, U:DUM], T.bp[:, 0:DUM - U], "bpa bpb", "bpe")
+        if last:
+            for h, bk in enumerate(("p0", "p2") if TRANS else ("p3", "p6")):
+                act(T.lwin[:, 384 * h:384 * h + 384], T[bk][:, 0:384], bk, "lwin", AF.Copy, -1.0 / 4096)
+            for q, (c, k) in enumerate(((col(10), "k0"), (col(16), "kb"), (col(17), "kc"))):
+                act(T.pct[:, S * q:S * q + S], T.cm[:, 0:S], "cm " + k, "pct", AF.Identity, 0.0, c)
         span = ((0, 12), (12, 16))
         rank_ps, rank_k = (T.p2[:, 0:12], T.p5[:, 32:36]), ("p2", "p5")
-        win_ps, win_k = (T.p1, T.p4), ("p1", "p4")
+        win_ps, win_k = (T.p0, T.p6), ("p0", "p6")
+        top_ps, top_k = (T.p6[:, 256:268], T.p3[:, 0:4]), ("p6", "p3")
 
         def best(h):
             a, b = span[h]
-            scan(T.sc[:, 16 * a:16 * b], T.rs[:, 16 * a:16 * b], T.p0[:, 16 * a:16 * b], A.mult, A.max, "rs p0", "sc%d" % h)
+            if h == 0:
+                act(T.sk[:, 0:S], T.p1[:, 0:S], "p1", "sk0")
+                op("v", lambda: v.transpose(T.skt[:], T.sk[:, 0:S]), "sk0", "skt", cost=96 * CYC)
+                op("v", lambda: v.tensor_tensor_scan(T.s32[:, 0:S], T.rs[:, 0:S], T.skt[:], 0.0, A.mult, A.max), "rs skt", "sc0", cost=96 * CYC)
+            else:
+                op("v", lambda: v.transpose(T.sc[:, 0:64], T.p4[:, 0:64]), "p4", "sct")
+                act(T.sk[:, S:P], T.p4[:, 0:64], "p4", "sk1")
+                scan(T.s32[:, S:P], T.rs[:, 0:64], T.sc[:, 0:64], A.mult, A.max, "rs sct", "sc1")
+            for half in range(2):
+                for par in range(2):
+                    mm(top_ps[h][:, half::2], T.lc[:, 2 * par + half, :], T.s32[:, 16 * a + 16 * par + 15:16 * b:32], "lc sc%d" % h, top_k[h],
+                       start=(par == 0), stop=(par == 1))
             mm(rank_ps[h], T.eye[:], T.cf1[:, a:b], "eye cf1", rank_k[h], start=True)
             mm(rank_ps[h], T.eye[:], T.c32[:, a:b], "eye c32", rank_k[h])
 
         def propose(h):
             a, b = span[h]
-            top = T.sc[:, 16 * a + 15:16 * b:16]
-            ts(T.scb[:, a:b], top, 1.0 / 4096, A.mult, "sc%d" % h, "scb%d" % h, -144.0, A.add)
-            ts(T.prop[:, a:b], top, 143.5 * 4096, A.is_gt, "sc%d" % h, "prop%d" % h)
-            for r in range(16):
-                mm(win_ps[h][:, r:16 * (b - a):16], T.wt[:, r, :], T.scb[:, a:b], "wt scb%d" % h, win_k[h], stop=(r == 15))
+            ts(T.prop[:, a:b], top_ps[h], 2048.0, A.is_gt, top_k[h], "prop%d" % h)
+            if h == 0:
+                ts(T.scb[:, a:b], top_ps[h], 1.0 / 4096, A.mult, top_k[h], "scb")
+            else:
+                for c in range(4):
+                    ts(T.xs[:, 16 * c:16 * c + 16], T.dg[:, 0:16], top_ps[h][:, c:c + 1], A.mult, "dg " + top_k[h], "xs", 1.0 / 4096, A.mult)
+            mm(win_ps[h][:, 0:16 * (b - a)], T.eye[:], T.sk[:, 16 * a:16 * b], "eye sk%d" % h, win_k[h], start=True)
+            if h == 0:
+                for r in range(16):
+                    mm(win_ps[h][:, r:S:16], T.wt[:, r, :], T.scb[:, a:b], "wt scb", win_k[h], stop=(r == 15))
+            else:
+                mm(win_ps[h][:, 0:64], HX["hm"], T.xs[:], "hm xs", win_k[h], stop=True)
+
+        if not TRANS:
+            win_ps, win_k = (T.p1, T.p4), ("p1", "p4")
+
+            def best(h):
+                a, b = span[h]
+                scan(T.sc[:, 16 * a:16 * b], T.rs[:, 16 * a:16 * b], T.p0[:, 16 * a:16 * b], A.mult, A.max, "rs p0", "sc%d" % h)
+                if h == 0:
+                    mm(T.p0[:, 192:P], T.eye[:], T.sk[:, 192:P], "eye ckw", "p0", start=True)
+                mm(rank_ps[h], T.eye[:], T.cf1[:, a:b], "eye cf1", rank_k[h], start=True)
+                mm(rank_ps[h], T.eye[:], T.c32[:, a:b], "eye c32", rank_k[h])
+
+            def propose(h):
+                a, b = span[h]
+                top = T.sc[:, 16 * a + 15:16 * b:16]
+                ts(T.scb[:, a:b], top, 1.0 / 4096, A.mult, "sc%d" % h, "scb%d" % h, -143.0, A.add)
+                ts(T.prop[:, a:b], top, 143.5 * 4096, A.is_gt, "sc%d" % h, "prop%d" % h)
+                for r in range(16):
+                    mm(win_ps[h][:, r:16 * (b - a):16], T.wt[:, r, :], T.scb[:, a:b], "wt scb%d" % h, win_k[h], stop=(r == 15))
 
         def order(h):
             a, b = span[h]
@@ -463,36 +614,25 @@ def rank_program(g, core, T, topo):
             tt(wa[:, S:S + 1024].indirect(T.ofl[:, a:b]), T.yy[:, 16 * a:16 * b], al[:, 16 * a:16 * b], A.max,
                "ofl%d yy%d %s" % (h, h, alk), cpa)
 
-        def tail(q):
-            tt(T.cmp[:, 192:P, q::4], T.p7[:, 256:512], T.sm[:, 16 * 192 + q:16 * P:4], A.is_gt, "p7 sm_5 sm_6 sm_7", "cmp_3%d" % q)
-
-        def tail_counts(q):
-            for k in range(q, 16, 4):
-                mm(T.p4[:, 0:64], sel(k), T.cmp[:, 192:P, k], "zz cmp_3%d" % q, "p4")
-
         best(0)
-        mm(T.p0[:, 192:P], T.eye[:], T.ckw[:, 192:P], "eye ckw", "p0", start=True)
+        compare(3, range(0, 4))
         propose(0)
-        tail(0)
         order(0)
-        tail(1)
-        tail(2)
-        for q in range(3):
-            tail_counts(q)
-        tail(3)
-        for r in range(16):
-            mm(T.p0[:, 192:P], sel(r), T.cmp[:, 192 + r:P:16, :], "zz cmp_30 cmp_31 cmp_32 cmp_33", "p0", stop=(r == 15))
-        tail_counts(3)
+        compare(3, range(4, 16))
+        if TRANS:
+            best(1)
         winners(0)
-        place(0, 0, 6)
-        best(1)
+        place(0, 0, 4)
+        if not TRANS:
+            best(1)
         if t == 1:
             dma("y", T.b1t[:, U:DUM], T.b1[:, 0:DUM - U], "sc1", "b1c")
-            dma("y", T.b2t[:, U:DUM], T.b2[:, 0:DUM - U], "", "b2c")
+            dma("y", T.b2t[:, U:DUM], T.b2[:, 0:DUM - U], "sc1", "b2c")
         propose(1)
         order(1)
-        place(0, 6, 12)
+        place(0, 4, 8)
         winners(1)
+        place(0, 8, 12)
         mm(T.p0[:, 0:S], T.eye[:], T.mka[:], "eye mka", "p0", start=True)
         mm(T.p0[:, 0:S], T.bo[:], T.pca[:], "bo pca", "p0")
         mm(T.p1[:, 0:S], T.bo[:], T.pcb[:], "bo pcb", "p1", start=True)
@@ -512,71 +652,88 @@ def rank_program(g, core, T, topo):
             at = starts[c] + q * n
             mm(T.p2[:, 48 * c:S], T.bo[:], T.eq[:, at:at + n], "bo " + key, "p2", stop=stop)
 
+        EQV, early = EQVS[t], EARLY[t]
+
+        def lengths():
+            ts(T.ew[:], T.ra[:, 15::16], 1.0 / 15, A.mult, "ra", "ew", 0.25, A.add)
+            for q in range(3):
+                act(T.d4[:, q::4], Dw.indirect(T.ew[:, 4 * q:4 * q + 4]), DK + " ew", "d4")
+
+        if early:
+            lengths()
         for c in (2, 3):
+            if c in EQV:
+                continue
             n, at = S - 48 * c, starts[c] - starts[2]
             for q in range(3):
                 x = 64 * q + 16 * c + 15
                 act(T.ab[:, at + q * n:at + q * n + n], T.p3[:, 48 * c - 96:96], "p3 ra", "ab%d" % c, AF.Abs, -1.0, T.ra[:, x:x + 1])
             act(T.eq[:, starts[c]:starts[c] + 3 * n], T.ab[:, at:at + 3 * n], "wc nwc ab%d" % c, "eq%d" % c, AF.Relu,
                 T.wc[:, 4 + c:5 + c], T.wc[:, c:c + 1])
-        for c in (0, 1):
-            for q in range(3):
-                n, x = S - 48 * c, 64 * q + 16 * c + 15
-                at = starts[c] + q * n
-                ts(T.eq[:, at:at + n], T.p1[:, 48 * c:S], T.ra[:, x:x + 1], A.is_equal, "p1 ra wc", "eq%d%d" % (c, q), T.wc[:, c:c + 1], A.mult)
-                if (c, q) == (1, 1):
-                    for k in range(3):
-                        weigh(2, k, "eq2")
-                weigh(c, q, "eq%d%d" % (c, q))
-        for q in range(3):
-            weigh(3, q, "eq3", q == 2)
-        ts(T.ew[:], T.ra[:, 15::16], 1.0 / 15, A.mult, "ra", "ew", 0.25, A.add)
-        scan(T.ts[:], T.r48[:], T.p2[:, 0:S], A.mult, A.max, "r48 p2", "ts")
-        for c in range(4):
-            ts(T.off[:, c::4], T.ew[:, c::4], T.ts[:, 48 * c + 47:48 * c + 48], A.max, "ew ts jk", "off%d" % c, T.jk[:, c:c + 1], A.min)
-        OFF = "off0 off1 off2 off3"
-        lst = lambda q: T.off[:, 4 * q:4 * q + 4]
-        for q in range(3):
-            act(T.d4[:, q::4], Dw.indirect(lst(q)), DK + " " + OFF, "d4")
-
-        def touch():
-            for q in range(3):
-                cp(T.tw[:, 0:DW].indirect(lst(q)), T.one[:], "one " + OFF, "twa twz")
-            op("g", lambda t=t: g.remote_dma(T.rt[:, t, :], T.tw[:, V - H:V], T.sem["rt%d" % t], T.sem["lt%d" % t],
-                                            topo.addr(after)[1], topo.addr(after)[0], bits(eng_a)), "twz", "", ("lt%d" % t, len(eng_a)))
-            op("g", None, "", "rt%d" % t, ("rt%d" % t, n_in_t))
-
-        if not last:
-            touch()
+        if not early:
+            lengths()
         zero = ([("Da", 0)] if rank > (rank - 1) % n_ranks else []) + ([("Dz", V - H)] if rank > (rank + 1) % n_ranks else [])
         for k, a in zero:
             act(T.D[:, a:a + H], T.D[:, a:a + H], k + " d4", k, AF.Copy, 0.0)
         if zero:
-            act(T.d3[:], Dw.indirect(T.off[:]), DK + " " + OFF, "d3")
+            act(T.d3[:], Dw.indirect(T.ew[:]), DK + " ew", "d3")
             base, bk = (lambda q: T.d3[:, 64 * q:64 * q + 64]), "d3"
         else:
             base, bk = (lambda q: T.d4[:, q::4]), "d4"
-        late = [] if t < 2 else ([0, 1, 2] if t == 2 else [t])
-        mm(T.p3[:, 0:48], T.eye[:], T.fls[:], "eye fls flsb", "p3", start=True)
-        for x in late[:-1]:
+        for c in EQV:
+            for q in range(3):
+                n, x = S - 48 * c, 64 * q + 16 * c + 15
+                at = starts[c] + q * n
+                ts(T.eq[:, at:at + n], T.p1[:, 48 * c:S], T.ra[:, x:x + 1], A.is_equal, "p1 ra wc", "eq%d%d" % (c, q), T.wc[:, c:c + 1], A.mult)
+                weigh(c, q, "eq%d%d" % (c, q), len(EQV) == 4 and (c, q) == (EQV[-1], 2))
+        rest = [c for c in (2, 3) if c not in EQV]
+        for c in rest:
+            for q in range(3):
+                weigh(c, q, "eq%d" % c, (c, q) == (rest[-1], 2))
+        nzu, nk = T.nz[:, 64 * u:64 * u + 64], "nz%d" % u
+        theta = lambda: scan(T.th[:], T.mul4[:], T.d4[:], A.mult, A.subtract, "mul4_0 mul4_1 mul4_2 mul4_3 d4", "th")
+        delta = lambda: tt(T.dlt[:], T.th[:, 3::4], nzu, A.max, "th " + nk, "dlt")
+        if early:
+            theta()
+        scan(T.ts[:], T.r48[:], T.p2[:, 0:S], A.mult, A.max, "r48 p2", "ts")
+        if early == 2:
+            delta()
+        for c in range(4):
+            ts(T.off[:, c::4], T.ew[:, c::4], T.ts[:, 48 * c + 47:48 * c + 48], A.max, "ew ts jk", "off%d" % c, T.jk[:, c:c + 1], A.min)
+        OFF = "off0 off1 off2 off3"
+        lst = lambda q: T.off[:, 4 * q:4 * q + 4]
+
+        def stands():
+            ts(T.sw[:], T.ts[:, 47::48], 0.0, A.is_equal, "ts", "sw", -1.0 / 4096, A.mult)
             for r in range(16):
-                mm(T.p3[:, 0:8], sel(r), T.rt[:, x, r::16], "zz rt%d" % x, "p3")
+                mm(T.p0[:, r:64:16], T.wt[:, r, :], T.sw[:], "wt sw", "p0", start=True, stop=True)
+
+        def touch():
+            win, one, keys = (T.lwin, T.onef, "lwin") if last else (T.tw, T.one, "twa twz")
+            for q in range(3):
+                cp(win[:, 0:DW].indirect(lst(q)), one[:], "one onef " + OFF, keys)
+                if q == 0 and early == 1:
+                    delta()
+            if t >= 2:
+                land = T.rf[:] if last else T.rt[:, t - 2, :]
+                op("g", lambda t=t: g.remote_dma(land, win[:, V - H:V], T.sem["rt%d" % t], T.sem["lt%d" % t],
+                                                topo.addr(after)[1], topo.addr(after)[0], bits(eng_a)), keys.split()[-1], "",
+                   ("lt%d" % t, len(eng_a)), cost=300.0, late=1500.0)
+                op("g", None, "", "rt%d" % t, ("rt%d" % t, n_in_t))
 
         def own_touch():
+            mm(T.p3[:, 0:48], T.eye[:], T.fls[:], "eye fls flsb", "p3", start=True)
             for r in range(16):
                 mm(T.p3[:, 0:48], sel(r), T.tw[:, r:U:16], "zz twa", "p3", stop=(r == 15))
 
         if not last:
+            touch()
             own_touch()
 
         def their_touch():
-            mm(T.p6[:, 0:8], T.eye[:], T.fown[:], "eye fown", "p6", start=True)
-            for r in range(16):
-                mm(T.p6[:, 0:8], sel(r), T.rt[:, t, r::16], "zz rt%d" % t, "p6", stop=(r == 15))
+            scan(T.sx[:], T.m4[:], T.rt[:, t - 2, :], A.mult, A.add, "m4 rt%d" % t, "sx")
+            tt(T.fl[:, na:na + 8], T.sx[:, 15::16], T.fown[:], A.is_gt, "sx fown", "flb")
 
-        nzu, nk = T.nz[:, 64 * u:64 * u + 64], "nz%d" % u
-        scan(T.th[:], T.mul4[:], T.d4[:], A.mult, A.subtract, "mul4_0 mul4_1 mul4_2 mul4_3 d4", "th")
-        tt(T.dlt[:], T.th[:, 3::4], nzu, A.max, "th " + nk, "dlt")
         c0, nc = 8 * (t + 1), (24, 32, 48, 48, 48)[t]
         na = min(nc, 48 - c0)
 
@@ -598,41 +755,61 @@ def rank_program(g, core, T, topo):
         def compact(h, a, b, home):
             ps, pk, ps2, pk2 = (T.p4, "p4", T.p3, "p3") if h == 0 else (T.p7, "p7", T.p6, "p6")
             cp(T.ofe[:, a:b], ps[:, a:b], pk, "ofe%d" % h)
-            act(T.lwin[:, 0:4608].indirect(T.ofe[:, a:b]), T.pos[:, 16 * (c0 + a):16 * (c0 + b)], "pos ofe%d" % h, "lwin", AF.Silu)
+            m = SPLIT[t][h]
+            act(T.lwin[:, 0:4608].indirect(T.ofe[:, a:m]), T.pos[:, 16 * (c0 + a):16 * (c0 + m)], "pos ofe%d" % h, "lwin", AF.Silu)
+            if t < 2:
+                ts(T.lxv[:, 15::16], T.own2[:], ps[:, m:m + 1], A.subtract, "own2 " + pk, "lxv", 16.0 * (c0 + m), A.add)
+            elif m < b:
+                cp(T.lwv[:, 0:4608].indirect(T.ofe[:, m:b]), T.pos[:, 16 * (c0 + m):16 * (c0 + b)], "pos ofe%d" % h, "lwv")
             return lambda: ts(T.fls[:, home:home + b - a], ps2[:, 64 + a:64 + b], 1024 + P - 0.5, A.is_gt, pk2, "fls" + "b" * h)
 
         def correct(q):
             tt(Dw.indirect(lst(q)), base(q), T.dlt[:], A.subtract if q == 0 else A.add, "dlt %s %s" % (bk, OFF), DK)
 
-        correct(0)
-        if not last:
-            ts(T.fl[:, 0:na], T.p3[:, c0:c0 + na], 0.0, A.is_gt, "p3", "fla")
+        def others():
             if t < 2:
                 ts(T.fls[:], T.p3[:, 0:48], 0.0, A.is_gt, "p3", "fls")
             else:
-                ts(T.fown[:], T.p3[:, 0:8], 0.0, A.is_gt, "p3", "fown")
+                ts(T.fown[:], T.p3[:, 0:8], -4e9, A.mult, "p3 c18", "fown", col(18), A.add)
                 ts(T.fl[:, na + 8:48], T.p3[:, 8:c0], 0.0, A.is_gt, "p3", "flc")
-        correct(1)
-        if not last:
-            ranks(0, 0, na, "fla")
-        correct(2)
-        if not last:
-            keep = compact(0, 0, na, c0)
+
+        if not early:
+            theta()
+            delta()
+        for step in POST[1 if early else 0]:
+            if step in "012":
+                correct(int(step))
+            elif not last:
+                {"f": lambda: ts(T.fl[:, 0:na], T.p3[:, c0:c0 + na], 0.0, A.is_gt, "p3", "fla"), "o": others,
+                 "r": lambda: ranks(0, 0, na, "fla")}[step]()
+        stands()
         op("g", lambda t=t: g.remote_dma_fused([
             RemoteDMATransfer(dst_ids=[dst(before)], dma_engine_mask=bits(half_b), remote_sem=T.sem["rd%d" % t],
                               src=T.D[:, 0:H], dst=T.rd[:, t, H:2 * H]),
             RemoteDMATransfer(dst_ids=[dst(after)], dma_engine_mask=bits(half_a), remote_sem=T.sem["rd%d" % t],
                               src=T.D[:, V - H:V], dst=T.rd[:, t, 0:H])], local_sem=T.sem["ld%d" % t]),
-           "Da Dz", "", ("ld%d" % t, len(half_a) + len(half_b)))
+           "Da Dz", "", ("ld%d" % t, len(half_a) + len(half_b)), cost=300.0, late=2000.0 + 1500.0 * (t == 0))
         op("g", None, "", "rd%d" % t, ("rd%d" % t, n_in_d))
         if last:
-            dma("y", T.yd[:, H:V // 2], T.D[:, H:V // 2], "Dm", "")
-            dma("s", T.yd[:, V // 2:V - H], T.D[:, V // 2:V - H], "Dm", "")
+            dma("y", T.yd[:, H:V // 2], T.D[:, H:V // 2], "Dm", "", V // 2)
+            dma("s", T.yd[:, V // 2:V - H], T.D[:, V // 2:V - H], "Dm", "", V // 2)
             touch()
-            own_touch()
+        else:
+            keep = compact(0, 0, na, c0)
+
+        def own_blocks():
+            act(T.p2[:, 0:H], T.D[:, 0:H], "Da", "p2")
+            act(T.p2[:, H:2 * H], T.D[:, V - H:V], "Dz", "p2")
+
+        if t != 2:
+            own_blocks()
+
+        def new_z():
+            tt(T.dm[:], T.p0[:, 0:64], T.dlt[:], A.mult, "p0 dlt", "dm")
+            tt(nzu, nzu, T.dm[:], A.subtract, "dm " + nk, nk)
 
         def forget():
-            tt(nzu, nzu, T.dlt[:], A.subtract, "dlt " + nk, nk)
+            new_z()
             ts(T.fil[:], T.ew[:, 0:4], float(V), A.is_lt, "ew", "fil")
             ts(T.gr[:], wb[:, 0:S], col(9), A.not_equal, trb + " c9", "gr")
             tt(T.blk[:], T.ts[:, 47::48], T.fil[:], A.min, "ts fil", "blk")
@@ -648,20 +825,25 @@ def rank_program(g, core, T, topo):
             slot_list()
 
         def take():
-            tt(T.D[:, 0:H], T.D[:, 0:H], T.rd[:, t, 0:H], A.add, "Da rd%d" % t, "Da")
-            tt(T.D[:, V - H:V], T.D[:, V - H:V], T.rd[:, t, H:2 * H], A.add, "Dz rd%d" % t, "Dz")
+            tt(T.D[:, 0:H], T.p2[:, 0:H], T.rd[:, t, 0:H], A.add, "p2 rd%d" % t, "Da")
+            tt(T.D[:, V - H:V], T.p2[:, H:2 * H], T.rd[:, t, H:2 * H], A.add, "p2 rd%d" % t, "Dz")
 
         if not last:
-            def next_lists():
-                scan(T.lx[:], T.mx[:], T.lwin[:, 0:P], A.max, A.min, "mx lwin", "lx")
-                ts(T.lw[:], T.lx[:, 15::16], 0.25, A.add, "lx", "lw")
-                if t >= 2:
-                    ts(T.lt[:], T.lx[:, 15::16], U - 0.5, A.is_ge, "lx", "lt", -float(U), A.mult)
-                cp(T.o2[:], T.b2t[:, 0:wide].indirect(T.lw[:]), "b2a b2b b2d lw" + " b2c" * (t >= 2), "o2")
-                if t >= 2:
-                    tt(T.lt2[:], T.lt[:], T.lx[:, 15::16], A.add, "lt lx", "lt2")
-
             wide = U if t < 2 else EXT
+            tab = lambda x: "%sa %sb %sd lw" % (x, x, x) + (" %sc" % x) * (t >= 2)
+
+            def next_lists(between):
+                if t >= 2:
+                    scan(T.lxv[:], T.mx[:], T.lwv[:, 0:P], A.max, A.min, "mx lwv", "lxv")
+                between()
+                n = 8 if t == 0 else 16
+                scan(T.lx[:, 0:16 * n], T.mx[:, 0:16 * n], T.lwin[:, 0:16 * n], A.max, A.min, "mx lwin", "lx")
+                tt(T.lm[:, 0:n], T.lx[:, 15:16 * n:16], T.lxv[:, 15:16 * n:16], A.min, "lx lxv", "lm")
+                if n < 16:
+                    ts(T.lw[:, n:16], T.lxv[:, 16 * n + 15::16], 0.25, A.add, "lxv", "lw2")
+                ts(T.lw[:, 0:n], T.lm[:, 0:n], 0.25, A.add, "lm lw2", "lw")
+                cp(T.o2[:, 0:64], T.b2t[:, 0:wide].indirect(T.lw[:, 0:4]), tab("b2"), "o2a")
+                cp(T.o1[:, 0:64], T.b1t[:, 0:wide].indirect(T.lw[:, 0:4]), tab("b1"), "o1a")
 
             if t < 2:
                 keep()
@@ -669,59 +851,50 @@ def rank_program(g, core, T, topo):
                 forget_count()
                 pack(P + 256 * t, 2 * P + 256 * t, "b1b b2b", ("bpb", "bpc")[t])
                 forget2()
-                next_lists()
+                next_lists(lambda: None)
                 take()
             else:
-                their_touch()
                 keep()
                 forget()
-                ts(T.fl[:, na:na + 8], T.p6[:, 0:8], 0.0, A.is_gt, "p6", "flb")
+                their_touch()
                 ranks(1, na, 48, "flb flc")
                 forget_count()
                 keep = compact(1, na, 48, 0)
-                keep()
-                if t == 3:
-                    output_constants()
+                if t == 2:
+                    own_blocks()
+                next_lists(keep if t == 2 else take)
+                (take if t == 2 else keep)()
                 forget2()
-                take()
-                next_lists()
-            cp(T.o1[:], T.b1t[:, 0:wide].indirect(T.lw[:]), "b1a b1b b1d lw" + " b1c" * (t >= 2), "o1")
         else:
-            forget()
-            forget_count()
-            ts(T.fown[:], T.p3[:, 0:8], 0.0, A.is_gt, "p3", "fown")
-            ts(T.fl[:, 8:48], T.p3[:, 8:48], 0.0, A.is_gt, "p3", "fla")
-            forget2()
-            take()
-            dma("y", T.yd[:, 0:H], T.D[:, 0:H], "Da", "")
-            dma("y", T.yd[:, V - H:V], T.D[:, V - H:V], "Dz", "")
-            their_touch()
+            new_z()
+            planes(lambda: wb[:, 0:S], S, trb)
             for x in range(3):
                 act(T.zo[:, x::3], T.nz[:, 64 * x:64 * x + 64], "nz%d" % x, "zo", AF.Copy, -1.0)
             dma("y", T.yz[:], T.zo[:], "zo", "")
-            slot_list_end(0)
-            slot_list_end(1)
-            ts(T.fl[:, 0:8], T.p6[:, 0:8], 0.0, A.is_gt, "p6 fla", "fl0")
-            for h in range(2):
-                bank, bk2 = (T.p6, "p6") if h == 0 else (T.p7, "p7")
-                mm(bank[:, 0:384], T.eye[:], T.zb[:], "eye zb", bk2, start=True)
-                for r in range(16):
-                    mm(bank[:, r:384:16], T.wt[:, r, :], T.fl[:, 24 * h:24 * h + 24], "wt fl0", bk2, stop=(r == 15))
-            for h in range(2):
-                act(T.fo[:, 384 * h:384 * h + 384], (T.p6 if h == 0 else T.p7)[:, 0:384], "p%d" % (6 + h), "fo", AF.Copy, -1.0 / 4096)
-            dma("s", T.yf[:], T.fo[0:128:16, :], "fo", "")
-            src, keys = (lambda: wb[:, 0:2 * S].indirect(T.ofs[:])), "ofs %s cp%d" % (trb, 1 - t % 2)
-            ts(T.f16[:], src(), col(9), A.is_equal, keys + " c9", "f16")
-            planes(src, S, keys)
-            mm(T.p0[:, 0:S], T.bo[:], T.pct[:, 0:S], "bo pct", "p0", start=True)
+            mm(T.p4[:, 0:S], T.bo[:], T.pct[:, 0:S], "bo pct", "p4", start=True)
             mm(T.p1[:, 0:2 * S], T.bo[:], T.pct[:, S:3 * S], "bo pct", "p1", start=True)
-            for m, d, o in (("hfa", "f16", 0), ("hq", "q16", 0), ("hf", "f16", 1), ("hf", "f16", 2), ("h1", "h16", 1), ("hm", "q16", 2), ("hq", "l16", 2)):
+            for m, d, o in (("h1", "h16", 1), ("hq", "q16", 0), ("hm", "q16", 2), ("hq", "l16", 2)):
                 for x in range(3):
-                    out = T.p0[:, x:S:3] if o == 0 else T.p1[:, S * (o - 1) + x:S * o:3]
-                    mm(out, T[m][:], T[d][:, 64 * x:64 * x + 64], m + " " + d, "p0" if o == 0 else "p1",
+                    out = T.p4[:, x:S:3] if o == 0 else T.p1[:, S * (o - 1) + x:S * o:3]
+                    mm(out, HX[m], T[d][:, 64 * x:64 * x + 64], m + " " + d, "p4" if o == 0 else "p1",
                        stop=(x == 2 and m == "hq"))
-            ts(T.t2[:], T.p0[:, 0:S], 1.0 / 15, A.mult, "p0", "t2", MAG, A.add)
-            act(T.t1[:, S:3 * S], T.p1[:, 0:2 * S], "p1", "t1b")
-            ts(T.t1[:, 0:S], T.t2[:], MAG, A.subtract, "t2", "t1a")
-            dma("y", T.yt[:], T.t1[0:128:16, :], "t1a t1b", "")
+            ts(T.gr[:], wb[:, 0:S], col(9), A.not_equal, trb + " c9", "gr")
+            ts(T.g0[:], nzu, 0.0, A.not_equal, nk, "g0")
+            tt(T.gr[:, 64 * u:64 * u + 64], T.gr[:, 64 * u:64 * u + 64], T.p0[:, 0:64], A.is_gt, "gr p0", "gr")
+            for x in range(3):
+                mm(T.p5[:, x:S:3], T.neye[:], T.one[:], "neye one", "p5", start=True)
+                if x == u:
+                    mm(T.p5[:, x:S:3], T.bq[:], T.g0[:], "bq g0", "p5")
+                mm(T.p5[:, x:S:3], T.bq[:], T.gr[:, 64 * x:64 * x + 64], "bq gr", "p5", stop=True)
+            act(T.t2[:, S:3 * S], T.p1[:, 0:2 * S], "p1", "t2b")
+            ts(T.t1[:, 0:S], T.p4[:, 0:S], 1.0 / 15, A.mult, "p4", "t1", MAG, A.add)
+            take()
+            dma("y", T.yd[:, 0:H], T.D[:, 0:H], "Da", "", V // 4)
+            dma("s", T.yd[:, V - H:V], T.D[:, V - H:V], "Dz", "", V // 4)
+            ts(T.t2[:, 0:S], T.t1[:, 0:S], MAG, A.subtract, "t1", "t2a")
+            for q in (1, 2, 0):
+                tt(T.t1[:, S * q:S * q + S], T.p5[:, 0:S], T.t2[:, S * q:S * q + S], A.min, "p5 t2a t2b", "t1%d" % q)
+            dma("y", T.yt[:], T.t1[0:128:16, :], "t10 t11 t12", "")
+            tt(T.lwin[:, 0:H], T.lwin[:, 0:H], T.rf[:], A.max, "lwin rt%d" % t, "lwin")
+            dma("s", T.yf[:], T.lwin[0:128:16, 0:U], "lwin", "")
     emit(g, T, ops)

@@ -7,19 +7,24 @@ V, U, H, S, P, RO = 3072, 768, 128, 192, 256, 5
 J, WALL, MARK, DW = 3072, 3136, 3144, 3152
 EXT, DUM = 1288, 1280
 MAG = 12582912.0
-CUTS = (0, 16, 40, 64, 96, 128, 160, 192, 224, 240, 256)
-LOOK = "g0 o2 g1 a0 le dl g2 a1 dp g3 o1 s0 a2 b8 g4 c0 s1 g5 b9 a3 a4 c1 g6 g7 a5 a6 c2 bl a7".split()
+CUTS = (0, 16, 40, 64, 96, 128, 160, 192, 200, 224, 240, 256)
+LOOK = "g0 o2 g1 a0 le dl g2 a1 g3 dp o1 s0 a2 g4 a3 b9 c0 s1 g5 a4 b10 a5 g6 c1 g7 g8 a6 a7 bl c2 a8".split()
 OWN = (0,)
-SPLIT = ((8,), (16,), (18, 38), (12, 34))
-EARLY = (2, 2, 0, 0, 2)
+SPLIT = ((8,), (16,), (24, 40), (16, 36))
+EARLY = (2, 2, 2, 2, 2)
+MIXED = (2, 1, 1, 1, 2)
 POST = ("0fo1r2", "01for2")
 RELAX = False
 DLS = False
 ARRANGE = True
-CYC, PEC, GA, SCA = 0.95, 0.42, 1.5, 3.5
+CYC, PEC, GA, SCA = 0.9, 0.42, 1.5, 3.5
 EQVS = tuple((0, 1, 3) if e else (0, 1) for e in EARLY)
-TRANS, STREAM = False, (16, 4)
-PARTS = "at wt pca pcb wc ab2 ab3 d4 zo pct thr msk lc xs".split() + ["cmp_%d_%d" % (j, k) for j in range(4) for k in range(16)]
+STREAM, PLACE = (4, 4), (4, 12)
+HINT = (1, 1, 1, 1, 1)
+LV, LS = " ~lv", " ~ls"
+WTV = 16
+DMA0, DMAB, REM = 900.0, 450.0, 1200.0
+PARTS = "at wt wtv m4 pca pcb wc ab2 ab3 d4 zo pct thr msk lc xs".split() + ["cmp_%d_%d" % (j, k) for j in range(4) for k in range(16)]
 F32, BF, F16, I32, U16 = "float32", "bfloat16", "float16", "int32", "uint16"
 
 
@@ -31,8 +36,8 @@ SCRATCH = {
     "D": sb(DW, F32), "b1t": sb(EXT, I32), "b2t": sb(EXT, I32), "bp": sb(EXT, F32), "at": sb(EXT, F32), "pos": sb(EXT, F32),
     "g2": sb(4096, F32), "sm": sb(4096, F32), "cmp": sb([256, 16], BF),
     "o1": sb(256, U16), "o2": sb(256, U16), "lw": sb(16, U16), "le": sb(16, U16), "lt": sb(32, F32),
-    "dl": sb(256, F32), "bl": sb(256, F32), "al": sb(256, F32), "yy": sb(256, F32), "sc": sb(256, F32),
-    "prop": sb(16, BF), "scb": sb(16, BF), "pu": sb(16, BF), "pcs": sb(24, BF), "ofl": sb(16, U16),
+    "dl": sb(256, F32), "bl": sb(256, F32), "al": sb(256, F32), "yy": sb(256, F32), "sc": sb(256, BF),
+    "prop": sb(16, BF), "pu": sb(16, BF), "pcs": sb(24, BF), "ofl": sb(16, U16),
     "w0": sb(1216, F32), "w1": sb(1216, F32), "ofs": sb(12, U16), "ofs32": sb(12, F32),
     "h16": sb(192, F16), "q16": sb(192, F16), "l16": sb(192, F16),
     "ra": sb(192, F32), "ew": sb(12, U16), "eq": sb(1440, BF), "ts": sb(192, F32), "off": sb(12, U16),
@@ -40,19 +45,19 @@ SCRATCH = {
     "sw": sb(4, BF), "dm": sb(64, F32), "g0": sb(64, BF), "onef": sb(64, F32),
     "tw": sb(DW, BF), "one": sb(64, BF), "gr": sb(192, BF), "fil": sb(4, F32), "blk": sb(4, BF),
     "fre": sb(12, BF), "fcs": sb(12, BF),
-    "fown": sb(8, F32), "sx": sb(128, BF), "m4": sb(128, BF), "fls": sb(48, BF), "fl": sb(48, BF), "fu": sb(48, BF), "lcs": sb(56, BF), "ofe": sb(48, U16),
-    "lwin": sb(4608, F32), "lwv": sb(4608, F32), "lx": sb(256, F32), "lxv": sb(256, F32), "lm": sb(16, F32),
+    "fown": sb(8, F32), "sx": sb(U + H, BF), "m4": sb(512, BF), "fls": sb(48, BF), "fl": sb(48, BF), "fu": sb(48, BF), "lcs": sb(56, BF), "ofe": sb(48, U16),
+    "lwin": sb(4608, F32), "lwv": sb(4608, F32), "lx": sb(256, F32), "lxv": sb(256, F32),
     "rd": sb([RO, 256], F32), "rt": sb([2, 128], BF), "rf": sb(128, F32),
     "zo": sb(192, F32), "t1": sb(576, F32), "t2": sb(576, F32),
     "ip": sb(8, I32), "col": sb(24, F32), "cm": sb(256, F32), "i128": sb(144, F32), "gi": sb(128, F32), "tmp": sb(16, F32), "tmp2": sb(128, F32),
     "dg": sb(256, F32), "mx": sb(256, F32), "rs": sb(256, BF), "mul4": sb(256, F32), "r4": sb(12, F32),
     "eye": sb(128, BF), "neye": sb(128, BF), "bo": sb(128, BF), "tri": sb(128, BF), "zz": sb(144, BF), "wt": sb([16, 128], BF),
     "dfill": sb(128, BF), "dflag": sb(128, BF), "e1k": sb(128, BF), "e512": sb(128, BF), "mgt": sb(128, BF), "ab": sb(432, F32),
-    "hx": sb([6, 128], F16), "lc": sb([4, 128], BF), "sk": sb(256, BF), "skt": sb(192, BF), "s32": sb(256, BF), "xs": sb(64, F16),
+    "hx": sb([6, 128], F16), "lc": sb([4, 128], BF), "ckw": sb(192, BF),
     "cka": sb(256, BF), "c32": sb(16, BF), "c64": sb(48, BF), "cf1": sb(16, BF), "ce1": sb(48, BF),
     "mka": sb(192, BF), "pca": sb(192, BF), "pcb": sb(192, BF), "pct": sb(576, BF), "wr": sb(64, F32), "thr": sb(192, BF),
     "r48": sb(192, F32), "bq": sb(128, BF),
-    "wc": sb(8, F32), "jk": sb(4, F32), "own": sb(12, F32), "own2": sb(16, F32), "cpd": sb(192, F32),
+    "wc": sb(8, F32), "jk": sb(4, F32), "own": sb(12, F32), "jd": sb(256, F32), "mxb": sb(256, BF), "bar": sb(48, F32), "cpd": sb(192, F32),
     "p0": ("psum", [128, 512], F32), "p1": ("psum", [128, 512], F32), "p2": ("psum", [128, 512], F32), "p3": ("psum", [128, 512], F32),
     "p4": ("psum", [128, 512], F32), "p5": ("psum", [128, 512], F32), "p6": ("psum", [128, 512], F32), "p7": ("psum", [128, 512], F32),
 }
@@ -67,7 +72,18 @@ def bank(k):
 is_bank = bank
 
 
-WAKE, TURNS, SLACK = 200.0, 3, 0.0
+WAKE, TURNS, SLACK, PLAY = 200.0, 3, 0.0, 0
+
+
+def hard(a, b):
+    if a["q"] != b["q"] or a["sem"] is not None or b["sem"] is not None:
+        return True
+    if a["q"] == "t":
+        return False
+    for k in a["w"]:
+        if k[0] != "~" and (k in b["r"] and not bank(k) or k in b["w"] and k not in b["r"] and k not in PARTS):
+            return True
+    return any(k in b["w"] and not (bank(k) and k in b["r"]) for k in a["r"])
 
 
 def arrange(ops):
@@ -95,8 +111,7 @@ def arrange(ops):
 
     def gap(j, i):
         a, b = ops[j], ops[i]
-        soft = a["q"] == b["q"] and a["sem"] is None and b["sem"] is None and (a["q"] == "t" or not set(a["w"]) & set(b["r"]) - set(b["w"]))
-        return a["late"] + (0.0 if soft or b["f"] is None else WAKE)
+        return a["late"] + (0.0 if b["f"] is None or not hard(a, b) else WAKE)
 
     def pack(order, before, wait, first):
         at, busy = [0.0] * n, {}
@@ -115,6 +130,43 @@ def arrange(ops):
             at[i] = x
         return at
 
+    def run(before, behind, wait, first, due):
+        at, left, ready = [0.0] * n, [len(x) for x in before], [first(i) for i in range(n)]
+        free, cand = {}, {}
+        for i in range(n):
+            if left[i] == 0:
+                cand.setdefault(ops[i]["q"], []).append(i)
+        for step in range(n):
+            now, q = min((max(free.get(q, 0.0), min(ready[i] for i in c)), q) for q, c in cand.items() if c)
+            i = min((j for j in cand[q] if ready[j] <= now), key=lambda j: (due[j], j))
+            for h in cand[q]:
+                if ready[h] > now and due[h] < due[i] and ready[h] < now + ops[i]["cost"]:
+                    go = max(now - due[i], now + ops[i]["cost"] - due[h])
+                    hold = max(ready[h] - due[h], ready[h] + ops[h]["cost"] - due[i])
+                    if hold < go:
+                        i = h
+            at[i] = max(now, ready[i])
+            cand[q].remove(i)
+            if ops[i]["cost"] > 0:
+                free[q] = at[i] + ops[i]["cost"]
+            for j in behind[i]:
+                ready[j] = max(ready[j], at[i] + ops[i]["cost"] + wait(i, j))
+                left[j] -= 1
+                if left[j] == 0:
+                    cand.setdefault(ops[j]["q"], []).append(j)
+        return at
+
+    def length(at):
+        return max(at[i] + ops[i]["cost"] + ops[i]["late"] for i in range(n))
+
+    if PLAY:
+        at = pack(list(range(n)), pre, gap, lambda i: 0.0)
+        best = (length(at), at)
+        for turn in range(PLAY):
+            back = run(post, pre, lambda j, i: gap(i, j), lambda i: ops[i]["late"], [-(at[i] + ops[i]["cost"]) for i in range(n)])
+            at = run(pre, post, gap, lambda i: 0.0, [-(back[i] + ops[i]["cost"]) for i in range(n)])
+            best = min(best, (length(at), at))
+        return [ops[i] for i in sorted(range(n), key=lambda i: (best[1][i], i))]
     order = list(range(n))
     for turn in range(TURNS):
         at = pack(order, pre, gap, lambda i: 0.0)
@@ -140,6 +192,8 @@ def emit(g, T, ops):
             if k in lastw:
                 deps.add((lastw[k], not bank(k)))
         for k in o["w"]:
+            if k[0] == "~":
+                continue
             if k in lastw:
                 deps.add((lastw[k], not (RELAX or k in o["r"] and bank(k) or (k in PARTS and not readers[k]))))
             for j in readers.get(k, []):
@@ -224,7 +278,7 @@ def rank_program(g, core, T, topo):
 
     def dma(q, out, in_, r, w, behind=0):
         e = g.sync if q == "y" else g.scalar
-        op(q, lambda: e.dma_start(out, in_), r, w, ("dm%d" % nd[0], 16), True, 60.0, 1200.0 + 128 * 4 * (size(out) + behind) / 300.0)
+        op(q, lambda: e.dma_start(out, in_), r, w, ("dm%d" % nd[0], 16), True, 60.0, DMA0 + 128 * 4 * (size(out) + behind) / DMAB)
         nd[0] += 1
 
     def ts(out, in0, s1, o0, r, w, s2=None, o1=None):
@@ -309,28 +363,22 @@ def rank_program(g, core, T, topo):
     ts(col(8), col(1), -4096.0, A.mult, "c1", "c8", -128.0 * 4096, A.add)
     ts(col(13), col(1), -2.0, A.mult, "c1", "c13", -256.0, A.add)
     ts(col(14), col(1), -4.0, A.mult, "c1", "c14", -768.0, A.add)
-    ts(T.tmp[:], T.cm[:, 0:16], col(1), A.is_equal, "cm c1", "tmp", -4096.0, A.mult)
+    ts(T.tmp[:], T.cm[:, 0:16], col(1), A.is_equal, "cm c1", "tmp", -1.0, A.mult)
     ts(col(3), col(2), 15.0, A.add, "c2", "c3")
     ts(col(9), col(4), float(MARK + 1), A.mult, "c4", "c9", (MARK - 1536) / 4096.0 - 1536, A.add)
-    if not TRANS:
-        act(T.sk[:], T.cm[:], "cm", "ckw", AF.Identity, -4096.0, 15.0 * 4096)
-    ts(T.ip[:, 2:3], T.ip[:, 0:1], 4, A.logical_shift_right, "ip0", "ip2", 1, A.bitwise_and)
-    cp(col(19), T.ip[:, 2:3], "ip2", "c19")
-    ts(col(20), col(19), 0.0, A.is_equal, "c19", "c20")
-    ts(col(21), col(0), 16.0, A.add, "c0", "c21")
-    ts(col(22), col(0), -16.0, A.add, "c0", "c22")
-    for par in range(2):
-        for half in range(2):
-            ts(T.lc[:, 2 * par + half, :], T.i128[:, 0:128], col((0, 22, 21, 0)[2 * par + half]), A.is_equal, "i128 c0 c19 c20 c21 c22", "lc",
-               col(20 - half), A.mult)
+    act(T.ckw[:], T.cm[:, 0:S], "cm", "ckw", AF.Identity, -4096.0, -128.0 * 4096)
     act(T.cka[:], T.cm[:], "cm c8", "cka", AF.Identity, 0.0, col(8))
     ts(T.eye[:], T.i128[:, 0:128], col(0), A.is_equal, "i128 c0", "eye")
     ts(T.bo[:], T.gi[:], col(2), A.is_equal, "gi c2", "bo")
     ts(T.dg[:], T.cm[:], col(1), A.is_equal, "cm c1", "dg")
+    act(T.mx[:], T.dg[:], "dg", "mx", AF.Identity, 20000.0, -10000.0)
     act(T.cpd[:], T.cm[:, 0:S], "cm c9", "cpd", AF.Identity, 0.0, col(9))
     act(T.e512[:], T.eye[:], "eye", "e512", AF.Identity, 512.0)
     for r in range(16):
-        act(T.wt[:, r, :], T.bo[:], "bo tmp", "wt", AF.Identity, T.tmp[:, r:r + 1])
+        if r < WTV:
+            op("v", lambda r=r: v.tensor_scalar(T.wt[:, r, :], T.bo[:], T.tmp[:, r:r + 1], None, A.mult), "bo tmp", "wtv")
+        else:
+            act(T.wt[:, r, :], T.bo[:], "bo tmp", "wt", AF.Identity, T.tmp[:, r:r + 1])
     act(T.neye[:], T.eye[:], "eye", "neye", AF.Identity, -1.0)
     act(T.dfill[:], T.eye[:], "eye c13", "dfill", AF.Identity, col(13))
     ts(T.tmp2[:], T.cm[:, 0:128], col(1), A.is_gt, "cm c1", "tmp2")
@@ -341,6 +389,8 @@ def rank_program(g, core, T, topo):
     op("v", lambda: v.memset(T.r4[:, 0::4], 0.0), "r4", "r4")
     ts(T.rs[:], T.cm[:], 0.0, A.not_equal, "cm", "rs")
     tt(T.mgt[:], T.tri[:], T.bo[:], A.subtract, "tri bo", "mgt")
+    for c in range(4):
+        op("g", lambda c=c: g.affine_select(T.lc[:, c, :], T.tri[:], [[-1, 128]], A.not_equal, -32.0 * c, 0, 1), "tri", "lc", cost=390.0)
     slot_list()
     op("v", lambda: v.memset(T.D[:, WALL:MARK], 1e29), "Dj0", "Dj")
     ms(T.onef[:], 1.0, "onef")
@@ -383,15 +433,17 @@ def rank_program(g, core, T, topo):
     act(T.bq[:], T.bo[:], "bo", "bq", AF.Identity, 4096.0)
     ts(col(16), col(4), 24576.0, A.mult, "c4 c15", "kb", col(15), A.add)
     ts(col(17), col(4), 3584.0, A.mult, "c4", "kc")
-    act(T.m4[:], T.dg[:, 0:H], "dg", "m4", AF.Identity, -4.0, 4.0)
+    for h in range(2):
+        act(T.m4[:, P * h:P * h + P], T.dg[:], "dg", "m4", AF.Identity, -4.0, 4.0)
     ms(T.lt[:, 0:16], 0.25, "lt")
     scan(T.lt[:, 16:32], T.lt[:, 0:16], T.nz[:, 0:16], A.mult, A.add, "lt nz0", "lt2", 4.0 ** 16 / 2)
     tt(T.lt[:, 0:16], T.lt[:, 16:32], T.dg[:, 0:16], A.mult, "lt2 dg", "lt")
     op("v", lambda: v.tensor_reduce(col(18), T.lt[:, 0:16], AXX, A.add), "lt", "c18")
-    act(T.lwin[:, 0:P], T.cm[:], "cm", "lwin", AF.Silu, 0.0, float(DUM))
+    act(T.lwin[:, 0:P], T.cm[:], "cm", "lwin" + LS, AF.Silu, 0.0, float(DUM))
 
-    ts(T.own2[:], T.cm[:, 0:16], 8.0, A.mult, "cm c1", "own3", col(1), A.add)
-    ts(T.own2[:], T.own2[:], 2.0, A.mult, "own3", "own2")
+    act(T.p6[:, 0:P], T.pos[:, 0:P], "pos c1", "p6", AF.Identity, 1.0, col(1))
+    tt(T.jd[:], T.p6[:, 0:P], T.mx[:], A.min, "p6 mx", "jd")
+    ms(T.fl[:], 1.0, "fla flb flc")
     ts(T.jk[:], T.jk[:], float(J), A.add, "jk0", "jk")
     ts(T.own[:], T.own[:], 320.0, A.add, "own0", "own")
     ts(T.wc[:, 4:8], T.wc[:, 0:4], -1.0, A.mult, "wc", "nwc")
@@ -409,7 +461,7 @@ def rank_program(g, core, T, topo):
     act(T.mka[:], T.dg[:, 0:S], "dg", "mka", AF.Identity, 1048576.0, -1048576.0)
     act(T.e1k[:], T.eye[:], "eye", "e1k", AF.Identity, 1024.0)
     act(T.dflag[:], T.eye[:], "eye c14", "dflag", AF.Identity, col(14))
-    act(T.mx[:], T.dg[:], "dg", "mx", AF.Identity, 20000.0, -10000.0)
+    act(T.mxb[:], T.dg[:], "dg", "mxb", AF.Identity, 16384.0, -8192.0)
 
     def slot_list_end(step):
         if step == 0:
@@ -452,17 +504,18 @@ def rank_program(g, core, T, topo):
 
         def gath(i):
             a, b = CUTS[i], CUTS[i + 1]
-            (cp if i == 0 and t in OWN else act)(T.g2[:, 16 * a:16 * b], Dw.indirect(T.o2[:, a:b]), dk + " o2" + part(b), "g2_%d" % i)
+            own = i == 0 and t in OWN
+            (cp if own else act)(T.g2[:, 16 * a:16 * b], Dw.indirect(T.o2[:, a:b]), dk + " o2" + part(b), "g2_%d" % i + (LV if own else LS))
 
         def add(i):
             a, b = CUTS[i], CUTS[i + 1]
             tt(T.sm[:, 16 * a:16 * b], Dw.indirect(T.o1[:, a:b]), T.g2[:, 16 * a:16 * b], A.add,
-               dk + " o1%s g2_%d" % (part(b), i), "sm_%d" % i)
+               dk + " o1%s g2_%d" % (part(b), i), "sm_%d" % i + LV)
 
         def both(i):
             a, b = CUTS[i], CUTS[i + 1]
             gath(i)
-            act(T.sm[:, 16 * a:16 * b], Dw.indirect(T.o1[:, a:b]), dk + " o1" + part(b), "sm_%d" % i)
+            act(T.sm[:, 16 * a:16 * b], Dw.indirect(T.o1[:, a:b]), dk + " o1" + part(b), "sm_%d" % i + LS)
             op("g", lambda: g.dma_start(T.sm[:, 16 * a:16 * b], T.g2[:, 16 * a:16 * b], accum_op=A.add), "g2_%d sm_%d" % (i, i),
                "sm_%d" % i, ("a%s%d" % ("abcd"[adds[0]], t), 16), True, 700.0, 1300.0 + 60.0 * (b - a))
             adds[0] += 1
@@ -474,31 +527,33 @@ def rank_program(g, core, T, topo):
             for k0 in range(ks[0], ks[-1] + 1, step):
                 key = "cmp_%d_%d" % (j, k0)
                 for k in range(k0, k0 + step):
-                    tt(T.cmp[:, a:b, k], T.p7[:, a:b], T.sm[:, 16 * a + k:16 * b:16], A.is_gt, "p7 " + sums(j), key)
-                if not TRANS and k0 + step == 16:
+                    tt(T.cmp[:, a:b, k], T.p7[:, a:b], T.sm[:, 16 * a + k:16 * b:16], A.is_gt, "p7 " + sums(j), key + LV * (j < 3))
+                if k0 + step == 16:
                     keys = " ".join("cmp_%d_%d" % (j, x) for x in range(0, 16, step))
                     for r in range(16):
-                        mm(T.p0[:, a:b], sel(r), T.cmp[:, a + r:b:16, :], "zz " + keys, "p0", stop=(j >= 2 and r == 15))
+                        mm(T.p0[:, a:b] if j < 3 else top_ps[1], sel(r), T.cmp[:, a + r:b:16, :], "zz " + keys, top_k[j // 3],
+                           stop=(j >= 2 and r == 15))
                 for k in range(k0, k0 + step):
-                    mm(out, sel(k), T.cmp[:, a:b, k], "zz " + key, bk, stop=(TRANS and j >= 2 and k == 15))
+                    mm(out, sel(k), T.cmp[:, a:b, k], "zz " + key, bk)
 
-        if not TRANS:
-            mm(T.p0[:, 0:192], T.eye[:], T.sk[:, 0:192], "eye ckw", "p0", start=True)
+        top_ps, top_k = (T.p0[:, 0:S], T.p6[:, 384:448]), ("p0", "p6")
+        mm(top_ps[0], T.eye[:], T.ckw[:], "eye ckw", "p0", start=True)
         mm(T.p1[:, 0:192], T.eye[:], T.cka[:, 0:192], "eye cka", "p1", start=True)
         mm(T.p4[:, 0:64], T.eye[:], T.cka[:, 0:64], "eye cka", "p4", start=True)
         if last:
-            for h, bk in enumerate(("p0", "p2") if TRANS else ("p3", "p6")):
+            for h, bk in enumerate(("p3", "p2")):
                 for r in range(16):
                     mm(T[bk][:, r:384:16], T.wt[:, r, :], T.fls[:, 24 * h:24 * h + 24], "wt fls flsb", bk, start=True, stop=True)
+        mm(top_ps[1], T.eye[:], T.ckw[:, 0:64], "eye ckw", "p6", start=True)
 
         def entries():
             if t > 0:
-                act(T.bl[:], T.bp[:, 0:(512, U, EXT, EXT)[t - 1]].indirect(T.lw[:]), "bpa bpb bpc bpe bpd lw", "bl")
-                act(T.al[:], T.at[:, 0:EXT].indirect(T.lw[:]), "at0 at lw", "al")
+                act(T.bl[:], T.bp[:, 0:(512, U, EXT, EXT)[t - 1]].indirect(T.lw[:]), "bpa bpb bpc bpe bpd lw", "bl" + LS)
+                act(T.al[:], T.at[:, 0:EXT].indirect(T.lw[:]), "at0 at lw", "al" + LS)
 
         def edges():
-            ts(T.lt[:, 0:16], T.lm[:], U - 0.5, A.is_ge, "lm", "lt", -float(U), A.mult)
-            tt(T.lt[:, 16:32], T.lt[:, 0:16], T.lm[:], A.add, "lt lm", "lt2")
+            ts(T.lt[:, 0:16], T.lx[:, 15::16], U - 0.5, A.is_ge, "lx", "lt", -float(U), A.mult)
+            tt(T.lt[:, 16:32], T.lt[:, 0:16], T.lx[:, 15::16], A.add, "lt lx", "lt2")
             ts(T.le[:], T.lt[:, 16:32], 0.25, A.add, "lt2", "le")
 
         def fills():
@@ -517,7 +572,7 @@ def rank_program(g, core, T, topo):
                  "o1": lambda: cp(T.o1[:, 64:P], T.b1t[:, 0:wide].indirect(T.lw[:, 4:16]), tab("b1"), "o1b"),
                  "le": edges if t >= 3 else lambda: None,
                  "dl": lambda: (act if DLS else cp)(T.dl[:], Dw.indirect((T.le if t >= 3 else T.lw)[:]), dk + " le lw", "dl")}
-        always = {"dp": lambda: (act if t > 0 else cp)(T.p7[:, 0:P], (T.dl if t > 0 else T.D)[:, 0:P], "dl" if t > 0 else dk, "p7"),
+        always = {"dp": lambda: (act if t > 0 else cp)(T.p7[:, 0:P], (T.dl if t > 0 else T.D)[:, 0:P], "dl" if t > 0 else dk, "p7" + (LS if t > 0 else LV)),
                   "s0": lambda: slot_list_end(0), "s1": lambda: slot_list_end(1), "bl": entries}
         fills()
         for step in LOOK:
@@ -535,75 +590,44 @@ def rank_program(g, core, T, topo):
         if t == 2:
             act(T.bp[:, U:DUM], T.bp[:, 0:DUM - U], "bpa bpb", "bpe")
         if last:
-            for h, bk in enumerate(("p0", "p2") if TRANS else ("p3", "p6")):
-                act(T.lwin[:, 384 * h:384 * h + 384], T[bk][:, 0:384], bk, "lwin", AF.Copy, -1.0 / 4096)
+            for h, bk in enumerate(("p3", "p2")):
+                act(T.lwin[:, 384 * h:384 * h + 384], T[bk][:, 0:384], bk, "lwin", AF.Copy, -1.0)
             for q, (c, k) in enumerate(((col(10), "k0"), (col(16), "kb"), (col(17), "kc"))):
                 act(T.pct[:, S * q:S * q + S], T.cm[:, 0:S], "cm " + k, "pct", AF.Identity, 0.0, c)
         span = ((0, 12), (12, 16))
         rank_ps, rank_k = (T.p2[:, 0:12], T.p5[:, 32:36]), ("p2", "p5")
-        win_ps, win_k = (T.p0, T.p6), ("p0", "p6")
-        top_ps, top_k = (T.p6[:, 256:268], T.p3[:, 0:4]), ("p6", "p3")
+        win_ps, win_k = (T.p1, T.p4), ("p1", "p4")
 
         def best(h):
             a, b = span[h]
-            if h == 0:
-                act(T.sk[:, 0:S], T.p1[:, 0:S], "p1", "sk0")
-                op("v", lambda: v.transpose(T.skt[:], T.sk[:, 0:S]), "sk0", "skt", cost=96 * CYC)
-                op("v", lambda: v.tensor_tensor_scan(T.s32[:, 0:S], T.rs[:, 0:S], T.skt[:], 0.0, A.mult, A.max), "rs skt", "sc0", cost=96 * CYC)
-            else:
-                op("v", lambda: v.transpose(T.sc[:, 0:64], T.p4[:, 0:64]), "p4", "sct")
-                act(T.sk[:, S:P], T.p4[:, 0:64], "p4", "sk1")
-                scan(T.s32[:, S:P], T.rs[:, 0:64], T.sc[:, 0:64], A.mult, A.max, "rs sct", "sc1")
-            for half in range(2):
-                for par in range(2):
-                    mm(top_ps[h][:, half::2], T.lc[:, 2 * par + half, :], T.s32[:, 16 * a + 16 * par + 15:16 * b:32], "lc sc%d" % h, top_k[h],
-                       start=(par == 0), stop=(par == 1))
+            scan(T.sc[:, 16 * a:16 * b], T.rs[:, 16 * a:16 * b], top_ps[h], A.mult, A.max, "rs " + top_k[h], "sc%d" % h)
             mm(rank_ps[h], T.eye[:], T.cf1[:, a:b], "eye cf1", rank_k[h], start=True)
-            mm(rank_ps[h], T.eye[:], T.c32[:, a:b], "eye c32", rank_k[h])
+            mm(rank_ps[h], T.eye[:], T.c32[:, 0:b - a], "eye c32", rank_k[h])
 
         def propose(h):
             a, b = span[h]
-            ts(T.prop[:, a:b], top_ps[h], 2048.0, A.is_gt, top_k[h], "prop%d" % h)
-            if h == 0:
-                ts(T.scb[:, a:b], top_ps[h], 1.0 / 4096, A.mult, top_k[h], "scb")
-            else:
-                for c in range(4):
-                    ts(T.xs[:, 16 * c:16 * c + 16], T.dg[:, 0:16], top_ps[h][:, c:c + 1], A.mult, "dg " + top_k[h], "xs", 1.0 / 4096, A.mult)
-            mm(win_ps[h][:, 0:16 * (b - a)], T.eye[:], T.sk[:, 16 * a:16 * b], "eye sk%d" % h, win_k[h], start=True)
-            if h == 0:
-                for r in range(16):
-                    mm(win_ps[h][:, r:S:16], T.wt[:, r, :], T.scb[:, a:b], "wt scb", win_k[h], stop=(r == 15))
-            else:
-                mm(win_ps[h][:, 0:64], HX["hm"], T.xs[:], "hm xs", win_k[h], stop=True)
-
-        if not TRANS:
-            win_ps, win_k = (T.p1, T.p4), ("p1", "p4")
-
-            def best(h):
-                a, b = span[h]
-                scan(T.sc[:, 16 * a:16 * b], T.rs[:, 16 * a:16 * b], T.p0[:, 16 * a:16 * b], A.mult, A.max, "rs p0", "sc%d" % h)
-                if h == 0:
-                    mm(T.p0[:, 192:P], T.eye[:], T.sk[:, 192:P], "eye ckw", "p0", start=True)
-                mm(rank_ps[h], T.eye[:], T.cf1[:, a:b], "eye cf1", rank_k[h], start=True)
-                mm(rank_ps[h], T.eye[:], T.c32[:, a:b], "eye c32", rank_k[h])
-
-            def propose(h):
-                a, b = span[h]
-                top = T.sc[:, 16 * a + 15:16 * b:16]
-                ts(T.scb[:, a:b], top, 1.0 / 4096, A.mult, "sc%d" % h, "scb%d" % h, -143.0, A.add)
-                ts(T.prop[:, a:b], top, 143.5 * 4096, A.is_gt, "sc%d" % h, "prop%d" % h)
-                for r in range(16):
-                    mm(win_ps[h][:, r:16 * (b - a):16], T.wt[:, r, :], T.scb[:, a:b], "wt scb%d" % h, win_k[h], stop=(r == 15))
+            top = T.sc[:, 16 * a + 15:16 * b:16]
+            act(T.prop[:, a:b], top, "sc%d" % h, "prop%d" % h, AF.Sign)
+            for r in range(16):
+                mm(win_ps[h][:, r:16 * (b - a):16], T.wt[:, r, :], top, "wt wtv sc%d" % h, win_k[h], stop=(r == 15))
 
         def order(h):
             a, b = span[h]
-            scan(T.pcs[:, a + 1:b + 1], T.one[:, a:b], T.prop[:, a:b], A.mult, A.add, "one pcs0 prop%d" % h, "pcs%d" % h,
-                 0.0 if h == 0 else T.pcs[:, a:a + 1])
-            tt(T.pu[:, a:b], T.prop[:, a:b], T.c32[:, a:b], A.mult, "c32 prop%d" % h, "pu%d" % h)
-            mm(rank_ps[h], T.tri[:], T.prop[:, a:b], "tri prop%d" % h, rank_k[h])
-            mm(rank_ps[h], T.dfill[:], T.prop[:, a:b], "dfill prop%d" % h, rank_k[h])
-            mm(rank_ps[h], T.bo[:], T.pcs[:, a:b], "bo pcs0 pcs%d" % h, rank_k[h])
-            mm(rank_ps[h], T.neye[:], T.pu[:, a:b], "neye pu%d" % h, rank_k[h], stop=True)
+            if h == 0:
+                scan(T.pcs[:, 1:b + 1], T.one[:, 0:b], T.prop[:, 0:b], A.mult, A.add, "one pcs0 prop0", "pcs")
+                tt(T.pu[:, 0:b], T.prop[:, 0:b], T.c32[:, 0:b], A.mult, "c32 prop0", "pu")
+                act(T.pu[:, b:16], T.one[:, 0:4], "one pcs", "sofar", AF.Identity, 0.0, T.pcs[:, b:b + 1])
+                mm(rank_ps[0], T.tri[:], T.prop[:, 0:b], "tri prop0", "p2")
+                mm(rank_ps[0], T.dfill[:], T.prop[:, 0:b], "dfill prop0", "p2")
+                mm(rank_ps[0], T.bo[:], T.pcs[:, 0:b], "bo pcs0 pcs", "p2")
+                mm(rank_ps[0], T.neye[:], T.pu[:, 0:b], "neye pu", "p2", stop=True)
+            else:
+                mm(rank_ps[1], T.bo[:], T.pu[:, a:b], "bo sofar", "p5")
+                mm(rank_ps[1], T.dfill[:], T.prop[:, a:b], "dfill prop1", "p5")
+                for c in range(4):
+                    mm(rank_ps[1][:, c:c + 1], T.lc[:, c, :], T.prop[:, a + c:a + c + 1], "lc prop1", "p5")
+                for c in range(1, 4):
+                    mm(rank_ps[1][:, c:4], T.bo[:], T.prop[:, a:b - c], "bo prop1", "p5", stop=(c == 3))
 
         def winners(h):
             a, b = span[h]
@@ -619,20 +643,18 @@ def rank_program(g, core, T, topo):
         propose(0)
         order(0)
         compare(3, range(4, 16))
-        if TRANS:
-            best(1)
         winners(0)
-        place(0, 0, 4)
-        if not TRANS:
-            best(1)
+        place(0, 0, PLACE[0])
+        best(1)
         if t == 1:
             dma("y", T.b1t[:, U:DUM], T.b1[:, 0:DUM - U], "sc1", "b1c")
             dma("y", T.b2t[:, U:DUM], T.b2[:, 0:DUM - U], "sc1", "b2c")
+        place(0, PLACE[0], PLACE[1])
         propose(1)
         order(1)
-        place(0, 4, 8)
+        if PLACE[1] < 12:
+            place(0, PLACE[1], 12)
         winners(1)
-        place(0, 8, 12)
         mm(T.p0[:, 0:S], T.eye[:], T.mka[:], "eye mka", "p0", start=True)
         mm(T.p0[:, 0:S], T.bo[:], T.pca[:], "bo pca", "p0")
         mm(T.p1[:, 0:S], T.bo[:], T.pcb[:], "bo pcb", "p1", start=True)
@@ -653,13 +675,14 @@ def rank_program(g, core, T, topo):
             mm(T.p2[:, 48 * c:S], T.bo[:], T.eq[:, at:at + n], "bo " + key, "p2", stop=stop)
 
         EQV, early = EQVS[t], EARLY[t]
+        vo, so = (" ~v", " ~s") if HINT[t] else ("", "")
 
         def lengths():
-            ts(T.ew[:], T.ra[:, 15::16], 1.0 / 15, A.mult, "ra", "ew", 0.25, A.add)
+            ts(T.ew[:], T.ra[:, 15::16], 1.0 / 15, A.mult, "ra", "ew" + vo, 0.25, A.add)
             for q in range(3):
-                act(T.d4[:, q::4], Dw.indirect(T.ew[:, 4 * q:4 * q + 4]), DK + " ew", "d4")
+                act(T.d4[:, q::4], Dw.indirect(T.ew[:, 4 * q:4 * q + 4]), DK + " ew", "d4" + so)
 
-        if early:
+        if len(EQV) == 4:
             lengths()
         for c in (2, 3):
             if c in EQV:
@@ -667,7 +690,9 @@ def rank_program(g, core, T, topo):
             n, at = S - 48 * c, starts[c] - starts[2]
             for q in range(3):
                 x = 64 * q + 16 * c + 15
-                act(T.ab[:, at + q * n:at + q * n + n], T.p3[:, 48 * c - 96:96], "p3 ra", "ab%d" % c, AF.Abs, -1.0, T.ra[:, x:x + 1])
+                act(T.ab[:, at + q * n:at + q * n + n], T.p3[:, 48 * c - 96:96], "p3 ra", "ab%d" % c + so, AF.Abs, -1.0, T.ra[:, x:x + 1])
+            if early and c == 2:
+                lengths()
             act(T.eq[:, starts[c]:starts[c] + 3 * n], T.ab[:, at:at + 3 * n], "wc nwc ab%d" % c, "eq%d" % c, AF.Relu,
                 T.wc[:, 4 + c:5 + c], T.wc[:, c:c + 1])
         if not early:
@@ -684,7 +709,7 @@ def rank_program(g, core, T, topo):
             for q in range(3):
                 n, x = S - 48 * c, 64 * q + 16 * c + 15
                 at = starts[c] + q * n
-                ts(T.eq[:, at:at + n], T.p1[:, 48 * c:S], T.ra[:, x:x + 1], A.is_equal, "p1 ra wc", "eq%d%d" % (c, q), T.wc[:, c:c + 1], A.mult)
+                ts(T.eq[:, at:at + n], T.p1[:, 48 * c:S], T.ra[:, x:x + 1], A.is_equal, "p1 ra wc", "eq%d%d" % (c, q) + vo, T.wc[:, c:c + 1], A.mult)
                 weigh(c, q, "eq%d%d" % (c, q), len(EQV) == 4 and (c, q) == (EQV[-1], 2))
         rest = [c for c in (2, 3) if c not in EQV]
         for c in rest:
@@ -704,35 +729,44 @@ def rank_program(g, core, T, topo):
         lst = lambda q: T.off[:, 4 * q:4 * q + 4]
 
         def stands():
-            ts(T.sw[:], T.ts[:, 47::48], 0.0, A.is_equal, "ts", "sw", -1.0 / 4096, A.mult)
+            act(T.sw[:], T.ts[:, 47::48], "ts", "sw", AF.Sign)
+            mm(T.p0[:, 0:64], T.eye[:], T.one[:], "eye one", "p0", start=True)
             for r in range(16):
-                mm(T.p0[:, r:64:16], T.wt[:, r, :], T.sw[:], "wt sw", "p0", start=True, stop=True)
+                mm(T.p0[:, r:64:16], T.wt[:, r, :], T.sw[:], "wt sw", "p0", stop=(r == 15))
 
         def touch():
             win, one, keys = (T.lwin, T.onef, "lwin") if last else (T.tw, T.one, "twa twz")
             for q in range(3):
-                cp(win[:, 0:DW].indirect(lst(q)), one[:], "one onef " + OFF, keys)
-                if q == 0 and early == 1:
-                    delta()
+                if mixed == 2:
+                    correct(q)
+                cp(win[:, 0:DW].indirect(lst(q)), one[:], "one onef " + OFF, keys + vo)
+                if mixed == 1:
+                    correct(q)
             if t >= 2:
                 land = T.rf[:] if last else T.rt[:, t - 2, :]
                 op("g", lambda t=t: g.remote_dma(land, win[:, V - H:V], T.sem["rt%d" % t], T.sem["lt%d" % t],
                                                 topo.addr(after)[1], topo.addr(after)[0], bits(eng_a)), keys.split()[-1], "",
-                   ("lt%d" % t, len(eng_a)), cost=300.0, late=1500.0)
+                   ("lt%d" % t, len(eng_a)), cost=300.0, late=REM)
                 op("g", None, "", "rt%d" % t, ("rt%d" % t, n_in_t))
 
-        def own_touch():
-            mm(T.p3[:, 0:48], T.eye[:], T.fls[:], "eye fls flsb", "p3", start=True)
-            for r in range(16):
-                mm(T.p3[:, 0:48], sel(r), T.tw[:, r:U:16], "zz twa", "p3", stop=(r == 15))
+        def own_touch(a, b, out, key):
+            op("v", lambda: v.tensor_tensor_scan(T.sx[:, 16 * a:16 * b], T.m4[:, 0:16 * (b - a)], T.tw[:, 16 * a:16 * b], 0.0, A.mult, A.add),
+               "m4 twa", "sx%d" % a, cost=CYC * max(64, 8 * (b - a)))
+            tt(out, T.sx[:, 16 * a + 15:16 * b:16], T.bar[:, a:b], A.is_gt, "sx%d bar" % a, key)
 
         if not last:
+            act(T.bar[:], T.fls[:], "fls flsb c18", "bar", AF.Identity, -4e9, col(18))
+
+        def correct(q):
+            tt(Dw.indirect(lst(q)), base(q), T.dlt[:], A.subtract if q == 0 else A.add, "dlt %s %s" % (bk, OFF), DK + vo)
+
+        mixed = MIXED[t]
+        if mixed or not last:
             touch()
-            own_touch()
 
         def their_touch():
-            scan(T.sx[:], T.m4[:], T.rt[:, t - 2, :], A.mult, A.add, "m4 rt%d" % t, "sx")
-            tt(T.fl[:, na:na + 8], T.sx[:, 15::16], T.fown[:], A.is_gt, "sx fown", "flb")
+            op("v", lambda t=t: v.tensor_tensor_scan(T.sx[:, U:U + H], T.m4[:, 0:H], T.rt[:, t - 2, :], 0.0, A.mult, A.add), "m4 rt%d" % t, "sxn")
+            tt(T.fl[:, na:na + 8], T.sx[:, U + 15:U + H:16], T.fown[:], A.is_gt, "sxn fown", "flb")
 
         c0, nc = 8 * (t + 1), (24, 32, 48, 48, 48)[t]
         na = min(nc, 48 - c0)
@@ -758,29 +792,27 @@ def rank_program(g, core, T, topo):
             m = SPLIT[t][h]
             act(T.lwin[:, 0:4608].indirect(T.ofe[:, a:m]), T.pos[:, 16 * (c0 + a):16 * (c0 + m)], "pos ofe%d" % h, "lwin", AF.Silu)
             if t < 2:
-                ts(T.lxv[:, 15::16], T.own2[:], ps[:, m:m + 1], A.subtract, "own2 " + pk, "lxv", 16.0 * (c0 + m), A.add)
+                ts(T.lxv[:], T.jd[:], ps[:, m:m + 1], A.subtract, "jd " + pk, "lxv", 16.0 * (c0 + m), A.add)
             elif m < b:
                 cp(T.lwv[:, 0:4608].indirect(T.ofe[:, m:b]), T.pos[:, 16 * (c0 + m):16 * (c0 + b)], "pos ofe%d" % h, "lwv")
             return lambda: ts(T.fls[:, home:home + b - a], ps2[:, 64 + a:64 + b], 1024 + P - 0.5, A.is_gt, pk2, "fls" + "b" * h)
 
-        def correct(q):
-            tt(Dw.indirect(lst(q)), base(q), T.dlt[:], A.subtract if q == 0 else A.add, "dlt %s %s" % (bk, OFF), DK)
-
         def others():
             if t < 2:
-                ts(T.fls[:], T.p3[:, 0:48], 0.0, A.is_gt, "p3", "fls")
+                own_touch(0, c0, T.fls[:, 0:c0], "flsb")
             else:
-                ts(T.fown[:], T.p3[:, 0:8], -4e9, A.mult, "p3 c18", "fown", col(18), A.add)
-                ts(T.fl[:, na + 8:48], T.p3[:, 8:c0], 0.0, A.is_gt, "p3", "flc")
+                own_touch(0, c0, T.fl[:, na:48], "flc flb")
+                act(T.fown[:], T.fl[:, na:na + 8], "flb c18", "fown", AF.Identity, -4e9, col(18))
 
         if not early:
             theta()
             delta()
         for step in POST[1 if early else 0]:
             if step in "012":
-                correct(int(step))
+                if not mixed:
+                    correct(int(step))
             elif not last:
-                {"f": lambda: ts(T.fl[:, 0:na], T.p3[:, c0:c0 + na], 0.0, A.is_gt, "p3", "fla"), "o": others,
+                {"f": lambda: own_touch(c0, c0 + (na if t >= 2 else SPLIT[t][0]), T.fl[:, 0:na if t >= 2 else SPLIT[t][0]], "fla"), "o": others,
                  "r": lambda: ranks(0, 0, na, "fla")}[step]()
         stands()
         op("g", lambda t=t: g.remote_dma_fused([
@@ -788,12 +820,13 @@ def rank_program(g, core, T, topo):
                               src=T.D[:, 0:H], dst=T.rd[:, t, H:2 * H]),
             RemoteDMATransfer(dst_ids=[dst(after)], dma_engine_mask=bits(half_a), remote_sem=T.sem["rd%d" % t],
                               src=T.D[:, V - H:V], dst=T.rd[:, t, 0:H])], local_sem=T.sem["ld%d" % t]),
-           "Da Dz", "", ("ld%d" % t, len(half_a) + len(half_b)), cost=300.0, late=2000.0 + 1500.0 * (t == 0))
+           "Da Dz", "", ("ld%d" % t, len(half_a) + len(half_b)), cost=300.0, late=REM + 500.0 + 1500.0 * (t == 0))
         op("g", None, "", "rd%d" % t, ("rd%d" % t, n_in_d))
         if last:
             dma("y", T.yd[:, H:V // 2], T.D[:, H:V // 2], "Dm", "", V // 2)
             dma("s", T.yd[:, V // 2:V - H], T.D[:, V // 2:V - H], "Dm", "", V // 2)
-            touch()
+            if not mixed:
+                touch()
         else:
             keep = compact(0, 0, na, c0)
 
@@ -811,9 +844,9 @@ def rank_program(g, core, T, topo):
         def forget():
             new_z()
             ts(T.fil[:], T.ew[:, 0:4], float(V), A.is_lt, "ew", "fil")
-            ts(T.gr[:], wb[:, 0:S], col(9), A.not_equal, trb + " c9", "gr")
+            act(T.gr[:], wb[:, 0:S], trb + " c9", "gr", AF.Abs, -1.0, col(9))
             tt(T.blk[:], T.ts[:, 47::48], T.fil[:], A.min, "ts fil", "blk")
-            ts(T.gr[:, 64 * u:64 * u + 64], nzu, 0.0, A.not_equal, nk + " gr", "gr")
+            act(T.gr[:, 64 * u:64 * u + 64], nzu, nk + " gr", "gr", AF.Sign, -1.0)
 
         def forget_count():
             for r in range(16):
@@ -833,15 +866,13 @@ def rank_program(g, core, T, topo):
             tab = lambda x: "%sa %sb %sd lw" % (x, x, x) + (" %sc" % x) * (t >= 2)
 
             def next_lists(between):
-                if t >= 2:
-                    scan(T.lxv[:], T.mx[:], T.lwv[:, 0:P], A.max, A.min, "mx lwv", "lxv")
+                two = t >= 2 and SPLIT[t] != (na, 48)
+                if two:
+                    mm(T.p3[:, 0:P], T.eye[:], T.mxb[:], "eye mxb", "p3", start=True, stop=True)
+                    tt(T.lxv[:], T.p3[:, 0:P], T.lwv[:, 0:P], A.min, "p3 lwv", "lxv")
                 between()
-                n = 8 if t == 0 else 16
-                scan(T.lx[:, 0:16 * n], T.mx[:, 0:16 * n], T.lwin[:, 0:16 * n], A.max, A.min, "mx lwin", "lx")
-                tt(T.lm[:, 0:n], T.lx[:, 15:16 * n:16], T.lxv[:, 15:16 * n:16], A.min, "lx lxv", "lm")
-                if n < 16:
-                    ts(T.lw[:, n:16], T.lxv[:, 16 * n + 15::16], 0.25, A.add, "lxv", "lw2")
-                ts(T.lw[:, 0:n], T.lm[:, 0:n], 0.25, A.add, "lm lw2", "lw")
+                scan(T.lx[:], T.mx[:] if t >= 2 and not two else T.lxv[:], T.lwin[:, 0:P], A.max, A.min, "mx lxv lwin", "lx")
+                ts(T.lw[:], T.lx[:, 15::16], 0.25, A.add, "lx", "lw")
                 cp(T.o2[:, 0:64], T.b2t[:, 0:wide].indirect(T.lw[:, 0:4]), tab("b2"), "o2a")
                 cp(T.o1[:, 0:64], T.b1t[:, 0:wide].indirect(T.lw[:, 0:4]), tab("b1"), "o1a")
 

@@ -8,23 +8,14 @@ J, WALL, MARK, DW = 3072, 3136, 3144, 3152
 EXT, DUM = 1288, 1280
 MAG = 12582912.0
 CUTS = (0, 16, 40, 64, 96, 128, 160, 192, 200, 224, 240, 256)
-LOOK = "g0 o2 g1 a0 le dl g2 a1 g3 dp o1 s0 a2 g4 a3 b9 c0 s1 g5 a4 b10 a5 g6 c1 g7 g8 a6 a7 bl c2 a8".split()
-OWN = (0,)
-SPLIT = ((8,), (16,), (24, 40), (16, 36))
-EARLY = (2, 2, 2, 2, 2)
-MIXED = (2, 1, 1, 1, 2)
-POST = ("0fo1r2", "01for2")
-RELAX = False
-DLS = False
-ARRANGE = True
-CYC, PEC, GA, SCA = 0.9, 0.42, 1.5, 3.5
-EQVS = tuple((0, 1, 3) if e else (0, 1) for e in EARLY)
-STREAM, PLACE = (4, 4), (4, 12)
-HINT = (1, 1, 1, 1, 1)
+LOOK = "g0 o2 o1 g1 le a0 dl g2 a1 g3 dp a2 g4 a3 b9 c0 g5 a4 b10 a5 g6 c1 g7 g8 a6 a7 bl c2 a8".split()
+HEAD = 64
+SPLIT = ((8,), (12,), (18, 38), (14, 34))
+EARLY = (True, True, False, False, True)
 LV, LS = " ~lv", " ~ls"
-WTV = 16
-DMA0, DMAB, REM = 900.0, 450.0, 1200.0
-PARTS = "at wt wtv m4 pca pcb wc ab2 ab3 d4 zo pct thr msk lc xs".split() + ["cmp_%d_%d" % (j, k) for j in range(4) for k in range(16)]
+CYC, PEC, GA, SCA, WAKE = 0.88, 0.42, 1.5, 3.7, 200.0
+DMA0, DMAB, REM = 900.0, 600.0, 1100.0
+PARTS = "at wt wm m4 pca pcb wc ab2 ab3 d4 zo pct thr lc xs0 xs1 xs2 xs3".split() + ["cmp_%d_%d" % (j, k) for j in range(4) for k in range(0, 16, 4)]
 F32, BF, F16, I32, U16 = "float32", "bfloat16", "float16", "int32", "uint16"
 
 
@@ -36,43 +27,36 @@ SCRATCH = {
     "D": sb(DW, F32), "b1t": sb(EXT, I32), "b2t": sb(EXT, I32), "bp": sb(EXT, F32), "at": sb(EXT, F32), "pos": sb(EXT, F32),
     "g2": sb(4096, F32), "sm": sb(4096, F32), "cmp": sb([256, 16], BF),
     "o1": sb(256, U16), "o2": sb(256, U16), "lw": sb(16, U16), "le": sb(16, U16), "lt": sb(32, F32),
-    "dl": sb(256, F32), "bl": sb(256, F32), "al": sb(256, F32), "yy": sb(256, F32), "sc": sb(256, BF),
+    "dl": sb(256, F32), "bl": sb(256, F32), "al": sb(256, F32), "yy": sb(256, F32), "sc": sb(256, BF), "xs": sb(256, BF),
     "prop": sb(16, BF), "pu": sb(16, BF), "pcs": sb(24, BF), "ofl": sb(16, U16),
     "w0": sb(1216, F32), "w1": sb(1216, F32), "ofs": sb(12, U16), "ofs32": sb(12, F32),
     "h16": sb(192, F16), "q16": sb(192, F16), "l16": sb(192, F16),
-    "ra": sb(192, F32), "ew": sb(12, U16), "eq": sb(1440, BF), "ts": sb(192, F32), "off": sb(12, U16),
+    "ra": sb(192, F32), "ew": sb(12, U16), "eq": sb(1440, BF), "ab": sb(432, F32), "ts": sb(192, F32), "off": sb(12, U16),
     "d4": sb(256, F32), "d3": sb(192, F32), "th": sb(256, F32), "dlt": sb(64, F32), "nz": sb(192, F32),
-    "sw": sb(4, BF), "dm": sb(64, F32), "g0": sb(64, BF), "onef": sb(64, F32),
-    "tw": sb(DW, BF), "one": sb(64, BF), "gr": sb(192, BF), "fil": sb(4, F32), "blk": sb(4, BF),
+    "sw": sb(4, BF), "g0": sb(64, BF), "tw": sb(DW, BF), "gr": sb(192, BF), "fil": sb(4, F32), "blk": sb(4, BF),
     "fre": sb(12, BF), "fcs": sb(12, BF),
-    "fown": sb(8, F32), "sx": sb(U + H, BF), "m4": sb(512, BF), "fls": sb(48, BF), "fl": sb(48, BF), "fu": sb(48, BF), "lcs": sb(56, BF), "ofe": sb(48, U16),
-    "lwin": sb(4608, F32), "lwv": sb(4608, F32), "lx": sb(256, F32), "lxv": sb(256, F32),
+    "bar": sb(48, F32), "fown": sb(8, F32), "sx": sb(U + H, BF), "fls": sb(48, BF), "fl": sb(48, BF), "fu": sb(48, BF),
+    "lcs": sb(56, BF), "ofe": sb(48, U16), "lwin": sb(4608, F32), "lwv": sb(4608, F32), "lx": sb(256, F32), "lxv": sb(256, F32),
     "rd": sb([RO, 256], F32), "rt": sb([2, 128], BF), "rf": sb(128, F32),
     "zo": sb(192, F32), "t1": sb(576, F32), "t2": sb(576, F32),
     "ip": sb(8, I32), "col": sb(24, F32), "cm": sb(256, F32), "i128": sb(144, F32), "gi": sb(128, F32), "tmp": sb(16, F32), "tmp2": sb(128, F32),
-    "dg": sb(256, F32), "mx": sb(256, F32), "rs": sb(256, BF), "mul4": sb(256, F32), "r4": sb(12, F32),
-    "eye": sb(128, BF), "neye": sb(128, BF), "bo": sb(128, BF), "tri": sb(128, BF), "zz": sb(144, BF), "wt": sb([16, 128], BF),
-    "dfill": sb(128, BF), "dflag": sb(128, BF), "e1k": sb(128, BF), "e512": sb(128, BF), "mgt": sb(128, BF), "ab": sb(432, F32),
-    "hx": sb([6, 128], F16), "lc": sb([4, 128], BF), "ckw": sb(192, BF),
-    "cka": sb(256, BF), "c32": sb(16, BF), "c64": sb(48, BF), "cf1": sb(16, BF), "ce1": sb(48, BF),
-    "mka": sb(192, BF), "pca": sb(192, BF), "pcb": sb(192, BF), "pct": sb(576, BF), "wr": sb(64, F32), "thr": sb(192, BF),
-    "r48": sb(192, F32), "bq": sb(128, BF),
-    "wc": sb(8, F32), "jk": sb(4, F32), "own": sb(12, F32), "jd": sb(256, F32), "mxb": sb(256, BF), "bar": sb(48, F32), "cpd": sb(192, F32),
+    "one": sb(64, BF), "onef": sb(64, F32), "dg": sb(256, F32), "mx": sb(256, F32), "mxb": sb(256, BF), "jd": sb(256, F32),
+    "rs": sb(256, BF), "rmn": sb(64, BF), "mul4": sb(256, F32), "m4": sb(512, BF), "r4": sb(12, F32), "r48": sb(48, F32),
+    "eye": sb(128, BF), "eyf": sb(128, F32), "neye": sb(128, BF), "bo": sb(128, BF), "nbo": sb(128, BF), "bq": sb(128, BF),
+    "tri": sb(128, BF), "zz": sb(144, BF), "wt": sb([16, 128], BF), "lc": sb([4, 128], BF), "wm": sb([4, 128], BF),
+    "dfill": sb(128, BF), "dflag": sb(128, BF), "e1k": sb(128, BF), "e512": sb(128, BF), "mgt": sb(128, BF), "hx": sb([6, 128], F16),
+    "ckw": sb(128, BF), "cka": sb(192, BF), "c32": sb(16, BF), "c64": sb(48, BF), "cf1": sb(16, BF), "ce1": sb(48, BF),
+    "mka": sb(64, BF), "pca": sb(192, BF), "pcb": sb(192, BF), "pct": sb(576, BF), "wr": sb(64, F32), "thr": sb(192, BF),
+    "wc": sb(4, F32), "jk": sb(4, F32), "own": sb(12, F32), "cpd": sb(192, F32),
     "p0": ("psum", [128, 512], F32), "p1": ("psum", [128, 512], F32), "p2": ("psum", [128, 512], F32), "p3": ("psum", [128, 512], F32),
     "p4": ("psum", [128, 512], F32), "p5": ("psum", [128, 512], F32), "p6": ("psum", [128, 512], F32), "p7": ("psum", [128, 512], F32),
 }
-SEMAPHORES = (["sv", "ss", "st", "sg"] + ["dm%d" % i for i in range(24)]
-              + [k + str(t) for k in ("ld", "lt", "rd", "rt", "aa", "ab", "ac", "ad") for t in range(RO)])
+SEMAPHORES = (["sv", "ss", "st", "sg"] + ["dm%d" % i for i in range(14)]
+              + [k + str(t) for k in ("ld", "rd", "aa", "ab") for t in range(RO)] + [k + str(t) for k in ("lt", "rt") for t in range(2, RO)])
 
 
 def bank(k):
     return k[0] == "p" and k[1:].isdigit()
-
-
-is_bank = bank
-
-
-WAKE, TURNS, SLACK, PLAY = 200.0, 3, 0.0, 0
 
 
 def hard(a, b):
@@ -111,6 +95,9 @@ def arrange(ops):
 
     def gap(j, i):
         a, b = ops[j], ops[i]
+        issue = {"~y", "~g", "~h"}
+        if set(a["w"]) & set(b["w"]) & issue and not set(a["r"] + a["w"]) & set(b["r"] + b["w"]) - issue:
+            return 0.0
         return a["late"] + (0.0 if b["f"] is None or not hard(a, b) else WAKE)
 
     def pack(order, before, wait, first):
@@ -123,58 +110,19 @@ def arrange(ops):
                 k = len(row)
                 while k > 0 and row[k - 1][1] > x:
                     k -= 1
-                while k < len(row) and row[k][0] < x + c - SLACK:
+                while k < len(row) and row[k][0] < x + c:
                     x = max(x, row[k][1])
                     k += 1
                 row.insert(k, (x, x + c))
             at[i] = x
         return at
 
-    def run(before, behind, wait, first, due):
-        at, left, ready = [0.0] * n, [len(x) for x in before], [first(i) for i in range(n)]
-        free, cand = {}, {}
-        for i in range(n):
-            if left[i] == 0:
-                cand.setdefault(ops[i]["q"], []).append(i)
-        for step in range(n):
-            now, q = min((max(free.get(q, 0.0), min(ready[i] for i in c)), q) for q, c in cand.items() if c)
-            i = min((j for j in cand[q] if ready[j] <= now), key=lambda j: (due[j], j))
-            for h in cand[q]:
-                if ready[h] > now and due[h] < due[i] and ready[h] < now + ops[i]["cost"]:
-                    go = max(now - due[i], now + ops[i]["cost"] - due[h])
-                    hold = max(ready[h] - due[h], ready[h] + ops[h]["cost"] - due[i])
-                    if hold < go:
-                        i = h
-            at[i] = max(now, ready[i])
-            cand[q].remove(i)
-            if ops[i]["cost"] > 0:
-                free[q] = at[i] + ops[i]["cost"]
-            for j in behind[i]:
-                ready[j] = max(ready[j], at[i] + ops[i]["cost"] + wait(i, j))
-                left[j] -= 1
-                if left[j] == 0:
-                    cand.setdefault(ops[j]["q"], []).append(j)
-        return at
-
-    def length(at):
-        return max(at[i] + ops[i]["cost"] + ops[i]["late"] for i in range(n))
-
-    if PLAY:
-        at = pack(list(range(n)), pre, gap, lambda i: 0.0)
-        best = (length(at), at)
-        for turn in range(PLAY):
-            back = run(post, pre, lambda j, i: gap(i, j), lambda i: ops[i]["late"], [-(at[i] + ops[i]["cost"]) for i in range(n)])
-            at = run(pre, post, gap, lambda i: 0.0, [-(back[i] + ops[i]["cost"]) for i in range(n)])
-            best = min(best, (length(at), at))
-        return [ops[i] for i in sorted(range(n), key=lambda i: (best[1][i], i))]
     order = list(range(n))
-    for turn in range(TURNS):
-        at = pack(order, pre, gap, lambda i: 0.0)
-        place = {j: k for k, j in enumerate(order)}
-        order.sort(key=lambda i: (-(at[i] + ops[i]["cost"]), -place[i]))
-        at = pack(order, post, lambda j, i: gap(i, j), lambda i: ops[i]["late"])
-        place = {j: k for k, j in enumerate(order)}
-        order.sort(key=lambda i: (-(at[i] + ops[i]["cost"]), -place[i]))
+    for turn in range(3):
+        for before, wait, first in ((pre, gap, lambda i: 0.0), (post, lambda j, i: gap(i, j), lambda i: ops[i]["late"])):
+            at = pack(order, before, wait, first)
+            place = {j: k for k, j in enumerate(order)}
+            order.sort(key=lambda i: (-(at[i] + ops[i]["cost"]), -place[i]))
     at = pack(order, pre, gap, lambda i: 0.0)
     place = {j: k for k, j in enumerate(order)}
     order.sort(key=lambda i: (at[i], place[i]))
@@ -182,8 +130,6 @@ def arrange(ops):
 
 
 def emit(g, T, ops):
-    if ARRANGE:
-        ops = arrange(ops)
     Q = {"v": g.vector, "s": g.scalar, "t": g.tensor, "g": g, "y": g.sync}
     lastw, readers, need, seen = {}, {}, [], {}
     for i, o in enumerate(ops):
@@ -195,16 +141,16 @@ def emit(g, T, ops):
             if k[0] == "~":
                 continue
             if k in lastw:
-                deps.add((lastw[k], not (RELAX or k in o["r"] and bank(k) or (k in PARTS and not readers[k]))))
+                deps.add((lastw[k], not (k in o["r"] and bank(k) or (k in PARTS and not readers[k]))))
             for j in readers.get(k, []):
-                deps.add((j, not (RELAX or k in o["r"] and bank(k))))
+                deps.add((j, not (k in o["r"] and bank(k))))
         best = {}
-        for j, hard in deps:
+        for j, must in deps:
             p = ops[j]
             if j == i:
                 continue
             if p["sem"] is None:
-                if p["q"] == o["q"] and o["sem"] is None and (o["q"] == "t" or not hard):
+                if p["q"] == o["q"] and o["sem"] is None and (o["q"] == "t" or not must):
                     continue
                 key = p["q"]
             else:
@@ -256,9 +202,7 @@ def rank_program(g, core, T, topo):
 
     def op(q, f, r, w, sem=None, dma=False, cost=64 * CYC, late=0.0):
         r, w = r.split(), w.split()
-        for k in list(r):
-            if is_bank(k):
-                w.append(k)
+        w += [k for k in r if bank(k)]
         ops.append({"q": q, "f": f, "r": r, "w": w, "sem": sem, "dma": dma, "cost": cost if f else 0.0, "late": late})
 
     def size(x):
@@ -267,18 +211,18 @@ def rank_program(g, core, T, topo):
             n *= d
         return n
 
-    LISTS = set("o1a o1b o2a o2b lw le ofl0 ofl1 ofs ew off0 ofe0 ofe1".split())
+    lists = set("o1a o1b o2a o2b lw lwa le ofl0 ofl1 ofs ew off0 ofe0 ofe1".split())
+    windows = "cp0 cp1 twa lwin lwv Da".split()
 
     def price(out, a, r, w, rate=1.0):
-        if LISTS & set(r.split()) and w[:3] not in ("off", "fil"):
-            if w.split()[0] in ("cp0", "cp1", "twa", "lwin", "lwv", "Da"):
-                return 55.0 + SCA * CYC * size(a)
-            return 55.0 + GA * CYC * size(out)
+        if lists & set(r.split()) and w[:3] not in ("off", "fil"):
+            return 55.0 + (SCA * CYC * size(a) if w.split()[0] in windows else GA * CYC * size(out))
         return CYC * max(64.0, rate * size(out))
 
     def dma(q, out, in_, r, w, behind=0):
-        e = g.sync if q == "y" else g.scalar
-        op(q, lambda: e.dma_start(out, in_), r, w, ("dm%d" % nd[0], 16), True, 60.0, DMA0 + 128 * 4 * (size(out) + behind) / DMAB)
+        e = {"y": g.sync, "s": g.scalar, "g": g}[q]
+        op(q, lambda: e.dma_start(out, in_), r, w, ("dm%d" % nd[0], 16), True, 1700.0 if q == "g" else 60.0,
+           DMA0 + 128 * 4 * (size(out) + behind) / DMAB)
         nd[0] += 1
 
     def ts(out, in0, s1, o0, r, w, s2=None, o1=None):
@@ -288,16 +232,19 @@ def rank_program(g, core, T, topo):
             op("v", lambda: v.tensor_scalar(out, in0, s1, s2, o0, o1), r, w, cost=price(out, in0, r, w))
 
     def tt(out, a, b, o, r, w):
-        op("v", lambda: v.tensor_tensor(out, a, b, o), r, w, cost=price(out, b, r, w, 1.0 if any(is_bank(k) for k in r.split()) else 2.0))
+        op("v", lambda: v.tensor_tensor(out, a, b, o), r, w, cost=price(out, b, r, w, 1.0 if any(bank(k) for k in r.split()) else 2.0))
 
     def cp(out, a, r, w):
         op("v", lambda: v.tensor_copy(out, a), r, w, cost=price(out, a, r, w))
 
-    def scan(out, d0, d1, o0, o1, r, w, first=0.0):
-        op("v", lambda: v.tensor_tensor_scan(out, d0, d1, first, o0, o1), r, w, cost=price(out, d0, r, w))
+    def scan(out, d0, d1, o0, o1, r, w, first=0.0, rate=1.0):
+        op("v", lambda: v.tensor_tensor_scan(out, d0, d1, first, o0, o1), r, w, cost=price(out, d0, r, w, rate))
 
-    def ms(out, c, w):
-        op("v", lambda: v.memset(out, c), "", w, cost=price(out, out, "", w))
+    def ms(out, c, w, r=""):
+        op("v", lambda: v.memset(out, c), r, w, cost=price(out, out, "", w))
+
+    def total(out, a, r, w):
+        op("v", lambda: v.tensor_reduce(out, a, AXX, A.add), r, w)
 
     def act(out, a, r, w, func=None, scale=None, bias=None):
         fn = AF.Copy if func is None else func
@@ -312,8 +259,11 @@ def rank_program(g, core, T, topo):
     def mm(out, l, rh, r, w, start=False, stop=False):
         op("t", lambda: pe.matmul(out, l, rh, start, stop), r, w, cost=PEC * max(64, size(out)))
 
-    def iota(out, pat, base, cmul, w, r=""):
-        op("g", lambda: g.iota(out, pat, base, cmul, allow_small_or_imprecise_dtypes=True), r, w, cost=130.0 + 2 * CYC * size(out))
+    def to_psum(out, a, r, w):
+        op("t", lambda: pe.matmul(out, T.eyf[:], a, True, True), "eyf " + r, w, cost=4 * PEC * size(out))
+
+    def iota(out, pat, base, cmul, w):
+        op("g", lambda: g.iota(out, pat, base, cmul, allow_small_or_imprecise_dtypes=True), "", w, cost=130.0 + 2 * CYC * size(out))
 
     def sel(r):
         return T.zz[:, 15 - r:143 - r]
@@ -334,11 +284,10 @@ def rank_program(g, core, T, topo):
                 mm(T.p5[:, 16 + 4 * u:20 + 4 * u], T.bo[:], T.fcs[:, 4 * w:4 * w + 4], "bo fcs", "p5", stop=(w == 2))
 
     dma("s", T.b2t[:, 0:P], T.b2[:, 0:P], "", "b2a", V * 5 // 8)
-    dma("s", T.b1t[:, 0:P], T.b1[:, 0:P], "", "b1a", V * 5 // 8)
-    dma("y", T.D[:, 0:V // 2], T.dist[:, 0:V // 2], "", "Da Dm", V // 2)
-    dma("y", T.D[:, V // 2:V], T.dist[:, V // 2:V], "", "Dz Dm2", V // 2)
+    dma("y", T.b1t[:, 0:P], T.b1[:, 0:P], "", "b1a ~y", V * 5 // 8)
+    dma("y", T.D[:, 0:V], T.dist[:], "", "Da Dm Dz ~y", 2 * P)
     dma("y", T.b1t[:, P:U], T.b1[:, P:U], "Da Dz", "b1b")
-    dma("y", T.b2t[:, P:U], T.b2[:, P:U], "Da Dz", "b2b")
+    dma("g", T.b2t[:, P:U], T.b2[:, P:U], "Da Dz", "b2b ~h")
 
     op("g", lambda: g.iota(T.ip[:, 0:1], [[0, 1]], 0, 1), "", "ip0")
     iota(T.cm[:], [[0, 16], [1, 16]], 0, 0, "cm")
@@ -346,7 +295,8 @@ def rank_program(g, core, T, topo):
     iota(T.gi[:], [[16, 8], [0, 16]], 0, 0, "gi")
     iota(T.c32[:], [[32, 16]], 0, 0, "c32")
     iota(T.c64[:], [[64, 48]], 0, 0, "c64")
-    iota(T.pos[:], [[1, EXT]], 0, 0, "pos")
+    iota(T.pos[:, 0:P], [[1, P]], 0, 0, "pos0")
+    iota(T.pos[:, P:EXT], [[1, EXT - P]], P, 0, "pos")
     ts(T.ip[:, 1:2], T.ip[:, 0:1], 15, A.bitwise_and, "ip0", "ip1")
     cp(col(0), T.ip[:, 0:1], "ip0", "c0")
     cp(col(1), T.ip[:, 1:2], "ip1", "c1")
@@ -366,33 +316,32 @@ def rank_program(g, core, T, topo):
     ts(T.tmp[:], T.cm[:, 0:16], col(1), A.is_equal, "cm c1", "tmp", -1.0, A.mult)
     ts(col(3), col(2), 15.0, A.add, "c2", "c3")
     ts(col(9), col(4), float(MARK + 1), A.mult, "c4", "c9", (MARK - 1536) / 4096.0 - 1536, A.add)
-    act(T.ckw[:], T.cm[:, 0:S], "cm", "ckw", AF.Identity, -4096.0, -128.0 * 4096)
-    act(T.cka[:], T.cm[:], "cm c8", "cka", AF.Identity, 0.0, col(8))
+    act(T.ckw[:], T.cm[:, 0:H], "cm", "ckw", AF.Identity, -4096.0, -128.0 * 4096)
+    act(T.cka[:], T.cm[:, 0:S], "cm c8", "cka", AF.Identity, 0.0, col(8))
     ts(T.eye[:], T.i128[:, 0:128], col(0), A.is_equal, "i128 c0", "eye")
+    ts(T.eyf[:], T.i128[:, 0:128], col(0), A.is_equal, "i128 c0", "eyf")
     ts(T.bo[:], T.gi[:], col(2), A.is_equal, "gi c2", "bo")
     ts(T.dg[:], T.cm[:], col(1), A.is_equal, "cm c1", "dg")
     act(T.mx[:], T.dg[:], "dg", "mx", AF.Identity, 20000.0, -10000.0)
     act(T.cpd[:], T.cm[:, 0:S], "cm c9", "cpd", AF.Identity, 0.0, col(9))
     act(T.e512[:], T.eye[:], "eye", "e512", AF.Identity, 512.0)
     for r in range(16):
-        if r < WTV:
-            op("v", lambda r=r: v.tensor_scalar(T.wt[:, r, :], T.bo[:], T.tmp[:, r:r + 1], None, A.mult), "bo tmp", "wtv")
-        else:
-            act(T.wt[:, r, :], T.bo[:], "bo tmp", "wt", AF.Identity, T.tmp[:, r:r + 1])
+        act(T.wt[:, r, :], T.bo[:], "bo tmp", "wt", AF.Identity, T.tmp[:, r:r + 1])
     act(T.neye[:], T.eye[:], "eye", "neye", AF.Identity, -1.0)
+    act(T.nbo[:], T.bo[:], "bo", "nbo", AF.Identity, -1.0)
     act(T.dfill[:], T.eye[:], "eye c13", "dfill", AF.Identity, col(13))
     ts(T.tmp2[:], T.cm[:, 0:128], col(1), A.is_gt, "cm c1", "tmp2")
     ts(T.zz[:], T.i128[:], col(3), A.is_equal, "i128 c3", "zz", 65536.0, A.mult)
     ms(T.r4[:], 1.0, "r4")
     ms(T.fre[:], 1.0, "fre")
     tt(T.tri[:], T.tmp2[:], T.bo[:], A.mult, "tmp2 bo", "tri")
-    op("v", lambda: v.memset(T.r4[:, 0::4], 0.0), "r4", "r4")
+    ms(T.r4[:, 0::4], 0.0, "r4", "r4")
     ts(T.rs[:], T.cm[:], 0.0, A.not_equal, "cm", "rs")
     tt(T.mgt[:], T.tri[:], T.bo[:], A.subtract, "tri bo", "mgt")
     for c in range(4):
         op("g", lambda c=c: g.affine_select(T.lc[:, c, :], T.tri[:], [[-1, 128]], A.not_equal, -32.0 * c, 0, 1), "tri", "lc", cost=390.0)
     slot_list()
-    op("v", lambda: v.memset(T.D[:, WALL:MARK], 1e29), "Dj0", "Dj")
+    ms(T.D[:, WALL:MARK], 1e29, "Dj", "Dj0")
     ms(T.onef[:], 1.0, "onef")
     ms(T.b1t[:, DUM:EXT], WALL, "b1d")
     ms(T.b2t[:, DUM:EXT], WALL, "b2d")
@@ -404,81 +353,84 @@ def rank_program(g, core, T, topo):
     for q, c in enumerate((0.0, -1.0, 1.0, 0.5)):
         act(T.mul4[:, q::4], T.cm[:, 0:64], "cm", "mul4_%d" % q, AF.Identity, 0.0, c)
     act(T.cf1[:], T.cm[:, 0:16], "cm c6", "cf1", AF.Identity, 0.0, col(6))
-    act(T.ce1[:], T.cm[:, 0:48], "cm c7", "ce1", AF.Identity, 0.0, col(7))
-    cp(T.o2[:], T.b2t[:, 0:P], "b2a", "o2a o2b")
-    cp(T.o1[:], T.b1t[:, 0:P], "b1a", "o1a o1b")
+    for a, b, k in ((0, HEAD, "a"), (HEAD, P, "b")):
+        cp(T.o2[:, a:b], T.b2t[:, a:b], "b2a", "o2" + k)
+        cp(T.o1[:, a:b], T.b1t[:, a:b], "b1a", "o1" + k)
     for name, c in (("hq", 4096.0), ("hh", 15.0), ("hl", 61440.0), ("hn", -61440.0), ("h1", 1.0), ("hm", -4096.0)):
         ts(HX[name], T.bo[:], c, A.mult, "bo", name)
-    for q, c in enumerate((20992.0, 368640.0, 53760.0)):
-        ts(col(10 + q), col(4), c, A.mult, "c4 c5", "k%d" % q, col(5) if q == 1 else 0.0, A.add)
+    ts(col(20), col(1), 2.0, A.is_equal, "c1", "c20", 1536.0, A.mult)
+    tt(col(21), col(20), col(5), A.add, "c20 c5", "c21")
+    for q, c in enumerate((-2048.0, 344064.0, 30720.0)):
+        ts(col(10 + q), col(4), c, A.mult, "c4 c21", "k%d" % q, col(21) if q == 1 else 0.0, A.add)
+    ts(col(19), col(4), 20992.0, A.mult, "c4", "ka")
+    act(T.rmn[:], T.rs[:, 0:64], "rs", "rmn", AF.Identity, 2.0 ** 41, -2.0 ** 40)
     for q in range(3):
         act(T.pca[:, 64 * q:64 * q + 64], T.cm[:, 0:64], "cm k%d" % q, "pca", AF.Identity, 0.0, col(10 + q))
         act(T.pcb[:, q::3], T.cm[:, 0:64], "cm k%d" % q, "pcb", AF.Identity, 0.0, col(10 + q))
     ms(T.th[:, 0:64], 1.0 / 3.0, "th")
-    op("v", lambda: v.tensor_tensor_scan(T.ts[:, 0:64], T.th[:, 0:64], T.nz[:, 0:64], 1e29, A.mult, A.add), "th nz0", "ts")
+    scan(T.ts[:, 0:64], T.th[:, 0:64], T.nz[:, 0:64], A.mult, A.add, "th nz0", "ts", 1e29)
     ms(T.r48[:], 1.0, "r48")
     ts(T.wr[:], T.ts[:, 0:64], 3.0 ** 64 * 2.0 ** 14 / 1e29, A.mult, "ts", "wr")
-    op("v", lambda: v.memset(T.r48[:, 0::48], 0.0), "r48", "r48")
+    ms(T.r48[:, 0:1], 0.0, "r48", "r48")
     tt(T.ts[:, 0:64], T.wr[:], T.dg[:, 0:64], A.mult, "wr dg", "ts")
     ts(T.th[:, 0:64], T.dg[:, 0:64], -1.0, A.add, "dg wr", "th", 1e29, A.mult)
     for c in range(4):
-        op("v", lambda c=c: v.tensor_reduce(T.wc[:, c:c + 1], T.ts[:, 16 * c:16 * c + 16], AXX, A.add), "ts", "wc")
+        total(T.wc[:, c:c + 1], T.ts[:, 16 * c:16 * c + 16], "ts ts0 ts1", "wc")
     ts(T.th[:, 64:128], T.th[:, 0:64], 1e7, A.mult, "th", "th2")
-    ts(T.th[:, 128:192], T.ts[:, 0:64], -2.25, A.mult, "ts", "th3")
+    ts(T.th[:, 128:192], T.ts[:, 0:64], -2.25, A.mult, "ts ts0 ts1", "th3")
     ts(T.jk[:], T.cm[:, 0:4], 16.0, A.mult, "cm c1", "jk0", col(1), A.add)
     ts(T.own[:], T.cm[:, 0:12], 16.0, A.mult, "cm c1", "own0", col(1), A.add)
     tt(T.th[:, 192:256], T.th[:, 64:128], T.th[:, 128:192], A.add, "th2 th3", "th4")
-
     ts(col(15), col(5), 1.0 / 15, A.mult, "c5", "c15")
-    act(T.bq[:], T.bo[:], "bo", "bq", AF.Identity, 4096.0)
     ts(col(16), col(4), 24576.0, A.mult, "c4 c15", "kb", col(15), A.add)
     ts(col(17), col(4), 3584.0, A.mult, "c4", "kc")
-    for h in range(2):
-        act(T.m4[:, P * h:P * h + P], T.dg[:], "dg", "m4", AF.Identity, -4.0, 4.0)
-    ms(T.lt[:, 0:16], 0.25, "lt")
-    scan(T.lt[:, 16:32], T.lt[:, 0:16], T.nz[:, 0:16], A.mult, A.add, "lt nz0", "lt2", 4.0 ** 16 / 2)
+    ms(T.lt[:, 0:16], 0.125, "lt")
+    scan(T.lt[:, 16:32], T.lt[:, 0:16], T.nz[:, 0:16], A.mult, A.add, "lt nz0", "lt2", 8.0 ** 16 * 0.625)
     tt(T.lt[:, 0:16], T.lt[:, 16:32], T.dg[:, 0:16], A.mult, "lt2 dg", "lt")
-    op("v", lambda: v.tensor_reduce(col(18), T.lt[:, 0:16], AXX, A.add), "lt", "c18")
+    total(col(18), T.lt[:, 0:16], "lt", "c18")
     act(T.lwin[:, 0:P], T.cm[:], "cm", "lwin" + LS, AF.Silu, 0.0, float(DUM))
-
-    act(T.p6[:, 0:P], T.pos[:, 0:P], "pos c1", "p6", AF.Identity, 1.0, col(1))
-    tt(T.jd[:], T.p6[:, 0:P], T.mx[:], A.min, "p6 mx", "jd")
     ms(T.fl[:], 1.0, "fla flb flc")
     ts(T.jk[:], T.jk[:], float(J), A.add, "jk0", "jk")
     ts(T.own[:], T.own[:], 320.0, A.add, "own0", "own")
-    ts(T.wc[:, 4:8], T.wc[:, 0:4], -1.0, A.mult, "wc", "nwc")
-
+    for c in range(4):
+        act(T.wm[:, c, :], T.bo[:], "bo wc", "wm", AF.Identity, T.wc[:, c:c + 1])
 
     def pack(a, b, r, w):
         ts(T.p1[:, 0:b - a], T.b2t[:, a:b], -1536.0 - 1535 * 4096, A.add, r, "p1 own_p1", 1.0 / 4096, A.mult)
         tt(T.bp[:, a:b], T.p1[:, 0:b - a], T.b1t[:, a:b], A.add, r + " p1 own_p1", w)
 
-
     pack(0, P, "b1a b2a", "bpa")
-    act(T.at[:, 0:P], T.pos[:, 0:P], "pos", "at0", AF.Identity, 1.0 / 4096, -1536.0 / 4096 - 1536)
+    act(T.at[:, 0:P], T.pos[:, 0:P], "pos0", "at0", AF.Identity, 1.0 / 4096, -1536.0 / 4096 - 1536)
     for q in range(3):
         act(T.thr[:, q::3], T.th[:, 192:256], "th4 th", "thr")
-    act(T.mka[:], T.dg[:, 0:S], "dg", "mka", AF.Identity, 1048576.0, -1048576.0)
-    act(T.e1k[:], T.eye[:], "eye", "e1k", AF.Identity, 1024.0)
-    act(T.dflag[:], T.eye[:], "eye c14", "dflag", AF.Identity, col(14))
-    act(T.mxb[:], T.dg[:], "dg", "mxb", AF.Identity, 16384.0, -8192.0)
+    act(T.mka[:], T.dg[:, 0:64], "dg", "mka", AF.Identity, 1048576.0, -1048576.0)
 
-    def slot_list_end(step):
-        if step == 0:
-            tt(T.ofs32[:], T.p5[:, 16:28], T.own[:], A.max, "p5 own", "ofs32")
-        else:
-            ts(T.ofs[:], T.ofs32[:], -320.0, A.add, "ofs32", "ofs")
+    def flag_constants():
+        act(T.m4[:, 0:P], T.dg[:], "dg", "m4 ~s", AF.Identity, -8.0, 8.0)
+        act(T.p6[:, 0:P], T.pos[:, 0:P], "pos0 c1", "p6 ~s", AF.Identity, 1.0, col(1))
+        tt(T.jd[:], T.p6[:, 0:P], T.mx[:], A.min, "p6 mx", "jd")
+        act(T.ce1[:], T.cm[:, 0:48], "cm c7", "ce1 ~s", AF.Identity, 0.0, col(7))
+        act(T.dflag[:], T.eye[:], "eye c14", "dflag ~s", AF.Identity, col(14))
+        act(T.e1k[:], T.eye[:], "eye", "e1k ~s", AF.Identity, 1024.0)
+
+    def later_constants():
+        for a in range(P, EXT, P):
+            b = min(EXT, a + P)
+            act(T.at[:, a:b], T.pos[:, a:b], "pos", "at ~s", AF.Identity, 1.0 / 4096, (-1536.0 - U * (a >= U)) / 4096 - 1536)
+        act(T.m4[:, P:2 * P], T.dg[:], "dg", "m4 ~s", AF.Identity, -8.0, 8.0)
+        act(T.mxb[:], T.dg[:], "dg", "mxb ~s", AF.Identity, 16384.0, -8192.0)
+        act(T.bq[:], T.bo[:], "bo", "bq ~s", AF.Identity, 4096.0)
 
     def planes(src, n, r):
         ts(T.h16[:, 0:n], src(), MAG, A.add, r, "h16", MAG, A.subtract)
         ts(T.q16[:, 0:n], src(), -1535.5, A.min, r, "q16", 1536.0, A.add)
         tt(T.l16[:, 0:n], src(), T.h16[:, 0:n], A.subtract, r + " h16", "l16")
 
-    def rows(outs, a, b, bank, stop):
-        mm(outs[1], HX["hh"], T.h16[:, a:b], "hh h16", bank[1])
-        mm(outs[0], HX["hq"], T.q16[:, a:b], "hq q16", bank[0], stop=stop and bank[0] != bank[2])
-        mm(outs[2], HX["hn"], T.q16[:, a:b], "hn q16", bank[2])
-        mm(outs[2], HX["hl"], T.l16[:, a:b], "hl l16", bank[2], stop=stop)
+    def rows(outs, a, b, bk):
+        mm(outs[1], HX["hh"], T.h16[:, a:b], "hh h16", bk[1], stop=bk[1] != bk[2])
+        mm(outs[0], HX["hq"], T.q16[:, a:b], "hq q16", bk[0], stop=bk[0] != bk[2])
+        mm(outs[2], HX["hn"], T.q16[:, a:b], "hn q16", bk[2])
+        mm(outs[2], HX["hl"], T.l16[:, a:b], "hl l16", bk[2], stop=True)
 
     eng_b, eng_a = topo.engines(core, before), topo.engines(core, after)
     half_b = eng_b[0::2]
@@ -494,105 +446,105 @@ def rank_program(g, core, T, topo):
         tra, trb = ("tr0", "tr1") if t % 2 == 0 else ("tr1", "tr0")
         cpa = "cp%d" % (t % 2)
         last = t == RO - 1
-        op("g", lambda wa=wa: g.affine_select(wa[:, S:2 * S], T.cpd[:], [[0, S]], A.is_ge, 0.0, 0, 0), "cpd", cpa, cost=540.0)
-        dk = DK + (" Dm2" if t == 0 else "")
+        op("g", lambda wa=wa: g.affine_select(wa[:, S:2 * S], T.cpd[:], [[0, S]], A.is_ge, 0.0, 0, 0), "cpd", cpa + " ~h" * (t > 0), cost=540.0)
         wide = U if t < 3 else EXT
         tab = lambda x: "%sa %sb %sd lw" % (x, x, x) + (" %sc" % x) * (t >= 3)
-        part = lambda b: "a" if b <= 64 else "b"
+        part = lambda b: "a" if b <= HEAD else "b"
         sums = lambda j: " ".join("sm_%d" % i for i in range(len(CUTS) - 1) if CUTS[i] // 64 == j)
         adds = [0]
 
         def gath(i):
             a, b = CUTS[i], CUTS[i + 1]
-            own = i == 0 and t in OWN
-            (cp if own else act)(T.g2[:, 16 * a:16 * b], Dw.indirect(T.o2[:, a:b]), dk + " o2" + part(b), "g2_%d" % i + (LV if own else LS))
+            own = i == 0 and t == 0
+            (cp if own else act)(T.g2[:, 16 * a:16 * b], Dw.indirect(T.o2[:, a:b]), DK + " o2" + part(b), "g2_%d" % i + (LV if own else LS))
 
         def add(i):
             a, b = CUTS[i], CUTS[i + 1]
             tt(T.sm[:, 16 * a:16 * b], Dw.indirect(T.o1[:, a:b]), T.g2[:, 16 * a:16 * b], A.add,
-               dk + " o1%s g2_%d" % (part(b), i), "sm_%d" % i + LV)
+               DK + " o1%s g2_%d" % (part(b), i), "sm_%d" % i + LV)
 
         def both(i):
             a, b = CUTS[i], CUTS[i + 1]
             gath(i)
-            act(T.sm[:, 16 * a:16 * b], Dw.indirect(T.o1[:, a:b]), dk + " o1" + part(b), "sm_%d" % i + LS)
+            act(T.sm[:, 16 * a:16 * b], Dw.indirect(T.o1[:, a:b]), DK + " o1" + part(b), "sm_%d" % i + LS)
             op("g", lambda: g.dma_start(T.sm[:, 16 * a:16 * b], T.g2[:, 16 * a:16 * b], accum_op=A.add), "g2_%d sm_%d" % (i, i),
-               "sm_%d" % i, ("a%s%d" % ("abcd"[adds[0]], t), 16), True, 700.0, 1300.0 + 60.0 * (b - a))
+               "sm_%d ~h" % i, ("a%s%d" % ("ab"[adds[0]], t), 16), True, 700.0, 1300.0 + 60.0 * (b - a))
             adds[0] += 1
 
-        def compare(j, ks=range(16)):
+        def compare(j, ks=range(0, 16, 4)):
+            a, b = 64 * j, 64 * j + 64
+            for k0 in ks:
+                for k in range(k0, k0 + 4):
+                    tt(T.cmp[:, a:b, k], T.p7[:, a:b], T.sm[:, 16 * a + k:16 * b:16], A.is_gt, "p7 " + sums(j), "cmp_%d_%d" % (j, k0) + LV)
+                if k0 == 12 and j < 3:
+                    wrapped(j, range(16))
+                if k0 < 12 or j < 3:
+                    counts(j, k0)
+
+        def counts(j, k0):
             a, b = 64 * j, 64 * j + 64
             out, bk = (T.p1[:, a:b], "p1") if j < 3 else (T.p4[:, 0:64], "p4")
-            step = STREAM[j == 3]
-            for k0 in range(ks[0], ks[-1] + 1, step):
-                key = "cmp_%d_%d" % (j, k0)
-                for k in range(k0, k0 + step):
-                    tt(T.cmp[:, a:b, k], T.p7[:, a:b], T.sm[:, 16 * a + k:16 * b:16], A.is_gt, "p7 " + sums(j), key + LV * (j < 3))
-                if k0 + step == 16:
-                    keys = " ".join("cmp_%d_%d" % (j, x) for x in range(0, 16, step))
-                    for r in range(16):
-                        mm(T.p0[:, a:b] if j < 3 else top_ps[1], sel(r), T.cmp[:, a + r:b:16, :], "zz " + keys, top_k[j // 3],
-                           stop=(j >= 2 and r == 15))
-                for k in range(k0, k0 + step):
-                    mm(out, sel(k), T.cmp[:, a:b, k], "zz " + key, bk)
+            for k in range(k0, k0 + 4):
+                mm(out, sel(k), T.cmp[:, a:b, k], "zz cmp_%d_%d" % (j, k0), bk)
 
-        top_ps, top_k = (T.p0[:, 0:S], T.p6[:, 384:448]), ("p0", "p6")
-        mm(top_ps[0], T.eye[:], T.ckw[:], "eye ckw", "p0", start=True)
-        mm(T.p1[:, 0:192], T.eye[:], T.cka[:, 0:192], "eye cka", "p1", start=True)
+        def wrapped(j, rs):
+            a, b = 64 * j, 64 * j + 64
+            keys = " ".join("cmp_%d_%d" % (j, x) for x in range(0, 16, 4))
+            for r in rs:
+                mm(T.p0[:, a:b] if j < 2 else T.p6[:, a:b], sel(r), T.cmp[:, a + r:b:16, :], "zz " + keys,
+                   "p0" if j < 2 else "p6" + " ~u" * (j == 3), stop=(j >= 1 and r == 15))
+
+        def top(a, b, key):
+            bk = "p0" if a < H else "p6"
+            scan(T.sc[:, a:b], T.rs[:, a:b], T[bk][:, a:b], A.mult, A.max, "rs " + bk, key + LV)
+
+        mm(T.p0[:, 0:H], T.eye[:], T.ckw[:], "eye ckw", "p0", start=True)
+        mm(T.p6[:, H:S], T.eye[:], T.ckw[:, 0:64], "eye ckw", "p6", start=True)
+        mm(T.p1[:, 0:S], T.eye[:], T.cka[:], "eye cka", "p1", start=True)
         mm(T.p4[:, 0:64], T.eye[:], T.cka[:, 0:64], "eye cka", "p4", start=True)
         if last:
             for h, bk in enumerate(("p3", "p2")):
                 for r in range(16):
                     mm(T[bk][:, r:384:16], T.wt[:, r, :], T.fls[:, 24 * h:24 * h + 24], "wt fls flsb", bk, start=True, stop=True)
-        mm(top_ps[1], T.eye[:], T.ckw[:, 0:64], "eye ckw", "p6", start=True)
 
         def entries():
-            if t > 0:
-                act(T.bl[:], T.bp[:, 0:(512, U, EXT, EXT)[t - 1]].indirect(T.lw[:]), "bpa bpb bpc bpe bpd lw", "bl" + LS)
-                act(T.al[:], T.at[:, 0:EXT].indirect(T.lw[:]), "at0 at lw", "al" + LS)
+            act(T.bl[:], T.bp[:, 0:(512, U, EXT, EXT)[t - 1]].indirect(T.lw[:]), "bpa bpb bpc bpe bpd lw lwa", "bl" + LS)
+            act(T.al[:], T.at[:, 0:EXT].indirect(T.lw[:]), "at0 at lw lwa", "al" + LS)
 
         def edges():
-            ts(T.lt[:, 0:16], T.lx[:, 15::16], U - 0.5, A.is_ge, "lx", "lt", -float(U), A.mult)
-            tt(T.lt[:, 16:32], T.lt[:, 0:16], T.lx[:, 15::16], A.add, "lt lx", "lt2")
-            ts(T.le[:], T.lt[:, 16:32], 0.25, A.add, "lt2", "le")
+            if t >= 3:
+                ts(T.lt[:, 0:16], T.lx[:, 15::16], U - 0.5, A.is_ge, "lx lxa", "lt", -float(U), A.mult)
+                tt(T.lt[:, 16:32], T.lt[:, 0:16], T.lx[:, 15::16], A.add, "lt lx lxa", "lt2")
+                ts(T.le[:], T.lt[:, 16:32], 0.25, A.add, "lt2", "le")
 
-        def fills():
-            if t in (0, 3):
-                iota(T.tw[:, V - H:V], [[0, H]], 0, 0, "twz")
-            if not last:
-                iota(T.tw[:, 0:U], [[0, U]], 0, 0, "twa")
-                if t > 0:
-                    iota(T.lwin[:, 0:P], [[0, P]], DUM, 0, "lwin")
-                if t >= 2:
-                    iota(T.lwv[:, 0:P], [[0, P]], DUM, 0, "lwv")
-            else:
-                iota(T.lwin[:, V - H:V], [[0, H]], 0, 0, "lwin")
-
-        later = {"o2": lambda: cp(T.o2[:, 64:P], T.b2t[:, 0:wide].indirect(T.lw[:, 4:16]), tab("b2"), "o2b"),
-                 "o1": lambda: cp(T.o1[:, 64:P], T.b1t[:, 0:wide].indirect(T.lw[:, 4:16]), tab("b1"), "o1b"),
-                 "le": edges if t >= 3 else lambda: None,
-                 "dl": lambda: (act if DLS else cp)(T.dl[:], Dw.indirect((T.le if t >= 3 else T.lw)[:]), dk + " le lw", "dl")}
-        always = {"dp": lambda: (act if t > 0 else cp)(T.p7[:, 0:P], (T.dl if t > 0 else T.D)[:, 0:P], "dl" if t > 0 else dk, "p7" + (LS if t > 0 else LV)),
-                  "s0": lambda: slot_list_end(0), "s1": lambda: slot_list_end(1), "bl": entries}
-        fills()
+        if t in (0, 3):
+            iota(T.tw[:, V - H:V], [[0, H]], 0, 0, "twz ~g")
+        if last:
+            iota(T.lwin[:, V - H:V], [[0, H]], 0, 0, "lwin")
+        else:
+            iota(T.tw[:, 0:U], [[0, U]], 0, 0, "twa ~g")
+            if t > 0:
+                iota(T.lwin[:, 0:P], [[0, P]], DUM, 0, "lwin")
+                iota(T.lwv[:, 0:P], [[0, P]], DUM, 0, "lwv")
+        made = {"o2": lambda: cp(T.o2[:, HEAD:P], T.b2t[:, 0:wide].indirect(T.lw[:, HEAD // 16:16]), tab("b2"), "o2b" + LV * (t >= 3)),
+                "o1": lambda: cp(T.o1[:, HEAD:P], T.b1t[:, 0:wide].indirect(T.lw[:, HEAD // 16:16]), tab("b1"), "o1b" + LV * (t >= 3)),
+                "dl": lambda: cp(T.dl[:], Dw.indirect((T.le if t >= 3 else T.lw)[:]), DK + " le lw lwa", "dl"),
+                "le": edges, "bl": entries}
         for step in LOOK:
-            if step in always:
-                always[step]()
-            elif step in later:
+            if step == "dp":
+                to_psum(T.p7[:, 0:P], (T.dl if t > 0 else T.D)[:, 0:P], "dl" if t > 0 else DK, "p7")
+            elif step in made:
                 if t > 0:
-                    later[step]()
+                    made[step]()
             else:
                 {"g": gath, "a": add, "b": both, "c": compare}[step[0]](int(step[1:]))
         bl, al, blk, alk = (T.bl, T.al, "bl", "al") if t > 0 else (T.bp, T.at, "bpa", "at0")
-        if t == 0:
-            act(T.at[:, P:U], T.pos[:, P:U], "pos", "at", AF.Identity, 1.0 / 4096, -1536.0 / 4096 - 1536)
-            act(T.at[:, U:EXT], T.pos[:, U:EXT], "pos", "at", AF.Identity, 1.0 / 4096, (-1536.0 - U) / 4096 - 1536)
         if t == 2:
             act(T.bp[:, U:DUM], T.bp[:, 0:DUM - U], "bpa bpb", "bpe")
         if last:
             for h, bk in enumerate(("p3", "p2")):
                 act(T.lwin[:, 384 * h:384 * h + 384], T[bk][:, 0:384], bk, "lwin", AF.Copy, -1.0)
-            for q, (c, k) in enumerate(((col(10), "k0"), (col(16), "kb"), (col(17), "kc"))):
+            for q, (c, k) in enumerate(((col(19), "ka"), (col(16), "kb"), (col(17), "kc"))):
                 act(T.pct[:, S * q:S * q + S], T.cm[:, 0:S], "cm " + k, "pct", AF.Identity, 0.0, c)
         span = ((0, 12), (12, 16))
         rank_ps, rank_k = (T.p2[:, 0:12], T.p5[:, 32:36]), ("p2", "p5")
@@ -600,27 +552,31 @@ def rank_program(g, core, T, topo):
 
         def best(h):
             a, b = span[h]
-            scan(T.sc[:, 16 * a:16 * b], T.rs[:, 16 * a:16 * b], top_ps[h], A.mult, A.max, "rs " + top_k[h], "sc%d" % h)
+            top(H if h == 0 else S, 16 * b, "sc%d" % h)
+            if h == 0:
+                mm(T.p6[:, S:P], T.eye[:], T.ckw[:, 0:64], "eye ckw", "p6", start=True)
             mm(rank_ps[h], T.eye[:], T.cf1[:, a:b], "eye cf1", rank_k[h], start=True)
             mm(rank_ps[h], T.eye[:], T.c32[:, 0:b - a], "eye c32", rank_k[h])
 
         def propose(h):
             a, b = span[h]
-            top = T.sc[:, 16 * a + 15:16 * b:16]
-            act(T.prop[:, a:b], top, "sc%d" % h, "prop%d" % h, AF.Sign)
-            for r in range(16):
-                mm(win_ps[h][:, r:16 * (b - a):16], T.wt[:, r, :], top, "wt wtv sc%d" % h, win_k[h], stop=(r == 15))
+            for c in range(a, b):
+                if c == b - 4:
+                    act(T.prop[:, a:b], T.sc[:, 16 * a + 15:16 * b:16], "sca sc%d" % h, "prop%d ~p" % h, AF.Sign)
+                act(T.xs[:, 16 * c:16 * c + 16], T.mka[:, 0:16], "mka " + ("sca" if c < 8 else "sc%d" % h), "xs%d ~p" % (c // 4),
+                    AF.Relu, 1.0, T.sc[:, 16 * c + 15:16 * c + 16])
+            mm(win_ps[h][:, 0:16 * (b - a)], T.nbo[:], T.xs[:, 16 * a:16 * b], "nbo " + ("xs0 xs1 xs2", "xs3")[h], win_k[h], stop=True)
 
         def order(h):
             a, b = span[h]
             if h == 0:
-                scan(T.pcs[:, 1:b + 1], T.one[:, 0:b], T.prop[:, 0:b], A.mult, A.add, "one pcs0 prop0", "pcs")
+                scan(T.pcs[:, 1:b + 1], T.one[:, 0:b], T.prop[:, 0:b], A.mult, A.add, "one pcs0 prop0", "pcs" + LV)
                 tt(T.pu[:, 0:b], T.prop[:, 0:b], T.c32[:, 0:b], A.mult, "c32 prop0", "pu")
                 act(T.pu[:, b:16], T.one[:, 0:4], "one pcs", "sofar", AF.Identity, 0.0, T.pcs[:, b:b + 1])
                 mm(rank_ps[0], T.tri[:], T.prop[:, 0:b], "tri prop0", "p2")
                 mm(rank_ps[0], T.dfill[:], T.prop[:, 0:b], "dfill prop0", "p2")
                 mm(rank_ps[0], T.bo[:], T.pcs[:, 0:b], "bo pcs0 pcs", "p2")
-                mm(rank_ps[0], T.neye[:], T.pu[:, 0:b], "neye pu", "p2", stop=True)
+                mm(rank_ps[0], T.neye[:], T.pu[:, 0:b], "neye pu", "p2 ~u", stop=True)
             else:
                 mm(rank_ps[1], T.bo[:], T.pu[:, a:b], "bo sofar", "p5")
                 mm(rank_ps[1], T.dfill[:], T.prop[:, a:b], "dfill prop1", "p5")
@@ -634,142 +590,138 @@ def rank_program(g, core, T, topo):
             tt(T.yy[:, 16 * a:16 * b], win_ps[h][:, 0:16 * (b - a)], bl[:, 16 * a:16 * b], A.add, win_k[h] + " " + blk, "yy%d" % h)
             cp(T.ofl[:, a:b], rank_ps[h], rank_k[h], "ofl%d" % h)
 
-        def place(h, a, b):
+        def place(h):
+            a, b = span[h]
             tt(wa[:, S:S + 1024].indirect(T.ofl[:, a:b]), T.yy[:, 16 * a:16 * b], al[:, 16 * a:16 * b], A.max,
                "ofl%d yy%d %s" % (h, h, alk), cpa)
 
+        top(0, H, "sca")
+        compare(3, (0,))
         best(0)
-        compare(3, range(0, 4))
+        compare(3, (4, 8, 12))
         propose(0)
+        wrapped(3, range(6))
         order(0)
-        compare(3, range(4, 16))
+        tt(T.ofs32[:], T.p5[:, 16:28], T.own[:], A.max, "p5 own", "ofs32" + LV)
+        ts(T.ofs[:], T.ofs32[:], -320.0, A.add, "ofs32", "ofs")
+        wrapped(3, range(6, 16))
+        counts(3, 12)
         winners(0)
-        place(0, 0, PLACE[0])
         best(1)
         if t == 1:
             dma("y", T.b1t[:, U:DUM], T.b1[:, 0:DUM - U], "sc1", "b1c")
             dma("y", T.b2t[:, U:DUM], T.b2[:, 0:DUM - U], "sc1", "b2c")
-        place(0, PLACE[0], PLACE[1])
+        place(0)
         propose(1)
         order(1)
-        if PLACE[1] < 12:
-            place(0, PLACE[1], 12)
         winners(1)
-        mm(T.p0[:, 0:S], T.eye[:], T.mka[:], "eye mka", "p0", start=True)
-        mm(T.p0[:, 0:S], T.bo[:], T.pca[:], "bo pca", "p0")
+        diag = ("p6", "p0", "p7")
+        for q in range(3):
+            mm(T[diag[q]][:, 0:64], T.eye[:], T.mka[:], "eye mka", diag[q], start=True)
+            mm(T[diag[q]][:, 0:64], T.bo[:], T.pca[:, 64 * q:64 * q + 64], "bo pca", diag[q])
         mm(T.p1[:, 0:S], T.bo[:], T.pcb[:], "bo pcb", "p1", start=True)
         mm(T.p3[:, 0:96], T.bo[:], T.pcb[:, 96:S], "bo pcb", "p3", start=True)
         mm(T.p2[:, 0:S], T.eye[:], T.thr[:], "eye thr", "p2", start=True)
-        place(1, 12, 16)
+        place(1)
         planes(lambda: wa[:, 0:2 * S].indirect(T.ofs[:, 4 * u:4 * u + 4]), 64, "ofs %s %s" % (tra, cpa))
         act(wb[:, 0:S], wa[:, 0:2 * S].indirect(T.ofs[:]), "ofs %s %s" % (tra, cpa), trb)
-        rows([T.p0[:, 64 * q:64 * q + 64] for q in range(3)], 0, 64, ["p0"] * 3, True)
-        rows([T.p1[:, q:S:3] for q in range(3)], 0, 64, ["p1"] * 3, True)
-        rows([T.p3[:, q:96:3] for q in range(3)], 32, 64, ["p3"] * 3, True)
-        scan(T.ra[:], T.rs[:, 0:S], T.p0[:, 0:S], A.mult, A.max, "rs p0", "ra")
+        rows([T[diag[q]][:, 0:64] for q in range(3)], 0, 64, diag)
+        rows([T.p1[:, q:S:3] for q in range(3)], 0, 64, ["p1"] * 3)
+        rows([T.p3[:, q:96:3] for q in range(3)], 32, 64, ["p3"] * 3)
+        for q in (1, 0, 2):
+            scan(T.ra[:, 64 * q:64 * q + 64], T.rmn[:], T[diag[q]][:, 0:64], A.min, A.max, "rmn " + diag[q], "ra%d ~v" % q)
         starts = (0, 576, 1008, 1296)
+        early = EARLY[t]
+        mine, rest = ((0, 1, 3), (2,)) if early else ((0, 1), (2, 3))
 
         def weigh(c, q, key, stop=False):
             n = S - 48 * c
             at = starts[c] + q * n
-            mm(T.p2[:, 48 * c:S], T.bo[:], T.eq[:, at:at + n], "bo " + key, "p2", stop=stop)
+            mm(T.p2[:, 48 * c:S], T.wm[:, c, :], T.eq[:, at:at + n], "wm " + key, "p2", stop=stop)
 
-        EQV, early = EQVS[t], EARLY[t]
-        vo, so = (" ~v", " ~s") if HINT[t] else ("", "")
+        def lengths(qs):
+            if qs[0] == 0:
+                ts(T.ew[:], T.ra[:, 15::16], 1.0 / 15, A.mult, "ra0 ra1 ra2", "ew ~v", 1536.25, A.add)
+            for q in qs:
+                act(T.d4[:, q::4], Dw.indirect(T.ew[:, 4 * q:4 * q + 4]), DK + " ew", "d4 ~s")
 
-        def lengths():
-            ts(T.ew[:], T.ra[:, 15::16], 1.0 / 15, A.mult, "ra", "ew" + vo, 0.25, A.add)
-            for q in range(3):
-                act(T.d4[:, q::4], Dw.indirect(T.ew[:, 4 * q:4 * q + 4]), DK + " ew", "d4" + so)
+        def on_scalar():
+            for c in rest:
+                for q in (1, 0, 2):
+                    n, x = S - 48 * c, 64 * q + 16 * c + 15
+                    at = starts[c] - starts[2] + q * n
+                    act(T.ab[:, at:at + n], T.p3[:, 48 * c - 96:96], "p3 ra%d" % q, "ab%d ~s" % c, AF.Abs, -1.0, T.ra[:, x:x + 1])
+            if early:
+                lengths((0,))
+            for c in rest:
+                n, at = S - 48 * c, starts[c] - starts[2]
+                act(T.eq[:, starts[c]:starts[c] + 3 * n], T.ab[:, at:at + 3 * n], "ab%d" % c, "eq%d ~s" % c, AF.Relu, -1.0, 1.0)
+            if early:
+                lengths((1, 2))
 
-        if len(EQV) == 4:
-            lengths()
-        for c in (2, 3):
-            if c in EQV:
-                continue
-            n, at = S - 48 * c, starts[c] - starts[2]
-            for q in range(3):
-                x = 64 * q + 16 * c + 15
-                act(T.ab[:, at + q * n:at + q * n + n], T.p3[:, 48 * c - 96:96], "p3 ra", "ab%d" % c + so, AF.Abs, -1.0, T.ra[:, x:x + 1])
-            if early and c == 2:
-                lengths()
-            act(T.eq[:, starts[c]:starts[c] + 3 * n], T.ab[:, at:at + 3 * n], "wc nwc ab%d" % c, "eq%d" % c, AF.Relu,
-                T.wc[:, 4 + c:5 + c], T.wc[:, c:c + 1])
+        for q in (1, 0, 2):
+            for c in mine:
+                n, x = S - 48 * c, 64 * q + 16 * c + 15
+                at = starts[c] + q * n
+                if (c, q) == (0, 2):
+                    for y in rest:
+                        for z in range(3):
+                            weigh(y, z, "eq%d" % y)
+                ts(T.eq[:, at:at + n], T.p1[:, 48 * c:S], T.ra[:, x:x + 1], A.is_equal, "p1 ra%d" % q, "eq%d%d ~v" % (c, q))
+                weigh(c, q, "eq%d%d" % (c, q), (c, q) == (mine[-1], 2))
+                if (c, q) == (0, 1):
+                    on_scalar()
         if not early:
-            lengths()
+            lengths((0, 1, 2))
         zero = ([("Da", 0)] if rank > (rank - 1) % n_ranks else []) + ([("Dz", V - H)] if rank > (rank + 1) % n_ranks else [])
         for k, a in zero:
             act(T.D[:, a:a + H], T.D[:, a:a + H], k + " d4", k, AF.Copy, 0.0)
         if zero:
-            act(T.d3[:], Dw.indirect(T.ew[:]), DK + " ew", "d3")
+            act(T.d3[:], Dw.indirect(T.ew[:]), DK + " ew", "d3 ~s")
             base, bk = (lambda q: T.d3[:, 64 * q:64 * q + 64]), "d3"
         else:
             base, bk = (lambda q: T.d4[:, q::4]), "d4"
-        for c in EQV:
-            for q in range(3):
-                n, x = S - 48 * c, 64 * q + 16 * c + 15
-                at = starts[c] + q * n
-                ts(T.eq[:, at:at + n], T.p1[:, 48 * c:S], T.ra[:, x:x + 1], A.is_equal, "p1 ra wc", "eq%d%d" % (c, q) + vo, T.wc[:, c:c + 1], A.mult)
-                weigh(c, q, "eq%d%d" % (c, q), len(EQV) == 4 and (c, q) == (EQV[-1], 2))
-        rest = [c for c in (2, 3) if c not in EQV]
-        for c in rest:
-            for q in range(3):
-                weigh(c, q, "eq%d" % c, (c, q) == (rest[-1], 2))
+        if t == 0:
+            flag_constants()
         nzu, nk = T.nz[:, 64 * u:64 * u + 64], "nz%d" % u
-        theta = lambda: scan(T.th[:], T.mul4[:], T.d4[:], A.mult, A.subtract, "mul4_0 mul4_1 mul4_2 mul4_3 d4", "th")
-        delta = lambda: tt(T.dlt[:], T.th[:, 3::4], nzu, A.max, "th " + nk, "dlt")
+        theta = lambda: scan(T.th[:], T.mul4[:], T.d4[:], A.mult, A.subtract, "mul4_0 mul4_1 mul4_2 mul4_3 d4", "th" + " ~v" * (not early))
+        delta = lambda: tt(T.dlt[:], T.th[:, 3::4], nzu, A.max, "th " + nk, "dlt" + " ~v" * (not early))
         if early:
             theta()
-        scan(T.ts[:], T.r48[:], T.p2[:, 0:S], A.mult, A.max, "r48 p2", "ts")
-        if early == 2:
+        for c in range(4):
+            scan(T.ts[:, 48 * c:48 * c + 48], T.r48[:], T.p2[:, 48 * c:48 * c + 48], A.mult, A.max, "r48 p2", "ts%d ~w" % c)
+        if early:
             delta()
         for c in range(4):
-            ts(T.off[:, c::4], T.ew[:, c::4], T.ts[:, 48 * c + 47:48 * c + 48], A.max, "ew ts jk", "off%d" % c, T.jk[:, c:c + 1], A.min)
+            ts(T.off[:, c::4], T.ew[:, c::4], T.ts[:, 48 * c + 47:48 * c + 48], A.max, "ew ts%d jk" % c, "off%d ~w" % c, T.jk[:, c:c + 1], A.min)
         OFF = "off0 off1 off2 off3"
         lst = lambda q: T.off[:, 4 * q:4 * q + 4]
+        win, one, wk = (T.lwin, T.onef, "lwin") if last else (T.tw, T.one, "twa twz")
 
-        def stands():
-            act(T.sw[:], T.ts[:, 47::48], "ts", "sw", AF.Sign)
-            mm(T.p0[:, 0:64], T.eye[:], T.one[:], "eye one", "p0", start=True)
-            for r in range(16):
-                mm(T.p0[:, r:64:16], T.wt[:, r, :], T.sw[:], "wt sw", "p0", stop=(r == 15))
-
-        def touch():
-            win, one, keys = (T.lwin, T.onef, "lwin") if last else (T.tw, T.one, "twa twz")
-            for q in range(3):
-                if mixed == 2:
-                    correct(q)
-                cp(win[:, 0:DW].indirect(lst(q)), one[:], "one onef " + OFF, keys + vo)
-                if mixed == 1:
-                    correct(q)
-            if t >= 2:
-                land = T.rf[:] if last else T.rt[:, t - 2, :]
-                op("g", lambda t=t: g.remote_dma(land, win[:, V - H:V], T.sem["rt%d" % t], T.sem["lt%d" % t],
-                                                topo.addr(after)[1], topo.addr(after)[0], bits(eng_a)), keys.split()[-1], "",
-                   ("lt%d" % t, len(eng_a)), cost=300.0, late=REM)
-                op("g", None, "", "rt%d" % t, ("rt%d" % t, n_in_t))
-
-        def own_touch(a, b, out, key):
-            op("v", lambda: v.tensor_tensor_scan(T.sx[:, 16 * a:16 * b], T.m4[:, 0:16 * (b - a)], T.tw[:, 16 * a:16 * b], 0.0, A.mult, A.add),
-               "m4 twa", "sx%d" % a, cost=CYC * max(64, 8 * (b - a)))
-            tt(out, T.sx[:, 16 * a + 15:16 * b:16], T.bar[:, a:b], A.is_gt, "sx%d bar" % a, key)
-
-        if not last:
-            act(T.bar[:], T.fls[:], "fls flsb c18", "bar", AF.Identity, -4e9, col(18))
+        def touch(q):
+            cp(win[:, 0:DW].indirect(lst(q)), one[:], "one onef " + OFF, wk + " ~v")
 
         def correct(q):
-            tt(Dw.indirect(lst(q)), base(q), T.dlt[:], A.subtract if q == 0 else A.add, "dlt %s %s" % (bk, OFF), DK + vo)
+            tt(Dw.indirect(lst(q)), base(q), T.dlt[:], A.subtract if q == 0 else A.add, "dlt %s %s" % (bk, OFF), DK + " ~v" * (t < 2))
 
-        mixed = MIXED[t]
-        if mixed or not last:
-            touch()
+        def tell():
+            land, src = T.rf[:] if last else T.rt[:, t - 2, :], win[:, V - H:V]
+            op("g", lambda t=t: g.remote_dma(land, src, T.sem["rt%d" % t], T.sem["lt%d" % t], topo.addr(after)[1], topo.addr(after)[0], bits(eng_a)),
+               wk.split()[-1], "", ("lt%d" % t, len(eng_a)), cost=300.0, late=REM)
+            op("g", None, "", "rt%d" % t, ("rt%d" % t, n_in_t))
+
+        def own_touch(a, b, out, key, skip=0):
+            scan(T.sx[:, 16 * a:16 * b], T.m4[:, 0:16 * (b - a)], T.tw[:, 16 * a:16 * b], A.mult, A.add, "m4 twa", "sx%d" % a, rate=0.5)
+            if skip:
+                tt(T.fown[:], T.bar[:, a:a + skip], T.sx[:, 16 * a + 15:16 * (a + skip):16], A.subtract, "sx%d bar" % a, "fown")
+            tt(out, T.sx[:, 16 * (a + skip) + 15:16 * b:16], T.bar[:, a + skip:b], A.is_gt, "sx%d bar" % a, key)
 
         def their_touch():
-            op("v", lambda t=t: v.tensor_tensor_scan(T.sx[:, U:U + H], T.m4[:, 0:H], T.rt[:, t - 2, :], 0.0, A.mult, A.add), "m4 rt%d" % t, "sxn")
+            scan(T.sx[:, U:U + H], T.m4[:, 0:H], T.rt[:, t - 2, :], A.mult, A.add, "m4 rt%d" % t, "sxn", rate=0.5)
             tt(T.fl[:, na:na + 8], T.sx[:, U + 15:U + H:16], T.fown[:], A.is_gt, "sxn fown", "flb")
 
-        c0, nc = 8 * (t + 1), (24, 32, 48, 48, 48)[t]
-        na = min(nc, 48 - c0)
+        c0 = 8 * (t + 1)
+        na = (24, 32, 24, 16, 0)[t]
 
         def ranks(h, a, b, keys):
             ps, pk, ps2, pk2 = (T.p4, "p4", T.p3, "p3") if h == 0 else (T.p7, "p7", T.p6, "p6")
@@ -790,62 +742,67 @@ def rank_program(g, core, T, topo):
             ps, pk, ps2, pk2 = (T.p4, "p4", T.p3, "p3") if h == 0 else (T.p7, "p7", T.p6, "p6")
             cp(T.ofe[:, a:b], ps[:, a:b], pk, "ofe%d" % h)
             m = SPLIT[t][h]
-            act(T.lwin[:, 0:4608].indirect(T.ofe[:, a:m]), T.pos[:, 16 * (c0 + a):16 * (c0 + m)], "pos ofe%d" % h, "lwin", AF.Silu)
+            act(T.lwin[:, 0:4608].indirect(T.ofe[:, a:m]), T.pos[:, 16 * (c0 + a):16 * (c0 + m)], "pos0 pos ofe%d" % h, "lwin ~s", AF.Silu)
+            if t == 0:
+                later_constants()
+            e = b if t >= 2 else c0
+            if m < e:
+                cp(T.lwv[:, 0:4608].indirect(T.ofe[:, m:e]), T.pos[:, 16 * (c0 + m):16 * (c0 + e)], "pos ofe%d" % h, "lwv")
             if t < 2:
-                ts(T.lxv[:], T.jd[:], ps[:, m:m + 1], A.subtract, "jd " + pk, "lxv", 16.0 * (c0 + m), A.add)
-            elif m < b:
-                cp(T.lwv[:, 0:4608].indirect(T.ofe[:, m:b]), T.pos[:, 16 * (c0 + m):16 * (c0 + b)], "pos ofe%d" % h, "lwv")
+                out, key = (T.lxv[:], "lxv") if m == e else (T.p6[:, 0:P], "p6 own_p6")
+                ts(out, T.jd[:], ps[:, e:e + 1], A.subtract, "jd " + pk, key, 16.0 * (c0 + e), A.add)
             return lambda: ts(T.fls[:, home:home + b - a], ps2[:, 64 + a:64 + b], 1024 + P - 0.5, A.is_gt, pk2, "fls" + "b" * h)
 
-        def others():
-            if t < 2:
-                own_touch(0, c0, T.fls[:, 0:c0], "flsb")
-            else:
-                own_touch(0, c0, T.fl[:, na:48], "flc flb")
-                act(T.fown[:], T.fl[:, na:na + 8], "flb c18", "fown", AF.Identity, -4e9, col(18))
-
-        if not early:
-            theta()
-            delta()
-        for step in POST[1 if early else 0]:
-            if step in "012":
-                if not mixed:
-                    correct(int(step))
-            elif not last:
-                {"f": lambda: own_touch(c0, c0 + (na if t >= 2 else SPLIT[t][0]), T.fl[:, 0:na if t >= 2 else SPLIT[t][0]], "fla"), "o": others,
-                 "r": lambda: ranks(0, 0, na, "fla")}[step]()
-        stands()
+        if not last:
+            act(T.bar[:], T.fls[:], "fls flsb c18", "bar", AF.Identity, -1e15, col(18))
+        if t < 2:
+            for q in range(3):
+                for step in ((correct, touch), (touch, correct))[t]:
+                    step(q)
+            own_touch(c0, 2 * c0, T.fl[:, 0:c0], "fla")
+            own_touch(0, c0, T.fls[:, 0:c0], "flsb")
+            ranks(0, 0, na, "fla")
+        elif not last:
+            for step in (lambda: touch(0), theta, lambda: touch(1), delta, lambda: touch(2), tell, lambda: correct(0)):
+                step()
+            own_touch(c0, 48, T.fl[:, 0:na], "fla")
+            own_touch(0, c0, T.fl[:, na + 8:48], "flc", 8)
+            correct(1)
+            ranks(0, 0, na, "fla")
+            correct(2)
+        else:
+            for q in range(3):
+                correct(q)
+        act(T.sw[:], T.ts[:, 47::48], "ts0 ts1 ts2 ts3", "sw", AF.Sign)
+        mm(T.p0[:, 0:64], T.eye[:], T.one[:], "eye one", "p0", start=True)
+        for r in range(16):
+            mm(T.p0[:, r:64:16], T.wt[:, r, :], T.sw[:], "wt sw", "p0", stop=(r == 15))
         op("g", lambda t=t: g.remote_dma_fused([
             RemoteDMATransfer(dst_ids=[dst(before)], dma_engine_mask=bits(half_b), remote_sem=T.sem["rd%d" % t],
                               src=T.D[:, 0:H], dst=T.rd[:, t, H:2 * H]),
             RemoteDMATransfer(dst_ids=[dst(after)], dma_engine_mask=bits(half_a), remote_sem=T.sem["rd%d" % t],
                               src=T.D[:, V - H:V], dst=T.rd[:, t, 0:H])], local_sem=T.sem["ld%d" % t]),
-           "Da Dz", "", ("ld%d" % t, len(half_a) + len(half_b)), cost=300.0, late=REM + 500.0 + 1500.0 * (t == 0))
+           "Da Dz", "~g", ("ld%d" % t, len(half_a) + len(half_b)), cost=300.0, late=REM + 500.0 + 1500.0 * (t == 0))
         op("g", None, "", "rd%d" % t, ("rd%d" % t, n_in_d))
         if last:
-            dma("y", T.yd[:, H:V // 2], T.D[:, H:V // 2], "Dm", "", V // 2)
-            dma("s", T.yd[:, V // 2:V - H], T.D[:, V // 2:V - H], "Dm", "", V // 2)
-            if not mixed:
-                touch()
+            dma("y", T.yd[:, H:V - H], T.D[:, H:V - H], "Dm", "")
+            for q in range(3):
+                touch(q)
+            tell()
         else:
             keep = compact(0, 0, na, c0)
-
-        def own_blocks():
-            act(T.p2[:, 0:H], T.D[:, 0:H], "Da", "p2")
-            act(T.p2[:, H:2 * H], T.D[:, V - H:V], "Dz", "p2")
-
-        if t != 2:
-            own_blocks()
+        to_psum(T.p2[:, 0:H], T.D[:, 0:H], "Da", "p2")
+        to_psum(T.p2[:, H:2 * H], T.D[:, V - H:V], "Dz", "p2")
 
         def new_z():
-            tt(T.dm[:], T.p0[:, 0:64], T.dlt[:], A.mult, "p0 dlt", "dm")
-            tt(nzu, nzu, T.dm[:], A.subtract, "dm " + nk, nk)
+            tt(T.th[:, 0:64], T.p0[:, 0:64], T.dlt[:], A.mult, "p0 dlt", "th")
+            tt(nzu, nzu, T.th[:, 0:64], A.subtract, "th " + nk, nk)
 
         def forget():
             new_z()
             ts(T.fil[:], T.ew[:, 0:4], float(V), A.is_lt, "ew", "fil")
             act(T.gr[:], wb[:, 0:S], trb + " c9", "gr", AF.Abs, -1.0, col(9))
-            tt(T.blk[:], T.ts[:, 47::48], T.fil[:], A.min, "ts fil", "blk")
+            tt(T.blk[:], T.ts[:, 47::48], T.fil[:], A.min, "ts0 ts1 ts2 ts3 fil", "blk")
             act(T.gr[:, 64 * u:64 * u + 64], nzu, nk + " gr", "gr", AF.Sign, -1.0)
 
         def forget_count():
@@ -853,7 +810,7 @@ def rank_program(g, core, T, topo):
                 mm(T.p5[:, 0:12], sel(r), T.gr[:, r::16], "zz gr", "p5", start=(r == 0))
             mm(T.p5[:, 4 * u:4 * u + 4], T.eye[:], T.blk[:], "eye blk", "p5", stop=True)
 
-        def forget2():
+        def free_slots():
             ts(T.fre[:], T.p5[:, 0:12], 0.0, A.is_equal, "p5", "fre")
             slot_list()
 
@@ -861,41 +818,39 @@ def rank_program(g, core, T, topo):
             tt(T.D[:, 0:H], T.p2[:, 0:H], T.rd[:, t, 0:H], A.add, "p2 rd%d" % t, "Da")
             tt(T.D[:, V - H:V], T.p2[:, H:2 * H], T.rd[:, t, H:2 * H], A.add, "p2 rd%d" % t, "Dz")
 
-        if not last:
-            wide = U if t < 2 else EXT
-            tab = lambda x: "%sa %sb %sd lw" % (x, x, x) + (" %sc" % x) * (t >= 2)
+        def next_lists(between):
+            if t >= 2:
+                mm(T.p3[:, 0:P], T.eye[:], T.mxb[:], "eye mxb", "p3", start=True, stop=True)
+                tt(T.lxv[:], T.p3[:, 0:P], T.lwv[:, 0:P], A.min, "p3 lwv", "lxv")
+            elif t == 1:
+                tt(T.lxv[:], T.p6[:, 0:P], T.lwv[:, 0:P], A.min, "p6 own_p6 lwv", "lxv")
+            between()
+            for a, b, k in ((0, HEAD, "a"), (HEAD, P, "")):
+                scan(T.lx[:, a:b], T.lxv[:, a:b], T.lwin[:, a:b], A.max, A.min, "lxv lwin", "lx%s ~x" % k)
+            for a, b, k in ((0, HEAD, "a"), (HEAD, P, "")):
+                ts(T.lw[:, a // 16:b // 16], T.lx[:, a + 15:b:16], 0.25, A.add, "lx" + k, "lw%s ~x" % k)
+            for o, table, x in ((T.o2, T.b2t, "2"), (T.o1, T.b1t, "1")):
+                cp(o[:, 0:HEAD], table[:, 0:U if t < 2 else EXT].indirect(T.lw[:, 0:HEAD // 16]),
+                   "b%sa b%sb b%sd lwa" % (x, x, x) + (" b%sc" % x) * (t >= 2), "o%sa" % x)
 
-            def next_lists(between):
-                two = t >= 2 and SPLIT[t] != (na, 48)
-                if two:
-                    mm(T.p3[:, 0:P], T.eye[:], T.mxb[:], "eye mxb", "p3", start=True, stop=True)
-                    tt(T.lxv[:], T.p3[:, 0:P], T.lwv[:, 0:P], A.min, "p3 lwv", "lxv")
-                between()
-                scan(T.lx[:], T.mx[:] if t >= 2 and not two else T.lxv[:], T.lwin[:, 0:P], A.max, A.min, "mx lxv lwin", "lx")
-                ts(T.lw[:], T.lx[:, 15::16], 0.25, A.add, "lx", "lw")
-                cp(T.o2[:, 0:64], T.b2t[:, 0:wide].indirect(T.lw[:, 0:4]), tab("b2"), "o2a")
-                cp(T.o1[:, 0:64], T.b1t[:, 0:wide].indirect(T.lw[:, 0:4]), tab("b1"), "o1a")
-
-            if t < 2:
-                keep()
-                forget()
-                forget_count()
-                pack(P + 256 * t, 2 * P + 256 * t, "b1b b2b", ("bpb", "bpc")[t])
-                forget2()
-                next_lists(lambda: None)
-                take()
-            else:
-                keep()
-                forget()
-                their_touch()
-                ranks(1, na, 48, "flb flc")
-                forget_count()
-                keep = compact(1, na, 48, 0)
-                if t == 2:
-                    own_blocks()
-                next_lists(keep if t == 2 else take)
-                (take if t == 2 else keep)()
-                forget2()
+        if t < 2:
+            keep()
+            forget()
+            forget_count()
+            pack(P + 256 * t, 2 * P + 256 * t, "b1b b2b", ("bpb", "bpc")[t])
+            free_slots()
+            next_lists(lambda: None)
+            take()
+        elif not last:
+            keep()
+            forget()
+            their_touch()
+            ranks(1, na, 48, "flb flc")
+            forget_count()
+            keep = compact(1, na, 48, 0)
+            next_lists(keep if t == 2 else take)
+            (take if t == 2 else keep)()
+            free_slots()
         else:
             new_z()
             planes(lambda: wb[:, 0:S], S, trb)
@@ -928,4 +883,4 @@ def rank_program(g, core, T, topo):
             dma("y", T.yt[:], T.t1[0:128:16, :], "t10 t11 t12", "")
             tt(T.lwin[:, 0:H], T.lwin[:, 0:H], T.rf[:], A.max, "lwin rt%d" % t, "lwin")
             dma("s", T.yf[:], T.lwin[0:128:16, 0:U], "lwin", "")
-    emit(g, T, ops)
+    emit(g, T, arrange(ops))

@@ -4,18 +4,30 @@ from concourse.mybir import AluOpType as A, ActivationFunctionType as AF, AxisLi
 AXX = AxisListType.X
 
 V, U, H, S, P, RO = 3072, 768, 128, 192, 256, 5
-J, WALL, MARK, DW = 3072, 3136, 3144, 3152
+J, WALL, MARK, DW = 3072, 3264, 3272, 3280
 EXT, DUM = 1288, 1280
 MAG = 12582912.0
-CUTS = (0, 16, 40, 64, 96, 128, 160, 192, 200, 224, 240, 256)
-LOOK = "g0 o2 o1 g1 le a0 dl g2 a1 g3 dp a2 g4 a3 b9 c0 g5 a4 b10 a5 g6 c1 g7 g8 a6 a7 bl c2 a8".split()
+LOOKS = [((0, 16, 40, 64, 96, 128, 160, 192, 200, 224, 240, 256),
+          "g0 g1 a0 g2 a1 g3 dp a2 g4 a3 b9 c0 g5 a4 b10 a5 g6 c1 g7 g8 a6 a7 c2 a8".split()),
+         ((0, 32, 64, 96, 128, 160, 192, 200, 224, 240, 256),
+          "g0 o1 o2 dl dp a0 g1 a1 g2 a2 c0 g3 a3 b8 g4 a4 c1 b9 g5 a5 g6 a6 c2 g7 a7 bl".split())]
+TOP = 4
+OWN = 1
+MID = 6
+SOON = 0
+WT = 16
+HALF = 0
+BEFORE, AFTER = 0, 0
+LATE = 12
+BEHIND = 512
 HEAD = 64
 SPLIT = ((8,), (12,), (18, 38), (14, 34))
-EARLY = (True, True, False, False, True)
+TEST = "s0 s1 s2 c3 ew b3 a3 c2 c1 c0 l0 l1 l2 d0 d1 d2".split()
+TOUCH = 0.7310586
 LV, LS = " ~lv", " ~ls"
-CYC, PEC, GA, SCA, WAKE = 0.88, 0.42, 1.5, 3.7, 200.0
-DMA0, DMAB, REM = 900.0, 600.0, 1100.0
-PARTS = "at wt wm m4 pca pcb wc ab2 ab3 d4 zo pct thr lc xs0 xs1 xs2 xs3".split() + ["cmp_%d_%d" % (j, k) for j in range(4) for k in range(0, 16, 4)]
+CYC, PEC, GA, SCA, WAKE = 0.88, 0.6, 1.5, 3.7, 200.0
+DMA0, DMAB, REM, TELL = 900.0, 600.0, 1100.0, 1200.0
+PARTS = "at wt wm m4 d4 zo pct thr e3c lc xs0 xs1 xs2 xs3".split() + ["cmp_%d_%d" % (j, k) for j in range(4) for k in range(0, 16, 4)]
 F32, BF, F16, I32, U16 = "float32", "bfloat16", "float16", "int32", "uint16"
 
 
@@ -24,35 +36,36 @@ def sb(n, d):
 
 
 SCRATCH = {
-    "D": sb(DW, F32), "b1t": sb(EXT, I32), "b2t": sb(EXT, I32), "bp": sb(EXT, F32), "at": sb(EXT, F32), "pos": sb(EXT, F32),
+    "D": sb(U + DW, F32), "b1t": sb(EXT, I32), "b2t": sb(EXT, I32), "bp": sb(EXT, F32), "at": sb(EXT, F32), "pos": sb(EXT, F32),
     "g2": sb(4096, F32), "sm": sb(4096, F32), "cmp": sb([256, 16], BF),
-    "o1": sb(256, U16), "o2": sb(256, U16), "lw": sb(16, U16), "le": sb(16, U16), "lt": sb(32, F32),
+    "o1": sb(256, U16), "o2": sb(256, U16), "lw": sb(16, U16), "lt": sb(16, F32),
     "dl": sb(256, F32), "bl": sb(256, F32), "al": sb(256, F32), "yy": sb(256, F32), "sc": sb(256, BF), "xs": sb(256, BF),
     "prop": sb(16, BF), "pu": sb(16, BF), "pcs": sb(24, BF), "ofl": sb(16, U16),
     "w0": sb(1216, F32), "w1": sb(1216, F32), "ofs": sb(12, U16), "ofs32": sb(12, F32),
     "h16": sb(192, F16), "q16": sb(192, F16), "l16": sb(192, F16),
-    "ra": sb(192, F32), "ew": sb(12, U16), "eq": sb(1440, BF), "ab": sb(432, F32), "ts": sb(192, F32), "off": sb(12, U16),
-    "d4": sb(256, F32), "d3": sb(192, F32), "th": sb(256, F32), "dlt": sb(64, F32), "nz": sb(192, F32),
-    "sw": sb(4, BF), "g0": sb(64, BF), "tw": sb(DW, BF), "gr": sb(192, BF), "fil": sb(4, F32), "blk": sb(4, BF),
+    "ra": sb(192, F32), "ew": sb(12, U16), "eq": sb([30, 57], BF), "ab": sb(492, F32), "ts": sb(64, F32), "off": sb(12, U16),
+    "e3": sb([3, 78], F32), "o3": sb([3, 78], F32),
+    "d4": sb(192, F32), "d3": sb(192, F32), "th": sb(256, F32), "sd": sb(192, F32), "nz": sb(192, F32),
+    "sw": sb(4, BF), "g0": sb(64, BF), "tw": sb(DW, F32), "gr": sb(192, BF), "blk": sb(4, BF),
     "fre": sb(12, BF), "fcs": sb(12, BF),
     "bar": sb(48, F32), "fown": sb(8, F32), "sx": sb(U + H, BF), "fls": sb(48, BF), "fl": sb(48, BF), "fu": sb(48, BF),
     "lcs": sb(56, BF), "ofe": sb(48, U16), "lwin": sb(4608, F32), "lwv": sb(4608, F32), "lx": sb(256, F32), "lxv": sb(256, F32),
-    "rd": sb([RO, 256], F32), "rt": sb([2, 128], BF), "rf": sb(128, F32),
+    "rd": sb([RO, 256], F32), "rt": sb([RO, 8], U16), "twn": sb(DW, F32), "d2": sb(64, F32),
     "zo": sb(192, F32), "t1": sb(576, F32), "t2": sb(576, F32),
-    "ip": sb(8, I32), "col": sb(24, F32), "cm": sb(256, F32), "i128": sb(144, F32), "gi": sb(128, F32), "tmp": sb(16, F32), "tmp2": sb(128, F32),
-    "one": sb(64, BF), "onef": sb(64, F32), "dg": sb(256, F32), "mx": sb(256, F32), "mxb": sb(256, BF), "jd": sb(256, F32),
-    "rs": sb(256, BF), "rmn": sb(64, BF), "mul4": sb(256, F32), "m4": sb(512, BF), "r4": sb(12, F32), "r48": sb(48, F32),
+    "ip": sb(8, I32), "col": sb(24, F32), "cm": sb(256, F32), "i128": sb(144, F32), "gi": sb(128, F32), "tmp": sb(16, F32),
+    "one": sb(128, BF), "onef": sb(192, F32), "dg": sb(256, F32), "mx": sb(256, F32), "mxb": sb(256, BF), "jd": sb(256, F32),
+    "rs": sb(256, BF), "rmn": sb(64, BF), "mul4": sb(192, F32), "m4": sb(512, BF), "r4": sb(12, F32),
     "eye": sb(128, BF), "eyf": sb(128, F32), "neye": sb(128, BF), "bo": sb(128, BF), "nbo": sb(128, BF), "bq": sb(128, BF),
     "tri": sb(128, BF), "zz": sb(144, BF), "wt": sb([16, 128], BF), "lc": sb([4, 128], BF), "wm": sb([4, 128], BF),
     "dfill": sb(128, BF), "dflag": sb(128, BF), "e1k": sb(128, BF), "e512": sb(128, BF), "mgt": sb(128, BF), "hx": sb([6, 128], F16),
     "ckw": sb(128, BF), "cka": sb(192, BF), "c32": sb(16, BF), "c64": sb(48, BF), "cf1": sb(16, BF), "ce1": sb(48, BF),
-    "mka": sb(64, BF), "pca": sb(192, BF), "pcb": sb(192, BF), "pct": sb(576, BF), "wr": sb(64, F32), "thr": sb(192, BF),
-    "wc": sb(4, F32), "jk": sb(4, F32), "own": sb(12, F32), "cpd": sb(192, F32),
+    "mka": sb(64, BF), "pca": sb(64, BF), "pct": sb(576, BF), "thr": sb([4, 19], BF),
+    "wc": sb(12, F32), "jk": sb(4, F32), "own": sb(12, F32), "cpd": sb(192, F32),
     "p0": ("psum", [128, 512], F32), "p1": ("psum", [128, 512], F32), "p2": ("psum", [128, 512], F32), "p3": ("psum", [128, 512], F32),
     "p4": ("psum", [128, 512], F32), "p5": ("psum", [128, 512], F32), "p6": ("psum", [128, 512], F32), "p7": ("psum", [128, 512], F32),
 }
-SEMAPHORES = (["sv", "ss", "st", "sg"] + ["dm%d" % i for i in range(14)]
-              + [k + str(t) for k in ("ld", "rd", "aa", "ab") for t in range(RO)] + [k + str(t) for k in ("lt", "rt") for t in range(2, RO)])
+SEMAPHORES = (["sv", "ss", "st", "sg"] + ["dm%d" % i for i in range(16)]
+              + [k + str(t) for k in ("ld", "rd", "lt", "rt", "aa", "ab", "ac", "ad") for t in range(RO)])
 
 
 def bank(k):
@@ -131,7 +144,7 @@ def arrange(ops):
 
 def emit(g, T, ops):
     Q = {"v": g.vector, "s": g.scalar, "t": g.tensor, "g": g, "y": g.sync}
-    lastw, readers, need, seen = {}, {}, [], {}
+    lastw, readers, need, seen, knew = {}, {}, [], {}, []
     for i, o in enumerate(ops):
         deps = set()
         for k in o["r"]:
@@ -156,11 +169,16 @@ def emit(g, T, ops):
             else:
                 key = ("own", j)
             best[key] = max(best.get(key, -1), j)
-        mine = []
-        for key, j in best.items():
-            if seen.get((o["q"], key), -1) < j:
-                seen[(o["q"], key)] = j
+        mine, know = [], seen.setdefault(o["q"], {})
+        for key, j in sorted(best.items(), key=lambda x: -x[1]):
+            if know.get(key, -1) < j:
                 mine.append(j)
+                know = dict(know)
+                for x, y in list(knew[j].items()) + [(key, j)]:
+                    know[x] = max(know.get(x, -1), y)
+        if o["f"] is not None:
+            seen[o["q"]] = know
+        knew.append(know if o["f"] is not None else {})
         need.append(sorted(mine))
         for k in o["r"]:
             readers.setdefault(k, []).append(i)
@@ -211,8 +229,8 @@ def rank_program(g, core, T, topo):
             n *= d
         return n
 
-    lists = set("o1a o1b o2a o2b lw lwa le ofl0 ofl1 ofs ew off0 ofe0 ofe1".split())
-    windows = "cp0 cp1 twa lwin lwv Da".split()
+    lists = set("o1a o1b o2a o2b lw lwa le ofl0 ofl1 ofs ew off0 ofe0 ofe1 rt0 rt1 rt2 rt3 rt4".split())
+    windows = "cp0 cp1 twa twn lwin lwv Da".split()
 
     def price(out, a, r, w, rate=1.0):
         if lists & set(r.split()) and w[:3] not in ("off", "fil"):
@@ -268,7 +286,7 @@ def rank_program(g, core, T, topo):
     def sel(r):
         return T.zz[:, 15 - r:143 - r]
 
-    Dw = T.D[:, 0:DW]
+    D = Dw = T.D[:, U:U + DW]
     DK = "Da Dm Dz Dj"
     col = lambda i: T.col[:, i:i + 1]
     HX = {name: T.hx[:, i, :] for i, name in enumerate("hq hh hl hn h1 hm".split())}
@@ -277,7 +295,7 @@ def rank_program(g, core, T, topo):
         scan(T.fcs[:], T.r4[:], T.fre[:], A.mult, A.add, "r4 fre", "fcs")
         for u in range(3):
             for w in range(3):
-                mm(T.p5[:, 16 + 4 * u:20 + 4 * u], T.mgt[:], T.fre[:, 4 * w:4 * w + 4], "mgt fre", "p5", start=(w == 0))
+                mm(T.p5[:, 16 + 4 * u:20 + 4 * u], T.mgt[:], T.fre[:, 4 * w:4 * w + 4], "mgt fre", "p5 ~u", start=(w == 0))
                 if w <= u:
                     m = "e512" if w == u else "eye"
                     mm(T.p5[:, 16 + 4 * u:20 + 4 * u], T[m][:], T.fre[:, 4 * w:4 * w + 4], m + " fre", "p5")
@@ -285,73 +303,56 @@ def rank_program(g, core, T, topo):
 
     dma("s", T.b2t[:, 0:P], T.b2[:, 0:P], "", "b2a", V * 5 // 8)
     dma("y", T.b1t[:, 0:P], T.b1[:, 0:P], "", "b1a ~y", V * 5 // 8)
-    dma("y", T.D[:, 0:V], T.dist[:], "", "Da Dm Dz ~y", 2 * P)
-    dma("y", T.b1t[:, P:U], T.b1[:, P:U], "Da Dz", "b1b")
-    dma("g", T.b2t[:, P:U], T.b2[:, P:U], "Da Dz", "b2b ~h")
+    dma("y", D[:, 0:V], T.dist[:], "", "Da Dm Dz ~y", BEHIND)
 
     op("g", lambda: g.iota(T.ip[:, 0:1], [[0, 1]], 0, 1), "", "ip0")
     iota(T.cm[:], [[0, 16], [1, 16]], 0, 0, "cm")
     iota(T.i128[:], [[1, 144]], 0, 0, "i128")
     iota(T.gi[:], [[16, 8], [0, 16]], 0, 0, "gi")
     iota(T.c32[:], [[32, 16]], 0, 0, "c32")
-    iota(T.c64[:], [[64, 48]], 0, 0, "c64")
-    iota(T.pos[:, 0:P], [[1, P]], 0, 0, "pos0")
-    iota(T.pos[:, P:EXT], [[1, EXT - P]], P, 0, "pos")
+    iota(T.pos[:, 0:P], [[1, P]], 0, 0, "pos0 ~h")
+    iota(T.nz[:], [[0, S]], 0, 0, "nz0 nz1 nz2 ~h")
+    dma("g", T.b2t[:, P:P + HEAD], T.b2[:, P:P + HEAD], "", "b2e ~h", V)
     ts(T.ip[:, 1:2], T.ip[:, 0:1], 15, A.bitwise_and, "ip0", "ip1")
     cp(col(0), T.ip[:, 0:1], "ip0", "c0")
     cp(col(1), T.ip[:, 1:2], "ip1", "c1")
-    iota(T.nz[:], [[0, S]], 0, 0, "nz0 nz1 nz2")
-    iota(T.d4[:, 3::4], [[0, 64]], 0, 0, "d4")
-    iota(T.w0[:, 0:S], [[0, S]], 0, 0, "tr0")
-    ms(T.D[:, J:DW], 0.0, "Dj0")
+    ms(D[:, J:DW], 0.0, "Dj0")
     ms(T.one[:], 1.0, "one")
     tt(col(2), col(0), col(1), A.subtract, "c0 c1", "c2")
     ts(col(4), col(1), 0.0, A.is_equal, "c1", "c4")
     ts(col(5), col(1), 1.0, A.is_equal, "c1", "c5", -15.0, A.mult)
-    ts(col(6), col(1), 2.0, A.mult, "c1", "c6", 256.0, A.add)
-    ts(col(7), col(1), 4.0, A.mult, "c1", "c7", 768.0, A.add)
-    ts(col(8), col(1), -4096.0, A.mult, "c1", "c8", -128.0 * 4096, A.add)
-    ts(col(13), col(1), -2.0, A.mult, "c1", "c13", -256.0, A.add)
-    ts(col(14), col(1), -4.0, A.mult, "c1", "c14", -768.0, A.add)
-    ts(T.tmp[:], T.cm[:, 0:16], col(1), A.is_equal, "cm c1", "tmp", -1.0, A.mult)
+    for i, a, b in ((6, 2.0, 256.0), (7, 4.0, 768.0), (8, -4096.0, -128.0 * 4096), (13, -2.0, -256.0), (14, -4.0, -768.0)):
+        act(col(i), col(1), "c1", "c%d" % i, AF.Identity, a, b)
     ts(col(3), col(2), 15.0, A.add, "c2", "c3")
-    ts(col(9), col(4), float(MARK + 1), A.mult, "c4", "c9", (MARK - 1536) / 4096.0 - 1536, A.add)
+    act(col(9), col(4), "c4", "c9", AF.Identity, float(MARK + 1), (MARK - 1536) / 4096.0 - 1536)
     act(T.ckw[:], T.cm[:, 0:H], "cm", "ckw", AF.Identity, -4096.0, -128.0 * 4096)
     act(T.cka[:], T.cm[:, 0:S], "cm c8", "cka", AF.Identity, 0.0, col(8))
     ts(T.eye[:], T.i128[:, 0:128], col(0), A.is_equal, "i128 c0", "eye")
-    ts(T.eyf[:], T.i128[:, 0:128], col(0), A.is_equal, "i128 c0", "eyf")
+    act(T.eyf[:], T.eye[:], "eye", "eyf")
     ts(T.bo[:], T.gi[:], col(2), A.is_equal, "gi c2", "bo")
     ts(T.dg[:], T.cm[:], col(1), A.is_equal, "cm c1", "dg")
+    act(T.tmp[:], T.dg[:, 0:16], "dg", "tmp", AF.Copy, -1.0)
     act(T.mx[:], T.dg[:], "dg", "mx", AF.Identity, 20000.0, -10000.0)
     act(T.cpd[:], T.cm[:, 0:S], "cm c9", "cpd", AF.Identity, 0.0, col(9))
     act(T.e512[:], T.eye[:], "eye", "e512", AF.Identity, 512.0)
-    for r in range(16):
-        act(T.wt[:, r, :], T.bo[:], "bo tmp", "wt", AF.Identity, T.tmp[:, r:r + 1])
     act(T.neye[:], T.eye[:], "eye", "neye", AF.Identity, -1.0)
     act(T.nbo[:], T.bo[:], "bo", "nbo", AF.Identity, -1.0)
     act(T.dfill[:], T.eye[:], "eye c13", "dfill", AF.Identity, col(13))
-    ts(T.tmp2[:], T.cm[:, 0:128], col(1), A.is_gt, "cm c1", "tmp2")
+    ts(T.t2[:, 0:128], T.cm[:, 0:128], col(1), A.is_gt, "cm c1", "tmp2")
     ts(T.zz[:], T.i128[:], col(3), A.is_equal, "i128 c3", "zz", 65536.0, A.mult)
     ms(T.r4[:], 1.0, "r4")
     ms(T.fre[:], 1.0, "fre")
-    tt(T.tri[:], T.tmp2[:], T.bo[:], A.mult, "tmp2 bo", "tri")
+    tt(T.tri[:], T.t2[:, 0:128], T.bo[:], A.mult, "tmp2 bo", "tri")
     ms(T.r4[:, 0::4], 0.0, "r4", "r4")
-    ts(T.rs[:], T.cm[:], 0.0, A.not_equal, "cm", "rs")
+    act(T.rs[:], T.cm[:], "cm", "rs", AF.Sign)
     tt(T.mgt[:], T.tri[:], T.bo[:], A.subtract, "tri bo", "mgt")
     for c in range(4):
-        op("g", lambda c=c: g.affine_select(T.lc[:, c, :], T.tri[:], [[-1, 128]], A.not_equal, -32.0 * c, 0, 1), "tri", "lc", cost=390.0)
+        op("g", lambda c=c: g.affine_select(T.lc[:, c, :], T.tri[:], [[-1, 128]], A.not_equal, -32.0 * c, 0, 1), "tri", "lc ~h", cost=390.0)
     slot_list()
-    ms(T.D[:, WALL:MARK], 1e29, "Dj", "Dj0")
-    ms(T.onef[:], 1.0, "onef")
-    ms(T.b1t[:, DUM:EXT], WALL, "b1d")
-    ms(T.b2t[:, DUM:EXT], WALL, "b2d")
-    ms(T.bp[:, DUM:EXT], 1.0, "bpd")
+    ms(D[:, WALL:MARK], 1e29, "Dj", "Dj0")
     ms(T.pcs[:, 0:1], 0.0, "pcs0")
-    ms(T.lcs[:, 0:1], 0.0, "lcs0")
-    ms(T.fls[:, 0:16], 0.0, "flsb")
-    ms(T.fls[:, 16:48], 1.0, "fls")
-    for q, c in enumerate((0.0, -1.0, 1.0, 0.5)):
-        act(T.mul4[:, q::4], T.cm[:, 0:64], "cm", "mul4_%d" % q, AF.Identity, 0.0, c)
+    for q, c in enumerate((0.0, -1.0, 1.0)):
+        act(T.mul4[:, q::3], T.cm[:, 0:64], "cm", "mul4_%d" % q, AF.Identity, 0.0, c)
     act(T.cf1[:], T.cm[:, 0:16], "cm c6", "cf1", AF.Identity, 0.0, col(6))
     for a, b, k in ((0, HEAD, "a"), (HEAD, P, "b")):
         cp(T.o2[:, a:b], T.b2t[:, a:b], "b2a", "o2" + k)
@@ -360,55 +361,43 @@ def rank_program(g, core, T, topo):
         ts(HX[name], T.bo[:], c, A.mult, "bo", name)
     ts(col(20), col(1), 2.0, A.is_equal, "c1", "c20", 1536.0, A.mult)
     tt(col(21), col(20), col(5), A.add, "c20 c5", "c21")
-    for q, c in enumerate((-2048.0, 344064.0, 30720.0)):
-        ts(col(10 + q), col(4), c, A.mult, "c4 c21", "k%d" % q, col(21) if q == 1 else 0.0, A.add)
-    ts(col(19), col(4), 20992.0, A.mult, "c4", "ka")
+    act(col(11), col(4), "c4 c21", "k1", AF.Identity, 344064.0, col(21))
     act(T.rmn[:], T.rs[:, 0:64], "rs", "rmn", AF.Identity, 2.0 ** 41, -2.0 ** 40)
-    for q in range(3):
-        act(T.pca[:, 64 * q:64 * q + 64], T.cm[:, 0:64], "cm k%d" % q, "pca", AF.Identity, 0.0, col(10 + q))
-        act(T.pcb[:, q::3], T.cm[:, 0:64], "cm k%d" % q, "pcb", AF.Identity, 0.0, col(10 + q))
+    act(T.pca[:], T.cm[:, 0:64], "cm k1", "pca", AF.Identity, 0.0, col(11))
     ms(T.th[:, 0:64], 1.0 / 3.0, "th")
-    scan(T.ts[:, 0:64], T.th[:, 0:64], T.nz[:, 0:64], A.mult, A.add, "th nz0", "ts", 1e29)
-    ms(T.r48[:], 1.0, "r48")
-    ts(T.wr[:], T.ts[:, 0:64], 3.0 ** 64 * 2.0 ** 14 / 1e29, A.mult, "ts", "wr")
-    ms(T.r48[:, 0:1], 0.0, "r48", "r48")
-    tt(T.ts[:, 0:64], T.wr[:], T.dg[:, 0:64], A.mult, "wr dg", "ts")
-    ts(T.th[:, 0:64], T.dg[:, 0:64], -1.0, A.add, "dg wr", "th", 1e29, A.mult)
-    for c in range(4):
-        total(T.wc[:, c:c + 1], T.ts[:, 16 * c:16 * c + 16], "ts ts0 ts1", "wc")
-    ts(T.th[:, 64:128], T.th[:, 0:64], 1e7, A.mult, "th", "th2")
-    ts(T.th[:, 128:192], T.ts[:, 0:64], -2.25, A.mult, "ts ts0 ts1", "th3")
-    ts(T.jk[:], T.cm[:, 0:4], 16.0, A.mult, "cm c1", "jk0", col(1), A.add)
-    ts(T.own[:], T.cm[:, 0:12], 16.0, A.mult, "cm c1", "own0", col(1), A.add)
-    tt(T.th[:, 192:256], T.th[:, 64:128], T.th[:, 128:192], A.add, "th2 th3", "th4")
-    ts(col(15), col(5), 1.0 / 15, A.mult, "c5", "c15")
-    ts(col(16), col(4), 24576.0, A.mult, "c4 c15", "kb", col(15), A.add)
-    ts(col(17), col(4), 3584.0, A.mult, "c4", "kc")
-    ms(T.lt[:, 0:16], 0.125, "lt")
-    scan(T.lt[:, 16:32], T.lt[:, 0:16], T.nz[:, 0:16], A.mult, A.add, "lt nz0", "lt2", 8.0 ** 16 * 0.625)
-    tt(T.lt[:, 0:16], T.lt[:, 16:32], T.dg[:, 0:16], A.mult, "lt2 dg", "lt")
-    total(col(18), T.lt[:, 0:16], "lt", "c18")
-    act(T.lwin[:, 0:P], T.cm[:], "cm", "lwin" + LS, AF.Silu, 0.0, float(DUM))
-    ms(T.fl[:], 1.0, "fla flb flc")
-    ts(T.jk[:], T.jk[:], float(J), A.add, "jk0", "jk")
-    ts(T.own[:], T.own[:], 320.0, A.add, "own0", "own")
+    scan(T.ts[:], T.th[:, 0:64], D[:, J:J + 64], A.mult, A.add, "th Dj0", "ts", 1e29)
+    tt(T.lt[:], T.ts[:, 48:64], T.dg[:, 0:16], A.mult, "ts dg", "lt")
+    total(col(10), T.lt[:], "lt", "c10")
+    act(T.wc[:, 4:8], T.ts[:, 15::16], "ts c10", "wc0", AF.Identity, col(10))
+    act(T.wc[:, 0:4], T.wc[:, 4:8], "wc0", "wc", AF.Copy, 3.0 ** 128 * 2.0 ** 14 / 1e58)
+    act(T.wc[:, 8:12], T.wc[:, 0:4], "wc", "wb", AF.Identity, -5.25, -1e6)
+    act(T.jk[:], T.cm[:, 0:4], "cm c1", "jk0", AF.Identity, 16.0, col(1))
+    act(T.own[:], T.cm[:, 0:12], "cm c1", "own0", AF.Identity, 16.0, col(1))
+    act(T.own[:], T.own[:], "own0", "own", AF.Identity, 1.0, 320.0)
+    act(col(18), col(10), "c10", "c18", AF.Square, 3.0 ** 64 / 1e29 * (0.625 * TOUCH) ** 0.5)
+    act(T.lwin[:, 0:H], T.one[:], "one", "lwin" + LS, AF.Silu, 0.0, float(DUM))
+    act(T.lwin[:, H:P], T.one[:], "one lwin", "lwin" + LS, AF.Identity, 0.0, float(DUM))
     for c in range(4):
         act(T.wm[:, c, :], T.bo[:], "bo wc", "wm", AF.Identity, T.wc[:, c:c + 1])
 
-    def pack(a, b, r, w):
-        ts(T.p1[:, 0:b - a], T.b2t[:, a:b], -1536.0 - 1535 * 4096, A.add, r, "p1 own_p1", 1.0 / 4096, A.mult)
-        tt(T.bp[:, a:b], T.p1[:, 0:b - a], T.b1t[:, a:b], A.add, r + " p1 own_p1", w)
+    def pack(a, b, r, w, bk="p1"):
+        ts(T[bk][:, 0:b - a], T.b2t[:, a:b], -1536.0 - 1535 * 4096, A.add, r, bk + " own_p1", 1.0 / 4096, A.mult)
+        tt(T.bp[:, a:b], T[bk][:, 0:b - a], T.b1t[:, a:b], A.add, r + " own_p1 " + bk, w)
 
     pack(0, P, "b1a b2a", "bpa")
     act(T.at[:, 0:P], T.pos[:, 0:P], "pos0", "at0", AF.Identity, 1.0 / 4096, -1536.0 / 4096 - 1536)
+    for c in range(4):
+        act(T.thr[:, c, 0:16], T.dg[:, 0:16], "dg wb", "thr", AF.Identity, T.wc[:, 8 + c:9 + c], 1e6)
     for q in range(3):
-        act(T.thr[:, q::3], T.th[:, 192:256], "th4 th", "thr")
+        act(T.thr[:, :, 16 + q], T.jk[:], "jk0", "thr", AF.Identity, 1.0, 128.0 - 64 * q)
+    for q in range(3):
+        act(T.e3[:, q, 2 - q:78 - q], T.thr[:], "thr", "e3c", AF.Identity, -1.0, -4000.0)
     act(T.mka[:], T.dg[:, 0:64], "dg", "mka", AF.Identity, 1048576.0, -1048576.0)
 
     def flag_constants():
-        act(T.m4[:, 0:P], T.dg[:], "dg", "m4 ~s", AF.Identity, -8.0, 8.0)
-        act(T.p6[:, 0:P], T.pos[:, 0:P], "pos0 c1", "p6 ~s", AF.Identity, 1.0, col(1))
-        tt(T.jd[:], T.p6[:, 0:P], T.mx[:], A.min, "p6 mx", "jd")
+        act(T.m4[:, 0:P], T.dg[:], "dg", "m4 ~s", AF.Identity, -9.0, 9.0)
+        act(T.p3[:, 0:P], T.pos[:, 0:P], "pos0 c1", "p3 ~s", AF.Identity, 1.0, col(1))
+        tt(T.jd[:], T.p3[:, 0:P], T.mx[:], A.min, "p3 mx", "jd")
         act(T.ce1[:], T.cm[:, 0:48], "cm c7", "ce1 ~s", AF.Identity, 0.0, col(7))
         act(T.dflag[:], T.eye[:], "eye c14", "dflag ~s", AF.Identity, col(14))
         act(T.e1k[:], T.eye[:], "eye", "e1k ~s", AF.Identity, 1024.0)
@@ -417,13 +406,13 @@ def rank_program(g, core, T, topo):
         for a in range(P, EXT, P):
             b = min(EXT, a + P)
             act(T.at[:, a:b], T.pos[:, a:b], "pos", "at ~s", AF.Identity, 1.0 / 4096, (-1536.0 - U * (a >= U)) / 4096 - 1536)
-        act(T.m4[:, P:2 * P], T.dg[:], "dg", "m4 ~s", AF.Identity, -8.0, 8.0)
+        act(T.m4[:, P:2 * P], T.dg[:], "dg", "m4 ~s", AF.Identity, -9.0, 9.0)
         act(T.mxb[:], T.dg[:], "dg", "mxb ~s", AF.Identity, 16384.0, -8192.0)
         act(T.bq[:], T.bo[:], "bo", "bq ~s", AF.Identity, 4096.0)
 
     def planes(src, n, r):
         ts(T.h16[:, 0:n], src(), MAG, A.add, r, "h16", MAG, A.subtract)
-        ts(T.q16[:, 0:n], src(), -1535.5, A.min, r, "q16", 1536.0, A.add)
+        ts(T.q16[:, 0:n], src(), -1535.5, A.min, r, "q16", 1536.0 - 1.0 / 32, A.add)
         tt(T.l16[:, 0:n], src(), T.h16[:, 0:n], A.subtract, r + " h16", "l16")
 
     def rows(outs, a, b, bk):
@@ -446,7 +435,8 @@ def rank_program(g, core, T, topo):
         tra, trb = ("tr0", "tr1") if t % 2 == 0 else ("tr1", "tr0")
         cpa = "cp%d" % (t % 2)
         last = t == RO - 1
-        op("g", lambda wa=wa: g.affine_select(wa[:, S:2 * S], T.cpd[:], [[0, S]], A.is_ge, 0.0, 0, 0), "cpd", cpa + " ~h" * (t > 0), cost=540.0)
+        CUTS, LOOK = LOOKS[min(t, len(LOOKS) - 1)]
+        op("g", lambda wa=wa: g.affine_select(wa[:, S:2 * S], T.cpd[:], [[0, S]], A.is_ge, 0.0, 0, 0), "cpd", cpa + " ~h", cost=540.0)
         wide = U if t < 3 else EXT
         tab = lambda x: "%sa %sb %sd lw" % (x, x, x) + (" %sc" % x) * (t >= 3)
         part = lambda b: "a" if b <= HEAD else "b"
@@ -455,7 +445,7 @@ def rank_program(g, core, T, topo):
 
         def gath(i):
             a, b = CUTS[i], CUTS[i + 1]
-            own = i == 0 and t == 0
+            own = i == 0 and t < OWN
             (cp if own else act)(T.g2[:, 16 * a:16 * b], Dw.indirect(T.o2[:, a:b]), DK + " o2" + part(b), "g2_%d" % i + (LV if own else LS))
 
         def add(i):
@@ -468,8 +458,17 @@ def rank_program(g, core, T, topo):
             gath(i)
             act(T.sm[:, 16 * a:16 * b], Dw.indirect(T.o1[:, a:b]), DK + " o1" + part(b), "sm_%d" % i + LS)
             op("g", lambda: g.dma_start(T.sm[:, 16 * a:16 * b], T.g2[:, 16 * a:16 * b], accum_op=A.add), "g2_%d sm_%d" % (i, i),
-               "sm_%d ~h" % i, ("a%s%d" % ("ab"[adds[0]], t), 16), True, 700.0, 1300.0 + 60.0 * (b - a))
+               "sm_%d ~h" % i, ("a%s%d" % ("abcd"[adds[0]], t), 16), True, 700.0, 1300.0 + 60.0 * (b - a))
             adds[0] += 1
+
+        def hand(i):
+            a, b = CUTS[i], CUTS[i + 1]
+            act(T.sm[:, 16 * a:16 * b], Dw.indirect(T.o1[:, a:b]), DK + " o1" + part(b), "sm_%d" % i + LS)
+            to_psum(T.p3[:, 0:16 * (b - a)], T.sm[:, 16 * a:16 * b], "sm_%d" % i, "p3")
+
+        def plain(i):
+            a, b = CUTS[i], CUTS[i + 1]
+            tt(T.sm[:, 16 * a:16 * b], T.p3[:, 0:16 * (b - a)], T.g2[:, 16 * a:16 * b], A.add, "p3 g2_%d" % i, "sm_%d" % i + LV)
 
         def compare(j, ks=range(0, 16, 4)):
             a, b = 64 * j, 64 * j + 64
@@ -478,7 +477,7 @@ def rank_program(g, core, T, topo):
                     tt(T.cmp[:, a:b, k], T.p7[:, a:b], T.sm[:, 16 * a + k:16 * b:16], A.is_gt, "p7 " + sums(j), "cmp_%d_%d" % (j, k0) + LV)
                 if k0 == 12 and j < 3:
                     wrapped(j, range(16))
-                if k0 < 12 or j < 3:
+                if k0 < LATE or j < 3:
                     counts(j, k0)
 
         def counts(j, k0):
@@ -502,48 +501,54 @@ def rank_program(g, core, T, topo):
         mm(T.p6[:, H:S], T.eye[:], T.ckw[:, 0:64], "eye ckw", "p6", start=True)
         mm(T.p1[:, 0:S], T.eye[:], T.cka[:], "eye cka", "p1", start=True)
         mm(T.p4[:, 0:64], T.eye[:], T.cka[:, 0:64], "eye cka", "p4", start=True)
-        if last:
-            for h, bk in enumerate(("p3", "p2")):
-                for r in range(16):
-                    mm(T[bk][:, r:384:16], T.wt[:, r, :], T.fls[:, 24 * h:24 * h + 24], "wt fls flsb", bk, start=True, stop=True)
 
         def entries():
             act(T.bl[:], T.bp[:, 0:(512, U, EXT, EXT)[t - 1]].indirect(T.lw[:]), "bpa bpb bpc bpe bpd lw lwa", "bl" + LS)
             act(T.al[:], T.at[:, 0:EXT].indirect(T.lw[:]), "at0 at lw lwa", "al" + LS)
 
-        def edges():
-            if t >= 3:
-                ts(T.lt[:, 0:16], T.lx[:, 15::16], U - 0.5, A.is_ge, "lx lxa", "lt", -float(U), A.mult)
-                tt(T.lt[:, 16:32], T.lt[:, 0:16], T.lx[:, 15::16], A.add, "lt lx lxa", "lt2")
-                ts(T.le[:], T.lt[:, 16:32], 0.25, A.add, "lt2", "le")
-
-        if t in (0, 3):
-            iota(T.tw[:, V - H:V], [[0, H]], 0, 0, "twz ~g")
-        if last:
-            iota(T.lwin[:, V - H:V], [[0, H]], 0, 0, "lwin")
-        else:
+        if t >= 3:
+            iota(T.twn[:, V - H:V], [[0, H]], 0, 0, "twn ~g")
+        if 0 < t < RO - 1:
             iota(T.tw[:, 0:U], [[0, U]], 0, 0, "twa ~g")
-            if t > 0:
-                iota(T.lwin[:, 0:P], [[0, P]], DUM, 0, "lwin")
-                iota(T.lwv[:, 0:P], [[0, P]], DUM, 0, "lwv")
+            iota(T.lwin[:, 0:P], [[0, P]], DUM, 0, "lwin")
+            iota(T.lwv[:, 0:P], [[0, P]], DUM, 0, "lwv")
         made = {"o2": lambda: cp(T.o2[:, HEAD:P], T.b2t[:, 0:wide].indirect(T.lw[:, HEAD // 16:16]), tab("b2"), "o2b" + LV * (t >= 3)),
-                "o1": lambda: cp(T.o1[:, HEAD:P], T.b1t[:, 0:wide].indirect(T.lw[:, HEAD // 16:16]), tab("b1"), "o1b" + LV * (t >= 3)),
-                "dl": lambda: cp(T.dl[:], Dw.indirect((T.le if t >= 3 else T.lw)[:]), DK + " le lw lwa", "dl"),
-                "le": edges, "bl": entries}
+                "o1": lambda: cp(T.o1[:], T.b1t[:, 0:wide].indirect(T.lw[:]), tab("b1") + " lwa", "o1a o1b" + LV * (t >= 3)),
+                "dl": lambda: cp(T.dl[:], (T.D[:, 0:EXT] if t >= 3 else Dw).indirect(T.lw[:]), DK + " Dx Dy lw lwa", "dl"),
+                "bl": entries}
         for step in LOOK:
             if step == "dp":
-                to_psum(T.p7[:, 0:P], (T.dl if t > 0 else T.D)[:, 0:P], "dl" if t > 0 else DK, "p7")
+                to_psum(T.p7[:, 0:P], (T.dl if t > 0 else D)[:, 0:P], "dl" if t > 0 else DK, "p7")
             elif step in made:
-                if t > 0:
+                if t > (BEFORE if step[0] == "o" else 0):
                     made[step]()
             else:
-                {"g": gath, "a": add, "b": both, "c": compare}[step[0]](int(step[1:]))
+                {"g": gath, "a": add, "b": both, "h": hand, "p": plain, "c": compare}[step[0]](int(step[1:]))
+        if t == 0:
+            dma("y", T.b1t[:, P:U], T.b1[:, P:U], "cmp_2_0", "b1b", U - P)
+            dma("y", T.b2t[:, P + HEAD:U], T.b2[:, P + HEAD:U], "cmp_2_0 b2e", "b2b", U - P)
+            iota(T.w0[:, 0:S], [[0, S]], 0, 0, "tr0 ~h")
+            iota(T.eq[:, :, 48:57], [[0, 30], [0, 9]], 0, 0, "eqz ~h")
+            iota(T.tw[:, 0:U], [[0, U]], 0, 0, "twa ~g ~h")
+            iota(T.onef[:], [[0, S]], 1, 0, "onef ~h")
+            iota(T.fls[:, 0:16], [[0, 16]], 0, 0, "flsb ~h")
+            iota(T.fls[:, 16:48], [[0, 32]], 1, 0, "fls ~h")
+            iota(T.fl[:], [[0, 48]], 1, 0, "fla flb flc ~h")
+            iota(T.lcs[:, 0:1], [[0, 1]], 0, 0, "lcs0 ~h")
+            for x, c, k in ((T.b1t, WALL, "b1d"), (T.b2t, WALL, "b2d"), (T.bp, 1, "bpd")):
+                iota(x[:, DUM:EXT], [[0, EXT - DUM]], c, 0, k + " ~h")
+            iota(T.c64[:], [[64, 48]], 0, 0, "c64 ~h")
+            iota(T.pos[:, P:EXT], [[1, EXT - P]], P, 0, "pos ~h")
+            iota(T.twn[:, V - H:V], [[0, H]], 0, 0, "twn ~g")
+            iota(T.D[:, 0:U // 2], [[0, U // 2]], 0, 0, "Dy")
         bl, al, blk, alk = (T.bl, T.al, "bl", "al") if t > 0 else (T.bp, T.at, "bpa", "at0")
         if t == 2:
             act(T.bp[:, U:DUM], T.bp[:, 0:DUM - U], "bpa bpb", "bpe")
         if last:
-            for h, bk in enumerate(("p3", "p2")):
-                act(T.lwin[:, 384 * h:384 * h + 384], T[bk][:, 0:384], bk, "lwin", AF.Copy, -1.0)
+            act(col(19), col(4), "c4 al", "ka", AF.Copy, 23040.0)
+            act(col(15), col(5), "c5 al", "c15", AF.Copy, 1.0 / 15)
+            act(col(16), col(4), "c4 c15", "kb", AF.Identity, 24576.0, col(15))
+            act(col(17), col(4), "c4 al", "kc", AF.Copy, 1536.0)
             for q, (c, k) in enumerate(((col(19), "ka"), (col(16), "kb"), (col(17), "kc"))):
                 act(T.pct[:, S * q:S * q + S], T.cm[:, 0:S], "cm " + k, "pct", AF.Identity, 0.0, c)
         span = ((0, 12), (12, 16))
@@ -573,10 +578,10 @@ def rank_program(g, core, T, topo):
                 scan(T.pcs[:, 1:b + 1], T.one[:, 0:b], T.prop[:, 0:b], A.mult, A.add, "one pcs0 prop0", "pcs" + LV)
                 tt(T.pu[:, 0:b], T.prop[:, 0:b], T.c32[:, 0:b], A.mult, "c32 prop0", "pu")
                 act(T.pu[:, b:16], T.one[:, 0:4], "one pcs", "sofar", AF.Identity, 0.0, T.pcs[:, b:b + 1])
-                mm(rank_ps[0], T.tri[:], T.prop[:, 0:b], "tri prop0", "p2")
-                mm(rank_ps[0], T.dfill[:], T.prop[:, 0:b], "dfill prop0", "p2")
-                mm(rank_ps[0], T.bo[:], T.pcs[:, 0:b], "bo pcs0 pcs", "p2")
-                mm(rank_ps[0], T.neye[:], T.pu[:, 0:b], "neye pu", "p2 ~u", stop=True)
+                mm(rank_ps[0], T.tri[:], T.prop[:, 0:b], "tri prop0", rank_k[0])
+                mm(rank_ps[0], T.dfill[:], T.prop[:, 0:b], "dfill prop0", rank_k[0])
+                mm(rank_ps[0], T.bo[:], T.pcs[:, 0:b], "bo pcs0 pcs", rank_k[0])
+                mm(rank_ps[0], T.neye[:], T.pu[:, 0:b], "neye pu", rank_k[0] + " ~u", stop=True)
             else:
                 mm(rank_ps[1], T.bo[:], T.pu[:, a:b], "bo sofar", "p5")
                 mm(rank_ps[1], T.dfill[:], T.prop[:, a:b], "dfill prop1", "p5")
@@ -587,137 +592,133 @@ def rank_program(g, core, T, topo):
 
         def winners(h):
             a, b = span[h]
-            tt(T.yy[:, 16 * a:16 * b], win_ps[h][:, 0:16 * (b - a)], bl[:, 16 * a:16 * b], A.add, win_k[h] + " " + blk, "yy%d" % h)
-            cp(T.ofl[:, a:b], rank_ps[h], rank_k[h], "ofl%d" % h)
+            cp(T.ofl[:, a:b], rank_ps[h], rank_k[h], "ofl%d" % h + " ~w" * h)
+            tt(T.yy[:, 16 * a:16 * b], win_ps[h][:, 0:16 * (b - a)], bl[:, 16 * a:16 * b], A.add, win_k[h] + " " + blk, "yy%d" % h + " ~w" * h)
 
-        def place(h):
-            a, b = span[h]
+        def place(h, a, b):
             tt(wa[:, S:S + 1024].indirect(T.ofl[:, a:b]), T.yy[:, 16 * a:16 * b], al[:, 16 * a:16 * b], A.max,
-               "ofl%d yy%d %s" % (h, h, alk), cpa)
+               "ofl%d yy%d %s" % (h, h, alk), cpa + LV)
 
         top(0, H, "sca")
-        compare(3, (0,))
+        compare(3, range(0, TOP, 4))
         best(0)
-        compare(3, (4, 8, 12))
+        compare(3, range(TOP, 16, 4))
         propose(0)
-        wrapped(3, range(6))
+        wrapped(3, range(MID))
         order(0)
         tt(T.ofs32[:], T.p5[:, 16:28], T.own[:], A.max, "p5 own", "ofs32" + LV)
         ts(T.ofs[:], T.ofs32[:], -320.0, A.add, "ofs32", "ofs")
-        wrapped(3, range(6, 16))
-        counts(3, 12)
+        wrapped(3, range(MID, 16))
+        for k0 in range(LATE, 16, 4):
+            counts(3, k0)
         winners(0)
+        if SOON:
+            place(0, 0, SOON)
         best(1)
         if t == 1:
             dma("y", T.b1t[:, U:DUM], T.b1[:, 0:DUM - U], "sc1", "b1c")
             dma("y", T.b2t[:, U:DUM], T.b2[:, 0:DUM - U], "sc1", "b2c")
-        place(0)
+        place(0, SOON, 12)
+        if t == 0:
+            flag_constants()
+        if t in (1, 2):
+            act(T.twn[:, 0:DW].indirect(T.rt[:, t - 1, :]), T.onef[:, 0:H], "onef al rt%d" % (t - 1), "twn", AF.Silu)
         propose(1)
         order(1)
         winners(1)
         diag = ("p6", "p0", "p7")
         for q in range(3):
             mm(T[diag[q]][:, 0:64], T.eye[:], T.mka[:], "eye mka", diag[q], start=True)
-            mm(T[diag[q]][:, 0:64], T.bo[:], T.pca[:, 64 * q:64 * q + 64], "bo pca", diag[q])
-        mm(T.p1[:, 0:S], T.bo[:], T.pcb[:], "bo pcb", "p1", start=True)
-        mm(T.p3[:, 0:96], T.bo[:], T.pcb[:, 96:S], "bo pcb", "p3", start=True)
-        mm(T.p2[:, 0:S], T.eye[:], T.thr[:], "eye thr", "p2", start=True)
-        place(1)
+        mm(T.p0[:, 0:64], T.bo[:], T.pca[:], "bo pca", "p0")
+        mm(T.p1[:, 1:S:3], T.bo[:], T.pca[:], "bo pca", "p1", start=True)
+        mm(T.p3[:, 1:S:3], T.bo[:], T.pca[:], "bo pca", "p3", start=True)
+        mm(T.p2[:, 0:76], T.eye[:], T.thr[:], "eye thr", "p2", start=True)
+        place(1, 12, 16)
+        if t < 2:
+            for a in (P * (t + 1), P * (t + 1) + H):
+                pack(a, a + H, "b1b b2b", ("bpb", "bpc")[t], "p4")
         planes(lambda: wa[:, 0:2 * S].indirect(T.ofs[:, 4 * u:4 * u + 4]), 64, "ofs %s %s" % (tra, cpa))
         act(wb[:, 0:S], wa[:, 0:2 * S].indirect(T.ofs[:]), "ofs %s %s" % (tra, cpa), trb)
         rows([T[diag[q]][:, 0:64] for q in range(3)], 0, 64, diag)
         rows([T.p1[:, q:S:3] for q in range(3)], 0, 64, ["p1"] * 3)
-        rows([T.p3[:, q:96:3] for q in range(3)], 32, 64, ["p3"] * 3)
+        rows([T.p3[:, q:S:3] for q in range(3)], 0, 64, ["p3"] * 3)
         for q in (1, 0, 2):
-            scan(T.ra[:, 64 * q:64 * q + 64], T.rmn[:], T[diag[q]][:, 0:64], A.min, A.max, "rmn " + diag[q], "ra%d ~v" % q)
-        starts = (0, 576, 1008, 1296)
-        early = EARLY[t]
-        mine, rest = ((0, 1, 3), (2,)) if early else ((0, 1), (2, 3))
+            scan(T.ra[:, 64 * q:64 * q + 64], T.rmn[:], T[diag[q]][:, 0:64], A.min, A.max, "rmn " + diag[q], "ra%d" % q + " ~v" * (q < 2))
+        line = lambda c, q: 10 * q + (0, 4, 7, 9, 10)[c]
+        tt(T.ab[:, 480:484], T.ra[:, 15:64:16], T.ra[:, 79:128:16], A.add, "ra0 ra1", "sum ~v")
+        tt(T.ab[:, 484:488], T.ra[:, 15:64:16], T.ra[:, 79:128:16], A.subtract, "ra0 ra1", "gap ~v")
+        act(T.ab[:, 488:492], T.ab[:, 484:488], "gap", "gap2 ~s", AF.Square)
 
-        def weigh(c, q, key, stop=False):
-            n = S - 48 * c
-            at = starts[c] + q * n
-            mm(T.p2[:, 48 * c:S], T.wm[:, c, :], T.eq[:, at:at + n], "wm " + key, "p2", stop=stop)
+        def square(c):
+            act(T.ab[:, 48 * line(c, 0):48 * line(c + 1, 0)], T.p3[:, 48 * c:S], "p3 sum", "ab%d ~s" % c, AF.Square, -2.0, T.ab[:, 480 + c:481 + c])
 
-        def lengths(qs):
-            if qs[0] == 0:
+        def length(q):
+            act(T.d4[:, q::3], Dw.indirect(T.ew[:, 4 * q:4 * q + 4]), DK + " ew", "d4 ~s")
+
+        def equal(c, q, stop):
+            out = T.eq[:, line(c, q % 3):line(c + 1, q % 3), 0:48]
+            if q < 3:
+                x = 64 * q + 16 * c + 15
+                ts(out, T.p1[:, 48 * c:S], T.ra[:, x:x + 1], A.is_equal, "p1 ra%d" % q, "eq%d%d ~v" % (c, q))
+            else:
+                ts(out, T.ab[:, 48 * line(c, 0):48 * line(c + 1, 0)], T.ab[:, 488 + c:489 + c], A.is_equal, "ab%d gap2" % c, "eq%d0 ~v" % c)
+            for x in range(3):
+                mm(T.p2[:, 19 * c:76], T.wm[:, c, :], T.eq[:, line(c, q % 3):line(c + 1, q % 3), x::3], "wm eqz eq%d%d" % (c, q % 3), "p2",
+                   stop=stop and x == 2)
+
+        for step in TEST:
+            if step == "ew":
                 ts(T.ew[:], T.ra[:, 15::16], 1.0 / 15, A.mult, "ra0 ra1 ra2", "ew ~v", 1536.25, A.add)
-            for q in qs:
-                act(T.d4[:, q::4], Dw.indirect(T.ew[:, 4 * q:4 * q + 4]), DK + " ew", "d4 ~s")
-
-        def on_scalar():
-            for c in rest:
-                for q in (1, 0, 2):
-                    n, x = S - 48 * c, 64 * q + 16 * c + 15
-                    at = starts[c] - starts[2] + q * n
-                    act(T.ab[:, at:at + n], T.p3[:, 48 * c - 96:96], "p3 ra%d" % q, "ab%d ~s" % c, AF.Abs, -1.0, T.ra[:, x:x + 1])
-            if early:
-                lengths((0,))
-            for c in rest:
-                n, at = S - 48 * c, starts[c] - starts[2]
-                act(T.eq[:, starts[c]:starts[c] + 3 * n], T.ab[:, at:at + 3 * n], "ab%d" % c, "eq%d ~s" % c, AF.Relu, -1.0, 1.0)
-            if early:
-                lengths((1, 2))
-
-        for q in (1, 0, 2):
-            for c in mine:
-                n, x = S - 48 * c, 64 * q + 16 * c + 15
-                at = starts[c] + q * n
-                if (c, q) == (0, 2):
-                    for y in rest:
-                        for z in range(3):
-                            weigh(y, z, "eq%d" % y)
-                ts(T.eq[:, at:at + n], T.p1[:, 48 * c:S], T.ra[:, x:x + 1], A.is_equal, "p1 ra%d" % q, "eq%d%d ~v" % (c, q))
-                weigh(c, q, "eq%d%d" % (c, q), (c, q) == (mine[-1], 2))
-                if (c, q) == (0, 1):
-                    on_scalar()
-        if not early:
-            lengths((0, 1, 2))
+            elif step[0] in "sl":
+                {"s": square, "l": length}[step[0]](int(step[1]))
+            else:
+                equal(int(step[1]), "abcd".index(step[0]), step == TEST[-1])
+        act(T.e3[:, :, 18::19], T.ra[:, 15::16], "ra0 ra1 ra2 e3c", "e3w", AF.Identity, 1.0 / 15, 1536.0 - J)
         zero = ([("Da", 0)] if rank > (rank - 1) % n_ranks else []) + ([("Dz", V - H)] if rank > (rank + 1) % n_ranks else [])
         for k, a in zero:
-            act(T.D[:, a:a + H], T.D[:, a:a + H], k + " d4", k, AF.Copy, 0.0)
-        if zero:
-            act(T.d3[:], Dw.indirect(T.ew[:]), DK + " ew", "d3 ~s")
-            base, bk = (lambda q: T.d3[:, 64 * q:64 * q + 64]), "d3"
-        else:
-            base, bk = (lambda q: T.d4[:, q::4]), "d4"
-        if t == 0:
-            flag_constants()
+            act(D[:, a:a + H], D[:, a:a + H], k + " d4", k, AF.Copy, 0.0)
+        act(T.d3[:], Dw.indirect(T.ew[:]), DK + " ew", "d3 ~s")
         nzu, nk = T.nz[:, 64 * u:64 * u + 64], "nz%d" % u
-        theta = lambda: scan(T.th[:], T.mul4[:], T.d4[:], A.mult, A.subtract, "mul4_0 mul4_1 mul4_2 mul4_3 d4", "th" + " ~v" * (not early))
-        delta = lambda: tt(T.dlt[:], T.th[:, 3::4], nzu, A.max, "th " + nk, "dlt" + " ~v" * (not early))
-        if early:
-            theta()
-        for c in range(4):
-            scan(T.ts[:, 48 * c:48 * c + 48], T.r48[:], T.p2[:, 48 * c:48 * c + 48], A.mult, A.max, "r48 p2", "ts%d ~w" % c)
-        if early:
-            delta()
-        for c in range(4):
-            ts(T.off[:, c::4], T.ew[:, c::4], T.ts[:, 48 * c + 47:48 * c + 48], A.max, "ew ts%d jk" % c, "off%d ~w" % c, T.jk[:, c:c + 1], A.min)
-        OFF = "off0 off1 off2 off3"
-        lst = lambda q: T.off[:, 4 * q:4 * q + 4]
-        win, one, wk = (T.lwin, T.onef, "lwin") if last else (T.tw, T.one, "twa twz")
+        dlt = T.sd[:, 64:128]
+        scan(T.th[:, 0:S], T.mul4[:], T.d4[:], A.mult, A.subtract, "mul4_0 mul4_1 mul4_2 d4", "th")
+        for q in (1, 2, 0):
+            scan(T.o3[:, q, 2 - q:76], T.e3[:, q, 2 - q:76], T.p2[:, 0:74 + q], A.max, A.min, "e3c e3w p2", "o3%d" % q)
+        tt(T.d2[:], T.th[:, 2:S:3], nzu, A.max, "th " + nk, "d2")
+        if t in (0, 2, 3):
+            ts(T.off[:, 4:12], T.o3[:, 1:3, 18::19], J + 0.25, A.add, "o31 o32", "off1")
+            ts(T.off[:, 0:4], T.o3[:, 0, 18::19], J + 0.25, A.add, "o30", "off0")
+        else:
+            ts(T.off[:], T.o3[:, :, 18::19], J + 0.25, A.add, "o30 o31 o32", "off0 off1")
+        for q, k in enumerate(("sda", "dlt", "sdc")):
+            if q < HALF:
+                act(T.sd[:, 64 * q:64 * q + 64], T.d2[:], "d2", k, AF.Copy, 0.5 if q else -0.5)
+            else:
+                ts(T.sd[:, 64 * q:64 * q + 64], T.d2[:], 0.5 if q else -0.5, A.mult, "d2", k)
 
-        def touch(q):
-            cp(win[:, 0:DW].indirect(lst(q)), one[:], "one onef " + OFF, wk + " ~v")
+        def touch():
+            act(T.tw[:, 0:DW].indirect(T.off[:]), T.onef[:], "onef off0 off1", "twa ~s", AF.Silu)
 
-        def correct(q):
-            tt(Dw.indirect(lst(q)), base(q), T.dlt[:], A.subtract if q == 0 else A.add, "dlt %s %s" % (bk, OFF), DK + " ~v" * (t < 2))
+        def correct():
+            tt(Dw.indirect(T.off[:]), T.d3[:], T.sd[:], A.add, "dlt sda sdc d3 off0 off1", DK)
 
         def tell():
-            land, src = T.rf[:] if last else T.rt[:, t - 2, :], win[:, V - H:V]
+            land, src = T.rt[:, t, :], T.off[:, 4:12]
             op("g", lambda t=t: g.remote_dma(land, src, T.sem["rt%d" % t], T.sem["lt%d" % t], topo.addr(after)[1], topo.addr(after)[0], bits(eng_a)),
-               wk.split()[-1], "", ("lt%d" % t, len(eng_a)), cost=300.0, late=REM)
+               "off1", "~g", ("lt%d" % t, len(eng_a)), cost=300.0 + 1500.0 * (t == 0), late=TELL)
             op("g", None, "", "rt%d" % t, ("rt%d" % t, n_in_t))
 
+        def hear():
+            act(T.twn[:, 0:DW].indirect(T.rt[:, t, :]), T.onef[:, 0:H], "onef rt%d" % t, "twn ~s", AF.Silu)
+
         def own_touch(a, b, out, key, skip=0):
-            scan(T.sx[:, 16 * a:16 * b], T.m4[:, 0:16 * (b - a)], T.tw[:, 16 * a:16 * b], A.mult, A.add, "m4 twa", "sx%d" % a, rate=0.5)
-            if skip:
-                tt(T.fown[:], T.bar[:, a:a + skip], T.sx[:, 16 * a + 15:16 * (a + skip):16], A.subtract, "sx%d bar" % a, "fown")
-            tt(out, T.sx[:, 16 * (a + skip) + 15:16 * b:16], T.bar[:, a + skip:b], A.is_gt, "sx%d bar" % a, key)
+            scan(T.sx[:, 16 * a:16 * b], T.m4[:, 0:16 * (b - a)], T.tw[:, 16 * a:16 * b], A.mult, A.add, "m4 twa", "sx%d" % a + " ~w" * skip)
+            if key == "fown":
+                tt(out, T.bar[:, a:b], T.sx[:, 16 * a + 15:16 * b:16], A.subtract, "sx%d bar" % a, key)
+            else:
+                tt(out, T.sx[:, 16 * a + 15:16 * b:16], T.bar[:, a:b], A.is_gt, "sx%d bar" % a, key)
 
         def their_touch():
-            scan(T.sx[:, U:U + H], T.m4[:, 0:H], T.rt[:, t - 2, :], A.mult, A.add, "m4 rt%d" % t, "sxn", rate=0.5)
+            scan(T.sx[:, U:U + H], T.m4[:, 0:H], T.twn[:, V - H:V], A.mult, A.add, "m4 twn", "sxn")
             tt(T.fl[:, na:na + 8], T.sx[:, U + 15:U + H:16], T.fown[:], A.is_gt, "sxn fown", "flb")
 
         c0 = 8 * (t + 1)
@@ -727,13 +728,13 @@ def rank_program(g, core, T, topo):
             ps, pk, ps2, pk2 = (T.p4, "p4", T.p3, "p3") if h == 0 else (T.p7, "p7", T.p6, "p6")
             mm(ps[:, a:b], T.eye[:], T.ce1[:, a:b], "eye ce1", pk, start=True)
             mm(ps[:, a:b], T.eye[:], T.c64[:, a:b], "eye c64", pk)
-            scan(T.lcs[:, a + 1:b + 1], T.one[:, a:b], T.fl[:, a:b], A.mult, A.add, "one lcs0 " + keys, "lcs%d" % h,
+            scan(T.lcs[:, a + 1:b + 1], T.one[:, a:b], T.fl[:, a:b], A.mult, A.add, "one lcs0 " + keys, "lcs%d" % h + " ~w" * (h == 0),
                  0.0 if h == 0 else T.lcs[:, a:a + 1])
-            tt(T.fu[:, a:b], T.fl[:, a:b], T.c64[:, a:b], A.mult, "c64 " + keys, "fu%d" % h)
+            tt(T.fu[:, a:b], T.fl[:, a:b], T.c64[:, a:b], A.mult, "c64 " + keys, "fu%d" % h + " ~w" * (h == 0))
             mm(ps[:, a:b], T.tri[:], T.fl[:, a:b], "tri " + keys, pk)
             mm(ps[:, a:b], T.dflag[:], T.fl[:, a:b], "dflag " + keys, pk)
             mm(ps[:, a:b], T.bo[:], T.lcs[:, a:b], "bo lcs0 lcs%d" % h, pk)
-            mm(ps[:, a:b], T.neye[:], T.fu[:, a:b], "neye fu%d" % h, pk, stop=True)
+            mm(ps[:, a:b], T.neye[:], T.fu[:, a:b], "neye fu%d" % h, pk + " ~u", stop=True)
             mm(ps2[:, 64 + a:64 + b], T.tri[:], T.fl[:, a:b], "tri " + keys, pk2, start=True)
             mm(ps2[:, 64 + a:64 + b], T.e1k[:], T.fl[:, a:b], "e1k " + keys, pk2)
             mm(ps2[:, 64 + a:64 + b], T.bo[:], T.lcs[:, a:b], "bo lcs0 lcs%d" % h, pk2, stop=True)
@@ -749,65 +750,70 @@ def rank_program(g, core, T, topo):
             if m < e:
                 cp(T.lwv[:, 0:4608].indirect(T.ofe[:, m:e]), T.pos[:, 16 * (c0 + m):16 * (c0 + e)], "pos ofe%d" % h, "lwv")
             if t < 2:
-                out, key = (T.lxv[:], "lxv") if m == e else (T.p6[:, 0:P], "p6 own_p6")
+                out, key = (T.lxv[:], "lxv lxva") if m == e else (T.p6[:, 0:P], "p6 own_p6")
                 ts(out, T.jd[:], ps[:, e:e + 1], A.subtract, "jd " + pk, key, 16.0 * (c0 + e), A.add)
             return lambda: ts(T.fls[:, home:home + b - a], ps2[:, 64 + a:64 + b], 1024 + P - 0.5, A.is_gt, pk2, "fls" + "b" * h)
 
         if not last:
             act(T.bar[:], T.fls[:], "fls flsb c18", "bar", AF.Identity, -1e15, col(18))
+        if t != 1:
+            tell()
+        touch()
+        correct()
+        if t in (2, 3):
+            hear()
         if t < 2:
-            for q in range(3):
-                for step in ((correct, touch), (touch, correct))[t]:
-                    step(q)
             own_touch(c0, 2 * c0, T.fl[:, 0:c0], "fla")
             own_touch(0, c0, T.fls[:, 0:c0], "flsb")
             ranks(0, 0, na, "fla")
         elif not last:
-            for step in (lambda: touch(0), theta, lambda: touch(1), delta, lambda: touch(2), tell, lambda: correct(0)):
-                step()
             own_touch(c0, 48, T.fl[:, 0:na], "fla")
-            own_touch(0, c0, T.fl[:, na + 8:48], "flc", 8)
-            correct(1)
+            own_touch(0, 8, T.fown[:], "fown")
             ranks(0, 0, na, "fla")
-            correct(2)
+            own_touch(8, c0, T.fl[:, na + 8:48], "flc", 1)
         else:
-            for q in range(3):
-                correct(q)
-        act(T.sw[:], T.ts[:, 47::48], "ts0 ts1 ts2 ts3", "sw", AF.Sign)
-        mm(T.p0[:, 0:64], T.eye[:], T.one[:], "eye one", "p0", start=True)
+            act(T.lwin[:, 0:H], T.tw[:, 0:H], "twa", "lwin", AF.Copy, -1.0)
+            act(T.lwin[:, H:U], T.tw[:, H:U], "lwin twa", "lwb ~s", AF.Sign)
+            hear()
+        if t == 0:
+            for r in range(16):
+                act(T.wt[:, r, :], T.bo[:], "bo tmp " + ("xs3" if r < WT else "twa"), "wt", AF.Identity, T.tmp[:, r:r + 1])
+        act(T.sw[:], T.o3[:, 0, 18::19], "o30", "sw", AF.Sign, 1.0, 0.5)
+        mm(T.p0[:, 0:64], T.eye[:], T.one[:, 0:64], "eye one", "p0", start=True)
         for r in range(16):
             mm(T.p0[:, r:64:16], T.wt[:, r, :], T.sw[:], "wt sw", "p0", stop=(r == 15))
         op("g", lambda t=t: g.remote_dma_fused([
             RemoteDMATransfer(dst_ids=[dst(before)], dma_engine_mask=bits(half_b), remote_sem=T.sem["rd%d" % t],
-                              src=T.D[:, 0:H], dst=T.rd[:, t, H:2 * H]),
+                              src=D[:, 0:H], dst=T.rd[:, t, H:2 * H]),
             RemoteDMATransfer(dst_ids=[dst(after)], dma_engine_mask=bits(half_a), remote_sem=T.sem["rd%d" % t],
-                              src=T.D[:, V - H:V], dst=T.rd[:, t, 0:H])], local_sem=T.sem["ld%d" % t]),
-           "Da Dz", "~g", ("ld%d" % t, len(half_a) + len(half_b)), cost=300.0, late=REM + 500.0 + 1500.0 * (t == 0))
+                              src=D[:, V - H:V], dst=T.rd[:, t, 0:H])], local_sem=T.sem["ld%d" % t]),
+           "Da Dz", "~g", ("ld%d" % t, len(half_a) + len(half_b)), cost=300.0, late=REM + 500.0)
         op("g", None, "", "rd%d" % t, ("rd%d" % t, n_in_d))
-        if last:
-            dma("y", T.yd[:, H:V - H], T.D[:, H:V - H], "Dm", "")
-            for q in range(3):
-                touch(q)
+        if t == 1:
             tell()
+        if last:
+            dma("y", T.yd[:, H:V - H], D[:, H:V - H], "Dm", "")
         else:
             keep = compact(0, 0, na, c0)
-        to_psum(T.p2[:, 0:H], T.D[:, 0:H], "Da", "p2")
-        to_psum(T.p2[:, H:2 * H], T.D[:, V - H:V], "Dz", "p2")
+
+        to_psum(T.p2[:, 0:H], D[:, 0:H], "Da", "p2")
+        to_psum(T.p2[:, H:2 * H], D[:, V - H:V], "Dz", "p2")
+        if t in (2, 3):
+            act(T.D[:, U // 2:U], D[:, U // 2:U], "Dm", "Dx")
 
         def new_z():
-            tt(T.th[:, 0:64], T.p0[:, 0:64], T.dlt[:], A.mult, "p0 dlt", "th")
+            tt(T.th[:, 0:64], T.p0[:, 0:64], dlt, A.mult, "p0 dlt", "th")
             tt(nzu, nzu, T.th[:, 0:64], A.subtract, "th " + nk, nk)
 
         def forget():
             new_z()
-            ts(T.fil[:], T.ew[:, 0:4], float(V), A.is_lt, "ew", "fil")
             act(T.gr[:], wb[:, 0:S], trb + " c9", "gr", AF.Abs, -1.0, col(9))
-            tt(T.blk[:], T.ts[:, 47::48], T.fil[:], A.min, "ts0 ts1 ts2 ts3 fil", "blk")
+            tt(T.blk[:], T.o3[:, 0, 18::19], T.e3[:, 0, 18::19], A.is_gt, "o30 e3w", "blk")
             act(T.gr[:, 64 * u:64 * u + 64], nzu, nk + " gr", "gr", AF.Sign, -1.0)
 
         def forget_count():
             for r in range(16):
-                mm(T.p5[:, 0:12], sel(r), T.gr[:, r::16], "zz gr", "p5", start=(r == 0))
+                mm(T.p5[:, 0:12], sel(r), T.gr[:, r::16], "zz gr", "p5 ~u", start=(r == 0))
             mm(T.p5[:, 4 * u:4 * u + 4], T.eye[:], T.blk[:], "eye blk", "p5", stop=True)
 
         def free_slots():
@@ -815,29 +821,29 @@ def rank_program(g, core, T, topo):
             slot_list()
 
         def take():
-            tt(T.D[:, 0:H], T.p2[:, 0:H], T.rd[:, t, 0:H], A.add, "p2 rd%d" % t, "Da")
-            tt(T.D[:, V - H:V], T.p2[:, H:2 * H], T.rd[:, t, H:2 * H], A.add, "p2 rd%d" % t, "Dz")
+            tt(D[:, 0:H], T.p2[:, 0:H], T.rd[:, t, 0:H], A.add, "p2 rd%d" % t, "Da" + " ~x" * (last or t < AFTER))
+            tt(D[:, V - H:V], T.p2[:, H:2 * H], T.rd[:, t, H:2 * H], A.add, "p2 rd%d" % t, "Dz")
 
         def next_lists(between):
             if t >= 2:
-                mm(T.p3[:, 0:P], T.eye[:], T.mxb[:], "eye mxb", "p3", start=True, stop=True)
-                tt(T.lxv[:], T.p3[:, 0:P], T.lwv[:, 0:P], A.min, "p3 lwv", "lxv")
-            elif t == 1:
-                tt(T.lxv[:], T.p6[:, 0:P], T.lwv[:, 0:P], A.min, "p6 own_p6 lwv", "lxv")
+                mm(T.p1[:, 0:P], T.eye[:], T.mxb[:], "eye mxb", "p1", start=True, stop=True)
+            for a, b, k in ((0, HEAD, "a"), (HEAD, P, "")) if t > 0 else ():
+                bk = "p1" if t >= 2 else "p6"
+                tt(T.lxv[:, a:b], T[bk][:, a:b], T.lwv[:, a:b], A.min, bk + " own_p6 lwv", "lxv%s ~x" % k)
             between()
             for a, b, k in ((0, HEAD, "a"), (HEAD, P, "")):
-                scan(T.lx[:, a:b], T.lxv[:, a:b], T.lwin[:, a:b], A.max, A.min, "lxv lwin", "lx%s ~x" % k)
+                scan(T.lx[:, a:b], T.lxv[:, a:b], T.lwin[:, a:b], A.max, A.min, "lxv%s lwin" % k, "lx%s ~x" % k)
             for a, b, k in ((0, HEAD, "a"), (HEAD, P, "")):
                 ts(T.lw[:, a // 16:b // 16], T.lx[:, a + 15:b:16], 0.25, A.add, "lx" + k, "lw%s ~x" % k)
-            for o, table, x in ((T.o2, T.b2t, "2"), (T.o1, T.b1t, "1")):
-                cp(o[:, 0:HEAD], table[:, 0:U if t < 2 else EXT].indirect(T.lw[:, 0:HEAD // 16]),
-                   "b%sa b%sb b%sd lwa" % (x, x, x) + (" b%sc" % x) * (t >= 2), "o%sa" % x)
+            cp(T.o2[:, 0:HEAD], T.b2t[:, 0:U if t < 2 else EXT].indirect(T.lw[:, 0:HEAD // 16]), "b2a b2b b2d lwa" + " b2c" * (t >= 2), "o2a ~x")
+            if t < BEFORE:
+                cp(T.o1[:], T.b1t[:, 0:U].indirect(T.lw[:]), "b1a b1b b1d lw lwa", "o1a o1b ~x")
+                cp(T.o2[:, HEAD:P], T.b2t[:, 0:U].indirect(T.lw[:, HEAD // 16:16]), "b2a b2b b2d lw", "o2b ~x")
 
         if t < 2:
             keep()
             forget()
             forget_count()
-            pack(P + 256 * t, 2 * P + 256 * t, "b1b b2b", ("bpb", "bpc")[t])
             free_slots()
             next_lists(lambda: None)
             take()
@@ -851,11 +857,16 @@ def rank_program(g, core, T, topo):
             next_lists(keep if t == 2 else take)
             (take if t == 2 else keep)()
             free_slots()
+            if t == 3:
+                for h, bk in enumerate(("p3", "p2")):
+                    for r in range(16):
+                        mm(T[bk][:, r:384:16], T.wt[:, r, :], T.fls[:, 24 * h:24 * h + 24], "wt fls flsb", bk, start=True, stop=True)
+                    act(T.tw[:, 384 * h:384 * h + 384], T[bk][:, 0:384], bk, "twa", AF.Copy, -1.0)
         else:
             new_z()
             planes(lambda: wb[:, 0:S], S, trb)
             for x in range(3):
-                act(T.zo[:, x::3], T.nz[:, 64 * x:64 * x + 64], "nz%d" % x, "zo", AF.Copy, -1.0)
+                act(T.zo[:, x::3], T.nz[:, 64 * x:64 * x + 64], "nz%d" % x, "zo", AF.Copy, -0.5)
             dma("y", T.yz[:], T.zo[:], "zo", "")
             mm(T.p4[:, 0:S], T.bo[:], T.pct[:, 0:S], "bo pct", "p4", start=True)
             mm(T.p1[:, 0:2 * S], T.bo[:], T.pct[:, S:3 * S], "bo pct", "p1", start=True)
@@ -868,19 +879,19 @@ def rank_program(g, core, T, topo):
             ts(T.g0[:], nzu, 0.0, A.not_equal, nk, "g0")
             tt(T.gr[:, 64 * u:64 * u + 64], T.gr[:, 64 * u:64 * u + 64], T.p0[:, 0:64], A.is_gt, "gr p0", "gr")
             for x in range(3):
-                mm(T.p5[:, x:S:3], T.neye[:], T.one[:], "neye one", "p5", start=True)
+                mm(T.p5[:, x:S:3], T.neye[:], T.one[:, 0:64], "neye one", "p5", start=True)
                 if x == u:
                     mm(T.p5[:, x:S:3], T.bq[:], T.g0[:], "bq g0", "p5")
                 mm(T.p5[:, x:S:3], T.bq[:], T.gr[:, 64 * x:64 * x + 64], "bq gr", "p5", stop=True)
             act(T.t2[:, S:3 * S], T.p1[:, 0:2 * S], "p1", "t2b")
             ts(T.t1[:, 0:S], T.p4[:, 0:S], 1.0 / 15, A.mult, "p4", "t1", MAG, A.add)
-            take()
-            dma("y", T.yd[:, 0:H], T.D[:, 0:H], "Da", "", V // 4)
-            dma("s", T.yd[:, V - H:V], T.D[:, V - H:V], "Dz", "", V // 4)
             ts(T.t2[:, 0:S], T.t1[:, 0:S], MAG, A.subtract, "t1", "t2a")
             for q in (1, 2, 0):
-                tt(T.t1[:, S * q:S * q + S], T.p5[:, 0:S], T.t2[:, S * q:S * q + S], A.min, "p5 t2a t2b", "t1%d" % q)
+                tt(T.t1[:, S * q:S * q + S], T.p5[:, 0:S], T.t2[:, S * q:S * q + S], A.min, "p5 t2a t2b", "t1%d ~x" % q)
             dma("y", T.yt[:], T.t1[0:128:16, :], "t10 t11 t12", "")
-            tt(T.lwin[:, 0:H], T.lwin[:, 0:H], T.rf[:], A.max, "lwin rt%d" % t, "lwin")
-            dma("s", T.yf[:], T.lwin[0:128:16, 0:U], "lwin", "")
+            take()
+            dma("y", T.yd[:, 0:H], D[:, 0:H], "Da", "", V // 4)
+            dma("s", T.yd[:, V - H:V], D[:, V - H:V], "Dz", "", V // 4)
+            tt(T.lwin[:, 0:H], T.twn[:, V - H:V], T.lwin[:, 0:H], A.is_gt, "lwin twn", "lwin")
+            dma("s", T.yf[:], T.lwin[0:128:16, 0:U], "lwin lwb", "")
     emit(g, T, arrange(ops))

from concourse.bass import DstId, RemoteDMATransfer
from concourse.mybir import AluOpType as A, ActivationFunctionType as AF, AxisListType

AXX = AxisListType.X

V, U, H, S, P, RO = 3072, 768, 128, 192, 256, 5
J, WALL, MARK, DW = 3072, 3264, 3272, 3280
EXT, DUM = 1288, 1280
MAG = 12582912.0
LOOKS = [((0, 16, 40, 64, 96, 128, 160, 192, 200, 224, 240, 256),
          "g0 g1 a0 g2 a1 g3 dp a2 g4 a3 b9 c0 g5 a4 b10 a5 g6 c1 g7 g8 a6 a7 c2 a8".split()),
         ((0, 32, 64, 96, 128, 160, 192, 200, 224, 240, 256),
          "g0 o1 o2 dl dp a0 g1 a1 g2 a2 c0 g3 a3 b8 g4 a4 c1 b9 g5 a5 g6 a6 c2 g7 a7 bl".split())]
TOP = 4
OWN = 1
MID = 6
SOON = 0
WT = 16
HALF = 0
BEFORE, AFTER = 0, 0
LATE = 12
BEHIND = 512
HEAD = 64
SPLIT = ((8,), (12,), (18, 38), (14, 34))
TEST = "s0 s1 s2 c3 ew b3 a3 c2 c1 c0 l0 l1 l2 d0 d1 d2".split()
TOUCH = 0.7310586
LV, LS = " ~lv", " ~ls"
CYC, PEC, GA, SCA, WAKE = 0.88, 0.6, 1.5, 3.7, 200.0
DMA0, DMAB, REM, TELL = 900.0, 600.0, 1100.0, 1200.0
PARTS = "at wt wm m4 d4 zo pct thr e3c lc xs0 xs1 xs2 xs3".split() + ["cmp_%d_%d" % (j, k) for j in range(4) for k in range(0, 16, 4)]
F32, BF, F16, I32, U16 = "float32", "bfloat16", "float16", "int32", "uint16"


def sb(n, d):
    return ("sbuf", [128] + (n if isinstance(n, list) else [n]), d)


SCRATCH = {
    "D": sb(U + DW, F32), "b1t": sb(EXT, I32), "b2t": sb(EXT, I32), "bp": sb(EXT, F32), "at": sb(EXT, F32), "pos": sb(EXT, F32),
    "g2": sb(4096, F32), "sm": sb(4096, F32), "cmp": sb([256, 16], BF),
    "o1": sb(256, U16), "o2": sb(256, U16), "lw": sb(16, U16), "lt": sb(16, F32),
    "dl": sb(256, F32), "bl": sb(256, F32), "al": sb(256, F32), "yy": sb(256, F32), "sc": sb(256, BF), "xs": sb(256, BF),
    "prop": sb(16, BF), "pu": sb(16, BF), "pcs": sb(24, BF), "ofl": sb(16, U16),
    "w0": sb(1216, F32), "w1": sb(1216, F32), "ofs": sb(12, U16), "ofs32": sb(12, F32),
    "h16": sb(192, F16), "q16": sb(192, F16), "l16": sb(192, F16),
    "ra": sb(192, F32), "ew": sb(12, U16), "eq": sb([30, 57], BF), "ab": sb(492, F32), "ts": sb(64, F32), "off": sb(12, U16),
    "e3": sb([3, 78], F32), "o3": sb([3, 78], F32),
    "d4": sb(192, F32), "d3": sb(192, F32), "th": sb(256, F32), "sd": sb(192, F32), "nz": sb(192, F32),
    "sw": sb(4, BF), "g0": sb(64, BF), "tw": sb(DW, F32), "gr": sb(192, BF), "blk": sb(4, BF),
    "fre": sb(12, BF), "fcs": sb(12, BF),
    "bar": sb(48, F32), "fown": sb(8, F32), "sx": sb(U + H, BF), "fls": sb(48, BF), "fl": sb(48, BF), "fu": sb(48, BF),
    "lcs": sb(56, BF), "ofe": sb(48, U16), "lwin": sb(4608, F32), "lwv": sb(4608, F32), "lx": sb(256, F32), "lxv": sb(256, F32),
    "rd": sb([RO, 256], F32), "rt": sb([RO, 8], U16), "twn": sb(DW, F32), "d2": sb(64, F32),
    "zo": sb(192, F32), "t1": sb(576, F32), "t2": sb(576, F32),
    "ip": sb(8, I32), "col": sb(24, F32), "cm": sb(256, F32), "i128": sb(144, F32), "gi": sb(128, F32), "tmp": sb(16, F32),
    "one": sb(128, BF), "onef": sb(192, F32), "dg": sb(256, F32), "mx": sb(256, F32), "mxb": sb(256, BF), "jd": sb(256, F32),
    "rs": sb(256, BF), "rmn": sb(64, BF), "mul4": sb(192, F32), "m4": sb(512, BF), "r4": sb(12, F32),
    "eye": sb(128, BF), "eyf": sb(128, F32), "neye": sb(128, BF), "bo": sb(128, BF), "nbo": sb(128, BF), "bq": sb(128, BF),
    "tri": sb(128, BF), "zz": sb(144, BF), "wt": sb([16, 128], BF), "lc": sb([4, 128], BF), "wm": sb([4, 128], BF),
    "dfill": sb(128, BF), "dflag": sb(128, BF), "e1k": sb(128, BF), "e512": sb(128, BF), "mgt": sb(128, BF), "hx": sb([6, 128], F16),
    "ckw": sb(128, BF), "cka": sb(192, BF), "c32": sb(16, BF), "c64": sb(48, BF), "cf1": sb(16, BF), "ce1": sb(48, BF),
    "mka": sb(64, BF), "pca": sb(64, BF), "pct": sb(576, BF), "thr": sb([4, 19], BF),
    "wc": sb(12, F32), "jk": sb(4, F32), "own": sb(12, F32), "cpd": sb(192, F32),
    "p0": ("psum", [128, 512], F32), "p1": ("psum", [128, 512], F32), "p2": ("psum", [128, 512], F32), "p3": ("psum", [128, 512], F32),
    "p4": ("psum", [128, 512], F32), "p5": ("psum", [128, 512], F32), "p6": ("psum", [128, 512], F32), "p7": ("psum", [128, 512], F32),
}
SEMAPHORES = (["sv", "ss", "st", "sg"] + ["dm%d" % i for i in range(16)]
              + [k + str(t) for k in ("ld", "rd", "lt", "rt", "aa", "ab", "ac", "ad") for t in range(RO)])


def bank(k):
    return k[0] == "p" and k[1:].isdigit()


def hard(a, b):
    if a["q"] != b["q"] or a["sem"] is not None or b["sem"] is not None:
        return True
    if a["q"] == "t":
        return False
    for k in a["w"]:
        if k[0] != "~" and (k in b["r"] and not bank(k) or k in b["w"] and k not in b["r"] and k not in PARTS):
            return True
    return any(k in b["w"] and not (bank(k) and k in b["r"]) for k in a["r"])


def arrange(ops):
    n = len(ops)
    lastw, readers, sent = {}, {}, {}
    pre, post = [set() for o in ops], [[] for o in ops]
    for i, o in enumerate(ops):
        for k in o["r"] + o["w"]:
            if k in lastw:
                pre[i].add(lastw[k])
        for k in o["w"]:
            pre[i].update(readers.get(k, []))
        if o["f"] is None:
            pre[i].add(sent[o["sem"][0][1:]])
        elif o["sem"] is not None and o["sem"][0][0] == "l":
            sent[o["sem"][0][1:]] = i
        pre[i].discard(i)
        for j in pre[i]:
            post[j].append(i)
        for k in o["r"]:
            readers.setdefault(k, []).append(i)
        for k in o["w"]:
            lastw[k] = i
            readers[k] = []

    def gap(j, i):
        a, b = ops[j], ops[i]
        issue = {"~y", "~g", "~h"}
        if set(a["w"]) & set(b["w"]) & issue and not set(a["r"] + a["w"]) & set(b["r"] + b["w"]) - issue:
            return 0.0
        return a["late"] + (0.0 if b["f"] is None or not hard(a, b) else WAKE)

    def pack(order, before, wait, first):
        at, busy = [0.0] * n, {}
        for i in order:
            c = ops[i]["cost"]
            x = max([first(i)] + [at[j] + ops[j]["cost"] + wait(j, i) for j in before[i]])
            if c > 0:
                row = busy.setdefault(ops[i]["q"], [])
                k = len(row)
                while k > 0 and row[k - 1][1] > x:
                    k -= 1
                while k < len(row) and row[k][0] < x + c:
                    x = max(x, row[k][1])
                    k += 1
                row.insert(k, (x, x + c))
            at[i] = x
        return at

    order = list(range(n))
    for turn in range(3):
        for before, wait, first in ((pre, gap, lambda i: 0.0), (post, lambda j, i: gap(i, j), lambda i: ops[i]["late"])):
            at = pack(order, before, wait, first)
            place = {j: k for k, j in enumerate(order)}
            order.sort(key=lambda i: (-(at[i] + ops[i]["cost"]), -place[i]))
    at = pack(order, pre, gap, lambda i: 0.0)
    place = {j: k for k, j in enumerate(order)}
    order.sort(key=lambda i: (at[i], place[i]))
    return [ops[i] for i in order]


def emit(g, T, ops):
    Q = {"v": g.vector, "s": g.scalar, "t": g.tensor, "g": g, "y": g.sync}
    lastw, readers, need, seen, knew = {}, {}, [], {}, []
    for i, o in enumerate(ops):
        deps = set()
        for k in o["r"]:
            if k in lastw:
                deps.add((lastw[k], not bank(k)))
        for k in o["w"]:
            if k[0] == "~":
                continue
            if k in lastw:
                deps.add((lastw[k], not (k in o["r"] and bank(k) or (k in PARTS and not readers[k]))))
            for j in readers.get(k, []):
                deps.add((j, not (k in o["r"] and bank(k))))
        best = {}
        for j, must in deps:
            p = ops[j]
            if j == i:
                continue
            if p["sem"] is None:
                if p["q"] == o["q"] and o["sem"] is None and (o["q"] == "t" or not must):
                    continue
                key = p["q"]
            else:
                key = ("own", j)
            best[key] = max(best.get(key, -1), j)
        mine, know = [], seen.setdefault(o["q"], {})
        for key, j in sorted(best.items(), key=lambda x: -x[1]):
            if know.get(key, -1) < j:
                mine.append(j)
                know = dict(know)
                for x, y in list(knew[j].items()) + [(key, j)]:
                    know[x] = max(know.get(x, -1), y)
        if o["f"] is not None:
            seen[o["q"]] = know
        knew.append(know if o["f"] is not None else {})
        need.append(sorted(mine))
        for k in o["r"]:
            readers.setdefault(k, []).append(i)
        for k in o["w"]:
            lastw[k] = i
            readers[k] = []
    wanted = set(j for m in need for j in m)
    count, token, total = {}, {}, {}
    for i, o in enumerate(ops):
        if o["sem"] is not None:
            token[i] = o["sem"]
            total[o["sem"][0]] = o["sem"][1]
        elif i in wanted:
            count[o["q"]] = count.get(o["q"], 0) + 1
            token[i] = ("s" + o["q"], count[o["q"]])
            total["s" + o["q"]] = count[o["q"]]
    for i, o in enumerate(ops):
        if o["f"] is None:
            continue
        for j in need[i]:
            Q[o["q"]].wait_ge(T.sem[token[j][0]], token[j][1])
        ins = o["f"]()
        if o["dma"]:
            ins.then_inc(T.sem[o["sem"][0]], 16)
        elif o["sem"] is None and i in token:
            ins.then_inc(T.sem[token[i][0]], 1)
    for name, n in total.items():
        g.wait_ge(T.sem[name], n)


def rank_program(g, core, T, topo):
    rank = T.rank_of(core)
    if rank is None:
        return
    n_ranks = len(T.cores)
    before, after = T.cores[(rank - 1) % n_ranks], T.cores[(rank + 1) % n_ranks]
    ops, nd = [], [0]
    v, s, pe = g.vector, g.scalar, g.tensor

    def op(q, f, r, w, sem=None, dma=False, cost=64 * CYC, late=0.0):
        r, w = r.split(), w.split()
        w += [k for k in r if bank(k)]
        ops.append({"q": q, "f": f, "r": r, "w": w, "sem": sem, "dma": dma, "cost": cost if f else 0.0, "late": late})

    def size(x):
        n = 1
        for d in x.shape[1:]:
            n *= d
        return n

    lists = set("o1a o1b o2a o2b lw lwa le ofl0 ofl1 ofs ew off0 ofe0 ofe1 rt0 rt1 rt2 rt3 rt4".split())
    windows = "cp0 cp1 twa twn lwin lwv Da".split()

    def price(out, a, r, w, rate=1.0):
        if lists & set(r.split()) and w[:3] not in ("off", "fil"):
            return 55.0 + (SCA * CYC * size(a) if w.split()[0] in windows else GA * CYC * size(out))
        return CYC * max(64.0, rate * size(out))

    def dma(q, out, in_, r, w, behind=0):
        e = {"y": g.sync, "s": g.scalar, "g": g}[q]
        op(q, lambda: e.dma_start(out, in_), r, w, ("dm%d" % nd[0], 16), True, 1700.0 if q == "g" else 60.0,
           DMA0 + 128 * 4 * (size(out) + behind) / DMAB)
        nd[0] += 1

    def ts(out, in0, s1, o0, r, w, s2=None, o1=None):
        if o1 is None:
            op("v", lambda: v.tensor_scalar(out, in0, s1, None, o0), r, w, cost=price(out, in0, r, w))
        else:
            op("v", lambda: v.tensor_scalar(out, in0, s1, s2, o0, o1), r, w, cost=price(out, in0, r, w))

    def tt(out, a, b, o, r, w):
        op("v", lambda: v.tensor_tensor(out, a, b, o), r, w, cost=price(out, b, r, w, 1.0 if any(bank(k) for k in r.split()) else 2.0))

    def cp(out, a, r, w):
        op("v", lambda: v.tensor_copy(out, a), r, w, cost=price(out, a, r, w))

    def scan(out, d0, d1, o0, o1, r, w, first=0.0, rate=1.0):
        op("v", lambda: v.tensor_tensor_scan(out, d0, d1, first, o0, o1), r, w, cost=price(out, d0, r, w, rate))

    def ms(out, c, w, r=""):
        op("v", lambda: v.memset(out, c), r, w, cost=price(out, out, "", w))

    def total(out, a, r, w):
        op("v", lambda: v.tensor_reduce(out, a, AXX, A.add), r, w)

    def act(out, a, r, w, func=None, scale=None, bias=None):
        fn = AF.Copy if func is None else func
        c = price(out, a, r, w) + (1300.0 if fn == AF.Silu and bias is not None else 0.0)
        if scale is None:
            op("s", lambda: s.activation(out, a, fn), r, w, cost=c)
        elif bias is not None:
            op("s", lambda: s.activation(out, a, fn, bias=bias, scale=scale), r, w, cost=c)
        else:
            op("s", lambda: s.activation(out, a, fn, scale=scale), r, w, cost=c)

    def mm(out, l, rh, r, w, start=False, stop=False):
        op("t", lambda: pe.matmul(out, l, rh, start, stop), r, w, cost=PEC * max(64, size(out)))

    def to_psum(out, a, r, w):
        op("t", lambda: pe.matmul(out, T.eyf[:], a, True, True), "eyf " + r, w, cost=4 * PEC * size(out))

    def iota(out, pat, base, cmul, w):
        op("g", lambda: g.iota(out, pat, base, cmul, allow_small_or_imprecise_dtypes=True), "", w, cost=130.0 + 2 * CYC * size(out))

    def sel(r):
        return T.zz[:, 15 - r:143 - r]

    D = Dw = T.D[:, U:U + DW]
    DK = "Da Dm Dz Dj"
    col = lambda i: T.col[:, i:i + 1]
    HX = {name: T.hx[:, i, :] for i, name in enumerate("hq hh hl hn h1 hm".split())}

    def slot_list():
        scan(T.fcs[:], T.r4[:], T.fre[:], A.mult, A.add, "r4 fre", "fcs")
        for u in range(3):
            for w in range(3):
                mm(T.p5[:, 16 + 4 * u:20 + 4 * u], T.mgt[:], T.fre[:, 4 * w:4 * w + 4], "mgt fre", "p5 ~u", start=(w == 0))
                if w <= u:
                    m = "e512" if w == u else "eye"
                    mm(T.p5[:, 16 + 4 * u:20 + 4 * u], T[m][:], T.fre[:, 4 * w:4 * w + 4], m + " fre", "p5")
                mm(T.p5[:, 16 + 4 * u:20 + 4 * u], T.bo[:], T.fcs[:, 4 * w:4 * w + 4], "bo fcs", "p5", stop=(w == 2))

    dma("s", T.b2t[:, 0:P], T.b2[:, 0:P], "", "b2a", V * 5 // 8)
    dma("y", T.b1t[:, 0:P], T.b1[:, 0:P], "", "b1a ~y", V * 5 // 8)
    dma("y", D[:, 0:V], T.dist[:], "", "Da Dm Dz ~y", BEHIND)

    op("g", lambda: g.iota(T.ip[:, 0:1], [[0, 1]], 0, 1), "", "ip0")
    iota(T.cm[:], [[0, 16], [1, 16]], 0, 0, "cm")
    iota(T.i128[:], [[1, 144]], 0, 0, "i128")
    iota(T.gi[:], [[16, 8], [0, 16]], 0, 0, "gi")
    iota(T.c32[:], [[32, 16]], 0, 0, "c32")
    iota(T.pos[:, 0:P], [[1, P]], 0, 0, "pos0 ~h")
    iota(T.nz[:], [[0, S]], 0, 0, "nz0 nz1 nz2 ~h")
    dma("g", T.b2t[:, P:P + HEAD], T.b2[:, P:P + HEAD], "", "b2e ~h", V)
    ts(T.ip[:, 1:2], T.ip[:, 0:1], 15, A.bitwise_and, "ip0", "ip1")
    cp(col(0), T.ip[:, 0:1], "ip0", "c0")
    cp(col(1), T.ip[:, 1:2], "ip1", "c1")
    ms(D[:, J:DW], 0.0, "Dj0")
    ms(T.one[:], 1.0, "one")
    tt(col(2), col(0), col(1), A.subtract, "c0 c1", "c2")
    ts(col(4), col(1), 0.0, A.is_equal, "c1", "c4")
    ts(col(5), col(1), 1.0, A.is_equal, "c1", "c5", -15.0, A.mult)
    for i, a, b in ((6, 2.0, 256.0), (7, 4.0, 768.0), (8, -4096.0, -128.0 * 4096), (13, -2.0, -256.0), (14, -4.0, -768.0)):
        act(col(i), col(1), "c1", "c%d" % i, AF.Identity, a, b)
    ts(col(3), col(2), 15.0, A.add, "c2", "c3")
    act(col(9), col(4), "c4", "c9", AF.Identity, float(MARK + 1), (MARK - 1536) / 4096.0 - 1536)
    act(T.ckw[:], T.cm[:, 0:H], "cm", "ckw", AF.Identity, -4096.0, -128.0 * 4096)
    act(T.cka[:], T.cm[:, 0:S], "cm c8", "cka", AF.Identity, 0.0, col(8))
    ts(T.eye[:], T.i128[:, 0:128], col(0), A.is_equal, "i128 c0", "eye")
    act(T.eyf[:], T.eye[:], "eye", "eyf")
    ts(T.bo[:], T.gi[:], col(2), A.is_equal, "gi c2", "bo")
    ts(T.dg[:], T.cm[:], col(1), A.is_equal, "cm c1", "dg")
    act(T.tmp[:], T.dg[:, 0:16], "dg", "tmp", AF.Copy, -1.0)
    act(T.mx[:], T.dg[:], "dg", "mx", AF.Identity, 20000.0, -10000.0)
    act(T.cpd[:], T.cm[:, 0:S], "cm c9", "cpd", AF.Identity, 0.0, col(9))
    act(T.e512[:], T.eye[:], "eye", "e512", AF.Identity, 512.0)
    act(T.neye[:], T.eye[:], "eye", "neye", AF.Identity, -1.0)
    act(T.nbo[:], T.bo[:], "bo", "nbo", AF.Identity, -1.0)
    act(T.dfill[:], T.eye[:], "eye c13", "dfill", AF.Identity, col(13))
    ts(T.t2[:, 0:128], T.cm[:, 0:128], col(1), A.is_gt, "cm c1", "tmp2")
    ts(T.zz[:], T.i128[:], col(3), A.is_equal, "i128 c3", "zz", 65536.0, A.mult)
    ms(T.r4[:], 1.0, "r4")
    ms(T.fre[:], 1.0, "fre")
    tt(T.tri[:], T.t2[:, 0:128], T.bo[:], A.mult, "tmp2 bo", "tri")
    ms(T.r4[:, 0::4], 0.0, "r4", "r4")
    act(T.rs[:], T.cm[:], "cm", "rs", AF.Sign)
    tt(T.mgt[:], T.tri[:], T.bo[:], A.subtract, "tri bo", "mgt")
    for c in range(4):
        op("g", lambda c=c: g.affine_select(T.lc[:, c, :], T.tri[:], [[-1, 128]], A.not_equal, -32.0 * c, 0, 1), "tri", "lc ~h", cost=390.0)
    slot_list()
    ms(D[:, WALL:MARK], 1e29, "Dj", "Dj0")
    ms(T.pcs[:, 0:1], 0.0, "pcs0")
    for q, c in enumerate((0.0, -1.0, 1.0)):
        act(T.mul4[:, q::3], T.cm[:, 0:64], "cm", "mul4_%d" % q, AF.Identity, 0.0, c)
    act(T.cf1[:], T.cm[:, 0:16], "cm c6", "cf1", AF.Identity, 0.0, col(6))
    for a, b, k in ((0, HEAD, "a"), (HEAD, P, "b")):
        cp(T.o2[:, a:b], T.b2t[:, a:b], "b2a", "o2" + k)
        cp(T.o1[:, a:b], T.b1t[:, a:b], "b1a", "o1" + k)
    for name, c in (("hq", 4096.0), ("hh", 15.0), ("hl", 61440.0), ("hn", -61440.0), ("h1", 1.0), ("hm", -4096.0)):
        ts(HX[name], T.bo[:], c, A.mult, "bo", name)
    ts(col(20), col(1), 2.0, A.is_equal, "c1", "c20", 1536.0, A.mult)
    tt(col(21), col(20), col(5), A.add, "c20 c5", "c21")
    act(col(11), col(4), "c4 c21", "k1", AF.Identity, 344064.0, col(21))
    act(T.rmn[:], T.rs[:, 0:64], "rs", "rmn", AF.Identity, 2.0 ** 41, -2.0 ** 40)
    act(T.pca[:], T.cm[:, 0:64], "cm k1", "pca", AF.Identity, 0.0, col(11))
    ms(T.th[:, 0:64], 1.0 / 3.0, "th")
    scan(T.ts[:], T.th[:, 0:64], D[:, J:J + 64], A.mult, A.add, "th Dj0", "ts", 1e29)
    tt(T.lt[:], T.ts[:, 48:64], T.dg[:, 0:16], A.mult, "ts dg", "lt")
    total(col(10), T.lt[:], "lt", "c10")
    act(T.wc[:, 4:8], T.ts[:, 15::16], "ts c10", "wc0", AF.Identity, col(10))
    act(T.wc[:, 0:4], T.wc[:, 4:8], "wc0", "wc", AF.Copy, 3.0 ** 128 * 2.0 ** 14 / 1e58)
    act(T.wc[:, 8:12], T.wc[:, 0:4], "wc", "wb", AF.Identity, -5.25, -1e6)
    act(T.jk[:], T.cm[:, 0:4], "cm c1", "jk0", AF.Identity, 16.0, col(1))
    act(T.own[:], T.cm[:, 0:12], "cm c1", "own0", AF.Identity, 16.0, col(1))
    act(T.own[:], T.own[:], "own0", "own", AF.Identity, 1.0, 320.0)
    act(col(18), col(10), "c10", "c18", AF.Square, 3.0 ** 64 / 1e29 * (0.625 * TOUCH) ** 0.5)
    act(T.lwin[:, 0:H], T.one[:], "one", "lwin" + LS, AF.Silu, 0.0, float(DUM))
    act(T.lwin[:, H:P], T.one[:], "one lwin", "lwin" + LS, AF.Identity, 0.0, float(DUM))
    for c in range(4):
        act(T.wm[:, c, :], T.bo[:], "bo wc", "wm", AF.Identity, T.wc[:, c:c + 1])

    def pack(a, b, r, w, bk="p1"):
        ts(T[bk][:, 0:b - a], T.b2t[:, a:b], -1536.0 - 1535 * 4096, A.add, r, bk + " own_p1", 1.0 / 4096, A.mult)
        tt(T.bp[:, a:b], T[bk][:, 0:b - a], T.b1t[:, a:b], A.add, r + " own_p1 " + bk, w)

    pack(0, P, "b1a b2a", "bpa")
    act(T.at[:, 0:P], T.pos[:, 0:P], "pos0", "at0", AF.Identity, 1.0 / 4096, -1536.0 / 4096 - 1536)
    for c in range(4):
        act(T.thr[:, c, 0:16], T.dg[:, 0:16], "dg wb", "thr", AF.Identity, T.wc[:, 8 + c:9 + c], 1e6)
    for q in range(3):
        act(T.thr[:, :, 16 + q], T.jk[:], "jk0", "thr", AF.Identity, 1.0, 128.0 - 64 * q)
    for q in range(3):
        act(T.e3[:, q, 2 - q:78 - q], T.thr[:], "thr", "e3c", AF.Identity, -1.0, -4000.0)
    act(T.mka[:], T.dg[:, 0:64], "dg", "mka", AF.Identity, 1048576.0, -1048576.0)

    def flag_constants():
        act(T.m4[:, 0:P], T.dg[:], "dg", "m4 ~s", AF.Identity, -9.0, 9.0)
        act(T.p3[:, 0:P], T.pos[:, 0:P], "pos0 c1", "p3 ~s", AF.Identity, 1.0, col(1))
        tt(T.jd[:], T.p3[:, 0:P], T.mx[:], A.min, "p3 mx", "jd")
        act(T.ce1[:], T.cm[:, 0:48], "cm c7", "ce1 ~s", AF.Identity, 0.0, col(7))
        act(T.dflag[:], T.eye[:], "eye c14", "dflag ~s", AF.Identity, col(14))
        act(T.e1k[:], T.eye[:], "eye", "e1k ~s", AF.Identity, 1024.0)

    def later_constants():
        for a in range(P, EXT, P):
            b = min(EXT, a + P)
            act(T.at[:, a:b], T.pos[:, a:b], "pos", "at ~s", AF.Identity, 1.0 / 4096, (-1536.0 - U * (a >= U)) / 4096 - 1536)
        act(T.m4[:, P:2 * P], T.dg[:], "dg", "m4 ~s", AF.Identity, -9.0, 9.0)
        act(T.mxb[:], T.dg[:], "dg", "mxb ~s", AF.Identity, 16384.0, -8192.0)
        act(T.bq[:], T.bo[:], "bo", "bq ~s", AF.Identity, 4096.0)

    def planes(src, n, r):
        ts(T.h16[:, 0:n], src(), MAG, A.add, r, "h16", MAG, A.subtract)
        ts(T.q16[:, 0:n], src(), -1535.5, A.min, r, "q16", 1536.0 - 1.0 / 32, A.add)
        tt(T.l16[:, 0:n], src(), T.h16[:, 0:n], A.subtract, r + " h16", "l16")

    def rows(outs, a, b, bk):
        mm(outs[1], HX["hh"], T.h16[:, a:b], "hh h16", bk[1], stop=bk[1] != bk[2])
        mm(outs[0], HX["hq"], T.q16[:, a:b], "hq q16", bk[0], stop=bk[0] != bk[2])
        mm(outs[2], HX["hn"], T.q16[:, a:b], "hn q16", bk[2])
        mm(outs[2], HX["hl"], T.l16[:, a:b], "hl l16", bk[2], stop=True)

    eng_b, eng_a = topo.engines(core, before), topo.engines(core, after)
    half_b = eng_b[0::2]
    half_a = [e for e in eng_a if e not in half_b][:len(half_b)]
    bits = lambda es: sum(1 << e for e in es)
    dst = lambda c: DstId(rid=topo.addr(c)[0], pnc=topo.addr(c)[1])
    n_in_t = len(topo.engines(before, core))
    n_in_d = len(topo.engines(before, core)) // 2 + len(topo.engines(after, core)) // 2

    for t in range(RO):
        u = t % 3
        wa, wb = (T.w0, T.w1) if t % 2 == 0 else (T.w1, T.w0)
        tra, trb = ("tr0", "tr1") if t % 2 == 0 else ("tr1", "tr0")
        cpa = "cp%d" % (t % 2)
        last = t == RO - 1
        CUTS, LOOK = LOOKS[min(t, len(LOOKS) - 1)]
        op("g", lambda wa=wa: g.affine_select(wa[:, S:2 * S], T.cpd[:], [[0, S]], A.is_ge, 0.0, 0, 0), "cpd", cpa + " ~h", cost=540.0)
        wide = U if t < 3 else EXT
        tab = lambda x: "%sa %sb %sd lw" % (x, x, x) + (" %sc" % x) * (t >= 3)
        part = lambda b: "a" if b <= HEAD else "b"
        sums = lambda j: " ".join("sm_%d" % i for i in range(len(CUTS) - 1) if CUTS[i] // 64 == j)
        adds = [0]

        def gath(i):
            a, b = CUTS[i], CUTS[i + 1]
            own = i == 0 and t < OWN
            (cp if own else act)(T.g2[:, 16 * a:16 * b], Dw.indirect(T.o2[:, a:b]), DK + " o2" + part(b), "g2_%d" % i + (LV if own else LS))

        def add(i):
            a, b = CUTS[i], CUTS[i + 1]
            tt(T.sm[:, 16 * a:16 * b], Dw.indirect(T.o1[:, a:b]), T.g2[:, 16 * a:16 * b], A.add,
               DK + " o1%s g2_%d" % (part(b), i), "sm_%d" % i + LV)

        def both(i):
            a, b = CUTS[i], CUTS[i + 1]
            gath(i)
            act(T.sm[:, 16 * a:16 * b], Dw.indirect(T.o1[:, a:b]), DK + " o1" + part(b), "sm_%d" % i + LS)
            op("g", lambda: g.dma_start(T.sm[:, 16 * a:16 * b], T.g2[:, 16 * a:16 * b], accum_op=A.add), "g2_%d sm_%d" % (i, i),
               "sm_%d ~h" % i, ("a%s%d" % ("abcd"[adds[0]], t), 16), True, 700.0, 1300.0 + 60.0 * (b - a))
            adds[0] += 1

        def hand(i):
            a, b = CUTS[i], CUTS[i + 1]
            act(T.sm[:, 16 * a:16 * b], Dw.indirect(T.o1[:, a:b]), DK + " o1" + part(b), "sm_%d" % i + LS)
            to_psum(T.p3[:, 0:16 * (b - a)], T.sm[:, 16 * a:16 * b], "sm_%d" % i, "p3")

        def plain(i):
            a, b = CUTS[i], CUTS[i + 1]
            tt(T.sm[:, 16 * a:16 * b], T.p3[:, 0:16 * (b - a)], T.g2[:, 16 * a:16 * b], A.add, "p3 g2_%d" % i, "sm_%d" % i + LV)

        def compare(j, ks=range(0, 16, 4)):
            a, b = 64 * j, 64 * j + 64
            for k0 in ks:
                for k in range(k0, k0 + 4):
                    tt(T.cmp[:, a:b, k], T.p7[:, a:b], T.sm[:, 16 * a + k:16 * b:16], A.is_gt, "p7 " + sums(j), "cmp_%d_%d" % (j, k0) + LV)
                if k0 == 12 and j < 3:
                    wrapped(j, range(16))
                if k0 < LATE or j < 3:
                    counts(j, k0)

        def counts(j, k0):
            a, b = 64 * j, 64 * j + 64
            out, bk = (T.p1[:, a:b], "p1") if j < 3 else (T.p4[:, 0:64], "p4")
            for k in range(k0, k0 + 4):
                mm(out, sel(k), T.cmp[:, a:b, k], "zz cmp_%d_%d" % (j, k0), bk)

        def wrapped(j, rs):
            a, b = 64 * j, 64 * j + 64
            keys = " ".join("cmp_%d_%d" % (j, x) for x in range(0, 16, 4))
            for r in rs:
                mm(T.p0[:, a:b] if j < 2 else T.p6[:, a:b], sel(r), T.cmp[:, a + r:b:16, :], "zz " + keys,
                   "p0" if j < 2 else "p6" + " ~u" * (j == 3), stop=(j >= 1 and r == 15))

        def top(a, b, key):
            bk = "p0" if a < H else "p6"
            scan(T.sc[:, a:b], T.rs[:, a:b], T[bk][:, a:b], A.mult, A.max, "rs " + bk, key + LV)

        mm(T.p0[:, 0:H], T.eye[:], T.ckw[:], "eye ckw", "p0", start=True)
        mm(T.p6[:, H:S], T.eye[:], T.ckw[:, 0:64], "eye ckw", "p6", start=True)
        mm(T.p1[:, 0:S], T.eye[:], T.cka[:], "eye cka", "p1", start=True)
        mm(T.p4[:, 0:64], T.eye[:], T.cka[:, 0:64], "eye cka", "p4", start=True)

        def entries():
            act(T.bl[:], T.bp[:, 0:(512, U, EXT, EXT)[t - 1]].indirect(T.lw[:]), "bpa bpb bpc bpe bpd lw lwa", "bl" + LS)
            act(T.al[:], T.at[:, 0:EXT].indirect(T.lw[:]), "at0 at lw lwa", "al" + LS)

        if t >= 3:
            iota(T.twn[:, V - H:V], [[0, H]], 0, 0, "twn ~g")
        if 0 < t < RO - 1:
            iota(T.tw[:, 0:U], [[0, U]], 0, 0, "twa ~g")
            iota(T.lwin[:, 0:P], [[0, P]], DUM, 0, "lwin")
            iota(T.lwv[:, 0:P], [[0, P]], DUM, 0, "lwv")
        made = {"o2": lambda: cp(T.o2[:, HEAD:P], T.b2t[:, 0:wide].indirect(T.lw[:, HEAD // 16:16]), tab("b2"), "o2b" + LV * (t >= 3)),
                "o1": lambda: cp(T.o1[:], T.b1t[:, 0:wide].indirect(T.lw[:]), tab("b1") + " lwa", "o1a o1b" + LV * (t >= 3)),
                "dl": lambda: cp(T.dl[:], (T.D[:, 0:EXT] if t >= 3 else Dw).indirect(T.lw[:]), DK + " Dx Dy lw lwa", "dl"),
                "bl": entries}
        for step in LOOK:
            if step == "dp":
                to_psum(T.p7[:, 0:P], (T.dl if t > 0 else D)[:, 0:P], "dl" if t > 0 else DK, "p7")
            elif step in made:
                if t > (BEFORE if step[0] == "o" else 0):
                    made[step]()
            else:
                {"g": gath, "a": add, "b": both, "h": hand, "p": plain, "c": compare}[step[0]](int(step[1:]))
        if t == 0:
            dma("y", T.b1t[:, P:U], T.b1[:, P:U], "cmp_2_0", "b1b", U - P)
            dma("y", T.b2t[:, P + HEAD:U], T.b2[:, P + HEAD:U], "cmp_2_0 b2e", "b2b", U - P)
            iota(T.w0[:, 0:S], [[0, S]], 0, 0, "tr0 ~h")
            iota(T.eq[:, :, 48:57], [[0, 30], [0, 9]], 0, 0, "eqz ~h")
            iota(T.tw[:, 0:U], [[0, U]], 0, 0, "twa ~g ~h")
            iota(T.onef[:], [[0, S]], 1, 0, "onef ~h")
            iota(T.fls[:, 0:16], [[0, 16]], 0, 0, "flsb ~h")
            iota(T.fls[:, 16:48], [[0, 32]], 1, 0, "fls ~h")
            iota(T.fl[:], [[0, 48]], 1, 0, "fla flb flc ~h")
            iota(T.lcs[:, 0:1], [[0, 1]], 0, 0, "lcs0 ~h")
            for x, c, k in ((T.b1t, WALL, "b1d"), (T.b2t, WALL, "b2d"), (T.bp, 1, "bpd")):
                iota(x[:, DUM:EXT], [[0, EXT - DUM]], c, 0, k + " ~h")
            iota(T.c64[:], [[64, 48]], 0, 0, "c64 ~h")
            iota(T.pos[:, P:EXT], [[1, EXT - P]], P, 0, "pos ~h")
            iota(T.twn[:, V - H:V], [[0, H]], 0, 0, "twn ~g")
            iota(T.D[:, 0:U // 2], [[0, U // 2]], 0, 0, "Dy")
        bl, al, blk, alk = (T.bl, T.al, "bl", "al") if t > 0 else (T.bp, T.at, "bpa", "at0")
        if t == 2:
            act(T.bp[:, U:DUM], T.bp[:, 0:DUM - U], "bpa bpb", "bpe")
        if last:
            act(col(19), col(4), "c4 al", "ka", AF.Copy, 23040.0)
            act(col(15), col(5), "c5 al", "c15", AF.Copy, 1.0 / 15)
            act(col(16), col(4), "c4 c15", "kb", AF.Identity, 24576.0, col(15))
            act(col(17), col(4), "c4 al", "kc", AF.Copy, 1536.0)
            for q, (c, k) in enumerate(((col(19), "ka"), (col(16), "kb"), (col(17), "kc"))):
                act(T.pct[:, S * q:S * q + S], T.cm[:, 0:S], "cm " + k, "pct", AF.Identity, 0.0, c)
        span = ((0, 12), (12, 16))
        rank_ps, rank_k = (T.p2[:, 0:12], T.p5[:, 32:36]), ("p2", "p5")
        win_ps, win_k = (T.p1, T.p4), ("p1", "p4")

        def best(h):
            a, b = span[h]
            top(H if h == 0 else S, 16 * b, "sc%d" % h)
            if h == 0:
                mm(T.p6[:, S:P], T.eye[:], T.ckw[:, 0:64], "eye ckw", "p6", start=True)
            mm(rank_ps[h], T.eye[:], T.cf1[:, a:b], "eye cf1", rank_k[h], start=True)
            mm(rank_ps[h], T.eye[:], T.c32[:, 0:b - a], "eye c32", rank_k[h])

        def propose(h):
            a, b = span[h]
            for c in range(a, b):
                if c == b - 4:
                    act(T.prop[:, a:b], T.sc[:, 16 * a + 15:16 * b:16], "sca sc%d" % h, "prop%d ~p" % h, AF.Sign)
                act(T.xs[:, 16 * c:16 * c + 16], T.mka[:, 0:16], "mka " + ("sca" if c < 8 else "sc%d" % h), "xs%d ~p" % (c // 4),
                    AF.Relu, 1.0, T.sc[:, 16 * c + 15:16 * c + 16])
            mm(win_ps[h][:, 0:16 * (b - a)], T.nbo[:], T.xs[:, 16 * a:16 * b], "nbo " + ("xs0 xs1 xs2", "xs3")[h], win_k[h], stop=True)

        def order(h):
            a, b = span[h]
            if h == 0:
                scan(T.pcs[:, 1:b + 1], T.one[:, 0:b], T.prop[:, 0:b], A.mult, A.add, "one pcs0 prop0", "pcs" + LV)
                tt(T.pu[:, 0:b], T.prop[:, 0:b], T.c32[:, 0:b], A.mult, "c32 prop0", "pu")
                act(T.pu[:, b:16], T.one[:, 0:4], "one pcs", "sofar", AF.Identity, 0.0, T.pcs[:, b:b + 1])
                mm(rank_ps[0], T.tri[:], T.prop[:, 0:b], "tri prop0", rank_k[0])
                mm(rank_ps[0], T.dfill[:], T.prop[:, 0:b], "dfill prop0", rank_k[0])
                mm(rank_ps[0], T.bo[:], T.pcs[:, 0:b], "bo pcs0 pcs", rank_k[0])
                mm(rank_ps[0], T.neye[:], T.pu[:, 0:b], "neye pu", rank_k[0] + " ~u", stop=True)
            else:
                mm(rank_ps[1], T.bo[:], T.pu[:, a:b], "bo sofar", "p5")
                mm(rank_ps[1], T.dfill[:], T.prop[:, a:b], "dfill prop1", "p5")
                for c in range(4):
                    mm(rank_ps[1][:, c:c + 1], T.lc[:, c, :], T.prop[:, a + c:a + c + 1], "lc prop1", "p5")
                for c in range(1, 4):
                    mm(rank_ps[1][:, c:4], T.bo[:], T.prop[:, a:b - c], "bo prop1", "p5", stop=(c == 3))

        def winners(h):
            a, b = span[h]
            cp(T.ofl[:, a:b], rank_ps[h], rank_k[h], "ofl%d" % h + " ~w" * h)
            tt(T.yy[:, 16 * a:16 * b], win_ps[h][:, 0:16 * (b - a)], bl[:, 16 * a:16 * b], A.add, win_k[h] + " " + blk, "yy%d" % h + " ~w" * h)

        def place(h, a, b):
            tt(wa[:, S:S + 1024].indirect(T.ofl[:, a:b]), T.yy[:, 16 * a:16 * b], al[:, 16 * a:16 * b], A.max,
               "ofl%d yy%d %s" % (h, h, alk), cpa + LV)

        top(0, H, "sca")
        compare(3, range(0, TOP, 4))
        best(0)
        compare(3, range(TOP, 16, 4))
        propose(0)
        wrapped(3, range(MID))
        order(0)
        tt(T.ofs32[:], T.p5[:, 16:28], T.own[:], A.max, "p5 own", "ofs32" + LV)
        ts(T.ofs[:], T.ofs32[:], -320.0, A.add, "ofs32", "ofs")
        wrapped(3, range(MID, 16))
        for k0 in range(LATE, 16, 4):
            counts(3, k0)
        winners(0)
        if SOON:
            place(0, 0, SOON)
        best(1)
        if t == 1:
            dma("y", T.b1t[:, U:DUM], T.b1[:, 0:DUM - U], "sc1", "b1c")
            dma("y", T.b2t[:, U:DUM], T.b2[:, 0:DUM - U], "sc1", "b2c")
        place(0, SOON, 12)
        if t == 0:
            flag_constants()
        if t in (1, 2):
            act(T.twn[:, 0:DW].indirect(T.rt[:, t - 1, :]), T.onef[:, 0:H], "onef al rt%d" % (t - 1), "twn", AF.Silu)
        propose(1)
        order(1)
        winners(1)
        diag = ("p6", "p0", "p7")
        for q in range(3):
            mm(T[diag[q]][:, 0:64], T.eye[:], T.mka[:], "eye mka", diag[q], start=True)
        mm(T.p0[:, 0:64], T.bo[:], T.pca[:], "bo pca", "p0")
        mm(T.p1[:, 1:S:3], T.bo[:], T.pca[:], "bo pca", "p1", start=True)
        mm(T.p3[:, 1:S:3], T.bo[:], T.pca[:], "bo pca", "p3", start=True)
        mm(T.p2[:, 0:76], T.eye[:], T.thr[:], "eye thr", "p2", start=True)
        place(1, 12, 16)
        if t < 2:
            for a in (P * (t + 1), P * (t + 1) + H):
                pack(a, a + H, "b1b b2b", ("bpb", "bpc")[t], "p4")
        planes(lambda: wa[:, 0:2 * S].indirect(T.ofs[:, 4 * u:4 * u + 4]), 64, "ofs %s %s" % (tra, cpa))
        act(wb[:, 0:S], wa[:, 0:2 * S].indirect(T.ofs[:]), "ofs %s %s" % (tra, cpa), trb)
        rows([T[diag[q]][:, 0:64] for q in range(3)], 0, 64, diag)
        rows([T.p1[:, q:S:3] for q in range(3)], 0, 64, ["p1"] * 3)
        rows([T.p3[:, q:S:3] for q in range(3)], 0, 64, ["p3"] * 3)
        for q in (1, 0, 2):
            scan(T.ra[:, 64 * q:64 * q + 64], T.rmn[:], T[diag[q]][:, 0:64], A.min, A.max, "rmn " + diag[q], "ra%d" % q + " ~v" * (q < 2))
        line = lambda c, q: 10 * q + (0, 4, 7, 9, 10)[c]
        tt(T.ab[:, 480:484], T.ra[:, 15:64:16], T.ra[:, 79:128:16], A.add, "ra0 ra1", "sum ~v")
        tt(T.ab[:, 484:488], T.ra[:, 15:64:16], T.ra[:, 79:128:16], A.subtract, "ra0 ra1", "gap ~v")
        act(T.ab[:, 488:492], T.ab[:, 484:488], "gap", "gap2 ~s", AF.Square)

        def square(c):
            act(T.ab[:, 48 * line(c, 0):48 * line(c + 1, 0)], T.p3[:, 48 * c:S], "p3 sum", "ab%d ~s" % c, AF.Square, -2.0, T.ab[:, 480 + c:481 + c])

        def length(q):
            act(T.d4[:, q::3], Dw.indirect(T.ew[:, 4 * q:4 * q + 4]), DK + " ew", "d4 ~s")

        def equal(c, q, stop):
            out = T.eq[:, line(c, q % 3):line(c + 1, q % 3), 0:48]
            if q < 3:
                x = 64 * q + 16 * c + 15
                ts(out, T.p1[:, 48 * c:S], T.ra[:, x:x + 1], A.is_equal, "p1 ra%d" % q, "eq%d%d ~v" % (c, q))
            else:
                ts(out, T.ab[:, 48 * line(c, 0):48 * line(c + 1, 0)], T.ab[:, 488 + c:489 + c], A.is_equal, "ab%d gap2" % c, "eq%d0 ~v" % c)
            for x in range(3):
                mm(T.p2[:, 19 * c:76], T.wm[:, c, :], T.eq[:, line(c, q % 3):line(c + 1, q % 3), x::3], "wm eqz eq%d%d" % (c, q % 3), "p2",
                   stop=stop and x == 2)

        for step in TEST:
            if step == "ew":
                ts(T.ew[:], T.ra[:, 15::16], 1.0 / 15, A.mult, "ra0 ra1 ra2", "ew ~v", 1536.25, A.add)
            elif step[0] in "sl":
                {"s": square, "l": length}[step[0]](int(step[1]))
            else:
                equal(int(step[1]), "abcd".index(step[0]), step == TEST[-1])
        act(T.e3[:, :, 18::19], T.ra[:, 15::16], "ra0 ra1 ra2 e3c", "e3w", AF.Identity, 1.0 / 15, 1536.0 - J)
        zero = ([("Da", 0)] if rank > (rank - 1) % n_ranks else []) + ([("Dz", V - H)] if rank > (rank + 1) % n_ranks else [])
        for k, a in zero:
            act(D[:, a:a + H], D[:, a:a + H], k + " d4", k, AF.Copy, 0.0)
        act(T.d3[:], Dw.indirect(T.ew[:]), DK + " ew", "d3 ~s")
        nzu, nk = T.nz[:, 64 * u:64 * u + 64], "nz%d" % u
        dlt = T.sd[:, 64:128]
        scan(T.th[:, 0:S], T.mul4[:], T.d4[:], A.mult, A.subtract, "mul4_0 mul4_1 mul4_2 d4", "th")
        for q in (1, 2, 0):
            scan(T.o3[:, q, 2 - q:76], T.e3[:, q, 2 - q:76], T.p2[:, 0:74 + q], A.max, A.min, "e3c e3w p2", "o3%d" % q)
        tt(T.d2[:], T.th[:, 2:S:3], nzu, A.max, "th " + nk, "d2")
        if t in (0, 2, 3):
            ts(T.off[:, 4:12], T.o3[:, 1:3, 18::19], J + 0.25, A.add, "o31 o32", "off1")
            ts(T.off[:, 0:4], T.o3[:, 0, 18::19], J + 0.25, A.add, "o30", "off0")
        else:
            ts(T.off[:], T.o3[:, :, 18::19], J + 0.25, A.add, "o30 o31 o32", "off0 off1")
        for q, k in enumerate(("sda", "dlt", "sdc")):
            if q < HALF:
                act(T.sd[:, 64 * q:64 * q + 64], T.d2[:], "d2", k, AF.Copy, 0.5 if q else -0.5)
            else:
                ts(T.sd[:, 64 * q:64 * q + 64], T.d2[:], 0.5 if q else -0.5, A.mult, "d2", k)

        def touch():
            act(T.tw[:, 0:DW].indirect(T.off[:]), T.onef[:], "onef off0 off1", "twa ~s", AF.Silu)

        def correct():
            tt(Dw.indirect(T.off[:]), T.d3[:], T.sd[:], A.add, "dlt sda sdc d3 off0 off1", DK)

        def tell():
            land, src = T.rt[:, t, :], T.off[:, 4:12]
            op("g", lambda t=t: g.remote_dma(land, src, T.sem["rt%d" % t], T.sem["lt%d" % t], topo.addr(after)[1], topo.addr(after)[0], bits(eng_a)),
               "off1", "~g", ("lt%d" % t, len(eng_a)), cost=300.0 + 1500.0 * (t == 0), late=TELL)
            op("g", None, "", "rt%d" % t, ("rt%d" % t, n_in_t))

        def hear():
            act(T.twn[:, 0:DW].indirect(T.rt[:, t, :]), T.onef[:, 0:H], "onef rt%d" % t, "twn ~s", AF.Silu)

        def own_touch(a, b, out, key, skip=0):
            scan(T.sx[:, 16 * a:16 * b], T.m4[:, 0:16 * (b - a)], T.tw[:, 16 * a:16 * b], A.mult, A.add, "m4 twa", "sx%d" % a + " ~w" * skip)
            if key == "fown":
                tt(out, T.bar[:, a:b], T.sx[:, 16 * a + 15:16 * b:16], A.subtract, "sx%d bar" % a, key)
            else:
                tt(out, T.sx[:, 16 * a + 15:16 * b:16], T.bar[:, a:b], A.is_gt, "sx%d bar" % a, key)

        def their_touch():
            scan(T.sx[:, U:U + H], T.m4[:, 0:H], T.twn[:, V - H:V], A.mult, A.add, "m4 twn", "sxn")
            tt(T.fl[:, na:na + 8], T.sx[:, U + 15:U + H:16], T.fown[:], A.is_gt, "sxn fown", "flb")

        c0 = 8 * (t + 1)
        na = (24, 32, 24, 16, 0)[t]

        def ranks(h, a, b, keys):
            ps, pk, ps2, pk2 = (T.p4, "p4", T.p3, "p3") if h == 0 else (T.p7, "p7", T.p6, "p6")
            mm(ps[:, a:b], T.eye[:], T.ce1[:, a:b], "eye ce1", pk, start=True)
            mm(ps[:, a:b], T.eye[:], T.c64[:, a:b], "eye c64", pk)
            scan(T.lcs[:, a + 1:b + 1], T.one[:, a:b], T.fl[:, a:b], A.mult, A.add, "one lcs0 " + keys, "lcs%d" % h + " ~w" * (h == 0),
                 0.0 if h == 0 else T.lcs[:, a:a + 1])
            tt(T.fu[:, a:b], T.fl[:, a:b], T.c64[:, a:b], A.mult, "c64 " + keys, "fu%d" % h + " ~w" * (h == 0))
            mm(ps[:, a:b], T.tri[:], T.fl[:, a:b], "tri " + keys, pk)
            mm(ps[:, a:b], T.dflag[:], T.fl[:, a:b], "dflag " + keys, pk)
            mm(ps[:, a:b], T.bo[:], T.lcs[:, a:b], "bo lcs0 lcs%d" % h, pk)
            mm(ps[:, a:b], T.neye[:], T.fu[:, a:b], "neye fu%d" % h, pk + " ~u", stop=True)
            mm(ps2[:, 64 + a:64 + b], T.tri[:], T.fl[:, a:b], "tri " + keys, pk2, start=True)
            mm(ps2[:, 64 + a:64 + b], T.e1k[:], T.fl[:, a:b], "e1k " + keys, pk2)
            mm(ps2[:, 64 + a:64 + b], T.bo[:], T.lcs[:, a:b], "bo lcs0 lcs%d" % h, pk2, stop=True)

        def compact(h, a, b, home):
            ps, pk, ps2, pk2 = (T.p4, "p4", T.p3, "p3") if h == 0 else (T.p7, "p7", T.p6, "p6")
            cp(T.ofe[:, a:b], ps[:, a:b], pk, "ofe%d" % h)
            m = SPLIT[t][h]
            act(T.lwin[:, 0:4608].indirect(T.ofe[:, a:m]), T.pos[:, 16 * (c0 + a):16 * (c0 + m)], "pos0 pos ofe%d" % h, "lwin ~s", AF.Silu)
            if t == 0:
                later_constants()
            e = b if t >= 2 else c0
            if m < e:
                cp(T.lwv[:, 0:4608].indirect(T.ofe[:, m:e]), T.pos[:, 16 * (c0 + m):16 * (c0 + e)], "pos ofe%d" % h, "lwv")
            if t < 2:
                out, key = (T.lxv[:], "lxv lxva") if m == e else (T.p6[:, 0:P], "p6 own_p6")
                ts(out, T.jd[:], ps[:, e:e + 1], A.subtract, "jd " + pk, key, 16.0 * (c0 + e), A.add)
            return lambda: ts(T.fls[:, home:home + b - a], ps2[:, 64 + a:64 + b], 1024 + P - 0.5, A.is_gt, pk2, "fls" + "b" * h)

        if not last:
            act(T.bar[:], T.fls[:], "fls flsb c18", "bar", AF.Identity, -1e15, col(18))
        if t != 1:
            tell()
        touch()
        correct()
        if t in (2, 3):
            hear()
        if t < 2:
            own_touch(c0, 2 * c0, T.fl[:, 0:c0], "fla")
            own_touch(0, c0, T.fls[:, 0:c0], "flsb")
            ranks(0, 0, na, "fla")
        elif not last:
            own_touch(c0, 48, T.fl[:, 0:na], "fla")
            own_touch(0, 8, T.fown[:], "fown")
            ranks(0, 0, na, "fla")
            own_touch(8, c0, T.fl[:, na + 8:48], "flc", 1)
        else:
            act(T.lwin[:, 0:H], T.tw[:, 0:H], "twa", "lwin", AF.Copy, -1.0)
            act(T.lwin[:, H:U], T.tw[:, H:U], "lwin twa", "lwb ~s", AF.Sign)
            hear()
        if t == 0:
            for r in range(16):
                act(T.wt[:, r, :], T.bo[:], "bo tmp " + ("xs3" if r < WT else "twa"), "wt", AF.Identity, T.tmp[:, r:r + 1])
        act(T.sw[:], T.o3[:, 0, 18::19], "o30", "sw", AF.Sign, 1.0, 0.5)
        mm(T.p0[:, 0:64], T.eye[:], T.one[:, 0:64], "eye one", "p0", start=True)
        for r in range(16):
            mm(T.p0[:, r:64:16], T.wt[:, r, :], T.sw[:], "wt sw", "p0", stop=(r == 15))
        op("g", lambda t=t: g.remote_dma_fused([
            RemoteDMATransfer(dst_ids=[dst(before)], dma_engine_mask=bits(half_b), remote_sem=T.sem["rd%d" % t],
                              src=D[:, 0:H], dst=T.rd[:, t, H:2 * H]),
            RemoteDMATransfer(dst_ids=[dst(after)], dma_engine_mask=bits(half_a), remote_sem=T.sem["rd%d" % t],
                              src=D[:, V - H:V], dst=T.rd[:, t, 0:H])], local_sem=T.sem["ld%d" % t]),
           "Da Dz", "~g", ("ld%d" % t, len(half_a) + len(half_b)), cost=300.0, late=REM + 500.0)
        op("g", None, "", "rd%d" % t, ("rd%d" % t, n_in_d))
        if t == 1:
            tell()
        if last:
            dma("y", T.yd[:, H:V - H], D[:, H:V - H], "Dm", "")
        else:
            keep = compact(0, 0, na, c0)

        to_psum(T.p2[:, 0:H], D[:, 0:H], "Da", "p2")
        to_psum(T.p2[:, H:2 * H], D[:, V - H:V], "Dz", "p2")
        if t in (2, 3):
            act(T.D[:, U // 2:U], D[:, U // 2:U], "Dm", "Dx")

        def new_z():
            tt(T.th[:, 0:64], T.p0[:, 0:64], dlt, A.mult, "p0 dlt", "th")
            tt(nzu, nzu, T.th[:, 0:64], A.subtract, "th " + nk, nk)

        def forget():
            new_z()
            act(T.gr[:], wb[:, 0:S], trb + " c9", "gr", AF.Abs, -1.0, col(9))
            tt(T.blk[:], T.o3[:, 0, 18::19], T.e3[:, 0, 18::19], A.is_gt, "o30 e3w", "blk")
            act(T.gr[:, 64 * u:64 * u + 64], nzu, nk + " gr", "gr", AF.Sign, -1.0)

        def forget_count():
            for r in range(16):
                mm(T.p5[:, 0:12], sel(r), T.gr[:, r::16], "zz gr", "p5 ~u", start=(r == 0))
            mm(T.p5[:, 4 * u:4 * u + 4], T.eye[:], T.blk[:], "eye blk", "p5", stop=True)

        def free_slots():
            ts(T.fre[:], T.p5[:, 0:12], 0.0, A.is_equal, "p5", "fre")
            slot_list()

        def take():
            tt(D[:, 0:H], T.p2[:, 0:H], T.rd[:, t, 0:H], A.add, "p2 rd%d" % t, "Da" + " ~x" * (last or t < AFTER))
            tt(D[:, V - H:V], T.p2[:, H:2 * H], T.rd[:, t, H:2 * H], A.add, "p2 rd%d" % t, "Dz")

        def next_lists(between):
            if t >= 2:
                mm(T.p1[:, 0:P], T.eye[:], T.mxb[:], "eye mxb", "p1", start=True, stop=True)
            for a, b, k in ((0, HEAD, "a"), (HEAD, P, "")) if t > 0 else ():
                bk = "p1" if t >= 2 else "p6"
                tt(T.lxv[:, a:b], T[bk][:, a:b], T.lwv[:, a:b], A.min, bk + " own_p6 lwv", "lxv%s ~x" % k)
            between()
            for a, b, k in ((0, HEAD, "a"), (HEAD, P, "")):
                scan(T.lx[:, a:b], T.lxv[:, a:b], T.lwin[:, a:b], A.max, A.min, "lxv%s lwin" % k, "lx%s ~x" % k)
            for a, b, k in ((0, HEAD, "a"), (HEAD, P, "")):
                ts(T.lw[:, a // 16:b // 16], T.lx[:, a + 15:b:16], 0.25, A.add, "lx" + k, "lw%s ~x" % k)
            cp(T.o2[:, 0:HEAD], T.b2t[:, 0:U if t < 2 else EXT].indirect(T.lw[:, 0:HEAD // 16]), "b2a b2b b2d lwa" + " b2c" * (t >= 2), "o2a ~x")
            if t < BEFORE:
                cp(T.o1[:], T.b1t[:, 0:U].indirect(T.lw[:]), "b1a b1b b1d lw lwa", "o1a o1b ~x")
                cp(T.o2[:, HEAD:P], T.b2t[:, 0:U].indirect(T.lw[:, HEAD // 16:16]), "b2a b2b b2d lw", "o2b ~x")

        if t < 2:
            keep()
            forget()
            forget_count()
            free_slots()
            next_lists(lambda: None)
            take()
        elif not last:
            keep()
            forget()
            their_touch()
            ranks(1, na, 48, "flb flc")
            forget_count()
            keep = compact(1, na, 48, 0)
            next_lists(keep if t == 2 else take)
            (take if t == 2 else keep)()
            free_slots()
            if t == 3:
                for h, bk in enumerate(("p3", "p2")):
                    for r in range(16):
                        mm(T[bk][:, r:384:16], T.wt[:, r, :], T.fls[:, 24 * h:24 * h + 24], "wt fls flsb", bk, start=True, stop=True)
                    act(T.tw[:, 384 * h:384 * h + 384], T[bk][:, 0:384], bk, "twa", AF.Copy, -1.0)
        else:
            new_z()
            planes(lambda: wb[:, 0:S], S, trb)
            for x in range(3):
                act(T.zo[:, x::3], T.nz[:, 64 * x:64 * x + 64], "nz%d" % x, "zo", AF.Copy, -0.5)
            dma("y", T.yz[:], T.zo[:], "zo", "")
            mm(T.p4[:, 0:S], T.bo[:], T.pct[:, 0:S], "bo pct", "p4", start=True)
            mm(T.p1[:, 0:2 * S], T.bo[:], T.pct[:, S:3 * S], "bo pct", "p1", start=True)
            for m, d, o in (("h1", "h16", 1), ("hq", "q16", 0), ("hm", "q16", 2), ("hq", "l16", 2)):
                for x in range(3):
                    out = T.p4[:, x:S:3] if o == 0 else T.p1[:, S * (o - 1) + x:S * o:3]
                    mm(out, HX[m], T[d][:, 64 * x:64 * x + 64], m + " " + d, "p4" if o == 0 else "p1",
                       stop=(x == 2 and m == "hq"))
            ts(T.gr[:], wb[:, 0:S], col(9), A.not_equal, trb + " c9", "gr")
            ts(T.g0[:], nzu, 0.0, A.not_equal, nk, "g0")
            tt(T.gr[:, 64 * u:64 * u + 64], T.gr[:, 64 * u:64 * u + 64], T.p0[:, 0:64], A.is_gt, "gr p0", "gr")
            for x in range(3):
                mm(T.p5[:, x:S:3], T.neye[:], T.one[:, 0:64], "neye one", "p5", start=True)
                if x == u:
                    mm(T.p5[:, x:S:3], T.bq[:], T.g0[:], "bq g0", "p5")
                mm(T.p5[:, x:S:3], T.bq[:], T.gr[:, 64 * x:64 * x + 64], "bq gr", "p5", stop=True)
            act(T.t2[:, S:3 * S], T.p1[:, 0:2 * S], "p1", "t2b")
            ts(T.t1[:, 0:S], T.p4[:, 0:S], 1.0 / 15, A.mult, "p4", "t1", MAG, A.add)
            ts(T.t2[:, 0:S], T.t1[:, 0:S], MAG, A.subtract, "t1", "t2a")
            for q in (1, 2, 0):
                tt(T.t1[:, S * q:S * q + S], T.p5[:, 0:S], T.t2[:, S * q:S * q + S], A.min, "p5 t2a t2b", "t1%d ~x" % q)
            dma("y", T.yt[:], T.t1[0:128:16, :], "t10 t11 t12", "")
            take()
            dma("y", T.yd[:, 0:H], D[:, 0:H], "Da", "", V // 4)
            dma("s", T.yd[:, V - H:V], D[:, V - H:V], "Dz", "", V // 4)
            tt(T.lwin[:, 0:H], T.twn[:, V - H:V], T.lwin[:, 0:H], A.is_gt, "lwin twn", "lwin")
            dma("s", T.yf[:], T.lwin[0:128:16, 0:U], "lwin lwb", "")
    emit(g, T, arrange(ops))
